import numpy as np, ml_dtypes
CORES = [16,18,20,22]
N = 4
BF = ml_dtypes.bfloat16
V, G, ST, RO = 1792, 1296, 7, 3
D, B, Q = 64, 256, 64
C, W = 256, 3088
def pack(xx, yy, nl, al):
    h = lambda a: np.ascontiguousarray(a).reshape(N, 128, V)
    return {"xf": h(xx).astype(np.float32).astype(BF), "lab": h(yy).astype(np.float32).astype(BF), "nb": h(nl).astype(np.int32), "asc": h(al).astype(np.int32)}
def signs(rng, *shape):
    return rng.integers(0, 2, shape) * 2 - 1
def both(c):
    return np.concatenate([c, np.roll(c, -1, axis=0)[..., :G]], axis=-1)
def alike(rng, c, want):
    o = np.argsort(c, axis=2, kind="stable"); n = np.sum(c < 0, axis=2)[:, :, None]; m = c.shape[2]
    j = np.where(want < 0, rng.random(want.shape) * n, n + rng.random(want.shape) * (m - n)).astype(np.int64)
    return np.take_along_axis(o, np.minimum(j, m - 1), 2)
def parts(rng):
    pat = signs(rng, 1, 8, 16, 1); c = signs(rng, N, 8, V)
    yy = c[:, :, None, :] * pat; yy = np.where(rng.random(yy.shape) < 0.1, -yy, yy)
    xx = rng.integers(0, 16, (N, 8, 16, V)); nl = rng.integers(0, W, (N, 8, 16, V))
    al = alike(rng, c, np.repeat(c[:, :, None, :], 16, axis=2).reshape(N, 8, 16 * V)).reshape(N, 8, 16, V)
    al = np.where(rng.random(al.shape) < 0.1, rng.integers(0, V, al.shape), al)
    r, g, i, v = np.indices((N, 8, 4, V))
    nl[r, g, rng.integers(1, 16, r.shape), al[:, :, :4]] = v
    share = rng.choice(np.array([0.1, 0.4, 0.7, 0.95]), (N, 8, 1))
    nl[:, :, 0] = alike(rng, both(c), np.where(rng.random((N, 8, V)) < share, -c, c))
    return xx, yy, nl, al
def setup_inputs(rng):
    return pack(*parts(rng))
def setup_inputs_spread(rng):
    s = (N, 8, 16, V)
    xx = np.minimum((16 * np.power(rng.random(s), np.exp2(rng.integers(-3, 4, (N, 8, 1, V))))).astype(np.int64), 15)
    yy = np.where(rng.random(s) < rng.random((N, 8, 1, V)), 1, -1)
    ex = rng.choice(np.array([0.4, 1.0, 2.5]), (N, 8, 1, 1)); ea = rng.choice(np.array([0.4, 1.0, 2.5]), (N, 8, 1, 1))
    nl = np.minimum((W * np.power(rng.random(s), ex)).astype(np.int64), W - 1)
    al = np.minimum((V * np.power(rng.random(s), ea)).astype(np.int64), V - 1)
    return pack(xx, yy, nl, al)
def setup_inputs_ends(rng):
    v = np.arange(V); odd = (np.arange(8) % 2)[None, :, None]; z = ST * (C - 1)
    pat = signs(rng, 1, 8, 16, 1); c = signs(rng, N, 8, V)
    kind = rng.integers(0, 10, (N, 8, V)); kind[..., 1] = 0; kind[..., V - 2] = 0; kind[..., 2] = 2; kind[..., V - 3] = 2; kind[..., V - 1] = 4
    nz = np.where(kind < 2, 16, np.where(kind < 4, 0, rng.integers(7, 10, kind.shape))); nz[..., V - 1] = 8
    o = np.argsort(rng.random((N, 8, 16, V)), axis=2)
    nl = np.where(kind[:, :, None, :] >= 7, rng.integers(0, W, o.shape), np.where(o < nz[:, :, None, :], 0, W - 1))
    nl[..., 0] = np.where((np.arange(16) == 0) | (np.arange(16) > 9), W - 1, 0)
    nl[..., G - 1] = rng.integers(1, G - 1, (N, 8, 16))
    ka = rng.integers(0, 10, (N, 8, V))[:, :, None, :]
    al = np.where(ka < 2, 0, np.where(ka < 4, V - 1, np.where(ka < 7, (V - 1) * rng.integers(0, 2, o.shape), rng.integers(0, V, o.shape))))
    bad = (v % ST < RO) & (rng.random((N, 8, V)) < np.where(odd == 1, 0.9, 0.2))
    bad[..., ST * (C - 2)] = True; bad[..., z:] = False; bad[..., 1] = False; bad[..., 2] = False; bad[..., G - 1] = False; bad[..., 0] = odd[..., 0] == 1
    c = np.where(bad, 1, c); c[..., 0] = 1; c[..., G - 1] = -1; c[..., z] = -c[..., V - 1]
    al = np.where(bad[:, :, None, :], 0, al); al[..., G - 1] = V - 1; al[..., z:] = V - 1; al[:, 0::2, :, 0] = V - 1
    nl[:, :, 0] = np.where(bad, W - 1, nl[:, :, 0]); nl[:, :, 0, z] = np.where(c[..., V - 1] > 0, 0, W - 1)
    kx = rng.integers(0, 5, (N, 8, V))[:, :, None, :]
    xx = np.where(kx == 0, 0, np.where(kx == 1, 15, 15 * rng.integers(0, 2, o.shape)))
    return pack(xx, c[:, :, None, :] * pat, nl, al)
def setup_inputs_corners(rng):
    xx, yy, nl, al = parts(rng); pat = signs(rng, 8, 16, 1)
    cand = np.arange(C) * ST; rest = np.flatnonzero(np.arange(V) % ST != 0); gh = V + np.flatnonzero(np.arange(G) % ST != 0)
    for r in range(N):
        turn = rng.permutation(8); few = int(rng.integers(1, 9))
        for g in range(8):
            nd, nf, nq = ((D, B, Q), (D + 1, B + 1, Q + 1), (C, B + 1, B), (D - 1, B - 1, Q - 1), (few, 16 * few, few), (0, 0, 0), (D, B, 0), (D, 1, 1))[int(turn[g])]
            o = rng.permutation(rest); hp, hm, hq = int(o[0]), int(o[1]), int(o[2])
            c = signs(rng, V); c[cand] = 1; c[hp] = 1; c[hq] = 1; c[hm] = -1; yy[r, g] = c * pat[g]
            nl[r, g, :, hp] = rng.permutation(np.array([hq] * 9 + [hm] * 7))
            will = np.sort(rng.permutation(C)[:nd]) * ST; die = will[:D]; late = will[D:]
            nl[r, g, 0, cand] = hm; nl[r, g, 0, will] = hq; al[r, g][:, cand] = hp
            al[r, g][:, late] = o[rng.integers(3 + nf, len(o), (16, len(late)))]
            if nd == 0: continue
            bs = np.sort(o[3:3 + nf]); m = 16 * len(die)
            al[r, g][:, die] = rng.permutation(np.concatenate([bs, bs[rng.integers(0, nf, m - nf)]])).reshape(16, -1)
            ask = np.zeros(nf, bool); ask[rng.permutation(min(nf, B))[:nq]] = True
            fresh = np.where(ask, gh[rng.integers(0, len(gh), (16, nf))], rest[rng.integers(0, len(rest), (16, nf))])
            dead = die[rng.integers(0, len(die), (16, nf))]
            li = np.where(np.arange(16)[:, None] == rng.integers(0, 16, nf), dead, fresh)
            t = rng.random(nf); li = np.where(~ask & (t < 0.2), fresh, np.where(~ask & (t < 0.3), dead, li))
            nl[r, g][:, bs] = li
    return pack(xx, yy, nl, al)
def setup_inputs_alike(rng):
    xx, yy, nl, al = parts(rng); me = np.arange(V)
    base = rng.integers(0, 16, (N, 8, 16, 4)); base[:, 0] = base[:, 0, :, :1]
    xx = np.take_along_axis(base, rng.integers(0, 4, (N, 8, 1, V)), 3)
    hub = rng.integers(0, W, (N, 8, 24)); hub[..., :4] = np.array([0, V - 1, V, W - 1]); hub[..., 4:8] = ST * np.arange(1, 5); hub[..., 8:12] = V + ST * np.arange(4)
    nl[:, 1::2] = np.take_along_axis(hub[:, 1::2], rng.integers(0, 24, (N, 4, 16 * V)), 2).reshape(N, 4, 16, V)
    nl[:, 2] = np.where(rng.random((N, 16, V)) < 0.3, me, nl[:, 2])
    nl[:, 4] = rng.integers(V, W, (N, 16, V)); nl[:, 6] = rng.integers(0, V, (N, 16, V))
    al[:, 3] = rng.choice(np.array([0, V - 1, V // 2, 3]), (N, 16, V))
    al[:, 5] = np.where(rng.random((N, 16, V)) < 0.5, me, al[:, 5]); al[:, 7] = al[:, 7, :1]
    return pack(xx, yy, nl, al)
def setup_inputs_shared(rng):
    xx, yy, nl, al = parts(rng); pat = signs(rng, 8, 16, 1); v = np.arange(V); K = B // 4; h = K // 2
    cand = np.flatnonzero(v % ST < RO); gh = V + np.flatnonzero(np.arange(G) % ST >= RO)
    q = np.arange(B) // 2 % K; far = np.arange(K) % h % 4 == 3
    for r in range(N):
        for g in range(8):
            m = np.sort(rng.permutation(C)[:2 * K]) * ST + RO; bs = np.stack([m, m + 1], axis=1).reshape(-1)
            o = rng.permutation(np.setdiff1d(v[v % ST >= RO], bs)); hp, hq, hm = int(o[0]), int(o[1]), int(o[2])
            u = o[3:3 + K]; rest = o[3 + K:]; old = rest[:64]; more = np.concatenate([rest, gh])
            die = np.sort(rng.permutation(C)[:D]) * ST
            ws = np.concatenate([rng.permutation(C)[:h] * ST + 1, rng.permutation(C)[:h] * ST + 2])
            c = signs(rng, V); c[cand] = 1; c[hp] = 1; c[hq] = 1; c[hm] = -1; yy[r, g] = c * pat[g]
            nl[r, g, :, hp] = rng.permutation(np.array([hq] * 9 + [hm] * 7))
            nl[r, g, 0, cand] = hm; nl[r, g, 0, die] = hq; nl[r, g, 0, ws] = hq
            al[r, g][:, cand] = hp; al[r, g][:, ws] = old[rng.integers(0, 64, (16, K))]
            al[r, g][:, die] = rng.permutation(np.concatenate([bs, bs[rng.integers(0, B, 16 * D - B)]])).reshape(16, -1)
            base = rng.integers(0, 13, (16, h)); base = np.where(far[:h], 15 * (base & 1), base); base = np.concatenate([base, base], axis=1)
            x = xx[r, g]
            x[:, bs] = base[:, q] + np.where(far[q], 0, rng.integers(0, 2, (16, B)))
            x[:, u] = np.where(far, base, base + 1)
            x[:, ws] = np.where(far, 15 - base, base + 2 * (np.arange(K) >= h))
            lu = np.where(far, u, more[rng.integers(0, len(more), (16, K))]); a = np.where(far, 15, rng.integers(0, 16, K))
            lu[a, np.arange(K)] = ws; lu[(a[:h] + 5) & 15, np.arange(h)] = np.where(far[:h], u[:h], ws[h:])
            nl[r, g][:, u] = lu
            li = more[rng.integers(0, len(more), (16, B))]; a = rng.integers(0, 16, B)
            li[a, np.arange(B)] = die[rng.integers(0, D, B)]; li[(a + rng.integers(1, 16, B)) & 15, np.arange(B)] = u[q]
            nl[r, g][:, bs] = li
    return pack(xx, yy, nl, al)
def check_inputs(d):
    bad = []
    for k, lo, hi in (("xf", 0, 15), ("lab", -1, 1), ("nb", 0, W - 1), ("asc", 0, V - 1)):
        a = np.asarray(d[k]).astype(np.float64)
        if not np.all((a >= lo) & (a <= hi)): bad.append("range of " + k)
        elif k == "xf" and not np.all(a == np.floor(a)): bad.append("xf holds whole numbers")
        elif k == "lab" and not np.all(np.abs(a) == 1): bad.append("lab holds -1 and 1")
    return bad
def take(tab, ix):
    return np.take_along_axis(tab, ix[:, :, None, :], 3)
def alive(lv, names):
    return np.take_along_axis(lv, names.reshape(N, 8, -1), 2).reshape(names.shape)
def apart(X, xb, names):
    return np.stack([np.sum(np.abs(take(X, names[:, :, i]) - xb), axis=2) for i in range(16)], axis=2)
def reference(xf, lab, nb, asc):
    X = both(xf.astype(np.float32).astype(np.int32).reshape(N, 8, 16, V)); Y = both(lab.astype(np.float32).astype(np.int32).reshape(N, 8, 16, V))
    nl = nb.astype(np.int64).reshape(N, 8, 16, V); al = asc.astype(np.int64).reshape(N, 8, 16, V)
    S = np.zeros((N, 8, 16, V), np.int32)
    for i in range(16): S = S + take(Y, nl[:, :, i])
    died = np.zeros((N, 8, V), np.int64); flag = np.zeros((N, 8, V), bool); last = np.zeros(N, np.int64); BIG = 1 << 20
    for t in range(RO):
        v = np.arange(C) * ST + t; av = al[:, :, :, v]
        e = take(Y, nl[:, :, 0, v]) - Y[:, :, :, v]; loss = np.zeros((N, 8, C), np.int64)
        for i in range(16):
            ya = take(Y, av[:, :, i]); sa = take(S, av[:, :, i])
            loss = loss + np.sum(ya * sa > 0, axis=2) - np.sum(ya * (sa + e) > 0, axis=2)
        will = loss <= (last & 7)[:, None, None]
        die = will & (np.add.accumulate(will.astype(np.int64), axis=2) <= D)
        died[:, :, v] = np.where(die, t + 1, died[:, :, v]); last = np.sum(die.astype(np.int64), axis=(1, 2))
        live = died == 0; lv = both(live)
        r, g, i, j = np.nonzero(np.repeat(die[:, :, None, :], 16, axis=2)); flag[r, g, av[r, g, i, j]] = True; flag = flag & live
        tr = flag & (np.add.accumulate(flag.astype(np.int64), axis=2) <= B); flag = flag & ~tr
        b = np.argsort(~tr, axis=2, kind="stable")[..., :B]; ok = np.take_along_axis(tr, b, 2)
        lb = take(nl, b); on = alive(lv, lb); xb = take(X, b)
        k = np.argmax(~on, axis=2); need = ok & np.any(~on, axis=2) & np.any(on, axis=2)
        iu = np.argmin(np.where(on, apart(X, xb, lb), BIG), axis=2); u = np.take_along_axis(lb, iu[:, :, None, :], 2)[:, :, 0]
        asks = need & (u >= V); served = asks & (np.add.accumulate(asks.astype(np.int64), axis=2) <= Q)
        far = take(np.roll(nl, -1, axis=0), np.maximum(u - V, 0)); far = np.where(far < G, V + far, -1)
        lu = np.where((u < V)[:, :, None, :], take(nl, np.minimum(u, V - 1)), far); nm = np.maximum(lu, 0)
        fit = (lu >= 0) & alive(lv, nm) & (lu != b[:, :, None, :]) & ((need & (u < V)) | served)[:, :, None, :]
        for i in range(16): fit = fit & (lu != lb[:, :, i:i + 1])
        iw = np.argmin(np.where(fit, apart(X, xb, nm), BIG), axis=2); w = np.take_along_axis(nm, iw[:, :, None, :], 2)[:, :, 0]
        r, g, s = np.nonzero(np.any(fit, axis=2)); bb = b[r, g, s]; ww = w[r, g, s]; kk = k[r, g, s]; old = nl[r, g, kk, bb]
        nl[r, g, kk, bb] = ww; S[r, g, :, bb] = S[r, g, :, bb] + Y[r, g, :, ww] - Y[r, g, :, old]
        m = ww < V; r, g, bb, ww = r[m], g[m], bb[m], ww[m]
        first = np.unique((r * 8 + g) * V + ww, return_index=True)[1]
        r, g, bb, ww = r[first], g[first], bb[first], ww[first]; al[r, g, (bb + t) & 15, ww] = bb
    return {"yn": nl.reshape(N, 128, V).astype(np.float32), "yd": died.astype(np.float32)}

@@ -1,0 +1,747 @@
+from concourse.mybir import AluOpType as ALU, AxisListType, ActivationFunctionType as AF
+
+V, G, W = 1792, 1296, 3088
+CEN = 1544.0
+NW = 2048 + 3 * G
+YD = 3104
+THR = 241.0 * 65536
+M32, M64 = 1.5 * 2 ** 28, 1.5 * 2 ** 29
+DML = 2176
+SC, SV, SVL = 272, 118, 64
+LV = (128, 80, 80)
+CV = 10
+RV = (8, 8, 8)
+
+F32, BF, F16, I32, U16 = "float32", "bfloat16", "float16", "int32", "uint16"
+SB = {
+    "NI": (V, I32), "NU": (V, U16), "N": (NW, F32), "N2": (G, F32), "A": (2048, I32),
+    "Y": (2 * YD, BF), "X": (3104, BF), "R": (2048, BF), "Z": (2048, BF), "DD": (V, BF),
+    "GV0": (2048, BF), "GV1": (2048, BF), "GA0": (2560, BF), "GA1": (2560, BF),
+    "MX0": (2048, BF), "MX1": (2048, BF), "EE": (17 * 256, BF), "RMP": (8192, BF),
+    "T1": (SC, BF), "T2": (SC, BF), "XS": (192 * 3, BF), "XL": (192 * 3, BF), "TX": (256, BF),
+    "IB": (128, BF), "NIB": (128, BF), "IBIG": (128, BF), "I64": (128, BF), "I16": (128, BF), "I31": (128, BF),
+    "I2": (256, BF), "IF": (128, F32), "JF": (128, F32), "BO": (128, BF), "NBO": (128, BF), "NB4": (128, BF),
+    "NB8": (128, BF), "NBU": (256, BF), "B8K": (16, BF),
+    "TRI16": (128, BF), "TRI": (128, BF), "ONES": (128, BF), "B8": (80, BF), "B8F": (16, F32), "SEL": (2048, BF),
+    "WM": (256, F32), "IOI": (256, F32), "IOS": (256, F32), "RAMP": (128, BF), "IO4": (64, BF), "TN": (128, F32),
+    "TM": (128, F32), "KR": (256, BF), "C15": (192, BF), "RB": (256, F32), "C256": (128, BF), "RZ": (128 * CV, BF),
+    "DM": (DML, BF), "DE": (DML, BF), "DS": (DML, BF), "MK": (16, BF), "SCB": (16, BF),
+    "sm": (16 * 48, F32), "si": (16 * 12, I32), "su": (16 * 12, U16), "sb": (16 * 8, BF),
+    "AU": (256, U16), "AH": (256, F16), "AT": (256, F16), "NH": (256, F16), "EB": (256, BF), "MP": (256, BF),
+    "MM": (256, BF), "RR": (256, BF), "X1": (256, F16), "X2": (256, BF), "PP": (17 * 128, BF), "DB": (256, BF),
+    "S1": (64, BF), "S2": (64, BF), "CS": (128, F32), "CS2": (128, F32), "DW": (128, F32), "F": (128, BF),
+    "FK": (128, BF), "CC": (144, BF), "CUM": (128, F32), "CMP": (256, BF), "CRP": (256, BF),
+    "LBU": (256, U16), "LBH": (256, F16), "XB": (256, BF), "LUU": (256, U16), "LUH": (256, F16),
+    "SC1": (512, F32), "BC": (256, F32), "BC2": (256, F32), "BT": (256, F32),
+    "OH": (256, F32), "NL": (256, F32), "RG": (256, BF), "YB": (256, BF), "YW": (256, BF), "YO": (256, BF),
+    "ZN": (256, BF), "RN": (256, BF), "WR": (256, F16), "NM": (256, BF), "BM": (256, F32), "AN": (256, F32),
+}
+SCRATCH = {k: ("sbuf", [128, n], d) for k, (n, d) in SB.items()}
+SCRATCH["LT"] = ("sbuf", [128, 16, 32], F32)
+for _k in range(8):
+    SCRATCH["p%d" % _k] = ("psum", [128, 512], F32)
+NDMA, NMSG = 16, 8
+SEMAPHORES = ["cv", "ca", "cp", "cg"] + ["d%d" % k for k in range(NDMA)] + ["r%d" % k for k in range(NMSG)] + \
+             ["l%d" % k for k in range(NMSG)]
+
+
+def rank_program(g, core, T, topo):
+    rank = T.rank_of(core)
+    if rank is None:
+        return
+    n = len(T.cores)
+    dst = T.cores[(rank - 1) % n]
+    rid, pid = topo.addr(dst)[0], topo.addr(dst)[1]
+    engs = topo.engines(core, dst)[::2]
+    mask = sum(1 << e for e in engs)
+    neng = len(engs)
+    Q = {"v": g.vector, "a": g.scalar, "p": g.tensor, "g": g, "s": g.sync}
+    ops, hist, cnt = [], {}, {"d": 0}
+
+    def ap(name, a=0, b=None, s=1, p0=0, p1=128):
+        b = T[name].shape[-1] if b is None else b
+        return (T[name][p0:p1, a:b:s] if s > 1 else T[name][p0:p1, a:b], name, a, b)
+
+    def ind(win, off):
+        return (win[0].indirect(off[0]), win[1], win[2], win[3], off)
+
+    def lt(a):
+        return (T["LT"][:, :, a:a + 16], "LT", 0, 512)
+
+    slots = {"sm": {}, "si": {}, "su": {}, "sb": {}}
+
+    def sl(buf, key, a=0, b=16):
+        k = slots[buf].setdefault(key, len(slots[buf]))
+        return ap(buf, 16 * k + a, 16 * k + b)
+
+    def sm(key, a=0, b=16):
+        return sl("sm", key, a, b)
+
+    def add(q, fn, reads, writes, sem=None):
+        i = len(ops)
+        deps = set()
+        acc = []
+        for w, xs in ((False, reads), (True, writes)):
+            for x in xs:
+                if isinstance(x, tuple):
+                    acc.append((x[1], x[2], x[3], w))
+                    if len(x) > 4:
+                        acc.append((x[4][1], x[4][2], x[4][3], False))
+        for name, a, b, w in acc:
+            ps = name[0] == "p" and name[1:].isdigit()
+            for (a2, b2, w2, j) in hist.get(name, []):
+                o = ops[j]
+                same = o["q"] == q and o["sem"] is None and sem is None
+                if same and q == "p":
+                    continue
+                if (ps and not same) or ((w or w2) and a < b2 and a2 < b):
+                    deps.add(j)
+        for name, a, b, w in acc:
+            hist.setdefault(name, []).append((a, b, w, i))
+        ops.append({"q": q, "fn": fn, "deps": deps, "sem": sem, "mark": False})
+
+    def x0(x):
+        return x[0] if isinstance(x, tuple) else x
+
+    def tt(o, a, b, op):
+        add("v", lambda: g.vector.tensor_tensor(o[0], a[0], b[0], op), [a, b], [o])
+
+    def ts(o, a, s1, op0, s2=None, op1=None):
+        if op1 is None:
+            add("v", lambda: g.vector.tensor_scalar(o[0], a[0], x0(s1), None, op0), [a, s1], [o])
+        else:
+            add("v", lambda: g.vector.tensor_scalar(o[0], a[0], x0(s1), x0(s2), op0, op1), [a, s1, s2], [o])
+
+    def cp(o, a):
+        add("v", lambda: g.vector.tensor_copy(o[0], a[0]), [a], [o])
+
+    def scan(o, d0, d1, op0, op1):
+        add("v", lambda: g.vector.tensor_tensor_scan(o[0], d0[0], d1[0], 0.0, op0, op1), [d0, d1], [o])
+
+    def ms(o, c):
+        add("v", lambda: g.vector.memset(o[0], c), [], [o])
+
+    def act(o, a, f=AF.Identity, bias=0.0, scale=1.0, acc=None):
+        add("a", lambda: g.scalar.activation(o[0], a[0], f, bias=x0(bias), scale=scale, accum_out=x0(acc)),
+            [a, bias], [o, acc])
+
+    def mm(o, l, r, start, stop):
+        add("p", lambda: g.tensor.matmul(o[0], l[0], r[0], start, stop), [l, r], [o])
+
+    def iota(o, pat, base, cm=0):
+        if SB[o[1]][1] == I32:
+            add("g", lambda: g.iota(o[0], pat, base, cm), [], [o])
+        else:
+            add("g", lambda: g.iota(o[0], pat, base, cm, allow_small_or_imprecise_dtypes=True), [], [o])
+
+    def sel(o, a, pat, op, fill, base, cm):
+        add("g", lambda: g.affine_select(o[0], a[0], pat, op, float(fill), base, cm), [a], [o])
+
+    def dma(q, o, a, reads, writes):
+        s = "d%d" % cnt["d"]
+        cnt["d"] += 1
+        add(q, lambda: Q[q].dma_start(o, a), reads, writes, sem=(s, 16, True))
+
+    def send(k, o, a):
+        add("g", lambda: g.remote_dma(o[0], a[0], T.sem["r%d" % k], T.sem["l%d" % k], pid, rid, mask), [a], [],
+            sem=("l%d" % k, neng, False))
+
+    def landed(k, o):
+        add("x", None, [], [o], sem=("r%d" % k, neng, False))
+
+    def P(k, a=0, b=512, s=1, p0=0, p1=128):
+        return ap("p%d" % k, a, b, s, p0, p1)
+
+    eq, ge, gt, le, ltn, ne = ALU.is_equal, ALU.is_ge, ALU.is_gt, ALU.is_le, ALU.is_lt, ALU.not_equal
+    ad, sub, mul, mx, mn = ALU.add, ALU.subtract, ALU.mult, ALU.max, ALU.min
+    zero = ap("C15", 64, 192)
+
+    def diag(name, val, base=0, step=-1):
+        src = zero
+        if SB[name][1] != BF:
+            src = ap(name)
+            iota(src, [[0, 128]], 0)
+        sel(ap(name), src, [[step, 128]], ne, val, base, 1)
+
+    def block(o, val, pat):
+        c = 1
+        for x in pat:
+            c *= x[1]
+        iota(o, [[0, c]], val)
+        sel(o, o, [[-x[0], x[1]] for x in pat], ge, 0, 0, 1)
+        sel(o, o, pat, ge, 0, 15, -1)
+
+    landed(0, ap("Y", V, W))
+    landed(1, ap("X", V, W))
+    for t in range(3):
+        landed(2 + t, ap("N", 2048 + G * t, 2048 + G * (t + 1)))
+        landed(5 + t, ap("XL", 192 * t, 192 * t + 192))
+    pieces = ((0, 2 * SC), (2 * SC, 4 * SC), (4 * SC, V))
+    dma("s", T["Y"][:, 0:G], T.lab[:, 0:G], [], [ap("Y", 0, G)])
+    dma("s", T["NI"][:, 0:2 * SC], T.nb[:, 0:2 * SC], [], [ap("NI", 0, 2 * SC)])
+    dma("s", T["Y"][:, G:V], T.lab[:, G:V], [], [ap("Y", G, V)])
+    iota(zero, [[0, 128]], 0)
+    diag("IB", 1.0)
+    diag("NIB", -1.0)
+    iota(sl("si", "p", 0, 1), [[0, 1]], 0, 1)
+    iota(sm("io16"), [[1, 16]], 0)
+    send(0, ap("Y", V, W), ap("Y", 0, G))
+    first = len(ops) - 1
+    for a, b in pieces[1:]:
+        dma("s", T["NI"][:, a:b], T.nb[:, a:b], [], [ap("NI", a, b)])
+        ops[-1]["deps"].add(first)
+    dma("s", T["A"][:, 0:V], T.asc[:, :], [], [ap("A", 0, V)])
+    dma("s", T["X"][:, 0:V], T.xf[:, :], [], [ap("X", 0, V)])
+    ms(ap("Y", W, YD), 0.0)
+    dma("s", T["Y"][:, YD:2 * YD], T["Y"][:, 0:YD], [ap("Y", 0, YD)], [ap("Y", YD, 2 * YD)])
+    ms(ap("DM"), 1.0)
+    ms(ap("X", W, W + 1), 31.0)
+    ms(ap("X", W + 1, 3104), 63.0)
+    ms(ap("N", V, 2048), float(W + 1))
+    ms(ap("R", V, 2048), 0.0)
+    ms(ap("XS"), 0.0)
+    act(ap("SEL"), ap("DM", 0, 2048), scale=0.0)
+    act(ap("PP"), ap("DM"), scale=0.0)
+    act(ap("DD"), ap("DM", 0, V), scale=0.0)
+    act(ap("RZ"), ap("DM", 0, 128 * CV), AF.Copy)
+    ts(sl("si", "q", 0, 1), sl("si", "p", 0, 1), 15, ALU.bitwise_and)
+    qf = sm("col", 0, 1)
+    cp(qf, sl("si", "q", 0, 1))
+    m0 = sm("col", 1, 2)
+    ts(m0, qf, 0.0, eq)
+    ts(sm("col", 2, 3), m0, 16.0, mul, qf, ad)
+    ts(sm("col", 2, 3), sm("col", 2, 3), -1.0, ad)
+    qt = [qf, sm("col", 2, 3)]
+    ts(sm("col", 3, 4), qf, 3.0, ad, qf, mul)
+    ts(sl("su", "ends", 0, 1), sm("col", 3, 4), 8.0, mul, 15.0, ad)
+    ts(ap("SCB"), sm("io16"), 16.0, mul, qf, ad)
+    ts(sm("dum"), ap("SCB"), float(V), ad)
+    ts(sm("sh"), ap("SCB"), 0.5, ad)
+    bc = sl("su", "bc")
+    cp(bc, sm("io16"))
+    ts(sm("rev"), sm("io16"), -1.0, mul, 15.0, ad)
+    ts(ap("MK"), sm("rev"), qf, ltn)
+    e8 = sm("col", 4, 5)
+    ms(e8, 0.0)
+    ms(ap("CC", 0, 1), 0.0)
+    ms(ap("DW", 112, 128), 0.0)
+    cp(ap("NU", *pieces[0]), ap("NI", *pieces[0]))
+    cp(ap("N", *pieces[0]), ap("NI", *pieces[0]))
+
+    def consts_a():
+        block(ap("B8", 0, 8), 1, [[16, 8]])
+        for q in range(16):
+            sel(ap("SEL", 128 * q + q, 128 * q + 128, 16), ap("B8", 0, 8), [[0, 8]], ge, 0, 0, 0)
+        diag("I64", 1.0 / 64)
+        diag("I31", 15.5)
+        iota(ap("ONES"), [[0, 128]], 1)
+        sel(ap("TRI"), ap("ONES"), [[1, 128]], ge, 0, 0, -1)
+        iota(ap("IO4"), [[4, 64]], 4)
+        iota(ap("C15", 0, 64), [[0, 64]], -15)
+        iota(ap("RAMP", 0, 16), [[2, 16]], -15)
+        iota(ap("RAMP", 16, 128), [[32, 112]], 32)
+        iota(ap("IOI"), [[0, 16], [1, 16]], 0)
+
+    def consts_b():
+        iota(ap("F", 0, 112), [[0, 112]], 0)
+        iota(ap("F", 112, 128), [[0, 16]], 1)
+        diag("TN", 2.0 / 32)
+        sel(ap("TN"), ap("TN"), [[-1, 128]], ne, -1.0 / 32, 1, 1)
+        sel(ap("TN"), ap("TN"), [[-1, 128]], ne, -1.0 / 32, -1, 1)
+        sel(ap("TN", 111, 112), ap("TN", 111, 112), [[0, 1]], ne, 1.0 / 32, -111, 1)
+        diag("TM", -2.0)
+        sel(ap("TM"), ap("TM"), [[-1, 128]], ne, 1.0, 1, 1)
+        sel(ap("TM"), ap("TM"), [[-1, 128]], ne, 1.0, -1, 1)
+        for col, off, val in ((0, 0, -1.0), (0, 1, 0.0), (15, 0, -13.0), (15, 1, 15.0), (15, -1, 0.0)):
+            sel(ap("TM", col, 128, 16), ap("TM", col, 128, 16), [[-16, 8]], ne, val, off - col, 1)
+        block(ap("BO"), 1, [[16, 8], [0, 16]])
+        sel(ap("TRI16"), ap("BO"), [[1, 128]], ge, 0, 0, -1)
+        iota(ap("C256"), [[0, 128]], 256)
+        iota(ap("RZ", 0, 128 * CV, 128), [[0, CV]], 0)
+        iota(ap("IOS"), [[1, 256]], 0)
+        diag("I16", 16.0)
+        for k, val in enumerate((65536, 131072, -65536, -512)):
+            block(ap("B8", 16 * k + 16, 16 * k + 24), val, [[16, 8]])
+        sel(ap("B8K", 0, 16, 2), ap("B8", 48, 56), [[0, 8]], ge, 0, 0, 0)
+        sel(ap("B8K", 1, 16, 2), ap("B8", 64, 72), [[0, 8]], ge, 0, 0, 0)
+        block(ap("NBU"), -65536, [[16, 8], [0, 32]])
+        sel(ap("NBU"), ap("NBU"), [[0, 8], [-1, 2], [0, 16]], ge, 0, 0, 0)
+        iota(ap("KR"), [[0, 16], [4096, 16]], 0)
+        sel(ap("KR"), ap("KR"), [[0, 256]], ne, CEN, -1, 1)
+        sel(ap("KR"), ap("KR"), [[0, 256]], ne, 0, -2, 1)
+        sel(ap("KR"), ap("KR"), [[0, 8], [1, 2], [0, 16]], ne, 496 * 512, -5, 2)
+        iota(ap("I2"), [[0, 256]], 0)
+        sel(ap("I2"), ap("I2"), [[-16, 8], [0, 2], [-1, 16]], ne, 1, 0, 1)
+        iota(ap("RB"), [[0, 256]], 0)
+        sel(ap("RB", 0, 256, 16), ap("RB", 0, 256, 16), [[0, 16]], ne, 2.0 ** 30, 0, 0)
+        block(ap("B8F", 0, 8), 1, [[16, 8]])
+        block(ap("NBO"), -65536, [[16, 8], [0, 16]])
+        sel(ap("NB8"), ap("NBO"), [[0, 8], [-1, 16]], ge, 0, 7, 0)
+        diag("IBIG", 2.0 ** 25)
+        diag("IF", 1.0)
+        diag("JF", 1.0, -127, 1)
+        for c in range(16):
+            o = 8 * c * (c + 1)
+            sel(ap("DM", o, o + 16), ap("MK"), [[0, 16]], ge, 0, 0, 0)
+
+    b8, b8a, b8b, b8n, b8k = [ap("B8", 16 * k, 16 * k + 8) for k in range(5)]
+    consts_a()
+    consts_b()
+    send(1, ap("X", V, W), ap("X", 0, G))
+
+    def zfrom(src, w, ycols, zout, bank):
+        ts(ap("T1", 0, w), src, 1.0, eq, 64.0, mul)
+        ts(ap("T2", 0, w), src, -1.0, eq)
+        mm(P(bank, 0, w), ap("IB"), ap("T1", 0, w), True, False)
+        mm(P(bank, 0, w), ap("NIB"), ap("T2", 0, w), False, True)
+        return lambda: tt(zout, P(bank, 0, w), ycols, mul)
+
+    yw = ap("Y", 0, W)
+
+    def cand(name, t):
+        return ap(name, t, t + 7 * 255 + 1, 7)
+
+    def prep_n1(t):
+        ts(ap("NH"), cand("N", t), -CEN, ad, m0, mul)
+        for q in range(16):
+            mm(P(4, 0, 16), ap("SEL", 128 * q, 128 * q + 128), ap("NH", q, 256, 16), q == 0, q == 15)
+
+    def prep_n2(t):
+        ts(sl("su", "n"), P(4, 0, 16), CEN, ad)
+        tt(ap("EB"), ind(yw, sl("su", "n")), ap("Y", YD + t, YD + t + 7 * 255 + 1, 7), sub)
+        ts(ap("MP"), ap("EB"), 2.0, eq)
+        ts(ap("MM"), ap("EB"), -2.0, eq)
+        mm(P(5, 0, 256), ap("NIB"), ap("MP"), True, False)
+        mm(P(5, 0, 256), ap("I64"), ap("MM"), False, True)
+
+    def prep_a(t):
+        ts(ap("AH"), cand("A", t), 16.0, ad)
+        for h in range(2):
+            mm(P(6, 128 * h, 128 * h + 128), ap("AH", 128 * h, 128 * h + 128), ap("IB"), True, True)
+
+    late = []
+    for c in range(7):
+        a = SC * c
+        w = min(SC, V - a)
+        sv = SV if c < 6 else SVL
+        bank = c & 1 if c < 6 else 7
+        gv, ga = "GV%d" % (c & 1), "GA%d" % (c & 1)
+        cp(ap(gv, 0, 16 * sv), ind(yw, ap("NU", a, a + sv)))
+        act(ap(ga, 0, 16 * (w - sv)), ind(yw, ap("NU", a + sv, a + w)), AF.Copy)
+        if c:
+            act(ap("R", a - SC, a), P((c - 1) & 1, 0, SC), AF.Copy)
+        for f in late:
+            f()
+        late = []
+        if c > 1:
+            e = a - 2 * SC
+            late.append(zfrom(ap("R", e, e + SC), SC, ap("Y", e, e + SC), ap("Z", e, e + SC), 2 + (c & 1)))
+        mm(P(bank, 0, w), ap("NIB"), ap("Y", a, a + w), True, False)
+        for i in range(16):
+            mm(P(bank, 0, sv), ap("IB"), ap(gv, i, 16 * sv, 16), False, False)
+        for i in range(16):
+            mm(P(bank, sv, w), ap("IB"), ap(ga, i, 16 * (w - sv), 16), False, i == 15)
+        if c in (0, 2):
+            cp(ap("NU", *pieces[1 + c // 2]), ap("NI", *pieces[1 + c // 2]))
+        if c in (1, 3):
+            cp(ap("N", *pieces[1 + c // 2]), ap("NI", *pieces[1 + c // 2]))
+        if c == 4:
+            prep_n1(0)
+            cp(ap("AU"), cand("A", 0))
+        if c == 5:
+            prep_n2(0)
+            prep_a(0)
+    e = 5 * SC
+    for f in late:
+        f()
+    fifth = zfrom(ap("R", e, e + SC), SC, ap("Y", e, e + SC), ap("Z", e, e + SC), 3)
+    cp(ap("AT"), P(6, 0, 256))
+    fifth()
+    e = 6 * SC
+    zfrom(P(7, 0, V - e), V - e, ap("Y", e, V), ap("Z", e, V), 2)()
+
+    def wrap(src, bank, a):
+        tt(ap("BC"), ind(src, bc), ap("WM"), mul)
+        for h in range(2):
+            mm(P(bank, a + 8 * h, a + 8 * h + 8), ap("BC", 128 * h, 128 * h + 128), ap("B8F", 0, 8), True, True)
+        return P(bank, a, a + 16)
+
+    def half(name, h):
+        return ap(name, 128 * h, 128 * h + 128)
+
+    def ones(k):
+        return ap("ONES", 0, 128, 1, 0, k)
+
+    xw = ap("X", 0, W + 2)
+    bu = sl("su", "b")
+
+    def newlists():
+        for h in range(2):
+            mm(P(7, 256 + 128 * h, 384 + 128 * h), half("BC2", h), ap("IF"), False, h == 1)
+
+    for t in range(3):
+        zw = ap("Z", 0, V)
+        lv = LV[t]
+        parts = {"v1": ("GV0", 0, lv // 2), "v2": ("GV1", lv // 2, lv), "a1": ("MX0", lv, 128),
+                 "a2": ("GA0", 128, 192), "a3": ("GA1", 192, 256)}
+
+        def zg(k):
+            gb, a, b = parts[k]
+            if b > a and k[0] == "v":
+                cp(ap(gb, 0, 16 * (b - a)), ind(zw, ap("AU", a, b)))
+            elif b > a:
+                act(ap(gb, 0, 16 * (b - a)), ind(zw, ap("AU", a, b)), AF.Copy)
+
+        def zsum(k, stop):
+            gb, a, b = parts[k]
+            for i in range(16 if b > a else 0):
+                mm(P(a >> 7, a & 127, b - (a & 128)), ap("IB"), ap(gb, i, 16 * (b - a), 16), False, stop and i == 15)
+
+        for k in ("a1", "a2", "a3"):
+            zg(k)
+        for h in range(2):
+            mm(P(h, 0, 128), ones(1), ap("C15", 64, 192, 1, 0, 1), True, False)
+        if t:
+            prep_a(t)
+            cp(ind(ap("N", 0, 2048), bu), ap("NL"))
+            prep_n1(t)
+            zsum("a1", False)
+            zg("v1")
+            prep_n2(t)
+            zsum("v1", False)
+            zsum("a2", False)
+            zg("v2")
+            cp(ap("AT"), P(6, 0, 256))
+        else:
+            zg("v1")
+            zg("v2")
+            for k in ("a1", "v1", "a2"):
+                zsum(k, False)
+            act(ap("R", 6 * SC, V), P(7, 0, V - 6 * SC), AF.Copy)
+            ts(ap("WM"), ap("IOI"), qf, eq)
+        zsum("v2", True)
+        zsum("a3", True)
+        for h in range(2):
+            ts(half("RR", h), P(h, 0, 128), M64, ad, -M64, ad)
+            tt(half("X1", h), P(h, 0, 128), half("MP", h), mul)
+            tt(half("X2", h), P(5, 128 * h, 128 * h + 128), half("RR", h), mul)
+            mm(P(3, 8 * h, 8 * h + 8), half("X1", h), b8, True, False)
+            mm(P(3, 8 * h, 8 * h + 8), half("X2", h), b8, False, True)
+        will = sl("sb", "will")
+        ts(will, P(3, 0, 16), e8, le, 2.0, mul)
+        mm(P(3, 16, 32), ap("TRI"), will, True, False)
+        mm(P(3, 24, 32), ap("ONES"), sl("sb", "will", 0, 8), False, True)
+        mm(P(2, 0, 64), ones(1), ap("C15", 0, 64, 1, 0, 1), True, False)
+        tt(sm("rank"), P(3, 16, 32), will, mul)
+        die = sl("sb", "die")
+        ng = len(range(t, G, 7))
+        for gi in range(8):
+            for h in range(2):
+                c = 8 * h + gi
+                ts(ap("PP", 128 * c + 64, 128 * c + 128), ap("IO4"), sm("rank", c, c + 1), eq, 2.0, mul)
+            for h in range(2):
+                c = 8 * h + gi
+                for j in range(2):
+                    o = 128 * c + 64 - 64 * j
+                    mm(P(2, 8 * gi, 8 * gi + 8), ap("PP", o, o + 128),
+                       ap("AT", 128 * h + 16 * gi + 8 * j, 128 * h + 16 * gi + 8 * j + 8), False,
+                       gi == 7 and h == 1 and j == 1)
+        ts(sm("ok"), sm("rank"), 256.0, le)
+        tt(die, sm("ok"), will, mul)
+        ts(ap("S2"), P(2, 0, 64), M32, ad, -M32, ad)
+        tt(ap("S1"), P(2, 0, 64), ap("S2"), sub)
+        act(ap("DB"), ind(die, bc), AF.Copy)
+        for c in range(64):
+            o = 128 * c
+            ts(ap("RMP", o, o + 128), ap("RAMP"), ap("S1", c, c + 1), mx, ap("S2", c, c + 1), mn)
+            gi = c >> 3
+            mm(P(0, 16 * gi, 16 * gi + 16, 1, 0, 112), ap("RMP", o + 16, o + 128), ap("RMP", o, o + 16),
+               c & 7 == 0, c & 7 == 7)
+            if c == 7:
+                mm(P(4, 0, 256), ap("NIB"), cand("X", t), True, False)
+                for h in range(2):
+                    mm(P(4, 128 * h, 128 * h + 128), half("DB", h), ap("I31"), False, h == 1)
+                for h in range(2):
+                    mm(P(5, 128 * h, 128 * h + 128), half("DB", h), ap("IB"), True, True)
+                act(ap("TX"), P(4, 0, 256), AF.Relu)
+                act(cand("DD", t), P(5, 0, 256), scale=(t + 1) / 2.0)
+            if c == 15:
+                mm(P(4, 0, 256), ap("IB"), cand("X", t), True, False)
+                mm(P(4, 0, 256), ap("IB"), ap("TX"), False, True)
+                act(ap("XS", 192 * t, 192 * t + ng), P(4, 0, ng), AF.Copy)
+                send(5 + t, ap("XL", 192 * t, 192 * t + 192), ap("XS", 192 * t, 192 * t + 192))
+                act(cand("X", t), P(4, 0, 256), AF.Copy)
+            if 23 <= c < 39:
+                q = c - 23
+                mm(P(6, 0, 112), ap("SEL", 128 * q, 128 * q + 128), ap("DD", q, V, 16), q == 0, q == 15)
+            if c == 39:
+                act(ap("DW", 0, 112), P(6, 0, 112), scale=65536.0)
+                act(ap("N2"), ap("N", 0, G), bias=float(V))
+                send(2 + t, ap("N", 2048 + G * t, 2048 + G * (t + 1)), ap("N2"))
+                act(ap("X", V + t, W, 7), ap("XL", 192 * t, 192 * t + ng), AF.Copy)
+        cp(ap("CS", 0, 128, 1, 0, 112), P(0, 0, 128, 1, 0, 112))
+        mm(P(1, 0, 112), ap("CS", 0, 128, 1, 0, 112), ap("TN", 0, 112, 1, 0, 112), True, True)
+        if t < 2:
+            mm(P(3, 0, 16), ap("ONES"), die, True, True)
+            add("v", lambda: g.vector.tensor_reduce(sm("col", 5, 6)[0], P(3, 0, 16)[0], AxisListType.X, ad),
+                [P(3, 0, 16)], [sm("col", 5, 6)])
+            ts(sl("si", "e", 0, 1), sm("col", 5, 6), 0.5, mul)
+        cp(ap("CS2", 0, 112), P(1, 0, 112))
+        mm(P(0, 0, 128), ap("IB"), ap("F"), True, False)
+        mm(P(0, 0, 112), ap("TM"), ap("CS2", 0, 112), False, True)
+        if t < 2:
+            ts(sl("si", "e", 1, 2), sl("si", "e", 0, 1), 7, ALU.bitwise_and)
+            cp(e8, sl("si", "e", 1, 2))
+        tt(ap("F"), P(0, 0, 128), ap("DW"), gt)
+        mm(P(1, 0, 128), ap("BO"), ap("F"), True, True)
+        mm(P(1, 128, 256), ap("TRI16"), ap("F"), True, True)
+        scan(ap("CC", 1, 129), P(1, 0, 128), ap("C256"), ad, mn)
+        for c in range(CV, 16):
+            act(ap("GA0", 128 * c, 128 * c + 128), ap("CC", 1, 129), AF.Sign, bias=sm("sh", c, c + 1), scale=-1.0,
+                acc=sm("acc", c, c + 1))
+        for c in range(CV):
+            ts(ap("MX0", 128 * c, 128 * c + 128), ap("CC", 1, 129), ap("SCB", c, c + 1), le)
+        scan(ap("MX1", 0, 128 * CV), ap("RZ", 0, 128 * CV), ap("MX0", 0, 128 * CV), mul, ad)
+        cu, cb = sl("su", "c"), sl("sb", "c")
+        tt(ap("CUM"), P(1, 128, 256), ap("CC", 0, 128), ad)
+        cp(sl("sb", "c", 0, CV), ap("MX1", 127, 128 * CV, 128))
+        ts(sl("sb", "c", CV, 16), sm("acc", CV, 16), 0.5, mul, 64.0, ad)
+        cp(cu, cb)
+        tt(ap("CMP"), ind(ap("CUM"), cu), ap("IOS"), le)
+        act(ap("CRP"), ind(ap("IOS", 0, 128), cu), AF.Copy)
+        if t < 2:
+            act(ap("BM"), ap("CRP"), bias=qt[t], scale=16.0)
+        mm(P(7, 0, 16), ap("I16"), cb, True, False)
+        for q in range(16):
+            mm(P(7, 0, 16), ap("SEL", 128 * q, 128 * q + 128), ap("CMP", q, 256, 16), False, q == 15)
+        if t < 2:
+            ts(ap("FK", 0, 112), ap("CUM", 0, 112), 256.0, gt)
+            tt(ap("F", 0, 112), ap("F", 0, 112), ap("FK", 0, 112), mul)
+        if t == 1:
+            cp(ind(ap("R"), bu), ap("RN"))
+        cp(bu, P(7, 0, 16))
+        cp(ap("LBU"), ind(ap("N", 0, 2048), bu))
+        act(ap("XB"), ind(xw, bu), AF.Copy)
+        act(ap("GA0", 0, 1024), ind(xw, ap("LBU", 128, 192)), AF.Copy)
+        act(ap("GA0", 1024, 2048), ind(xw, ap("LBU", 192, 256)), AF.Copy)
+        ts(ap("LBH"), ap("LBU"), -CEN, ad)
+        cp(ap("GV0"), ind(xw, ap("LBU", 0, 128)))
+        for h in range(2):
+            mm(P(7, 16 + 8 * h, 24 + 8 * h), half("CMP", h), b8, True, False)
+            mm(P(7, 16 + 8 * h, 24 + 8 * h), half("CRP", h), b8, False, True)
+        for h in range(2):
+            mm(P(7, 256 + 128 * h, 384 + 128 * h), half("LBH", h), ap("IB"), True, True)
+        mm(P(2, 0, 256), ap("IB"), ap("XB"), True, True)
+        if t < 2:
+            mm(P(2, 256, 512), ap("BO"), ap("CMP"), True, True)
+
+        def preload(banks):
+            for b in banks:
+                for j in range(4):
+                    mm(P(b, 128 * j, 128 * j + 128), ap("NIB"), half("XB", 1), j == 0, False)
+
+        def vmax(h, gb, i, mb, st):
+            tt(ap(mb, 128 * i, 128 * i + 128), P(2, 128 * h, 128 * h + 128), ap(gb, i, 2048, 16), mx)
+            mm(P(h, i, 8 * st, st), ap(mb, 128 * i, 128 * i + 128), b8b, False, False)
+
+        def adiff(b, gb, i0, s0=0):
+            for j in range(4):
+                mm(P(b, 128 * j + s0, 128 * j + 128), ap("IB"), ap(gb, 16 * s0 + i0 + j, 2048, 16), False, j == 3)
+            act(ap("MX1", 128 * i0, 128 * i0 + 512), P(b), AF.Abs)
+
+        def asum(i0, st, stop=False):
+            for i in range(i0, i0 + 4):
+                mm(P(1, i, 8 * st, st), ap("MX1", 128 * i, 128 * i + 128), b8a, False, stop and i == i0 + 3)
+
+        for h in range(2):
+            mm(P(h, 0, 256), ones(3), ap("KR", 0, 256, 1, 0, 3), True, False)
+        mm(P(0, 0, 256), half("XB", 0), ap("NBU"), False, False)
+        mm(P(1, 0, 256), half("LBH", 1), ap("I2"), False, False)
+        preload((3, 4, 5, 6))
+        for i in range(16):
+            mm(P(3 + i // 4, 128 * (i & 3), 128 * (i & 3) + 64), ap("IB"), ap("GA0", i, 1024, 16), False, False)
+        for k in range(4):
+            adiff(3 + k, "GA0", 4 * k, 64)
+            for i in range(4 * k, 4 * k + 4):
+                mm(P(0, i, 256, 16), ap("GV0", i, 2048, 16), ap("B8K"), False, False)
+            for i in range(4 * k, 4 * k + 4):
+                mm(P(1, 16 + i, 256, 32), ap("GA0", i, 2048, 16), b8k, False, False)
+            for i in range(4 * k, 4 * k + 4):
+                vmax(0, "GV0", i, "MX0", 32)
+            if k in (1, 2):
+                asum(4 * k - 4, 32)
+            if k == 3:
+                mm(P(0, 0, 256), half("LBH", 0), ap("I2"), False, True)
+        if t < 2:
+            ts(ap("NM"), P(2, 256, 512), qt[t], ne)
+        asum(8, 32)
+        asum(12, 32, True)
+        act(lt(0), P(7, 256, 512), AF.Copy)
+        act(lt(16), P(7, 256, 512), AF.Copy)
+        act(sm("bT"), P(7, 16, 32), bias=-CEN)
+        act(ap("BT"), ind(sm("bT"), bc), AF.Copy)
+        for h in range(2):
+            scan(ap("SC1", 256 * h, 256 * h + 256), ap("RB"), P(h, 0, 256), ad, mn)
+        if t < 2:
+            act(ap("RG"), ind(ap("R"), bu), AF.Copy)
+            act(ap("YB"), ind(yw, bu), AF.Copy)
+        ue, ke = ap("SC1", 15, 512, 32), ap("SC1", 31, 512, 32)
+        cp(sl("si", "u"), ue)
+        ts(sm("xx"), ue, THR, ltn, 65536.0, mul)
+        ts(sl("si", "k"), ke, 65536.0, mn, 0.0, mx)
+        ts(sl("si", "un"), sl("si", "u"), 4095, ALU.bitwise_and)
+        tt(sm("need"), sl("si", "k"), sm("xx"), ltn)
+        ts(sm("uf"), sl("si", "un"), -1791.5, ad)
+        tt(sm("w1"), sm("uf"), sm("need"), mul)
+        ts(sl("si", "row"), sl("si", "k"), 12, ALU.logical_shift_right)
+        asks = sl("sb", "asks")
+        ts(asks, sm("w1"), 0.0, gt)
+        mm(P(7, 32, 48), ap("TRI"), asks, True, False)
+        mm(P(7, 40, 48), ap("ONES"), sl("sb", "asks", 0, 8), False, True)
+        ts(sm("y2"), sm("w1"), 256.0 + G * t, ad)
+        ts(sm("m1"), sm("w1"), 0.0, mn)
+        tt(sm("y2"), sm("y2"), asks, mul)
+        ts(sl("si", "old"), sl("si", "k"), 4095, ALU.bitwise_and)
+        ts(sm("y1"), P(7, 32, 48), 64.0, le)
+        ts(sm("fk"), sl("si", "old"), 255.0 * 65536, ad)
+        tt(sm("y1"), sm("y1"), sm("y2"), mul)
+        tt(sm("y4"), sm("y1"), sm("m1"), ad)
+        wp = wrap(sm("y4"), 7, 48)
+        rv = RV[t]
+        dbanks = (3, 4, 6)[:(16 - rv) // 4]
+        for h, nb_ in enumerate(("NBO", "NB%d" % rv)):
+            mm(P(h, 0, 128), ones(2), ap("KR", 0, 128, 1, 0, 2), True, False)
+            mm(P(h, 0, 128), half("XB", h), ap(nb_), False, False)
+        tt(ap("OH"), ind(sl("si", "row"), bc), ap("IOI"), eq)
+        uu = sl("su", "u")
+        ts(uu, wp, 1791.75, ad)
+        ts(ap("LUU"), ind(ap("N", 0, 2048 + G * (t + 1)), uu), float(W + 1), mn)
+        act(ap("GA0", 0, 2048), ind(xw, ap("LUU", 0, 128)), AF.Copy)
+        act(ap("GA1", 0, 2048), ind(xw, ap("LUU", 128, 256)), AF.Copy)
+        ts(ap("LUH"), ap("LUU"), -CEN, ad)
+        for h in range(2):
+            mm(P(5, 128 * h, 128 * h + 128), half("LUH", h), ap("IB"), True, True)
+        if t < 2:
+            wo = wrap(sl("si", "old"), 7, 80)
+        preload(dbanks)
+        for r in range(17):
+            if r == 2 and t < 2:
+                cp(sl("su", "old"), wo)
+            tt(ap("EE", 256 * r, 256 * r + 256), P(5, 0, 256), lt(r) if r < 16 else ap("BT"), eq)
+            for h in range(2):
+                mm(P(h, 0, 128), ap("IBIG"), ap("EE", 256 * r + 128 * h, 256 * r + 128 * h + 128), False, False)
+        for i in range(16):
+            mm(P(0, i, 128, 16), ap("GA0", i, 2048, 16), b8n, False, False)
+        for k, b in enumerate(dbanks):
+            adiff(b, "GA1", rv + 4 * k)
+            for i in range(4 * k, 4 * k + 4):
+                vmax(0, "GA0", i, "MX0", 16)
+        for i in range(4 * len(dbanks), 16):
+            vmax(0, "GA0", i, "MX0", 16)
+        mm(P(0, 0, 128), half("LUH", 0), ap("IB"), False, True)
+        for i in range(rv):
+            mm(P(1, i, 128, 16), ap("GA1", i, 2048, 16), b8n, False, False)
+        for k in range(len(dbanks) - 1):
+            asum(rv + 4 * k, 16)
+        for i in range(rv):
+            vmax(1, "GA1", i, "MX1", 16)
+        asum(12, 16)
+        mm(P(1, 0, 128), half("LUH", 1), ap("IB"), False, True)
+        mm(P(7, 256, 512), ap("IB"), ap("LBH"), True, False)
+        if t < 2:
+            act(ap("YO"), ind(ap("Y", 0, YD), sl("su", "old")), AF.Copy)
+        for h in range(2):
+            scan(half("SC1", h), half("RB", 0), P(h, 0, 128), ad, mn)
+        tt(sl("si", "w"), ap("SC1", 15, 256, 16), sm("fk"), mn)
+        ts(sl("si", "wn"), sl("si", "w"), 4095, ALU.bitwise_and)
+        if t < 2:
+            ts(sm("un4"), sl("si", "w"), THR, ge, float(YD), mul)
+            tt(sm("pw"), sm("un4"), sl("si", "wn"), ad)
+            act(ap("AN"), ind(sm("pw"), bc), AF.Copy)
+            wp = wrap(sm("pw"), 3, 0)
+            for h in range(2):
+                mm(P(5, 128 - 128 * h, 256 - 128 * h), half("AN", h), ap("JF"), True, True)
+        tt(sm("dv"), sl("si", "wn"), sl("si", "old"), sub)
+        tt(ap("BC2"), ind(sm("dv"), bc), ap("OH"), mul)
+        if t == 2:
+            newlists()
+            ts(ap("NL"), P(7, 256, 512), CEN, ad)
+            cp(ind(ap("N", 0, 2048), bu), ap("NL"))
+            break
+        mm(P(6, 0, 256), ap("IB"), ap("NM"), True, True)
+        cp(sl("su", "w"), wp)
+        act(ap("YW"), ind(ap("Y"), sl("su", "w")), AF.Copy)
+        cp(sm("pww"), wp)
+        cp(ap("WR"), P(5, 0, 256))
+        mm(P(0, 0, 256), ap("IB"), ap("RG"), True, False)
+        mm(P(0, 0, 256), ap("NIB"), ap("YO"), False, False)
+        mm(P(0, 0, 256), ap("IB"), ap("YW"), False, True)
+        act(ap("RN"), P(0, 0, 256), AF.Copy)
+        newlists()
+        act(ap("NL"), P(7, 256, 512), bias=CEN)
+        ts(sl("su", "wa"), sm("pww"), float(V - 1), mn)
+        ts(sm("bad"), sm("pww"), float(V), ge)
+        tt(ap("AN"), ind(ap("A", 0, V), sl("su", "wa")), ap("BM"), sub)
+        for c in range(16):
+            o = 8 * c * (c + 1)
+            ts(ap("DE", o, o + 16 * c + 16), ap("WR", 240 - 16 * c, 256), sm("pww", c, c + 1), eq)
+        fin = zfrom(ap("RN"), 256, ap("YB"), ap("ZN"), 1)
+        tt(ap("X1"), P(6, 0, 256), ap("AN"), mul)
+        mm(P(6, 256, 512), ap("IF"), ap("BM"), True, False)
+        mm(P(6, 256, 512), ap("IB"), ap("X1"), False, True)
+        act(ap("AN"), P(6, 256, 512), AF.Copy)
+        scan(ap("DS"), ap("DE"), ap("DM"), ad, mul)
+        tt(sm("bad"), ind(ap("DS"), sl("su", "ends", 0, 1)), sm("bad"), ad)
+        fin()
+        ts(sm("bad"), sm("bad"), 0.0, gt, 16384.0, mul)
+        cp(ind(ap("Z"), bu), ap("ZN"))
+        tt(sm("bad"), sm("bad"), sm("pww"), ad)
+        tt(sm("bad"), sm("bad"), sm("dum"), mn)
+        cp(sl("su", "tg"), sm("bad"))
+        cp(ind(ap("A"), sl("su", "tg")), ap("AN"))
+        cp(ap("AU"), cand("A", t + 1))
+
+    for k, (a, b) in enumerate(((0, 896), (896, V))):
+        dma("sa"[k], T.yn[:, a:b], T["N"][:, a:b], [ap("N", a, b)], [])
+    dma("g", T.yd[:, :], T["DD"][0:128:16, :], [ap("DD")], [])
+
+    for o in ops:
+        best = {}
+        for j in o["deps"]:
+            if ops[j]["sem"] is None:
+                best[ops[j]["q"]] = max(best.get(ops[j]["q"], -1), j)
+        o["deps"] = [j for j in o["deps"] if ops[j]["sem"] is not None] + list(best.values())
+    done = {q: {} for q in Q}
+    for o in ops:
+        if o["q"] != "x":
+            for j in o["deps"]:
+                if ops[j]["sem"] is None and done[o["q"]].get(ops[j]["q"], -1) < j:
+                    done[o["q"]][ops[j]["q"]] = j
+                    ops[j]["mark"] = True
+    num, run = {}, {"v": 0, "a": 0, "p": 0, "g": 0}
+    for i, o in enumerate(ops):
+        if o["sem"] is None:
+            run[o["q"]] += o["mark"]
+            num[i] = run[o["q"]]
+    seen = {q: {} for q in Q}
+    waited = set()
+    for i, o in enumerate(ops):
+        q = o["q"]
+        if q == "x":
+            continue
+        for j in sorted(o["deps"]):
+            d = ops[j]
+            s, c = ("c" + d["q"], num[j]) if d["sem"] is None else d["sem"][:2]
+            if seen[q].get(s, 0) < c:
+                Q[q].wait_ge(T.sem[s], c)
+                seen[q][s] = c
+                waited.add(s)
+        h = o["fn"]()
+        if o["sem"] is not None:
+            if o["sem"][2]:
+                h.then_inc(T.sem[o["sem"][0]], 16)
+        elif o["mark"]:
+            h.then_inc(T.sem["c" + q], 1)
+    for o in ops:
+        if o["sem"] is not None and o["sem"][0] not in waited:
+            Q["g" if o["q"] == "x" else o["q"]].wait_ge(T.sem[o["sem"][0]], o["sem"][1])

@@ -7,9 +7,10 @@ YD = 3104
 THR = 241.0 * 65536
 M32, M64 = 1.5 * 2 ** 28, 1.5 * 2 ** 29
 DML = 2176
-SC, SV, SVL = 272, 118, 64
-LV = (128, 80, 80)
-CV = 10
+SC, SV, SVL = 272, 120, 72
+LV = (128, 86, 86)
+UV = 12
+CV = 9
 RV = (8, 8, 8)
 
 F32, BF, F16, I32, U16 = "float32", "bfloat16", "float16", "int32", "uint16"
@@ -18,13 +19,13 @@ SB = {
     "Y": (2 * YD, BF), "X": (3104, BF), "R": (2048, BF), "Z": (2048, BF), "DD": (V, BF),
     "GV0": (2048, BF), "GV1": (2048, BF), "GA0": (2560, BF), "GA1": (2560, BF),
     "MX0": (2048, BF), "MX1": (2048, BF), "EE": (17 * 256, BF), "RMP": (8192, BF),
-    "T1": (SC, BF), "T2": (SC, BF), "XS": (192 * 3, BF), "XL": (192 * 3, BF), "TX": (256, BF),
+    "T1": (3 * SC, BF), "T2": (3 * SC, BF), "XS": (192 * 3, BF), "XL": (192 * 3, BF), "TX": (256, BF),
     "IB": (128, BF), "NIB": (128, BF), "IBIG": (128, BF), "I64": (128, BF), "I16": (128, BF), "I31": (128, BF),
     "I2": (256, BF), "IF": (128, F32), "JF": (128, F32), "BO": (128, BF), "NBO": (128, BF), "NB4": (128, BF),
     "NB8": (128, BF), "NBU": (256, BF), "B8K": (16, BF),
     "TRI16": (128, BF), "TRI": (128, BF), "ONES": (128, BF), "B8": (80, BF), "B8F": (16, F32), "SEL": (2048, BF),
     "WM": (256, F32), "IOI": (256, F32), "IOS": (256, F32), "RAMP": (128, BF), "IO4": (64, BF), "TN": (128, F32),
-    "TM": (128, F32), "KR": (256, BF), "C15": (192, BF), "RB": (256, F32), "C256": (128, BF), "RZ": (128 * CV, BF),
+    "TM": (128, F32), "KR": (256, BF), "C15": (320, BF), "RB": (256, F32), "C256": (128, BF), "RZ": (128 * CV, BF),
     "DM": (DML, BF), "DE": (DML, BF), "DS": (DML, BF), "MK": (16, BF), "SCB": (16, BF),
     "sm": (16 * 48, F32), "si": (16 * 12, I32), "su": (16 * 12, U16), "sb": (16 * 8, BF),
     "AU": (256, U16), "AH": (256, F16), "AT": (256, F16), "NH": (256, F16), "EB": (256, BF), "MP": (256, BF),
@@ -238,6 +239,7 @@ def rank_program(g, core, T, topo):
         sel(ap("TRI"), ap("ONES"), [[1, 128]], ge, 0, 0, -1)
         iota(ap("IO4"), [[4, 64]], 4)
         iota(ap("C15", 0, 64), [[0, 64]], -15)
+        iota(ap("C15", 192, 320), [[0, 128]], 0)
         iota(ap("RAMP", 0, 16), [[2, 16]], -15)
         iota(ap("RAMP", 16, 128), [[32, 112]], 32)
         iota(ap("IOI"), [[0, 16], [1, 16]], 0)
@@ -260,6 +262,7 @@ def rank_program(g, core, T, topo):
         iota(ap("RZ", 0, 128 * CV, 128), [[0, CV]], 0)
         iota(ap("IOS"), [[1, 256]], 0)
         diag("I16", 16.0)
+        send(1, ap("X", V, W), ap("X", 0, G))
         for k, val in enumerate((65536, 131072, -65536, -512)):
             block(ap("B8", 16 * k + 16, 16 * k + 24), val, [[16, 8]])
         sel(ap("B8K", 0, 16, 2), ap("B8", 48, 56), [[0, 8]], ge, 0, 0, 0)
@@ -287,13 +290,13 @@ def rank_program(g, core, T, topo):
     b8, b8a, b8b, b8n, b8k = [ap("B8", 16 * k, 16 * k + 8) for k in range(5)]
     consts_a()
     consts_b()
-    send(1, ap("X", V, W), ap("X", 0, G))
 
     def zfrom(src, w, ycols, zout, bank):
-        ts(ap("T1", 0, w), src, 1.0, eq, 64.0, mul)
-        ts(ap("T2", 0, w), src, -1.0, eq)
-        mm(P(bank, 0, w), ap("IB"), ap("T1", 0, w), True, False)
-        mm(P(bank, 0, w), ap("NIB"), ap("T2", 0, w), False, True)
+        o = SC * (bank - 2)
+        ts(ap("T1", o, o + w), src, 1.0, eq, 64.0, mul)
+        ts(ap("T2", o, o + w), src, -1.0, eq)
+        mm(P(bank, 0, w), ap("IB"), ap("T1", o, o + w), True, False)
+        mm(P(bank, 0, w), ap("IB"), ap("T2", o, o + w), False, True)
         return lambda: tt(zout, P(bank, 0, w), ycols, mul)
 
     yw = ap("Y", 0, W)
@@ -306,10 +309,12 @@ def rank_program(g, core, T, topo):
         for q in range(16):
             mm(P(4, 0, 16), ap("SEL", 128 * q, 128 * q + 128), ap("NH", q, 256, 16), q == 0, q == 15)
 
-    def prep_n2(t):
+    def prep_n2(t, fill1, fill2):
         ts(sl("su", "n"), P(4, 0, 16), CEN, ad)
+        fill1()
         tt(ap("EB"), ind(yw, sl("su", "n")), ap("Y", YD + t, YD + t + 7 * 255 + 1, 7), sub)
-        ts(ap("MP"), ap("EB"), 2.0, eq)
+        fill2()
+        ts(ap("MP"), ap("EB"), 2.0, eq, -1.0, mul)
         ts(ap("MM"), ap("EB"), -2.0, eq)
         mm(P(5, 0, 256), ap("NIB"), ap("MP"), True, False)
         mm(P(5, 0, 256), ap("I64"), ap("MM"), False, True)
@@ -328,12 +333,12 @@ def rank_program(g, core, T, topo):
         gv, ga = "GV%d" % (c & 1), "GA%d" % (c & 1)
         cp(ap(gv, 0, 16 * sv), ind(yw, ap("NU", a, a + sv)))
         act(ap(ga, 0, 16 * (w - sv)), ind(yw, ap("NU", a + sv, a + w)), AF.Copy)
-        if c:
+        if 0 < c < 6:
             act(ap("R", a - SC, a), P((c - 1) & 1, 0, SC), AF.Copy)
         for f in late:
             f()
         late = []
-        if c > 1:
+        if 1 < c < 6:
             e = a - 2 * SC
             late.append(zfrom(ap("R", e, e + SC), SC, ap("Y", e, e + SC), ap("Z", e, e + SC), 2 + (c & 1)))
         mm(P(bank, 0, w), ap("NIB"), ap("Y", a, a + w), True, False)
@@ -341,24 +346,23 @@ def rank_program(g, core, T, topo):
             mm(P(bank, 0, sv), ap("IB"), ap(gv, i, 16 * sv, 16), False, False)
         for i in range(16):
             mm(P(bank, sv, w), ap("IB"), ap(ga, i, 16 * (w - sv), 16), False, i == 15)
-        if c in (0, 2):
-            cp(ap("NU", *pieces[1 + c // 2]), ap("NI", *pieces[1 + c // 2]))
         if c in (1, 3):
-            cp(ap("N", *pieces[1 + c // 2]), ap("NI", *pieces[1 + c // 2]))
+            cp(ap("NU", *pieces[1 + c // 2]), ap("NI", *pieces[1 + c // 2]))
+        if c in (2, 4):
+            cp(ap("N", *pieces[c // 2]), ap("NI", *pieces[c // 2]))
         if c == 4:
             prep_n1(0)
-            cp(ap("AU"), cand("A", 0))
         if c == 5:
-            prep_n2(0)
-            prep_a(0)
+            prep_n2(0, lambda: cp(ap("AU"), cand("A", 0)), lambda: prep_a(0))
+    e = 4 * SC
+    late = [zfrom(ap("R", e, e + SC), SC, ap("Y", e, e + SC), ap("Z", e, e + SC), 2)]
     e = 5 * SC
+    late.append(zfrom(P(1, 0, SC), SC, ap("Y", e, e + SC), ap("Z", e, e + SC), 3))
+    act(ap("R", e, e + SC), P(1, 0, SC), AF.Copy)
+    e = 6 * SC
+    late.append(zfrom(P(7, 0, V - e), V - e, ap("Y", e, V), ap("Z", e, V), 4))
     for f in late:
         f()
-    fifth = zfrom(ap("R", e, e + SC), SC, ap("Y", e, e + SC), ap("Z", e, e + SC), 3)
-    cp(ap("AT"), P(6, 0, 256))
-    fifth()
-    e = 6 * SC
-    zfrom(P(7, 0, V - e), V - e, ap("Y", e, V), ap("Z", e, V), 2)()
 
     def wrap(src, bank, a):
         tt(ap("BC"), ind(src, bc), ap("WM"), mul)
@@ -382,56 +386,55 @@ def rank_program(g, core, T, topo):
     for t in range(3):
         zw = ap("Z", 0, V)
         lv = LV[t]
-        parts = {"v1": ("GV0", 0, lv // 2), "v2": ("GV1", lv // 2, lv), "a1": ("MX0", lv, 128),
-                 "a2": ("GA0", 128, 192), "a3": ("GA1", 192, 256)}
+        mid = (lv + 32 + 256) // 4 * 2
+        parts = {"v0": (0, 48), "v1": (0 if t else 48, lv - 32), "v2": (lv - 32, lv), "a1": (mid, 256), "a2": (lv + 32, mid), "a3": (lv, lv + 32),
+                 "end": (lv - 32, lv + 32)}
 
         def zg(k):
-            gb, a, b = parts[k]
+            a, b = parts[k]
             if b > a and k[0] == "v":
-                cp(ap(gb, 0, 16 * (b - a)), ind(zw, ap("AU", a, b)))
+                cp(ap("RMP", 16 * a, 16 * b), ind(zw, ap("AU", a, b)))
             elif b > a:
-                act(ap(gb, 0, 16 * (b - a)), ind(zw, ap("AU", a, b)), AF.Copy)
+                act(ap("RMP", 16 * a, 16 * b), ind(zw, ap("AU", a, b)), AF.Copy)
 
         def zsum(k, stop):
-            gb, a, b = parts[k]
+            a, b = parts[k]
             for i in range(16 if b > a else 0):
-                mm(P(a >> 7, a & 127, b - (a & 128)), ap("IB"), ap(gb, i, 16 * (b - a), 16), False, stop and i == 15)
+                mm(P(0, a, b), ap("IB"), ap("RMP", 16 * a + i, 16 * b, 16), False, stop and i == 15)
 
         for k in ("a1", "a2", "a3"):
             zg(k)
-        for h in range(2):
-            mm(P(h, 0, 128), ones(1), ap("C15", 64, 192, 1, 0, 1), True, False)
+        mm(P(0, 0, 256), ones(1), ap("C15", 64, 320, 1, 0, 1), True, False)
         if t:
-            prep_a(t)
             cp(ind(ap("N", 0, 2048), bu), ap("NL"))
             prep_n1(t)
             zsum("a1", False)
             zg("v1")
-            prep_n2(t)
             zsum("v1", False)
             zsum("a2", False)
-            zg("v2")
-            cp(ap("AT"), P(6, 0, 256))
+            prep_n2(t, lambda: zg("v2"), lambda: (zsum("end", True), prep_a(t)))
         else:
-            zg("v1")
-            zg("v2")
-            for k in ("a1", "v1", "a2"):
+            for k in ("v0", "v1", "v2"):
+                zg(k)
+            for k in ("v0", "a1", "v1", "a2"):
                 zsum(k, False)
             act(ap("R", 6 * SC, V), P(7, 0, V - 6 * SC), AF.Copy)
             ts(ap("WM"), ap("IOI"), qf, eq)
-        zsum("v2", True)
-        zsum("a3", True)
+            zsum("end", True)
+        ts(ap("RR"), P(0, 0, 256), M64, ad, -M64, ad)
+        tt(ap("X1"), P(0, 0, 256), ap("MP"), mul)
+        tt(ap("X2"), P(5, 0, 256), ap("RR"), mul)
+        cp(ap("AT"), P(6, 0, 256))
+        mm(P(3, 0, 8), half("X1", 0), b8, True, False)
+        mm(P(3, 8, 16), half("X1", 1), b8, False, False)
         for h in range(2):
-            ts(half("RR", h), P(h, 0, 128), M64, ad, -M64, ad)
-            tt(half("X1", h), P(h, 0, 128), half("MP", h), mul)
-            tt(half("X2", h), P(5, 128 * h, 128 * h + 128), half("RR", h), mul)
-            mm(P(3, 8 * h, 8 * h + 8), half("X1", h), b8, True, False)
-            mm(P(3, 8 * h, 8 * h + 8), half("X2", h), b8, False, True)
+            mm(P(3, 8 * h, 8 * h + 8), half("X2", h), b8, False, h == 1)
         will = sl("sb", "will")
         ts(will, P(3, 0, 16), e8, le, 2.0, mul)
         mm(P(3, 16, 32), ap("TRI"), will, True, False)
         mm(P(3, 24, 32), ap("ONES"), sl("sb", "will", 0, 8), False, True)
-        mm(P(2, 0, 64), ones(1), ap("C15", 0, 64, 1, 0, 1), True, False)
+        for b in (2, 1):
+            mm(P(b, 0, 32), ones(1), ap("C15", 0, 32, 1, 0, 1), True, False)
         tt(sm("rank"), P(3, 16, 32), will, mul)
         die = sl("sb", "die")
         ng = len(range(t, G, 7))
@@ -443,16 +446,22 @@ def rank_program(g, core, T, topo):
                 c = 8 * h + gi
                 for j in range(2):
                     o = 128 * c + 64 - 64 * j
-                    mm(P(2, 8 * gi, 8 * gi + 8), ap("PP", o, o + 128),
+                    mm(P(2 - (gi >> 2), 8 * (gi & 3), 8 * (gi & 3) + 8), ap("PP", o, o + 128),
                        ap("AT", 128 * h + 16 * gi + 8 * j, 128 * h + 16 * gi + 8 * j + 8), False,
-                       gi == 7 and h == 1 and j == 1)
-        ts(sm("ok"), sm("rank"), 256.0, le)
-        tt(die, sm("ok"), will, mul)
-        ts(ap("S2"), P(2, 0, 64), M32, ad, -M32, ad)
-        tt(ap("S1"), P(2, 0, 64), ap("S2"), sub)
+                       gi & 3 == 3 and h == 1 and j == 1)
+            if gi == 5:
+                ts(sm("ok"), sm("rank"), 256.0, le)
+            if gi == 6:
+                ts(ap("S2", 0, 32), P(2, 0, 32), M32, ad, -M32, ad)
+                tt(die, sm("ok"), will, mul)
+        tt(ap("S1", 0, 32), P(2, 0, 32), ap("S2", 0, 32), sub)
         act(ap("DB"), ind(die, bc), AF.Copy)
         for c in range(64):
             o = 128 * c
+            if c == 8:
+                ts(ap("S2", 32, 64), P(1, 0, 32), M32, ad, -M32, ad)
+            if c == 12:
+                tt(ap("S1", 32, 64), P(1, 0, 32), ap("S2", 32, 64), sub)
             ts(ap("RMP", o, o + 128), ap("RAMP"), ap("S1", c, c + 1), mx, ap("S2", c, c + 1), mn)
             gi = c >> 3
             mm(P(0, 16 * gi, 16 * gi + 16, 1, 0, 112), ap("RMP", o + 16, o + 128), ap("RMP", o, o + 16),
@@ -481,18 +490,14 @@ def rank_program(g, core, T, topo):
                 act(ap("X", V + t, W, 7), ap("XL", 192 * t, 192 * t + ng), AF.Copy)
         cp(ap("CS", 0, 128, 1, 0, 112), P(0, 0, 128, 1, 0, 112))
         mm(P(1, 0, 112), ap("CS", 0, 128, 1, 0, 112), ap("TN", 0, 112, 1, 0, 112), True, True)
+        mm(P(2, 0, 128), ap("IB"), ap("F"), True, False)
+        if t == 1:
+            cp(ind(ap("R"), bu), ap("RN"))
+        cp(ap("CS2", 0, 112), P(1, 0, 112))
+        mm(P(2, 0, 112), ap("TM"), ap("CS2", 0, 112), False, True)
         if t < 2:
             mm(P(3, 0, 16), ap("ONES"), die, True, True)
-            add("v", lambda: g.vector.tensor_reduce(sm("col", 5, 6)[0], P(3, 0, 16)[0], AxisListType.X, ad),
-                [P(3, 0, 16)], [sm("col", 5, 6)])
-            ts(sl("si", "e", 0, 1), sm("col", 5, 6), 0.5, mul)
-        cp(ap("CS2", 0, 112), P(1, 0, 112))
-        mm(P(0, 0, 128), ap("IB"), ap("F"), True, False)
-        mm(P(0, 0, 112), ap("TM"), ap("CS2", 0, 112), False, True)
-        if t < 2:
-            ts(sl("si", "e", 1, 2), sl("si", "e", 0, 1), 7, ALU.bitwise_and)
-            cp(e8, sl("si", "e", 1, 2))
-        tt(ap("F"), P(0, 0, 128), ap("DW"), gt)
+        tt(ap("F"), P(2, 0, 128), ap("DW"), gt)
         mm(P(1, 0, 128), ap("BO"), ap("F"), True, True)
         mm(P(1, 128, 256), ap("TRI16"), ap("F"), True, True)
         scan(ap("CC", 1, 129), P(1, 0, 128), ap("C256"), ad, mn)
@@ -504,9 +509,10 @@ def rank_program(g, core, T, topo):
         scan(ap("MX1", 0, 128 * CV), ap("RZ", 0, 128 * CV), ap("MX0", 0, 128 * CV), mul, ad)
         cu, cb = sl("su", "c"), sl("sb", "c")
         tt(ap("CUM"), P(1, 128, 256), ap("CC", 0, 128), ad)
-        cp(sl("sb", "c", 0, CV), ap("MX1", 127, 128 * CV, 128))
+        ts(sl("su", "c", CV, 16), sm("acc", CV, 16), 0.5, mul, 64.0, ad)
+        cp(sl("su", "c", 0, CV), ap("MX1", 127, 128 * CV, 128))
         ts(sl("sb", "c", CV, 16), sm("acc", CV, 16), 0.5, mul, 64.0, ad)
-        cp(cu, cb)
+        cp(sl("sb", "c", 0, CV), ap("MX1", 127, 128 * CV, 128))
         tt(ap("CMP"), ind(ap("CUM"), cu), ap("IOS"), le)
         act(ap("CRP"), ind(ap("IOS", 0, 128), cu), AF.Copy)
         if t < 2:
@@ -516,15 +522,17 @@ def rank_program(g, core, T, topo):
             mm(P(7, 0, 16), ap("SEL", 128 * q, 128 * q + 128), ap("CMP", q, 256, 16), False, q == 15)
         if t < 2:
             ts(ap("FK", 0, 112), ap("CUM", 0, 112), 256.0, gt)
+            add("v", lambda: g.vector.tensor_reduce(sm("col", 5, 6)[0], P(3, 0, 16)[0], AxisListType.X, ad),
+                [P(3, 0, 16)], [sm("col", 5, 6)])
             tt(ap("F", 0, 112), ap("F", 0, 112), ap("FK", 0, 112), mul)
-        if t == 1:
-            cp(ind(ap("R"), bu), ap("RN"))
+            ts(sl("si", "e", 0, 1), sm("col", 5, 6), 0.5, mul)
         cp(bu, P(7, 0, 16))
         cp(ap("LBU"), ind(ap("N", 0, 2048), bu))
         act(ap("XB"), ind(xw, bu), AF.Copy)
-        act(ap("GA0", 0, 1024), ind(xw, ap("LBU", 128, 192)), AF.Copy)
+        act(ap("GA0", 16 * UV, 1024), ind(xw, ap("LBU", 128 + UV, 192)), AF.Copy)
         act(ap("GA0", 1024, 2048), ind(xw, ap("LBU", 192, 256)), AF.Copy)
         ts(ap("LBH"), ap("LBU"), -CEN, ad)
+        cp(ap("GA0", 0, 16 * UV), ind(xw, ap("LBU", 128, 128 + UV)))
         cp(ap("GV0"), ind(xw, ap("LBU", 0, 128)))
         for h in range(2):
             mm(P(7, 16 + 8 * h, 24 + 8 * h), half("CMP", h), b8, True, False)
@@ -562,19 +570,21 @@ def rank_program(g, core, T, topo):
             mm(P(3 + i // 4, 128 * (i & 3), 128 * (i & 3) + 64), ap("IB"), ap("GA0", i, 1024, 16), False, False)
         for k in range(4):
             adiff(3 + k, "GA0", 4 * k, 64)
-            for i in range(4 * k, 4 * k + 4):
-                mm(P(0, i, 256, 16), ap("GV0", i, 2048, 16), ap("B8K"), False, False)
-            for i in range(4 * k, 4 * k + 4):
-                mm(P(1, 16 + i, 256, 32), ap("GA0", i, 2048, 16), b8k, False, False)
+        for i in range(16):
+            mm(P(1, 16 + i, 256, 32), ap("GA0", i, 2048, 16), b8k, False, False)
+        for i in range(16):
+            mm(P(0, i, 256, 16), ap("GV0", i, 2048, 16), ap("B8K"), False, False)
+        for k in range(4):
             for i in range(4 * k, 4 * k + 4):
                 vmax(0, "GV0", i, "MX0", 32)
-            if k in (1, 2):
-                asum(4 * k - 4, 32)
+            if k < 3:
+                asum(4 * k, 32)
             if k == 3:
                 mm(P(0, 0, 256), half("LBH", 0), ap("I2"), False, True)
         if t < 2:
+            ts(sl("si", "e", 1, 2), sl("si", "e", 0, 1), 7, ALU.bitwise_and)
             ts(ap("NM"), P(2, 256, 512), qt[t], ne)
-        asum(8, 32)
+            cp(e8, sl("si", "e", 1, 2))
         asum(12, 32, True)
         act(lt(0), P(7, 256, 512), AF.Copy)
         act(lt(16), P(7, 256, 512), AF.Copy)
@@ -587,60 +597,61 @@ def rank_program(g, core, T, topo):
             act(ap("YB"), ind(yw, bu), AF.Copy)
         ue, ke = ap("SC1", 15, 512, 32), ap("SC1", 31, 512, 32)
         cp(sl("si", "u"), ue)
-        ts(sm("xx"), ue, THR, ltn, 65536.0, mul)
         ts(sl("si", "k"), ke, 65536.0, mn, 0.0, mx)
         ts(sl("si", "un"), sl("si", "u"), 4095, ALU.bitwise_and)
+        ts(sm("xx"), ue, THR, ltn, 65536.0, mul)
+        ts(sm("gh"), sl("si", "un"), float(V), ge, 256.0 + G * t, mul)
         tt(sm("need"), sl("si", "k"), sm("xx"), ltn)
-        ts(sm("uf"), sl("si", "un"), -1791.5, ad)
-        tt(sm("w1"), sm("uf"), sm("need"), mul)
+        tt(sm("y4"), sm("gh"), sl("si", "un"), ad)
         ts(sl("si", "row"), sl("si", "k"), 12, ALU.logical_shift_right)
-        asks = sl("sb", "asks")
-        ts(asks, sm("w1"), 0.0, gt)
-        mm(P(7, 32, 48), ap("TRI"), asks, True, False)
-        mm(P(7, 40, 48), ap("ONES"), sl("sb", "asks", 0, 8), False, True)
-        ts(sm("y2"), sm("w1"), 256.0 + G * t, ad)
-        ts(sm("m1"), sm("w1"), 0.0, mn)
-        tt(sm("y2"), sm("y2"), asks, mul)
-        ts(sl("si", "old"), sl("si", "k"), 4095, ALU.bitwise_and)
-        ts(sm("y1"), P(7, 32, 48), 64.0, le)
-        ts(sm("fk"), sl("si", "old"), 255.0 * 65536, ad)
-        tt(sm("y1"), sm("y1"), sm("y2"), mul)
-        tt(sm("y4"), sm("y1"), sm("m1"), ad)
         wp = wrap(sm("y4"), 7, 48)
+        asks = sl("sb", "asks")
+        ts(sm("y1"), sm("gh"), 1.0, mn)
+        ts(sl("si", "old"), sl("si", "k"), 4095, ALU.bitwise_and)
+        tt(asks, sm("y1"), sm("need"), mul)
+        mm(P(6, 0, 16), ap("TRI"), asks, True, False)
+        mm(P(6, 8, 16), ap("ONES"), sl("sb", "asks", 0, 8), False, True)
         rv = RV[t]
         dbanks = (3, 4, 6)[:(16 - rv) // 4]
         for h, nb_ in enumerate(("NBO", "NB%d" % rv)):
             mm(P(h, 0, 128), ones(2), ap("KR", 0, 128, 1, 0, 2), True, False)
             mm(P(h, 0, 128), half("XB", h), ap(nb_), False, False)
-        tt(ap("OH"), ind(sl("si", "row"), bc), ap("IOI"), eq)
         uu = sl("su", "u")
-        ts(uu, wp, 1791.75, ad)
+        ts(uu, wp, 2047.0 + G * (t + 1), mn)
         ts(ap("LUU"), ind(ap("N", 0, 2048 + G * (t + 1)), uu), float(W + 1), mn)
         act(ap("GA0", 0, 2048), ind(xw, ap("LUU", 0, 128)), AF.Copy)
         act(ap("GA1", 0, 2048), ind(xw, ap("LUU", 128, 256)), AF.Copy)
         ts(ap("LUH"), ap("LUU"), -CEN, ad)
         for h in range(2):
             mm(P(5, 128 * h, 128 * h + 128), half("LUH", h), ap("IB"), True, True)
-        if t < 2:
-            wo = wrap(sl("si", "old"), 7, 80)
+        tt(ap("OH"), ind(sl("si", "row"), bc), ap("IOI"), eq)
         preload(dbanks)
         for r in range(17):
-            if r == 2 and t < 2:
-                cp(sl("su", "old"), wo)
+            if r == 1:
+                ts(sm("y1"), P(6, 0, 16), 64.0, gt)
+            if r == 2:
+                tt(sm("y1"), sm("y1"), asks, mul)
+            if r == 3:
+                tt(sm("y1"), sm("y1"), sm("need"), ge)
+            if r == 4:
+                ts(sm("y1"), sm("y1"), -256.0 * 65536, mul, 255.0 * 65536, ad)
+            if r == 5:
+                tt(sm("fk"), sm("y1"), sl("si", "old"), ad)
             tt(ap("EE", 256 * r, 256 * r + 256), P(5, 0, 256), lt(r) if r < 16 else ap("BT"), eq)
             for h in range(2):
                 mm(P(h, 0, 128), ap("IBIG"), ap("EE", 256 * r + 128 * h, 256 * r + 128 * h + 128), False, False)
-        for i in range(16):
-            mm(P(0, i, 128, 16), ap("GA0", i, 2048, 16), b8n, False, False)
+            if r == 10:
+                for i in range(16):
+                    mm(P(0, i, 128, 16), ap("GA0", i, 2048, 16), b8n, False, False)
+        for i in range(8):
+            vmax(0, "GA0", i, "MX0", 16)
         for k, b in enumerate(dbanks):
             adiff(b, "GA1", rv + 4 * k)
-            for i in range(4 * k, 4 * k + 4):
-                vmax(0, "GA0", i, "MX0", 16)
-        for i in range(4 * len(dbanks), 16):
-            vmax(0, "GA0", i, "MX0", 16)
-        mm(P(0, 0, 128), half("LUH", 0), ap("IB"), False, True)
         for i in range(rv):
             mm(P(1, i, 128, 16), ap("GA1", i, 2048, 16), b8n, False, False)
+        for i in range(8, 16):
+            vmax(0, "GA0", i, "MX0", 16)
+        mm(P(0, 0, 128), half("LUH", 0), ap("IB"), False, True)
         for k in range(len(dbanks) - 1):
             asum(rv + 4 * k, 16)
         for i in range(rv):
@@ -648,20 +659,23 @@ def rank_program(g, core, T, topo):
         asum(12, 16)
         mm(P(1, 0, 128), half("LUH", 1), ap("IB"), False, True)
         mm(P(7, 256, 512), ap("IB"), ap("LBH"), True, False)
+        scan(half("SC1", 0), half("RB", 0), P(0, 0, 128), ad, mn)
         if t < 2:
-            act(ap("YO"), ind(ap("Y", 0, YD), sl("su", "old")), AF.Copy)
-        for h in range(2):
-            scan(half("SC1", h), half("RB", 0), P(h, 0, 128), ad, mn)
+            wo = wrap(sl("si", "old"), 6, 0)
+        scan(half("SC1", 1), half("RB", 0), P(1, 0, 128), ad, mn)
         tt(sl("si", "w"), ap("SC1", 15, 256, 16), sm("fk"), mn)
         ts(sl("si", "wn"), sl("si", "w"), 4095, ALU.bitwise_and)
         if t < 2:
-            ts(sm("un4"), sl("si", "w"), THR, ge, float(YD), mul)
+            cp(sl("su", "old"), wo)
+            act(ap("YO"), ind(ap("Y", 0, YD), sl("su", "old")), AF.Copy)
+        tt(sm("dv"), sl("si", "wn"), sl("si", "old"), sub)
+        if t < 2:
+            ts(sm("un4"), sm("dv"), 0.0, eq, float(YD), mul)
             tt(sm("pw"), sm("un4"), sl("si", "wn"), ad)
             act(ap("AN"), ind(sm("pw"), bc), AF.Copy)
             wp = wrap(sm("pw"), 3, 0)
             for h in range(2):
                 mm(P(5, 128 - 128 * h, 256 - 128 * h), half("AN", h), ap("JF"), True, True)
-        tt(sm("dv"), sl("si", "wn"), sl("si", "old"), sub)
         tt(ap("BC2"), ind(sm("dv"), bc), ap("OH"), mul)
         if t == 2:
             newlists()
@@ -672,33 +686,34 @@ def rank_program(g, core, T, topo):
         cp(sl("su", "w"), wp)
         act(ap("YW"), ind(ap("Y"), sl("su", "w")), AF.Copy)
         cp(sm("pww"), wp)
+        ts(sl("su", "wa"), wp, float(V - 1), mn)
+        ts(sm("bad"), wp, float(V), ge, 16384.0, mul)
+        tt(ap("BC"), ind(ap("A", 0, V), sl("su", "wa")), ap("BM"), sub)
+        tt(sm("bad"), sm("bad"), sm("pww"), ad)
         cp(ap("WR"), P(5, 0, 256))
         mm(P(0, 0, 256), ap("IB"), ap("RG"), True, False)
         mm(P(0, 0, 256), ap("NIB"), ap("YO"), False, False)
         mm(P(0, 0, 256), ap("IB"), ap("YW"), False, True)
-        act(ap("RN"), P(0, 0, 256), AF.Copy)
+        act(ap("TX"), P(0, 0, 256), AF.Square, bias=-3.5, scale=4.5)
+        act(P(1, 0, 256), ap("TX"), AF.Relu, bias=65.0, scale=-1.0)
+        if t == 0:
+            act(ap("RN"), P(0, 0, 256), AF.Copy)
         newlists()
         act(ap("NL"), P(7, 256, 512), bias=CEN)
-        ts(sl("su", "wa"), sm("pww"), float(V - 1), mn)
-        ts(sm("bad"), sm("pww"), float(V), ge)
-        tt(ap("AN"), ind(ap("A", 0, V), sl("su", "wa")), ap("BM"), sub)
         for c in range(16):
             o = 8 * c * (c + 1)
-            ts(ap("DE", o, o + 16 * c + 16), ap("WR", 240 - 16 * c, 256), sm("pww", c, c + 1), eq)
-        fin = zfrom(ap("RN"), 256, ap("YB"), ap("ZN"), 1)
-        tt(ap("X1"), P(6, 0, 256), ap("AN"), mul)
+            ts(ap("DE", o, o + 16 * c + 16), ap("WR", 240 - 16 * c, 256), sm("pww", c, c + 1), eq, 16384.0, mul)
+        tt(ap("X1"), P(6, 0, 256), ap("BC"), mul)
         mm(P(6, 256, 512), ap("IF"), ap("BM"), True, False)
         mm(P(6, 256, 512), ap("IB"), ap("X1"), False, True)
         act(ap("AN"), P(6, 256, 512), AF.Copy)
         scan(ap("DS"), ap("DE"), ap("DM"), ad, mul)
         tt(sm("bad"), ind(ap("DS"), sl("su", "ends", 0, 1)), sm("bad"), ad)
-        fin()
-        ts(sm("bad"), sm("bad"), 0.0, gt, 16384.0, mul)
-        cp(ind(ap("Z"), bu), ap("ZN"))
-        tt(sm("bad"), sm("bad"), sm("pww"), ad)
+        tt(ap("ZN"), P(1, 0, 256), ap("YB"), mul)
         tt(sm("bad"), sm("bad"), sm("dum"), mn)
         cp(sl("su", "tg"), sm("bad"))
         cp(ind(ap("A"), sl("su", "tg")), ap("AN"))
+        cp(ind(ap("Z"), bu), ap("ZN"))
         cp(ap("AU"), cand("A", t + 1))
 
     for k, (a, b) in enumerate(((0, 896), (896, V))):

@@ -1,47 +1,56 @@
 from concourse.mybir import AluOpType as ALU, AxisListType, ActivationFunctionType as AF
 
 V, G, W = 1792, 1296, 3088
-CEN = 1544.0
+CEN = 1552.0
 NW = 2048 + 3 * G
-YD = 3104
-THR = 241.0 * 65536
-M32, M64 = 1.5 * 2 ** 28, 1.5 * 2 ** 29
-DML = 2176
-SC, SV, SVL = 272, 120, 72
-LV = (128, 86, 86)
-UV = 12
-CV = 9
-RV = (8, 8, 8)
+YD, YL = 4096, 3104
+DK = 2 ** 17
+THR = 121.0 * DK
+M1, M32, M64 = 1.5 * 2 ** 23, 1.5 * 2 ** 28, 1.5 * 2 ** 29
+AO = 32.0
+SC = 288
+PW = (SC, SC, SC, SC, SC, 192, 96, 64)
+PV = (144, 136, 130, 120, 120, 80, 40, 28)
+NF = (2 * SC, 1040, 1296, 1552, V)
+LV = ((32, 32, 32, 32), (30, 26, 28, 32), (30, 26, 28, 32))
+UV = 4
+WV = 20
+RW = 130
+SX = (24, 33, 34)
+CV = 8
 
 F32, BF, F16, I32, U16 = "float32", "bfloat16", "float16", "int32", "uint16"
 SB = {
-    "NI": (V, I32), "NU": (V, U16), "N": (NW, F32), "N2": (G, F32), "A": (2048, I32),
-    "Y": (2 * YD, BF), "X": (3104, BF), "R": (2048, BF), "Z": (2048, BF), "DD": (V, BF),
-    "GV0": (2048, BF), "GV1": (2048, BF), "GA0": (2560, BF), "GA1": (2560, BF),
-    "MX0": (2048, BF), "MX1": (2048, BF), "EE": (17 * 256, BF), "RMP": (8192, BF),
+    "NI": (V, I32), "NU": (V, U16), "N": (NW, F32), "N2": (G, F32), "A": (V, I32), "AF": (V + 32, F32),
+    "Y": (YD + YL, BF), "X": (3104, BF), "R": (2048, BF), "Z": (2048, BF), "DD": (V, BF),
+    "GV0": (2304, BF), "GV1": (2304, BF), "GA0": (2816, BF), "GA1": (2816, BF),
+    "MX0": (2048, BF), "MX1": (2048, BF), "EE": (17 * 256, BF), "RMP": (64 * RW, BF),
     "T1": (3 * SC, BF), "T2": (3 * SC, BF), "XS": (192 * 3, BF), "XL": (192 * 3, BF), "TX": (256, BF),
-    "IB": (128, BF), "NIB": (128, BF), "IBIG": (128, BF), "I64": (128, BF), "I16": (128, BF), "I31": (128, BF),
-    "I2": (256, BF), "IF": (128, F32), "JF": (128, F32), "BO": (128, BF), "NBO": (128, BF), "NB4": (128, BF),
-    "NB8": (128, BF), "NBU": (256, BF), "B8K": (16, BF),
-    "TRI16": (128, BF), "TRI": (128, BF), "ONES": (128, BF), "B8": (80, BF), "B8F": (16, F32), "SEL": (2048, BF),
-    "WM": (256, F32), "IOI": (256, F32), "IOS": (256, F32), "RAMP": (128, BF), "IO4": (64, BF), "TN": (128, F32),
-    "TM": (128, F32), "KR": (256, BF), "C15": (320, BF), "RB": (256, F32), "C256": (128, BF), "RZ": (128 * CV, BF),
-    "DM": (DML, BF), "DE": (DML, BF), "DS": (DML, BF), "MK": (16, BF), "SCB": (16, BF),
+    "IB": (128, BF), "NIB": (128, BF), "IBIG": (128, BF), "I64": (128, BF), "I16": (128, BF),
+    "IF": (128, F32), "JF": (128, F32), "BO": (128, BF), "NBO": (128, BF),
+    "N128": (128, BF), "DQ": (256, BF), "B8K": (16, BF), "GH": (256, BF),
+    "TRI16": (128, BF), "TRI": (128, BF), "ONES": (128, BF), "B8": (80, BF), "B8F": (16, F32), "SEL": (144, BF),
+    "WM": (256, F32), "IOI": (256, F32), "IOS": (256, F32), "RAMP": (146, BF), "TRM": (128, BF),
+    "TRA": (128, BF), "N384": (128, BF), "IO4": (64, BF), "TN": (128, F32),
+    "TM": (128, F32), "KR": (256, BF), "C15": (192, BF), "RB": (128, F32), "C256": (128, BF), "RZ": (128 * CV, BF),
+    "DE": (384, BF), "DS": (384, BF), "MK": (256, BF), "RM": (128, BF), "SCB": (16, BF),
     "sm": (16 * 48, F32), "si": (16 * 12, I32), "su": (16 * 12, U16), "sb": (16 * 8, BF),
     "AU": (256, U16), "AH": (256, F16), "AT": (256, F16), "NH": (256, F16), "EB": (256, BF), "MP": (256, BF),
     "MM": (256, BF), "RR": (256, BF), "X1": (256, F16), "X2": (256, BF), "PP": (17 * 128, BF), "DB": (256, BF),
-    "S1": (64, BF), "S2": (64, BF), "CS": (128, F32), "CS2": (128, F32), "DW": (128, F32), "F": (128, BF),
-    "FK": (128, BF), "CC": (144, BF), "CUM": (128, F32), "CMP": (256, BF), "CRP": (256, BF),
+    "S1": (64, BF), "S2": (80, BF), "CS": (128, F32), "CS2": (128, F32), "DW": (128, BF), "F": (128, BF),
+    "TRQ": (128, BF), "CC": (144, BF), "CUM": (128, F32), "CMP": (256, BF), "CRP": (256, BF),
     "LBU": (256, U16), "LBH": (256, F16), "XB": (256, BF), "LUU": (256, U16), "LUH": (256, F16),
     "SC1": (512, F32), "BC": (256, F32), "BC2": (256, F32), "BT": (256, F32),
     "OH": (256, F32), "NL": (256, F32), "RG": (256, BF), "YB": (256, BF), "YW": (256, BF), "YO": (256, BF),
-    "ZN": (256, BF), "RN": (256, BF), "WR": (256, F16), "NM": (256, BF), "BM": (256, F32), "AN": (256, F32),
+    "ZN": (256, BF), "RN": (256, BF), "NM": (256, BF), "BM": (256, BF), "AN": (256, F32), "PB": (256, F32),
+    "WR": (256, F32), "YC": (768, BF),
 }
 SCRATCH = {k: ("sbuf", [128, n], d) for k, (n, d) in SB.items()}
 SCRATCH["LT"] = ("sbuf", [128, 16, 32], F32)
+SCRATCH["ZB"] = ("sbuf", [128, 2, 144], F16)
 for _k in range(8):
     SCRATCH["p%d" % _k] = ("psum", [128, 512], F32)
-NDMA, NMSG = 16, 8
+NDMA, NMSG = 16, 9
 SEMAPHORES = ["cv", "ca", "cp", "cg"] + ["d%d" % k for k in range(NDMA)] + ["r%d" % k for k in range(NMSG)] + \
              ["l%d" % k for k in range(NMSG)]
 
@@ -53,21 +62,26 @@ def rank_program(g, core, T, topo):
     n = len(T.cores)
     dst = T.cores[(rank - 1) % n]
     rid, pid = topo.addr(dst)[0], topo.addr(dst)[1]
-    engs = topo.engines(core, dst)[::2]
-    mask = sum(1 << e for e in engs)
-    neng = len(engs)
+    engs = topo.engines(core, dst)
+    engs = [engs[1::4] if 5 <= k < 8 else engs[::2] for k in range(NMSG)]
     Q = {"v": g.vector, "a": g.scalar, "p": g.tensor, "g": g, "s": g.sync}
     ops, hist, cnt = [], {}, {"d": 0}
 
     def ap(name, a=0, b=None, s=1, p0=0, p1=128):
         b = T[name].shape[-1] if b is None else b
-        return (T[name][p0:p1, a:b:s] if s > 1 else T[name][p0:p1, a:b], name, a, b)
+        return (T[name][p0:p1, a:b:s] if s > 1 else T[name][p0:p1, a:b], name, a, b, s)
 
     def ind(win, off):
-        return (win[0].indirect(off[0]), win[1], win[2], win[3], off)
+        return (win[0].indirect(off[0]), win[1], win[2], win[3], 1, off)
+
+    def cand(name, t):
+        return ap(name, t, t + 7 * 255 + 1, 7)
+
+    def whole(name, pattern):
+        return (pattern, name, 0, 1, 1)
 
     def lt(a):
-        return (T["LT"][:, :, a:a + 16], "LT", 0, 512)
+        return whole("LT", T["LT"][:, :, a:a + 16])
 
     slots = {"sm": {}, "si": {}, "su": {}, "sb": {}}
 
@@ -85,20 +99,21 @@ def rank_program(g, core, T, topo):
         for w, xs in ((False, reads), (True, writes)):
             for x in xs:
                 if isinstance(x, tuple):
-                    acc.append((x[1], x[2], x[3], w))
-                    if len(x) > 4:
-                        acc.append((x[4][1], x[4][2], x[4][3], False))
-        for name, a, b, w in acc:
+                    acc.append(x[1:5] + (w,))
+                    if len(x) > 5:
+                        acc.append(x[5][1:5] + (False,))
+        for name, a, b, s, w in acc:
             ps = name[0] == "p" and name[1:].isdigit()
-            for (a2, b2, w2, j) in hist.get(name, []):
+            for (a2, b2, s2, w2, j) in hist.get(name, []):
                 o = ops[j]
                 same = o["q"] == q and o["sem"] is None and sem is None
                 if same and q == "p":
                     continue
-                if (ps and not same) or ((w or w2) and a < b2 and a2 < b):
+                apart = same and s == s2 and (a - a2) % s
+                if (ps and not same) or ((w or w2) and a < b2 and a2 < b and not apart):
                     deps.add(j)
-        for name, a, b, w in acc:
-            hist.setdefault(name, []).append((a, b, w, i))
+        for name, a, b, s, w in acc:
+            hist.setdefault(name, []).append((a, b, s, w, i))
         ops.append({"q": q, "fn": fn, "deps": deps, "sem": sem, "mark": False})
 
     def x0(x):
@@ -126,6 +141,9 @@ def rank_program(g, core, T, topo):
         add("a", lambda: g.scalar.activation(o[0], a[0], f, bias=x0(bias), scale=scale, accum_out=x0(acc)),
             [a, bias], [o, acc])
 
+    def put(o, a):
+        add("a", lambda: g.scalar.activation(o[0], a[0], AF.Silu), [a], [o])
+
     def mm(o, l, r, start, stop):
         add("p", lambda: g.tensor.matmul(o[0], l[0], r[0], start, stop), [l, r], [o])
 
@@ -138,17 +156,18 @@ def rank_program(g, core, T, topo):
     def sel(o, a, pat, op, fill, base, cm):
         add("g", lambda: g.affine_select(o[0], a[0], pat, op, float(fill), base, cm), [a], [o])
 
-    def dma(q, o, a, reads, writes):
+    def dma(q, o, a, reads, writes, **how):
         s = "d%d" % cnt["d"]
         cnt["d"] += 1
-        add(q, lambda: Q[q].dma_start(o, a), reads, writes, sem=(s, 16, True))
+        add(q, lambda: Q[q].dma_start(o, a, **how), reads, writes, sem=(s, 16, True))
 
     def send(k, o, a):
+        mask = sum(1 << e for e in engs[k])
         add("g", lambda: g.remote_dma(o[0], a[0], T.sem["r%d" % k], T.sem["l%d" % k], pid, rid, mask), [a], [],
-            sem=("l%d" % k, neng, False))
+            sem=("l%d" % k, len(engs[k]), False))
 
     def landed(k, o):
-        add("x", None, [], [o], sem=("r%d" % k, neng, False))
+        add("x", None, [], [o], sem=("r%d" % k, len(engs[k]), False))
 
     def P(k, a=0, b=512, s=1, p0=0, p1=128):
         return ap("p%d" % k, a, b, s, p0, p1)
@@ -172,77 +191,96 @@ def rank_program(g, core, T, topo):
         sel(o, o, [[-x[0], x[1]] for x in pat], ge, 0, 0, 1)
         sel(o, o, pat, ge, 0, 15, -1)
 
-    landed(0, ap("Y", V, W))
+    landed(0, ap("Y", V, V + G // 2))
+    landed(8, ap("Y", V + G // 2, W))
     landed(1, ap("X", V, W))
     for t in range(3):
         landed(2 + t, ap("N", 2048 + G * t, 2048 + G * (t + 1)))
         landed(5 + t, ap("XL", 192 * t, 192 * t + 192))
     pieces = ((0, 2 * SC), (2 * SC, 4 * SC), (4 * SC, V))
-    dma("s", T["Y"][:, 0:G], T.lab[:, 0:G], [], [ap("Y", 0, G)])
+    for a, b in ((0, G // 2), (G // 2, G)):
+        dma("s", T["Y"][:, a:b], T.lab[:, a:b], [], [ap("Y", a, b)])
     dma("s", T["NI"][:, 0:2 * SC], T.nb[:, 0:2 * SC], [], [ap("NI", 0, 2 * SC)])
     dma("s", T["Y"][:, G:V], T.lab[:, G:V], [], [ap("Y", G, V)])
-    iota(zero, [[0, 128]], 0)
-    diag("IB", 1.0)
-    diag("NIB", -1.0)
+    b8, b8a, b8b, b8n, b8k = [ap("B8", 16 * k, 16 * k + 8) for k in range(5)]
+    ms(zero, 0.0)
     iota(sl("si", "p", 0, 1), [[0, 1]], 0, 1)
-    iota(sm("io16"), [[1, 16]], 0)
-    send(0, ap("Y", V, W), ap("Y", 0, G))
+    diag("IB", 1.0)
+    block(b8, 1, [[16, 8]])
+    send(0, ap("Y", V, V + G // 2), ap("Y", 0, G // 2))
+    send(8, ap("Y", V + G // 2, W), ap("Y", G // 2, G))
     first = len(ops) - 1
+    iota(ap("IOI"), [[0, 16], [1, 16]], 0)
     for a, b in pieces[1:]:
         dma("s", T["NI"][:, a:b], T.nb[:, a:b], [], [ap("NI", a, b)])
         ops[-1]["deps"].add(first)
     dma("s", T["A"][:, 0:V], T.asc[:, :], [], [ap("A", 0, V)])
-    dma("s", T["X"][:, 0:V], T.xf[:, :], [], [ap("X", 0, V)])
-    ms(ap("Y", W, YD), 0.0)
-    dma("s", T["Y"][:, YD:2 * YD], T["Y"][:, 0:YD], [ap("Y", 0, YD)], [ap("Y", YD, 2 * YD)])
-    ms(ap("DM"), 1.0)
-    ms(ap("X", W, W + 1), 31.0)
+    first = len(ops) - 1
+    ms(ap("X", 0, V), 16.0)
+    act(ap("AF", 0, V), ap("X", 0, V), AF.Silu, scale=AO / 16)
+    ms(ap("X", W, W + 1), 0.0)
     ms(ap("X", W + 1, 3104), 63.0)
-    ms(ap("N", V, 2048), float(W + 1))
-    ms(ap("R", V, 2048), 0.0)
-    ms(ap("XS"), 0.0)
-    act(ap("SEL"), ap("DM", 0, 2048), scale=0.0)
-    act(ap("PP"), ap("DM"), scale=0.0)
-    act(ap("DD"), ap("DM", 0, V), scale=0.0)
-    act(ap("RZ"), ap("DM", 0, 128 * CV), AF.Copy)
-    ts(sl("si", "q", 0, 1), sl("si", "p", 0, 1), 15, ALU.bitwise_and)
-    qf = sm("col", 0, 1)
-    cp(qf, sl("si", "q", 0, 1))
-    m0 = sm("col", 1, 2)
-    ts(m0, qf, 0.0, eq)
-    ts(sm("col", 2, 3), m0, 16.0, mul, qf, ad)
-    ts(sm("col", 2, 3), sm("col", 2, 3), -1.0, ad)
-    qt = [qf, sm("col", 2, 3)]
-    ts(sm("col", 3, 4), qf, 3.0, ad, qf, mul)
-    ts(sl("su", "ends", 0, 1), sm("col", 3, 4), 8.0, mul, 15.0, ad)
-    ts(ap("SCB"), sm("io16"), 16.0, mul, qf, ad)
-    ts(sm("dum"), ap("SCB"), float(V), ad)
-    ts(sm("sh"), ap("SCB"), 0.5, ad)
-    bc = sl("su", "bc")
-    cp(bc, sm("io16"))
-    ts(sm("rev"), sm("io16"), -1.0, mul, 15.0, ad)
-    ts(ap("MK"), sm("rev"), qf, ltn)
+    ms(ap("SEL"), 0.0)
     e8 = sm("col", 4, 5)
     ms(e8, 0.0)
     ms(ap("CC", 0, 1), 0.0)
-    ms(ap("DW", 112, 128), 0.0)
+    ms(ap("DW"), 0.0)
+    ts(sl("si", "q", 0, 1), sl("si", "p", 0, 1), 15, ALU.bitwise_and)
+    ts(ap("NIB"), ap("IB"), -1.0, mul)
+    qf = sm("col", 0, 1)
+    cp(qf, sl("si", "q", 0, 1))
+    cp(ap("SEL", 15, 143, 16), b8)
+    m0 = sm("col", 1, 2)
+    ts(m0, qf, 0.0, eq)
+    for o, val in ((b8a, DK), (b8b, 2 * DK), (b8n, -DK), (b8k, 512), (ap("B8K", 0, 8), -DK),
+                   (ap("B8K", 8, 16), 512), (ap("B8F", 0, 8), 1)):
+        ts(o, b8, float(val), mul)
+    ts(sm("col", 2, 3), m0, 16.0, mul, qf, ad)
+    ms(whole("ZB", T["ZB"][:, :, :]), 0.0)
+    ts(sm("col", 2, 3), sm("col", 2, 3), -1.0, ad)
+    qt = [qf, sm("col", 2, 3)]
+    nq, qa, dum = [[sm(k, j, j + 1) for j in range(2)] for k in ("nq", "qa", "dum")]
+    for j in range(2):
+        ts(nq[j], qt[j], -1.0, mul)
+        ts(qa[j], qt[j], AO, ad)
+        ts(dum[j], qf, float(V + 16 * j), ad)
+    for name, val in (("I64", 1.0 / 64), ("I16", 16.0), ("IBIG", 2.0 ** 26), ("N128", -128.0), ("N384", -384.0),
+                      ("IF", 1.0)):
+        act(ap(name), ap("IB"), scale=val)
+    for j in range(2):
+        ts(ap("DQ", 128 * j, 128 * j + 128), ap("NIB"), qa[j], mul)
     cp(ap("NU", *pieces[0]), ap("NI", *pieces[0]))
     cp(ap("N", *pieces[0]), ap("NI", *pieces[0]))
+    io16 = ap("IOI", 0, 16)
+    bc = sl("su", "bc")
+    cp(bc, io16)
+    for j in range(2):
+        ts(sl("su", "bp", 8 * j, 8 * j + 8), ap("IOI", 0, 8), 2.0, mul, float(j), ad)
+    ts(ap("SCB"), io16, 16.0, mul, qf, ad)
+    ts(ap("WM"), ap("IOI"), qf, eq)
+    ts(sm("sh"), ap("SCB"), 0.5, ad)
+    ts(ap("MK"), ap("IOI"), qf, ad, 15.0, gt)
+
+    def pick(q):
+        return ap("SEL", 15 - q, 143 - q)
 
     def consts_a():
-        block(ap("B8", 0, 8), 1, [[16, 8]])
-        for q in range(16):
-            sel(ap("SEL", 128 * q + q, 128 * q + 128, 16), ap("B8", 0, 8), [[0, 8]], ge, 0, 0, 0)
-        diag("I64", 1.0 / 64)
-        diag("I31", 15.5)
         iota(ap("ONES"), [[0, 128]], 1)
         sel(ap("TRI"), ap("ONES"), [[1, 128]], ge, 0, 0, -1)
-        iota(ap("IO4"), [[4, 64]], 4)
+        sel(ap("TRM"), ap("TRI"), [[-1, 128]], ne, -255, 0, 1)
+        sel(ap("TRA"), ap("TRI"), [[-1, 128]], ne, 256, 0, 1)
+        iota(ap("IO4"), [[2, 64]], -510)
         iota(ap("C15", 0, 64), [[0, 64]], -15)
-        iota(ap("C15", 192, 320), [[0, 128]], 0)
         iota(ap("RAMP", 0, 16), [[2, 16]], -15)
-        iota(ap("RAMP", 16, 128), [[32, 112]], 32)
-        iota(ap("IOI"), [[0, 16], [1, 16]], 0)
+        iota(ap("RAMP", 16, 130), [[32, 114]], 32)
+        iota(ap("RAMP", 130, 146), [[2, 16]], -17)
+        for t in range(3):
+            sel(ap("YC", 256 * t, 256 * t + 256), cand("Y", t), [[0, 256]], ge, 0, 0, 0)
+        iota(ap("PP"), [[0, 17 * 128]], 0)
+        iota(ap("DD"), [[0, V]], 0)
+        dma("g", T["X"][:, 0:V], T.xf[:, :], [], [ap("X", 0, V)], accum_op=ad)
+        ops[-1]["deps"].add(first)
+        iota(ap("XS"), [[0, 192 * 3]], 0)
 
     def consts_b():
         iota(ap("F", 0, 112), [[0, 112]], 0)
@@ -250,44 +288,44 @@ def rank_program(g, core, T, topo):
         diag("TN", 2.0 / 32)
         sel(ap("TN"), ap("TN"), [[-1, 128]], ne, -1.0 / 32, 1, 1)
         sel(ap("TN"), ap("TN"), [[-1, 128]], ne, -1.0 / 32, -1, 1)
-        sel(ap("TN", 111, 112), ap("TN", 111, 112), [[0, 1]], ne, 1.0 / 32, -111, 1)
         diag("TM", -2.0)
         sel(ap("TM"), ap("TM"), [[-1, 128]], ne, 1.0, 1, 1)
         sel(ap("TM"), ap("TM"), [[-1, 128]], ne, 1.0, -1, 1)
         for col, off, val in ((0, 0, -1.0), (0, 1, 0.0), (15, 0, -13.0), (15, 1, 15.0), (15, -1, 0.0)):
             sel(ap("TM", col, 128, 16), ap("TM", col, 128, 16), [[-16, 8]], ne, val, off - col, 1)
+        ta = ap("TM", 0, 32, 1, 0, 32)
+        iota(ta, [[0, 32]], 0)
+        for off, val in enumerate((-1.0, 2.0, -1.0)):
+            sel(ta, ta, [[-1, 32]], ne, val, -off, 1)
+        sel(ta, ta, [[16, 2], [0, 16]], ge, 0, 15, -1)
         block(ap("BO"), 1, [[16, 8], [0, 16]])
         sel(ap("TRI16"), ap("BO"), [[1, 128]], ge, 0, 0, -1)
+        sel(ap("TRQ"), ap("TRI16"), [[-1, 128]], ne, 256, 0, 1)
         iota(ap("C256"), [[0, 128]], 256)
+        iota(ap("RZ"), [[0, 128 * CV]], 1)
         iota(ap("RZ", 0, 128 * CV, 128), [[0, CV]], 0)
         iota(ap("IOS"), [[1, 256]], 0)
-        diag("I16", 16.0)
         send(1, ap("X", V, W), ap("X", 0, G))
-        for k, val in enumerate((65536, 131072, -65536, -512)):
-            block(ap("B8", 16 * k + 16, 16 * k + 24), val, [[16, 8]])
-        sel(ap("B8K", 0, 16, 2), ap("B8", 48, 56), [[0, 8]], ge, 0, 0, 0)
-        sel(ap("B8K", 1, 16, 2), ap("B8", 64, 72), [[0, 8]], ge, 0, 0, 0)
-        block(ap("NBU"), -65536, [[16, 8], [0, 32]])
-        sel(ap("NBU"), ap("NBU"), [[0, 8], [-1, 2], [0, 16]], ge, 0, 0, 0)
+        iota(ap("N", V, 2048), [[0, 256]], W + 1)
+        iota(ap("R", V, 2048), [[0, 256]], 0)
+        block(ap("NBO"), -DK, [[16, 8], [0, 16]])
+
+    def consts_c():
+        kinds = [[1, 2], [0, 128]]
         iota(ap("KR"), [[0, 16], [4096, 16]], 0)
         sel(ap("KR"), ap("KR"), [[0, 256]], ne, CEN, -1, 1)
-        sel(ap("KR"), ap("KR"), [[0, 256]], ne, 0, -2, 1)
-        sel(ap("KR"), ap("KR"), [[0, 8], [1, 2], [0, 16]], ne, 496 * 512, -5, 2)
-        iota(ap("I2"), [[0, 256]], 0)
-        sel(ap("I2"), ap("I2"), [[-16, 8], [0, 2], [-1, 16]], ne, 1, 0, 1)
-        iota(ap("RB"), [[0, 256]], 0)
-        sel(ap("RB", 0, 256, 16), ap("RB", 0, 256, 16), [[0, 16]], ne, 2.0 ** 30, 0, 0)
-        block(ap("B8F", 0, 8), 1, [[16, 8]])
-        block(ap("NBO"), -65536, [[16, 8], [0, 16]])
-        sel(ap("NB8"), ap("NBO"), [[0, 8], [-1, 16]], ge, 0, 7, 0)
-        diag("IBIG", 2.0 ** 25)
-        diag("IF", 1.0)
-        diag("JF", 1.0, -127, 1)
-        for c in range(16):
-            o = 8 * c * (c + 1)
-            sel(ap("DM", o, o + 16), ap("MK"), [[0, 16]], ge, 0, 0, 0)
+        sel(ap("KR"), ap("KR"), kinds, ne, -120 * DK, -4, 2)
+        sel(ap("KR"), ap("KR"), kinds, ne, 0, -5, 2)
+        sel(ap("KR"), ap("KR"), kinds, ne, 0, -7, 2)
+        iota(ap("RB"), [[0, 128]], 0)
+        sel(ap("RB", 0, 128, 16), ap("RB", 0, 128, 16), [[0, 8]], ne, 2.0 ** 30, 0, 0)
+        iota(ap("JF"), [[0, 128]], 0)
+        sel(ap("JF"), ap("JF"), [[-16, 2], [-32, 4], [1, 16]], ne, 1, -15, 1)
+        iota(ap("RM"), [[0, 128]], 1)
+        iota(ap("RM", 0, 128, 16), [[0, 8]], 0)
+        iota(ap("Y", W, YD), [[0, YD - W]], 0)
+        sel(ap("Y", YD, YD + YL), ap("Y", 0, YL), [[0, YL]], ge, 0, 0, 0)
 
-    b8, b8a, b8b, b8n, b8k = [ap("B8", 16 * k, 16 * k + 8) for k in range(5)]
     consts_a()
     consts_b()
 
@@ -301,68 +339,77 @@ def rank_program(g, core, T, topo):
 
     yw = ap("Y", 0, W)
 
-    def cand(name, t):
-        return ap(name, t, t + 7 * 255 + 1, 7)
-
     def prep_n1(t):
-        ts(ap("NH"), cand("N", t), -CEN, ad, m0, mul)
+        ts(ap("NH"), cand("N" if t else "NI", t), -CEN, ad, m0, mul)
         for q in range(16):
-            mm(P(4, 0, 16), ap("SEL", 128 * q, 128 * q + 128), ap("NH", q, 256, 16), q == 0, q == 15)
+            mm(P(4, 0, 16), pick(q), ap("NH", q, 256, 16), q == 0, q == 15)
 
     def prep_n2(t, fill1, fill2):
         ts(sl("su", "n"), P(4, 0, 16), CEN, ad)
         fill1()
-        tt(ap("EB"), ind(yw, sl("su", "n")), ap("Y", YD + t, YD + t + 7 * 255 + 1, 7), sub)
+        tt(ap("EB"), ind(yw, sl("su", "n")), ap("YC", 256 * t, 256 * t + 256), sub)
         fill2()
+
+    def prep_n3():
         ts(ap("MP"), ap("EB"), 2.0, eq, -1.0, mul)
         ts(ap("MM"), ap("EB"), -2.0, eq)
         mm(P(5, 0, 256), ap("NIB"), ap("MP"), True, False)
         mm(P(5, 0, 256), ap("I64"), ap("MM"), False, True)
 
     def prep_a(t):
-        ts(ap("AH"), cand("A", t), 16.0, ad)
+        if t:
+            ts(ap("AH"), cand("AF", t), M1 + 16 - AO, ad, -M1, ad)
+        else:
+            ts(ap("AH"), cand("A", t), 16.0, ad)
         for h in range(2):
             mm(P(6, 128 * h, 128 * h + 128), ap("AH", 128 * h, 128 * h + 128), ap("IB"), True, True)
 
     late = []
-    for c in range(7):
-        a = SC * c
-        w = min(SC, V - a)
-        sv = SV if c < 6 else SVL
-        bank = c & 1 if c < 6 else 7
-        gv, ga = "GV%d" % (c & 1), "GA%d" % (c & 1)
+    at = [sum(PW[:c]) for c in range(9)]
+    banks = (0, 1, 0, 1, 0, 1, 0, 7)
+
+    def zpiece(c, src, bank):
+        late.append(zfrom(src, PW[c], ap("Y", at[c], at[c + 1]), ap("Z", at[c], at[c + 1]), bank))
+
+    def rcopy(c):
+        act(ap("R", at[c], at[c + 1]), P(banks[c], 0, PW[c]), AF.Copy)
+
+    def nfloat(k):
+        cp(ap("N", NF[k], NF[k + 1]), ap("NI", NF[k], NF[k + 1]))
+
+    for c in range(8):
+        a, w, sv, bank = at[c], PW[c], PV[c], banks[c]
+        gv, ga, o = ("GV%d" % (c & 1), "GA%d" % (c & 1), 0) if c < 6 else ("GA%d" % (c & 1), "GA%d" % (c & 1), 16 * sv)
         cp(ap(gv, 0, 16 * sv), ind(yw, ap("NU", a, a + sv)))
-        act(ap(ga, 0, 16 * (w - sv)), ind(yw, ap("NU", a + sv, a + w)), AF.Copy)
-        if 0 < c < 6:
-            act(ap("R", a - SC, a), P((c - 1) & 1, 0, SC), AF.Copy)
-        for f in late:
-            f()
-        late = []
-        if 1 < c < 6:
-            e = a - 2 * SC
-            late.append(zfrom(ap("R", e, e + SC), SC, ap("Y", e, e + SC), ap("Z", e, e + SC), 2 + (c & 1)))
+        act(ap(ga, o, o + 16 * (w - sv)), ind(yw, ap("NU", a + sv, a + w)), AF.Copy)
+        if 0 < c < 7:
+            rcopy(c - 1)
         mm(P(bank, 0, w), ap("NIB"), ap("Y", a, a + w), True, False)
-        for i in range(16):
+        for i in range(16 if c < 6 else 0):
             mm(P(bank, 0, sv), ap("IB"), ap(gv, i, 16 * sv, 16), False, False)
+        while late:
+            late.pop()()
+        if c > 1:
+            zpiece(c - 2, ap("R", at[c - 2], at[c - 1]), 2 + (c & 1))
         for i in range(16):
-            mm(P(bank, sv, w), ap("IB"), ap(ga, i, 16 * (w - sv), 16), False, i == 15)
+            if c < 6:
+                mm(P(bank, sv, w), ap("IB"), ap(ga, i, 16 * (w - sv), 16), False, i == 15)
+            else:
+                mm(P(bank, 0, w), ap("IB"), ap(ga, i, 16 * w, 16), False, i == 15)
         if c in (1, 3):
             cp(ap("NU", *pieces[1 + c // 2]), ap("NI", *pieces[1 + c // 2]))
-        if c in (2, 4):
-            cp(ap("N", *pieces[c // 2]), ap("NI", *pieces[c // 2]))
-        if c == 4:
+        if c == 3:
             prep_n1(0)
-        if c == 5:
+        if c == 4:
             prep_n2(0, lambda: cp(ap("AU"), cand("A", 0)), lambda: prep_a(0))
-    e = 4 * SC
-    late = [zfrom(ap("R", e, e + SC), SC, ap("Y", e, e + SC), ap("Z", e, e + SC), 2)]
-    e = 5 * SC
-    late.append(zfrom(P(1, 0, SC), SC, ap("Y", e, e + SC), ap("Z", e, e + SC), 3))
-    act(ap("R", e, e + SC), P(1, 0, SC), AF.Copy)
-    e = 6 * SC
-    late.append(zfrom(P(7, 0, V - e), V - e, ap("Y", e, V), ap("Z", e, V), 4))
-    for f in late:
-        f()
+            prep_n3()
+    zpiece(6, P(0, 0, PW[6]), 2)
+    rcopy(6)
+    late.pop(0)()
+    nfloat(0)
+    zpiece(7, P(7, 0, PW[7]), 4)
+    while late:
+        late.pop(0)()
 
     def wrap(src, bank, a):
         tt(ap("BC"), ind(src, bc), ap("WM"), mul)
@@ -379,69 +426,55 @@ def rank_program(g, core, T, topo):
     xw = ap("X", 0, W + 2)
     bu = sl("su", "b")
 
+    def lists(t):
+        act(ap("N2"), ap("N", 0, G), bias=float(V))
+        send(2 + t, ap("N", 2048 + G * t, 2048 + G * (t + 1)), ap("N2"))
+
     def newlists():
         for h in range(2):
             mm(P(7, 256 + 128 * h, 384 + 128 * h), half("BC2", h), ap("IF"), False, h == 1)
 
     for t in range(3):
         zw = ap("Z", 0, V)
-        lv = LV[t]
-        mid = (lv + 32 + 256) // 4 * 2
-        parts = {"v0": (0, 48), "v1": (0 if t else 48, lv - 32), "v2": (lv - 32, lv), "a1": (mid, 256), "a2": (lv + 32, mid), "a3": (lv, lv + 32),
-                 "end": (lv - 32, lv + 32)}
-
-        def zg(k):
-            a, b = parts[k]
-            if b > a and k[0] == "v":
-                cp(ap("RMP", 16 * a, 16 * b), ind(zw, ap("AU", a, b)))
-            elif b > a:
-                act(ap("RMP", 16 * a, 16 * b), ind(zw, ap("AU", a, b)), AF.Copy)
-
-        def zsum(k, stop):
-            a, b = parts[k]
-            for i in range(16 if b > a else 0):
-                mm(P(0, a, b), ap("IB"), ap("RMP", 16 * a + i, 16 * b, 16), False, stop and i == 15)
-
-        for k in ("a1", "a2", "a3"):
-            zg(k)
-        mm(P(0, 0, 256), ones(1), ap("C15", 64, 320, 1, 0, 1), True, False)
-        if t:
-            cp(ind(ap("N", 0, 2048), bu), ap("NL"))
-            prep_n1(t)
-            zsum("a1", False)
-            zg("v1")
-            zsum("v1", False)
-            zsum("a2", False)
-            prep_n2(t, lambda: zg("v2"), lambda: (zsum("end", True), prep_a(t)))
+        for k in range(4):
+            a, m, b = 64 * k, 64 * k + LV[t][k], 64 * k + 64
+            cp(ap("RMP", 16 * a, 16 * m), ind(zw, ap("AU", a, m)))
+            act(ap("RMP", 16 * m, 16 * b), ind(zw, ap("AU", m, b)), AF.Copy)
+            for i in range(16):
+                mm(P(k // 3, a, b), ap("IB"), ap("RMP", 16 * a + i, 16 * b, 16), k % 3 + i == 0, k > 1 and i == 15)
+            if t and k == 0:
+                late.pop()()
+            if t and k == 1:
+                prep_a(t)
+        if t == 0:
+            rcopy(7)
         else:
-            for k in ("v0", "v1", "v2"):
-                zg(k)
-            for k in ("v0", "a1", "v1", "a2"):
-                zsum(k, False)
-            act(ap("R", 6 * SC, V), P(7, 0, V - 6 * SC), AF.Copy)
-            ts(ap("WM"), ap("IOI"), qf, eq)
-            zsum("end", True)
-        ts(ap("RR"), P(0, 0, 256), M64, ad, -M64, ad)
-        tt(ap("X1"), P(0, 0, 256), ap("MP"), mul)
-        tt(ap("X2"), P(5, 0, 256), ap("RR"), mul)
+            lists(t)
+        for k, a, b in ((0, 0, 192), (1, 192, 256)):
+            ts(ap("RR", a, b), P(k, a, b), M64, ad, -M64, ad)
+            tt(ap("X1", a, b), P(k, a, b), ap("MP", a, b), mul)
+            tt(ap("X2", a, b), P(5, a, b), ap("RR", a, b), mul)
         cp(ap("AT"), P(6, 0, 256))
-        mm(P(3, 0, 8), half("X1", 0), b8, True, False)
-        mm(P(3, 8, 16), half("X1", 1), b8, False, False)
         for h in range(2):
+            mm(P(3, 8 * h, 8 * h + 8), half("X1", h), b8, h == 0, False)
             mm(P(3, 8 * h, 8 * h + 8), half("X2", h), b8, False, h == 1)
         will = sl("sb", "will")
         ts(will, P(3, 0, 16), e8, le, 2.0, mul)
-        mm(P(3, 16, 32), ap("TRI"), will, True, False)
+        mm(P(3, 16, 32), ap("TRM"), will, True, False)
         mm(P(3, 24, 32), ap("ONES"), sl("sb", "will", 0, 8), False, True)
         for b in (2, 1):
             mm(P(b, 0, 32), ones(1), ap("C15", 0, 32, 1, 0, 1), True, False)
-        tt(sm("rank"), P(3, 16, 32), will, mul)
+        if t == 0:
+            nfloat(1)
+            lists(0)
         die = sl("sb", "die")
         ng = len(range(t, G, 7))
+        ts(die, P(3, 16, 32), -384.0, le, 2.0, mul)
+        act(ap("DB"), ind(die, bc), AF.Copy)
         for gi in range(8):
             for h in range(2):
                 c = 8 * h + gi
-                ts(ap("PP", 128 * c + 64, 128 * c + 128), ap("IO4"), sm("rank", c, c + 1), eq, 2.0, mul)
+                ts(ap("PP", 128 * c + 64, 128 * c + 128), ap("IO4"), P(3, 16 + c, 17 + c), eq, 2.0, mul)
             for h in range(2):
                 c = 8 * h + gi
                 for j in range(2):
@@ -450,57 +483,74 @@ def rank_program(g, core, T, topo):
                        ap("AT", 128 * h + 16 * gi + 8 * j, 128 * h + 16 * gi + 8 * j + 8), False,
                        gi & 3 == 3 and h == 1 and j == 1)
             if gi == 5:
-                ts(sm("ok"), sm("rank"), 256.0, le)
-            if gi == 6:
                 ts(ap("S2", 0, 32), P(2, 0, 32), M32, ad, -M32, ad)
-                tt(die, sm("ok"), will, mul)
-        tt(ap("S1", 0, 32), P(2, 0, 32), ap("S2", 0, 32), sub)
-        act(ap("DB"), ind(die, bc), AF.Copy)
-        for c in range(64):
-            o = 128 * c
-            if c == 8:
+                act(ap("S2", 64, 80), ap("S2", 0, 16), scale=-1.0)
+            if gi == 6:
+                tt(ap("S1", 0, 32), P(2, 0, 32), ap("S2", 0, 32), sub)
+        for h in range(2):
+            mm(P(5, 128 * h, 128 * h + 128), half("DB", h), ap("IB"), True, True)
+        mm(P(4, 0, 256), ap("IB"), cand("X", t), True, False)
+        for h in range(2):
+            mm(P(4, 128 * h, 128 * h + 128), half("DB", h), ap("N128"), False, h == 1)
+
+        def count(c, stop=False):
+            o = RW * c
+            mm(P(0, c >> 3 << 4, (c >> 3 << 4) + 16, 1, 0, 113), ap("RMP", o + 16, o + 129), ap("RMP", o, o + 16),
+               c == 16, stop)
+
+        for c in range(16, 64):
+            o = RW * c
+            if c == 22:
                 ts(ap("S2", 32, 64), P(1, 0, 32), M32, ad, -M32, ad)
-            if c == 12:
+            if c == 26:
                 tt(ap("S1", 32, 64), P(1, 0, 32), ap("S2", 32, 64), sub)
-            ts(ap("RMP", o, o + 128), ap("RAMP"), ap("S1", c, c + 1), mx, ap("S2", c, c + 1), mn)
-            gi = c >> 3
-            mm(P(0, 16 * gi, 16 * gi + 16, 1, 0, 112), ap("RMP", o + 16, o + 128), ap("RMP", o, o + 16),
-               c & 7 == 0, c & 7 == 7)
-            if c == 7:
-                mm(P(4, 0, 256), ap("NIB"), cand("X", t), True, False)
-                for h in range(2):
-                    mm(P(4, 128 * h, 128 * h + 128), half("DB", h), ap("I31"), False, h == 1)
-                for h in range(2):
-                    mm(P(5, 128 * h, 128 * h + 128), half("DB", h), ap("IB"), True, True)
-                act(ap("TX"), P(4, 0, 256), AF.Relu)
+            ts(ap("RMP", o, o + 129), ap("RAMP", 0, 129), ap("S1", c, c + 1), mx, ap("S2", c, c + 1), mn)
+            count(c)
+            if c % 3 == 0:
+                k = c // 3 - 6
+                o = RW * k
+                act(ap("RMP", o, o + 16), ap("RAMP", 130, 146), AF.Relu, bias=ap("S1", k, k + 1), scale=-1.0)
+                act(ap("RMP", o + 16, o + 129), ap("RAMP", 16, 129), AF.Relu, bias=ap("S2", 64 + k, 65 + k))
+                count(k, k == 15)
+            if c == SX[0]:
                 act(cand("DD", t), P(5, 0, 256), scale=(t + 1) / 2.0)
-            if c == 15:
-                mm(P(4, 0, 256), ap("IB"), cand("X", t), True, False)
-                mm(P(4, 0, 256), ap("IB"), ap("TX"), False, True)
-                act(ap("XS", 192 * t, 192 * t + ng), P(4, 0, ng), AF.Copy)
+            if c == SX[1]:
+                act(ap("XS", 192 * t, 192 * t + ng), P(4, 0, ng), AF.Relu)
                 send(5 + t, ap("XL", 192 * t, 192 * t + 192), ap("XS", 192 * t, 192 * t + 192))
-                act(cand("X", t), P(4, 0, 256), AF.Copy)
-            if 23 <= c < 39:
-                q = c - 23
-                mm(P(6, 0, 112), ap("SEL", 128 * q, 128 * q + 128), ap("DD", q, V, 16), q == 0, q == 15)
-            if c == 39:
-                act(ap("DW", 0, 112), P(6, 0, 112), scale=65536.0)
-                act(ap("N2"), ap("N", 0, G), bias=float(V))
-                send(2 + t, ap("N", 2048 + G * t, 2048 + G * (t + 1)), ap("N2"))
-                act(ap("X", V + t, W, 7), ap("XL", 192 * t, 192 * t + ng), AF.Copy)
-        cp(ap("CS", 0, 128, 1, 0, 112), P(0, 0, 128, 1, 0, 112))
-        mm(P(1, 0, 112), ap("CS", 0, 128, 1, 0, 112), ap("TN", 0, 112, 1, 0, 112), True, True)
+                if t == 0:
+                    consts_c()
+            if c == SX[2]:
+                mm(P(6, 0, 112), ap("I64"), ap("DW", 0, 112), True, False)
+            if SX[2] <= c < SX[2] + 16:
+                v = 7 * (c - SX[2]) + t
+                mm(P(6, v >> 4, 112, 7), pick(v & 15), ap("DD", v, V, 112), False, c == SX[2] + 15)
+        act(ap("DW", 0, 112), P(6, 0, 112), scale=65536.0)
+        act(cand("X", t), P(4, 0, 256), AF.Relu)
+        cp(ap("CS", 0, 128, 1, 0, 113), P(0, 0, 128, 1, 0, 113))
+        mm(P(1, 0, 112), ap("CS", 0, 128, 1, 0, 113), ap("TN", 0, 112, 1, 0, 113), True, True)
         mm(P(2, 0, 128), ap("IB"), ap("F"), True, False)
-        if t == 1:
-            cp(ind(ap("R"), bu), ap("RN"))
+
+        def fill(j):
+            if t == 0:
+                ts(cand("AF", 1 + j), cand("A", 1 + j), AO, ad)
+            if t == 1:
+                cp(ind(ap("R"), sl("su", "b", 8 * j, 8 * j + 8)), half("RN", j))
+
+        fill(0)
         cp(ap("CS2", 0, 112), P(1, 0, 112))
         mm(P(2, 0, 112), ap("TM"), ap("CS2", 0, 112), False, True)
+        fill(1)
         if t < 2:
             mm(P(3, 0, 16), ap("ONES"), die, True, True)
         tt(ap("F"), P(2, 0, 128), ap("DW"), gt)
         mm(P(1, 0, 128), ap("BO"), ap("F"), True, True)
         mm(P(1, 128, 256), ap("TRI16"), ap("F"), True, True)
+        if t == 0:
+            nfloat(2)
         scan(ap("CC", 1, 129), P(1, 0, 128), ap("C256"), ad, mn)
+        if t < 2:
+            mm(P(2, 0, 112), ap("TRQ"), ap("F", 0, 112), True, False)
+            mm(P(2, 0, 112), ap("IB"), ap("CC", 0, 112), False, True)
         for c in range(CV, 16):
             act(ap("GA0", 128 * c, 128 * c + 128), ap("CC", 1, 129), AF.Sign, bias=sm("sh", c, c + 1), scale=-1.0,
                 acc=sm("acc", c, c + 1))
@@ -511,210 +561,233 @@ def rank_program(g, core, T, topo):
         tt(ap("CUM"), P(1, 128, 256), ap("CC", 0, 128), ad)
         ts(sl("su", "c", CV, 16), sm("acc", CV, 16), 0.5, mul, 64.0, ad)
         cp(sl("su", "c", 0, CV), ap("MX1", 127, 128 * CV, 128))
-        ts(sl("sb", "c", CV, 16), sm("acc", CV, 16), 0.5, mul, 64.0, ad)
-        cp(sl("sb", "c", 0, CV), ap("MX1", 127, 128 * CV, 128))
         tt(ap("CMP"), ind(ap("CUM"), cu), ap("IOS"), le)
+        cp(cb, cu)
         act(ap("CRP"), ind(ap("IOS", 0, 128), cu), AF.Copy)
-        if t < 2:
-            act(ap("BM"), ap("CRP"), bias=qt[t], scale=16.0)
-        mm(P(7, 0, 16), ap("I16"), cb, True, False)
+        act(ap("X", V + t, W, 7), ap("XL", 192 * t, 192 * t + ng), AF.Copy)
         for q in range(16):
-            mm(P(7, 0, 16), ap("SEL", 128 * q, 128 * q + 128), ap("CMP", q, 256, 16), False, q == 15)
+            mm(P(7, 0, 16), pick(q), ap("CMP", q, 256, 16), q == 0, False)
+        mm(P(7, 0, 16), ap("I16"), cb, False, True)
         if t < 2:
-            ts(ap("FK", 0, 112), ap("CUM", 0, 112), 256.0, gt)
+            act(ap("F", 0, 112), P(2, 0, 112), AF.Relu, bias=-511.0)
             add("v", lambda: g.vector.tensor_reduce(sm("col", 5, 6)[0], P(3, 0, 16)[0], AxisListType.X, ad),
                 [P(3, 0, 16)], [sm("col", 5, 6)])
-            tt(ap("F", 0, 112), ap("F", 0, 112), ap("FK", 0, 112), mul)
             ts(sl("si", "e", 0, 1), sm("col", 5, 6), 0.5, mul)
+        if t == 0:
+            nfloat(3)
         cp(bu, P(7, 0, 16))
         cp(ap("LBU"), ind(ap("N", 0, 2048), bu))
         act(ap("XB"), ind(xw, bu), AF.Copy)
         act(ap("GA0", 16 * UV, 1024), ind(xw, ap("LBU", 128 + UV, 192)), AF.Copy)
         act(ap("GA0", 1024, 2048), ind(xw, ap("LBU", 192, 256)), AF.Copy)
         ts(ap("LBH"), ap("LBU"), -CEN, ad)
+        ts(ap("GH"), ap("LBU"), float(V), ge, 256.0 + G * t, mul)
         cp(ap("GA0", 0, 16 * UV), ind(xw, ap("LBU", 128, 128 + UV)))
-        cp(ap("GV0"), ind(xw, ap("LBU", 0, 128)))
+        cp(ap("GV0", 0, 2048), ind(xw, ap("LBU", 0, 128)))
         for h in range(2):
             mm(P(7, 16 + 8 * h, 24 + 8 * h), half("CMP", h), b8, True, False)
             mm(P(7, 16 + 8 * h, 24 + 8 * h), half("CRP", h), b8, False, True)
-        for h in range(2):
-            mm(P(7, 256 + 128 * h, 384 + 128 * h), half("LBH", h), ap("IB"), True, True)
-        mm(P(2, 0, 256), ap("IB"), ap("XB"), True, True)
-        if t < 2:
-            mm(P(2, 256, 512), ap("BO"), ap("CMP"), True, True)
+        mm(P(2, 0, 128), ap("IB"), half("XB", 0), True, True)
 
         def preload(banks):
             for b in banks:
                 for j in range(4):
                     mm(P(b, 128 * j, 128 * j + 128), ap("NIB"), half("XB", 1), j == 0, False)
 
-        def vmax(h, gb, i, mb, st):
-            tt(ap(mb, 128 * i, 128 * i + 128), P(2, 128 * h, 128 * h + 128), ap(gb, i, 2048, 16), mx)
-            mm(P(h, i, 8 * st, st), ap(mb, 128 * i, 128 * i + 128), b8b, False, False)
+        def vmax(gb, i):
+            tt(ap("MX0", 128 * i, 128 * i + 128), P(2, 0, 128), ap(gb, i, 2048, 16), mx)
+            mm(P(0, i, 128, 16), ap("MX0", 128 * i, 128 * i + 128), b8b, False, False)
 
         def adiff(b, gb, i0, s0=0):
             for j in range(4):
                 mm(P(b, 128 * j + s0, 128 * j + 128), ap("IB"), ap(gb, 16 * s0 + i0 + j, 2048, 16), False, j == 3)
             act(ap("MX1", 128 * i0, 128 * i0 + 512), P(b), AF.Abs)
 
-        def asum(i0, st, stop=False):
+        def asum(i0, stop=False):
             for i in range(i0, i0 + 4):
-                mm(P(1, i, 8 * st, st), ap("MX1", 128 * i, 128 * i + 128), b8a, False, stop and i == i0 + 3)
+                mm(P(1, i, 128, 16), ap("MX1", 128 * i, 128 * i + 128), b8a, False, stop and i == i0 + 3)
 
         for h in range(2):
-            mm(P(h, 0, 256), ones(3), ap("KR", 0, 256, 1, 0, 3), True, False)
-        mm(P(0, 0, 256), half("XB", 0), ap("NBU"), False, False)
-        mm(P(1, 0, 256), half("LBH", 1), ap("I2"), False, False)
+            mm(P(h, 0, 256), ones(4), ap("KR", 0, 256, 1, 0, 4), True, False)
+            mm(P(h, 0, 128), half("GH", h), ap("IB"), False, False)
+            mm(P(h, 128, 256), half("LBH", h), ap("IB"), False, False)
+        mm(P(0, 0, 128), half("XB", 0), ap("NBO"), False, False)
+        mm(P(1, 0, 128), half("LBH", 1), ap("IB"), False, False)
         preload((3, 4, 5, 6))
         for i in range(16):
             mm(P(3 + i // 4, 128 * (i & 3), 128 * (i & 3) + 64), ap("IB"), ap("GA0", i, 1024, 16), False, False)
         for k in range(4):
             adiff(3 + k, "GA0", 4 * k, 64)
         for i in range(16):
-            mm(P(1, 16 + i, 256, 32), ap("GA0", i, 2048, 16), b8k, False, False)
+            mm(P(1, 128 + i, 256, 16), ap("GA0", i, 2048, 16), b8k, False, False)
         for i in range(16):
             mm(P(0, i, 256, 16), ap("GV0", i, 2048, 16), ap("B8K"), False, False)
         for k in range(4):
             for i in range(4 * k, 4 * k + 4):
-                vmax(0, "GV0", i, "MX0", 32)
+                vmax("GV0", i)
             if k < 3:
-                asum(4 * k, 32)
-            if k == 3:
-                mm(P(0, 0, 256), half("LBH", 0), ap("I2"), False, True)
-        if t < 2:
-            ts(sl("si", "e", 1, 2), sl("si", "e", 0, 1), 7, ALU.bitwise_and)
-            ts(ap("NM"), P(2, 256, 512), qt[t], ne)
-            cp(e8, sl("si", "e", 1, 2))
-        asum(12, 32, True)
-        act(lt(0), P(7, 256, 512), AF.Copy)
-        act(lt(16), P(7, 256, 512), AF.Copy)
+                asum(4 * k)
+            if k == 2:
+                asum(12, True)
+        mm(P(0, 0, 128), half("LBH", 0), ap("IB"), False, True)
         act(sm("bT"), P(7, 16, 32), bias=-CEN)
         act(ap("BT"), ind(sm("bT"), bc), AF.Copy)
-        for h in range(2):
-            scan(ap("SC1", 256 * h, 256 * h + 256), ap("RB"), P(h, 0, 256), ad, mn)
         if t < 2:
-            act(ap("RG"), ind(ap("R"), bu), AF.Copy)
-            act(ap("YB"), ind(yw, bu), AF.Copy)
-        ue, ke = ap("SC1", 15, 512, 32), ap("SC1", 31, 512, 32)
+            mm(P(2, 256, 512), ap("BO"), ap("CMP"), True, True)
+        for h in range(2):
+            mm(P(5, 256 + 128 * h, 384 + 128 * h), half("LBH", h), ap("IB"), True, True)
+
+        def least(o, h, a):
+            scan(ap("SC1", o + 128 * h, o + 128 * h + 128), ap("RB"), P(h, a, a + 128), ad, mn)
+
+        least(0, 1, 0)
+        least(256, 1, 128)
+        least(0, 0, 0)
+        if t < 2:
+            act(ap("TX"), P(2, 256, 512), AF.Abs, bias=nq[t])
+            act(ap("NM"), ap("TX"), AF.Sign)
+            mm(P(3, 0, 256), ap("IB"), ap("CRP"), True, False)
+            mm(P(3, 0, 256), ap("N128"), ap("NM"), False, True)
+        act(lt(0), P(5, 256, 512), AF.Copy)
+        act(lt(16), P(5, 256, 512), AF.Copy)
+        if t < 2:
+            act(ap("BM"), P(3, 0, 256), AF.Relu)
+        ue, ke = ap("SC1", 15, 256, 16), ap("SC1", 271, 512, 16)
+        if t < 2:
+            ts(sl("si", "e", 1, 2), sl("si", "e", 0, 1), 7, ALU.bitwise_and)
         cp(sl("si", "u"), ue)
-        ts(sl("si", "k"), ke, 65536.0, mn, 0.0, mx)
-        ts(sl("si", "un"), sl("si", "u"), 4095, ALU.bitwise_and)
         ts(sm("xx"), ue, THR, ltn, 65536.0, mul)
-        ts(sm("gh"), sl("si", "un"), float(V), ge, 256.0 + G * t, mul)
-        tt(sm("need"), sl("si", "k"), sm("xx"), ltn)
-        tt(sm("y4"), sm("gh"), sl("si", "un"), ad)
-        ts(sl("si", "row"), sl("si", "k"), 12, ALU.logical_shift_right)
-        wp = wrap(sm("y4"), 7, 48)
+        ts(sl("si", "un"), sl("si", "u"), 8191, ALU.bitwise_and)
+        if t < 2:
+            cp(e8, sl("si", "e", 1, 2))
+        wp = wrap(sl("si", "un"), 7, 48)
+        least(256, 0, 128)
         asks = sl("sb", "asks")
-        ts(sm("y1"), sm("gh"), 1.0, mn)
-        ts(sl("si", "old"), sl("si", "k"), 4095, ALU.bitwise_and)
-        tt(asks, sm("y1"), sm("need"), mul)
-        mm(P(6, 0, 16), ap("TRI"), asks, True, False)
-        mm(P(6, 8, 16), ap("ONES"), sl("sb", "asks", 0, 8), False, True)
-        rv = RV[t]
-        dbanks = (3, 4, 6)[:(16 - rv) // 4]
-        for h, nb_ in enumerate(("NBO", "NB%d" % rv)):
-            mm(P(h, 0, 128), ones(2), ap("KR", 0, 128, 1, 0, 2), True, False)
-            mm(P(h, 0, 128), half("XB", h), ap(nb_), False, False)
+        ts(sm("y1"), sl("si", "un"), 2048.0, ge)
+        ts(sl("si", "k"), ke, 65536.0, mn)
+        for h in range(2):
+            mm(P(h, 0, 128), ones(4), ap("KR", 0, 128, 1, 0, 4), True, False)
+        mm(P(0, 0, 128), half("XB", 0), ap("NBO"), False, False)
         uu = sl("su", "u")
         ts(uu, wp, 2047.0 + G * (t + 1), mn)
+        need = sl("sb", "need")
+        tt(need, sl("si", "k"), sm("xx"), ltn)
         ts(ap("LUU"), ind(ap("N", 0, 2048 + G * (t + 1)), uu), float(W + 1), mn)
-        act(ap("GA0", 0, 2048), ind(xw, ap("LUU", 0, 128)), AF.Copy)
+        tt(asks, sm("y1"), need, mul)
         act(ap("GA1", 0, 2048), ind(xw, ap("LUU", 128, 256)), AF.Copy)
+        act(ap("GA0", 16 * WV, 2048), ind(xw, ap("LUU", WV, 128)), AF.Copy)
         ts(ap("LUH"), ap("LUU"), -CEN, ad)
         for h in range(2):
             mm(P(5, 128 * h, 128 * h + 128), half("LUH", h), ap("IB"), True, True)
-        tt(ap("OH"), ind(sl("si", "row"), bc), ap("IOI"), eq)
-        preload(dbanks)
+        mm(P(6, 0, 16), ap("TRA"), asks, True, False)
+        mm(P(6, 0, 16), ap("N384"), need, False, False)
+        mm(P(6, 8, 16), ap("ONES"), sl("sb", "asks", 0, 8), False, True)
+        cp(ap("GA0", 0, 16 * WV), ind(xw, ap("LUU", 0, WV)))
+        preload((4, 7, 3))
         for r in range(17):
+            if r == 0:
+                ts(sl("si", "old"), sl("si", "k"), 4095, ALU.bitwise_and)
             if r == 1:
-                ts(sm("y1"), P(6, 0, 16), 64.0, gt)
+                ts(sm("y1"), P(6, 0, 16), -65.0, gt, -2 * THR, mul)
             if r == 2:
-                tt(sm("y1"), sm("y1"), asks, mul)
+                ts(sm("fk"), sl("si", "old"), THR + YD, ad)
+                preload((6,))
             if r == 3:
-                tt(sm("y1"), sm("y1"), sm("need"), ge)
-            if r == 4:
-                ts(sm("y1"), sm("y1"), -256.0 * 65536, mul, 255.0 * 65536, ad)
-            if r == 5:
-                tt(sm("fk"), sm("y1"), sl("si", "old"), ad)
+                tt(sm("fk"), sm("fk"), sm("y1"), ad)
+            if r == 6:
+                ts(sl("si", "row"), sl("si", "k"), 12, ALU.logical_shift_right)
+            if r == 7 and t < 2:
+                ts(whole("ZB", T["ZB"][:, :, 15:143:16]), sl("si", "old"), -CEN, ad)
             tt(ap("EE", 256 * r, 256 * r + 256), P(5, 0, 256), lt(r) if r < 16 else ap("BT"), eq)
             for h in range(2):
                 mm(P(h, 0, 128), ap("IBIG"), ap("EE", 256 * r + 128 * h, 256 * r + 128 * h + 128), False, False)
-            if r == 10:
-                for i in range(16):
-                    mm(P(0, i, 128, 16), ap("GA0", i, 2048, 16), b8n, False, False)
-        for i in range(8):
-            vmax(0, "GA0", i, "MX0", 16)
-        for k, b in enumerate(dbanks):
-            adiff(b, "GA1", rv + 4 * k)
-        for i in range(rv):
-            mm(P(1, i, 128, 16), ap("GA1", i, 2048, 16), b8n, False, False)
-        for i in range(8, 16):
-            vmax(0, "GA0", i, "MX0", 16)
+            if r == 9:
+                mm(P(1, 0, 128), half("LUH", 1), ap("IB"), False, False)
+            if 10 <= r < 14:
+                adiff((4, 7, 3, 6)[r - 10], "GA1", 4 * (r - 10))
+        tt(ap("OH"), ind(sl("si", "row"), bc), ap("IOI"), eq)
+        for i in range(16):
+            mm(P(0, i, 128, 16), ap("GA0", i, 2048, 16), b8n, False, False)
+        for k in range(4):
+            for i in range(4 * k, 4 * k + 4):
+                vmax("GA0", i)
+            if k < 3:
+                asum(4 * k)
         mm(P(0, 0, 128), half("LUH", 0), ap("IB"), False, True)
-        for k in range(len(dbanks) - 1):
-            asum(rv + 4 * k, 16)
-        for i in range(rv):
-            vmax(1, "GA1", i, "MX1", 16)
-        asum(12, 16)
-        mm(P(1, 0, 128), half("LUH", 1), ap("IB"), False, True)
-        mm(P(7, 256, 512), ap("IB"), ap("LBH"), True, False)
-        scan(half("SC1", 0), half("RB", 0), P(0, 0, 128), ad, mn)
+        asum(12, True)
         if t < 2:
-            wo = wrap(sl("si", "old"), 6, 0)
-        scan(half("SC1", 1), half("RB", 0), P(1, 0, 128), ad, mn)
+            act(ap("RG"), ind(ap("R"), bu), AF.Copy)
+            act(ap("YB"), ind(yw, bu), AF.Copy)
+        if t < 2:
+            for h in range(2):
+                for q in range(16):
+                    mm(P(6, 8 * h, 8 * h + 8), whole("ZB", T["ZB"][:, h, 15 - q:143 - q]), ap("IB", q, 128, 16),
+                       h + q == 0, h + q == 16)
+        else:
+            mm(P(7, 256, 512), ap("IB"), ap("LBH"), True, False)
+        for h in range(2):
+            least(0, h, 0)
         tt(sl("si", "w"), ap("SC1", 15, 256, 16), sm("fk"), mn)
+        if t < 2:
+            ts(sl("si", "pw"), sl("si", "w"), 8191, ALU.bitwise_and)
         ts(sl("si", "wn"), sl("si", "w"), 4095, ALU.bitwise_and)
         if t < 2:
-            cp(sl("su", "old"), wo)
-            act(ap("YO"), ind(ap("Y", 0, YD), sl("su", "old")), AF.Copy)
+            cp(sm("pw"), sl("si", "pw"))
+            act(ap("PB"), ind(sm("pw"), bc), AF.Copy)
         tt(sm("dv"), sl("si", "wn"), sl("si", "old"), sub)
         if t < 2:
-            ts(sm("un4"), sm("dv"), 0.0, eq, float(YD), mul)
-            tt(sm("pw"), sm("un4"), sl("si", "wn"), ad)
-            act(ap("AN"), ind(sm("pw"), bc), AF.Copy)
-            wp = wrap(sm("pw"), 3, 0)
+            wp = wrap(sl("si", "pw"), 3, 0)
             for h in range(2):
-                mm(P(5, 128 - 128 * h, 256 - 128 * h), half("AN", h), ap("JF"), True, True)
+                for j in range(2):
+                    mm(P(5, 128 * j + 64 * h, 128 * j + 64 * h + 64), half("PB", h), ap("JF", 64 * j, 64 * j + 64), True, True)
+            mm(P(7, 256, 512), ap("IB"), ap("LBH"), True, False)
         tt(ap("BC2"), ind(sm("dv"), bc), ap("OH"), mul)
+        newlists()
         if t == 2:
-            newlists()
             ts(ap("NL"), P(7, 256, 512), CEN, ad)
             cp(ind(ap("N", 0, 2048), bu), ap("NL"))
             break
-        mm(P(6, 0, 256), ap("IB"), ap("NM"), True, True)
-        cp(sl("su", "w"), wp)
-        act(ap("YW"), ind(ap("Y"), sl("su", "w")), AF.Copy)
-        cp(sm("pww"), wp)
-        ts(sl("su", "wa"), wp, float(V - 1), mn)
-        ts(sm("bad"), wp, float(V), ge, 16384.0, mul)
-        tt(ap("BC"), ind(ap("A", 0, V), sl("su", "wa")), ap("BM"), sub)
-        tt(sm("bad"), sm("bad"), sm("pww"), ad)
-        cp(ap("WR"), P(5, 0, 256))
+        act(ap("WR"), P(5, 0, 256), scale=2.0 ** -14)
+        mm(P(4, 0, 256), ap("I16"), ap("BM"), True, False)
+        mm(P(4, 0, 256), ap("DQ", 128 * t, 128 * t + 128), ap("NM"), False, False)
         mm(P(0, 0, 256), ap("IB"), ap("RG"), True, False)
-        mm(P(0, 0, 256), ap("NIB"), ap("YO"), False, False)
-        mm(P(0, 0, 256), ap("IB"), ap("YW"), False, True)
-        act(ap("TX"), P(0, 0, 256), AF.Square, bias=-3.5, scale=4.5)
-        act(P(1, 0, 256), ap("TX"), AF.Relu, bias=65.0, scale=-1.0)
-        if t == 0:
-            act(ap("RN"), P(0, 0, 256), AF.Copy)
-        newlists()
+        cp(sl("su", "w"), wp)
+        ts(sl("su", "wa"), wp, float(V - 1), mn)
+        ts(sl("su", "old"), P(6, 0, 16), CEN, ad)
+        act(ap("YW"), ind(ap("Y"), sl("su", "w")), AF.Copy)
+        act(ap("YO"), ind(ap("Y", 0, YD), sl("su", "old")), AF.Copy)
+        ts(sm("pww"), wp, 2.0 ** -14, mul)
+        ts(sm("bad"), wp, float(V), ge)
+        tt(ap("X1"), ind(ap("AF", 0, V), sl("su", "wa")), ap("NM"), mul)
+        tt(sm("bad"), sm("bad"), sm("pww"), ad)
+        mm(P(0, 0, 256), ap("IB"), ap("YW"), False, False)
+        mm(P(4, 0, 256), ap("IB"), ap("X1"), False, True)
+        mm(P(0, 0, 256), ap("NIB"), ap("YO"), False, True)
         act(ap("NL"), P(7, 256, 512), bias=CEN)
-        for c in range(16):
-            o = 8 * c * (c + 1)
-            ts(ap("DE", o, o + 16 * c + 16), ap("WR", 240 - 16 * c, 256), sm("pww", c, c + 1), eq, 16384.0, mul)
-        tt(ap("X1"), P(6, 0, 256), ap("BC"), mul)
-        mm(P(6, 256, 512), ap("IF"), ap("BM"), True, False)
-        mm(P(6, 256, 512), ap("IB"), ap("X1"), False, True)
-        act(ap("AN"), P(6, 256, 512), AF.Copy)
-        scan(ap("DS"), ap("DE"), ap("DM"), ad, mul)
-        tt(sm("bad"), ind(ap("DS"), sl("su", "ends", 0, 1)), sm("bad"), ad)
-        tt(ap("ZN"), P(1, 0, 256), ap("YB"), mul)
-        tt(sm("bad"), sm("bad"), sm("dum"), mn)
-        cp(sl("su", "tg"), sm("bad"))
-        cp(ind(ap("A"), sl("su", "tg")), ap("AN"))
-        cp(ind(ap("Z"), bu), ap("ZN"))
-        cp(ap("AU"), cand("A", t + 1))
+        act(ap("AN"), P(4, 0, 256), bias=qa[t])
+        tt(ap("DE", 256, 384), ind(sm("pww"), sl("su", "bp", 8, 16)), ap("WR", 0, 128), eq)
+        tt(ap("DE", 0, 256), ind(sm("pww"), sl("su", "bp")), ap("WR"), eq)
+        scan(ap("DS", 256, 384), ap("RM"), ap("DE", 256, 384), mul, ad)
+        scan(ap("DS", 0, 256), ap("DE", 0, 256), ap("MK"), ad, mul)
+        bad, tg = [[ap(x[1], x[2] + j, x[3], 2) for j in range(2)] for x in (sm("bad"), sl("su", "tg"))]
+        tt(bad[1], bad[1], ap("DS", 271, 384, 16), ad)
+        for j in range(2):
+            tt(bad[j], bad[j], ap("DS", 128 * j + 15, 128 * j + 128, 16), ad)
+        for j in range(2):
+            ts(tg[j], bad[j], 16384.0, mul, dum[j], mn)
+        for k in range(7, -1, -1):
+            put(ind(ap("AF"), sl("su", "tg", 2 * k, 2 * k + 2)), ap("AN", 32 * k, 32 * k + 32))
+            if k == 7:
+                act(ap("TX"), P(0, 0, 256), AF.Square, bias=-3.5, scale=4.5)
+            if k == 6:
+                act(ap("ZN"), ap("TX"), AF.Relu, bias=65.0, scale=-1.0)
+            if k == 5 and t == 0:
+                act(ap("RN"), P(0, 0, 256), AF.Copy)
+        cp(ind(ap("N", 0, 2048), bu), ap("NL"))
+        prep_n1(t + 1)
+        tt(ind(ap("Z"), bu), ap("ZN"), ap("YB"), mul)
+        prep_n2(t + 1, lambda: None, lambda: ts(ap("AU"), cand("AF", t + 1), M1 - AO, ad, -M1, ad))
+        late = [prep_n3]
 
     for k, (a, b) in enumerate(((0, 896), (896, V))):
         dma("sa"[k], T.yn[:, a:b], T["N"][:, a:b], [ap("N", a, b)], [])

@@ -9,22 +9,21 @@ THR = 121.0 * DK
 M1, M32, M64 = 1.5 * 2 ** 23, 1.5 * 2 ** 28, 1.5 * 2 ** 29
 AO = 32.0
 SC = 288
-PW = (SC, SC, SC, SC, SC, 192, 96, 64)
-PV = (144, 136, 130, 120, 120, 80, 40, 28)
-NF = (2 * SC, 1040, 1296, 1552, V)
-LV = ((32, 32, 32, 32), (30, 26, 28, 32), (30, 26, 28, 32))
-UV = 4
-WV = 20
+PW = (192,) * 8 + (96, 96, 64)
+PV = (96, 84, 96, 92, 80, 92, 84, 84, 44, 44, 30)
+NF = (2 * SC, 1000, G, V)
+LV = ((32, 32, 32, 32), (32, 28, 32, 32), (32, 28, 32, 32))
+WV = 26
 RW = 130
-SX = (24, 33, 34)
+SX = (30, 63)
 CV = 8
 
 F32, BF, F16, I32, U16 = "float32", "bfloat16", "float16", "int32", "uint16"
 SB = {
     "NI": (V, I32), "NU": (V, U16), "N": (NW, F32), "N2": (G, F32), "A": (V, I32), "AF": (V + 32, F32),
     "Y": (YD + YL, BF), "X": (3104, BF), "R": (2048, BF), "Z": (2048, BF), "DD": (V, BF),
-    "GV0": (2304, BF), "GV1": (2304, BF), "GA0": (2816, BF), "GA1": (2816, BF),
-    "MX0": (2048, BF), "MX1": (2048, BF), "EE": (17 * 256, BF), "RMP": (64 * RW, BF),
+    "GV0": (2048, BF), "GV1": (128 * CV, BF), "GA0": (4608, BF), "GA1": (4608, BF),
+    "MX0": (2048, BF), "PBO": (128, BF), "B8J": (16, BF), "EE": (17 * 256, BF), "RMP": (64 * RW, BF),
     "T1": (3 * SC, BF), "T2": (3 * SC, BF), "XS": (192 * 3, BF), "XL": (192 * 3, BF), "TX": (256, BF),
     "IB": (128, BF), "NIB": (128, BF), "IBIG": (128, BF), "I64": (128, BF), "I16": (128, BF),
     "IF": (128, F32), "JF": (128, F32), "BO": (128, BF), "NBO": (128, BF),
@@ -32,21 +31,23 @@ SB = {
     "TRI16": (128, BF), "TRI": (128, BF), "ONES": (128, BF), "B8": (80, BF), "B8F": (16, F32), "SEL": (144, BF),
     "WM": (256, F32), "IOI": (256, F32), "IOS": (256, F32), "RAMP": (146, BF), "TRM": (128, BF),
     "TRA": (128, BF), "N384": (128, BF), "IO4": (64, BF), "TN": (128, F32),
-    "TM": (128, F32), "KR": (256, BF), "C15": (192, BF), "RB": (128, F32), "C256": (128, BF), "RZ": (128 * CV, BF),
+    "TM": (128, F32), "KR": (256, BF), "C15": (384, BF), "I2": (128, BF), "RB": (128, F32), "C256": (128, BF), "RZ": (128 * CV, BF),
     "DE": (384, BF), "DS": (384, BF), "MK": (256, BF), "RM": (128, BF), "SCB": (16, BF),
     "sm": (16 * 48, F32), "si": (16 * 12, I32), "su": (16 * 12, U16), "sb": (16 * 8, BF),
-    "AU": (256, U16), "AH": (256, F16), "AT": (256, F16), "NH": (256, F16), "EB": (256, BF), "MP": (256, BF),
+    "AU": (256, U16), "AH": (256, F16), "NH": (256, F16), "EB": (256, BF), "MP": (256, BF),
     "MM": (256, BF), "RR": (256, BF), "X1": (256, F16), "X2": (256, BF), "PP": (17 * 128, BF), "DB": (256, BF),
-    "S1": (64, BF), "S2": (80, BF), "CS": (128, F32), "CS2": (128, F32), "DW": (128, BF), "F": (128, BF),
+    "S1": (128, BF), "CS": (128, F32), "CS2": (128, F32), "DW": (128, BF), "F": (128, BF),
     "TRQ": (128, BF), "CC": (144, BF), "CUM": (128, F32), "CMP": (256, BF), "CRP": (256, BF),
     "LBU": (256, U16), "LBH": (256, F16), "XB": (256, BF), "LUU": (256, U16), "LUH": (256, F16),
-    "SC1": (512, F32), "BC": (256, F32), "BC2": (256, F32), "BT": (256, F32),
+    "SC1": (512, I32), "BC": (256, F32), "BC2": (256, F32), "BT": (256, F32),
     "OH": (256, F32), "NL": (256, F32), "RG": (256, BF), "YB": (256, BF), "YW": (256, BF), "YO": (256, BF),
     "ZN": (256, BF), "RN": (256, BF), "NM": (256, BF), "BM": (256, BF), "AN": (256, F32), "PB": (256, F32),
     "WR": (256, F32), "YC": (768, BF),
 }
 SCRATCH = {k: ("sbuf", [128, n], d) for k, (n, d) in SB.items()}
 SCRATCH["LT"] = ("sbuf", [128, 16, 32], F32)
+SCRATCH["AT"] = ("sbuf", [128, 32, 16], BF)
+SCRATCH["MX1"] = ("sbuf", [128, 16, 128], BF)
 SCRATCH["ZB"] = ("sbuf", [128, 2, 144], F16)
 for _k in range(8):
     SCRATCH["p%d" % _k] = ("psum", [128, 512], F32)
@@ -174,7 +175,7 @@ def rank_program(g, core, T, topo):
 
     eq, ge, gt, le, ltn, ne = ALU.is_equal, ALU.is_ge, ALU.is_gt, ALU.is_le, ALU.is_lt, ALU.not_equal
     ad, sub, mul, mx, mn = ALU.add, ALU.subtract, ALU.mult, ALU.max, ALU.min
-    zero = ap("C15", 64, 192)
+    zero = ap("C15", 256, 384)
 
     def diag(name, val, base=0, step=-1):
         src = zero
@@ -202,7 +203,7 @@ def rank_program(g, core, T, topo):
         dma("s", T["Y"][:, a:b], T.lab[:, a:b], [], [ap("Y", a, b)])
     dma("s", T["NI"][:, 0:2 * SC], T.nb[:, 0:2 * SC], [], [ap("NI", 0, 2 * SC)])
     dma("s", T["Y"][:, G:V], T.lab[:, G:V], [], [ap("Y", G, V)])
-    b8, b8a, b8b, b8n, b8k = [ap("B8", 16 * k, 16 * k + 8) for k in range(5)]
+    b8, b8b, b8n = [ap("B8", 16 * k, 16 * k + 8) for k in range(3)]
     ms(zero, 0.0)
     iota(sl("si", "p", 0, 1), [[0, 1]], 0, 1)
     diag("IB", 1.0)
@@ -232,7 +233,7 @@ def rank_program(g, core, T, topo):
     cp(ap("SEL", 15, 143, 16), b8)
     m0 = sm("col", 1, 2)
     ts(m0, qf, 0.0, eq)
-    for o, val in ((b8a, DK), (b8b, 2 * DK), (b8n, -DK), (b8k, 512), (ap("B8K", 0, 8), -DK),
+    for o, val in ((ap("B8J", 0, 8), DK), (ap("B8J", 8, 16), -4096), (b8b, 2 * DK), (b8n, -DK), (ap("B8K", 0, 8), -DK),
                    (ap("B8K", 8, 16), 512), (ap("B8F", 0, 8), 1)):
         ts(o, b8, float(val), mul)
     ts(sm("col", 2, 3), m0, 16.0, mul, qf, ad)
@@ -245,7 +246,7 @@ def rank_program(g, core, T, topo):
         ts(qa[j], qt[j], AO, ad)
         ts(dum[j], qf, float(V + 16 * j), ad)
     for name, val in (("I64", 1.0 / 64), ("I16", 16.0), ("IBIG", 2.0 ** 26), ("N128", -128.0), ("N384", -384.0),
-                      ("IF", 1.0)):
+                      ("IF", 1.0), ("I2", 2.0)):
         act(ap(name), ap("IB"), scale=val)
     for j in range(2):
         ts(ap("DQ", 128 * j, 128 * j + 128), ap("NIB"), qa[j], mul)
@@ -270,10 +271,10 @@ def rank_program(g, core, T, topo):
         sel(ap("TRM"), ap("TRI"), [[-1, 128]], ne, -255, 0, 1)
         sel(ap("TRA"), ap("TRI"), [[-1, 128]], ne, 256, 0, 1)
         iota(ap("IO4"), [[2, 64]], -510)
-        iota(ap("C15", 0, 64), [[0, 64]], -15)
+        iota(ap("C15", 0, 256), [[0, 256]], -15)
         iota(ap("RAMP", 0, 16), [[2, 16]], -15)
         iota(ap("RAMP", 16, 130), [[32, 114]], 32)
-        iota(ap("RAMP", 130, 146), [[2, 16]], -17)
+        iota(ap("RAMP", 130, 146), [[2, 16]], -13)
         for t in range(3):
             sel(ap("YC", 256 * t, 256 * t + 256), cand("Y", t), [[0, 256]], ge, 0, 0, 0)
         iota(ap("PP"), [[0, 17 * 128]], 0)
@@ -296,8 +297,8 @@ def rank_program(g, core, T, topo):
         ta = ap("TM", 0, 32, 1, 0, 32)
         iota(ta, [[0, 32]], 0)
         for off, val in enumerate((-1.0, 2.0, -1.0)):
-            sel(ta, ta, [[-1, 32]], ne, val, -off, 1)
-        sel(ta, ta, [[16, 2], [0, 16]], ge, 0, 15, -1)
+            sel(ta, ta, [[-1, 32]], ne, val, off, 1)
+        sel(ta, ta, [[-16, 2], [0, 16]], ge, 0, 0, 1)
         block(ap("BO"), 1, [[16, 8], [0, 16]])
         sel(ap("TRI16"), ap("BO"), [[1, 128]], ge, 0, 0, -1)
         sel(ap("TRQ"), ap("TRI16"), [[-1, 128]], ne, 256, 0, 1)
@@ -309,6 +310,7 @@ def rank_program(g, core, T, topo):
         iota(ap("N", V, 2048), [[0, 256]], W + 1)
         iota(ap("R", V, 2048), [[0, 256]], 0)
         block(ap("NBO"), -DK, [[16, 8], [0, 16]])
+        block(ap("PBO"), 4096, [[16, 8], [0, 16]])
 
     def consts_c():
         kinds = [[1, 2], [0, 128]]
@@ -350,23 +352,25 @@ def rank_program(g, core, T, topo):
         tt(ap("EB"), ind(yw, sl("su", "n")), ap("YC", 256 * t, 256 * t + 256), sub)
         fill2()
 
-    def prep_n3():
+    def masks():
         ts(ap("MP"), ap("EB"), 2.0, eq, -1.0, mul)
         ts(ap("MM"), ap("EB"), -2.0, eq)
+
+    def prep_n3():
         mm(P(5, 0, 256), ap("NIB"), ap("MP"), True, False)
         mm(P(5, 0, 256), ap("I64"), ap("MM"), False, True)
 
     def prep_a(t):
         if t:
             ts(ap("AH"), cand("AF", t), M1 + 16 - AO, ad, -M1, ad)
-        else:
-            ts(ap("AH"), cand("A", t), 16.0, ad)
+        mm(P(6, 0, 256), ap("ONES", 0, 128, 1, 0, 1), ap("C15", 0, 256, 1, 0, 1), True, False)
         for h in range(2):
-            mm(P(6, 128 * h, 128 * h + 128), ap("AH", 128 * h, 128 * h + 128), ap("IB"), True, True)
+            mm(P(6, 128 * h, 128 * h + 128), ap("AH", 128 * h, 128 * h + 128), ap("I2"), False, h == 1)
 
     late = []
-    at = [sum(PW[:c]) for c in range(9)]
-    banks = (0, 1, 0, 1, 0, 1, 0, 7)
+    last = len(PW) - 1
+    at = [sum(PW[:c]) for c in range(last + 2)]
+    banks = [c & 1 for c in range(last)] + [7]
 
     def zpiece(c, src, bank):
         late.append(zfrom(src, PW[c], ap("Y", at[c], at[c + 1]), ap("Z", at[c], at[c + 1]), bank))
@@ -377,39 +381,41 @@ def rank_program(g, core, T, topo):
     def nfloat(k):
         cp(ap("N", NF[k], NF[k + 1]), ap("NI", NF[k], NF[k + 1]))
 
-    for c in range(8):
+    for c in range(last + 1):
         a, w, sv, bank = at[c], PW[c], PV[c], banks[c]
-        gv, ga, o = ("GV%d" % (c & 1), "GA%d" % (c & 1), 0) if c < 6 else ("GA%d" % (c & 1), "GA%d" % (c & 1), 16 * sv)
-        cp(ap(gv, 0, 16 * sv), ind(yw, ap("NU", a, a + sv)))
-        act(ap(ga, o, o + 16 * (w - sv)), ind(yw, ap("NU", a + sv, a + w)), AF.Copy)
-        if 0 < c < 7:
+        one = w < 128
+        gb = ("GA0", "GA1", "RMP")[c % 3]
+        cp(ap(gb, 0, 16 * sv), ind(yw, ap("NU", a, a + sv)))
+        act(ap(gb, 16 * sv, 16 * w), ind(yw, ap("NU", a + sv, a + w)), AF.Copy)
+        if 0 < c < last:
             rcopy(c - 1)
         mm(P(bank, 0, w), ap("NIB"), ap("Y", a, a + w), True, False)
-        for i in range(16 if c < 6 else 0):
-            mm(P(bank, 0, sv), ap("IB"), ap(gv, i, 16 * sv, 16), False, False)
+        for i in range(0 if one else 16):
+            mm(P(bank, 0, sv), ap("IB"), ap(gb, i, 16 * sv, 16), False, False)
         while late:
             late.pop()()
         if c > 1:
             zpiece(c - 2, ap("R", at[c - 2], at[c - 1]), 2 + (c & 1))
+        o = 0 if one else sv
         for i in range(16):
-            if c < 6:
-                mm(P(bank, sv, w), ap("IB"), ap(ga, i, 16 * (w - sv), 16), False, i == 15)
-            else:
-                mm(P(bank, 0, w), ap("IB"), ap(ga, i, 16 * w, 16), False, i == 15)
-        if c in (1, 3):
-            cp(ap("NU", *pieces[1 + c // 2]), ap("NI", *pieces[1 + c // 2]))
-        if c == 3:
+            mm(P(bank, o, w), ap("IB"), ap(gb, 16 * o + i, 16 * w, 16), False, i == 15)
+        for a, b in pieces[1:]:
+            if c < last and a == at[c + 2]:
+                cp(ap("NU", a, b), ap("NI", a, b))
+        if c == last - 4:
             prep_n1(0)
-        if c == 4:
-            prep_n2(0, lambda: cp(ap("AU"), cand("A", 0)), lambda: prep_a(0))
-            prep_n3()
-    zpiece(6, P(0, 0, PW[6]), 2)
-    rcopy(6)
+        if c == last - 3:
+            prep_n2(0, lambda: None, lambda: None)
+    cp(ap("AU"), cand("A", 0))
+    zpiece(last - 1, P(banks[last - 1], 0, PW[last - 1]), 3 - (last & 1))
+    rcopy(last - 1)
     late.pop(0)()
-    nfloat(0)
-    zpiece(7, P(7, 0, PW[7]), 4)
-    while late:
-        late.pop(0)()
+    ts(ap("AH"), cand("A", 0), 16.0, ad)
+    zpiece(last, P(7, 0, PW[last]), 4)
+    late.pop(0)()
+    masks()
+    late.pop(0)()
+    prep_n3()
 
     def wrap(src, bank, a):
         tt(ap("BC"), ind(src, bc), ap("WM"), mul)
@@ -442,19 +448,19 @@ def rank_program(g, core, T, topo):
             act(ap("RMP", 16 * m, 16 * b), ind(zw, ap("AU", m, b)), AF.Copy)
             for i in range(16):
                 mm(P(k // 3, a, b), ap("IB"), ap("RMP", 16 * a + i, 16 * b, 16), k % 3 + i == 0, k > 1 and i == 15)
-            if t and k == 0:
-                late.pop()()
-            if t and k == 1:
+            if k == 1:
                 prep_a(t)
         if t == 0:
-            rcopy(7)
+            rcopy(last)
         else:
             lists(t)
         for k, a, b in ((0, 0, 192), (1, 192, 256)):
             ts(ap("RR", a, b), P(k, a, b), M64, ad, -M64, ad)
             tt(ap("X1", a, b), P(k, a, b), ap("MP", a, b), mul)
+            if k:
+                ts(whole("AT", T["AT"][:, :, 8:16]), P(6, 0, 256), M32, ad, -M32, ad)
             tt(ap("X2", a, b), P(5, a, b), ap("RR", a, b), mul)
-        cp(ap("AT"), P(6, 0, 256))
+        tt(whole("AT", T["AT"][:, :, 0:8]), P(6, 0, 256), whole("AT", T["AT"][:, :, 8:16]), sub)
         for h in range(2):
             mm(P(3, 8 * h, 8 * h + 8), half("X1", h), b8, h == 0, False)
             mm(P(3, 8 * h, 8 * h + 8), half("X2", h), b8, False, h == 1)
@@ -462,31 +468,25 @@ def rank_program(g, core, T, topo):
         ts(will, P(3, 0, 16), e8, le, 2.0, mul)
         mm(P(3, 16, 32), ap("TRM"), will, True, False)
         mm(P(3, 24, 32), ap("ONES"), sl("sb", "will", 0, 8), False, True)
-        for b in (2, 1):
-            mm(P(b, 0, 32), ones(1), ap("C15", 0, 32, 1, 0, 1), True, False)
         if t == 0:
-            nfloat(1)
-            lists(0)
+            nfloat(0)
         die = sl("sb", "die")
         ng = len(range(t, G, 7))
         ts(die, P(3, 16, 32), -384.0, le, 2.0, mul)
         act(ap("DB"), ind(die, bc), AF.Copy)
-        for gi in range(8):
+        for gi in (2, 3, 0, 1, 4, 5, 6, 7):
             for h in range(2):
                 c = 8 * h + gi
-                ts(ap("PP", 128 * c + 64, 128 * c + 128), ap("IO4"), P(3, 16 + c, 17 + c), eq, 2.0, mul)
+                ts(ap("PP", 128 * c + 64, 128 * c + 128), ap("IO4"), P(3, 16 + c, 17 + c), eq)
             for h in range(2):
                 c = 8 * h + gi
                 for j in range(2):
                     o = 128 * c + 64 - 64 * j
-                    mm(P(2 - (gi >> 2), 8 * (gi & 3), 8 * (gi & 3) + 8), ap("PP", o, o + 128),
-                       ap("AT", 128 * h + 16 * gi + 8 * j, 128 * h + 16 * gi + 8 * j + 8), False,
-                       gi & 3 == 3 and h == 1 and j == 1)
+                    mm(P((2, 1, 7, 7)[gi // 2], 16 * gi, 16 * gi + 16), ap("PP", o, o + 128),
+                       whole("AT", T["AT"][:, 2 * c + j, :]), gi in (0, 2, 4) and h + j == 0, gi in (1, 3, 7) and h + j == 2)
             if gi == 5:
-                ts(ap("S2", 0, 32), P(2, 0, 32), M32, ad, -M32, ad)
-                act(ap("S2", 64, 80), ap("S2", 0, 16), scale=-1.0)
-            if gi == 6:
-                tt(ap("S1", 0, 32), P(2, 0, 32), ap("S2", 0, 32), sub)
+                cp(ap("S1", 32, 64), P(1, 32, 64))
+        act(ap("S1", 0, 32), P(2, 0, 32), scale=-1.0)
         for h in range(2):
             mm(P(5, 128 * h, 128 * h + 128), half("DB", h), ap("IB"), True, True)
         mm(P(4, 0, 256), ap("IB"), cand("X", t), True, False)
@@ -498,44 +498,50 @@ def rank_program(g, core, T, topo):
             mm(P(0, c >> 3 << 4, (c >> 3 << 4) + 16, 1, 0, 113), ap("RMP", o + 16, o + 129), ap("RMP", o, o + 16),
                c == 16, stop)
 
+        def digit(c, j):
+            a = (c >> 3 << 4) + 8 * j + (c & 7)
+            return ap("S1", a, a + 1)
+
         for c in range(16, 64):
             o = RW * c
-            if c == 22:
-                ts(ap("S2", 32, 64), P(1, 0, 32), M32, ad, -M32, ad)
-            if c == 26:
-                tt(ap("S1", 32, 64), P(1, 0, 32), ap("S2", 32, 64), sub)
-            ts(ap("RMP", o, o + 129), ap("RAMP", 0, 129), ap("S1", c, c + 1), mx, ap("S2", c, c + 1), mn)
+            if c == 24:
+                cp(ap("S1", 64, 128), P(7, 64, 128))
+            ts(ap("RMP", o, o + 129), ap("RAMP", 0, 129), digit(c, 0), mx, digit(c, 1), mn)
             count(c)
             if c % 3 == 0:
                 k = c // 3 - 6
                 o = RW * k
-                act(ap("RMP", o, o + 16), ap("RAMP", 130, 146), AF.Relu, bias=ap("S1", k, k + 1), scale=-1.0)
-                act(ap("RMP", o + 16, o + 129), ap("RAMP", 16, 129), AF.Relu, bias=ap("S2", 64 + k, 65 + k))
+                act(ap("RMP", o, o + 16), ap("RAMP", 130, 146), AF.Relu, bias=digit(k, 0))
+                act(ap("RMP", o + 16, o + 129), ap("RAMP", 16, 129), AF.Relu, bias=digit(k, 1))
                 count(k, k == 15)
             if c == SX[0]:
                 act(cand("DD", t), P(5, 0, 256), scale=(t + 1) / 2.0)
             if c == SX[1]:
                 act(ap("XS", 192 * t, 192 * t + ng), P(4, 0, ng), AF.Relu)
                 send(5 + t, ap("XL", 192 * t, 192 * t + 192), ap("XS", 192 * t, 192 * t + 192))
-                if t == 0:
-                    consts_c()
-            if c == SX[2]:
-                mm(P(6, 0, 112), ap("I64"), ap("DW", 0, 112), True, False)
-            if SX[2] <= c < SX[2] + 16:
-                v = 7 * (c - SX[2]) + t
-                mm(P(6, v >> 4, 112, 7), pick(v & 15), ap("DD", v, V, 112), False, c == SX[2] + 15)
-        act(ap("DW", 0, 112), P(6, 0, 112), scale=65536.0)
+        def mask(a, b):
+            for v in range(t + 7 * a, 7 * b, 7):
+                mm(P(6, v >> 4, 112, 7), pick(v & 15), ap("DD", v, V, 112), False, v > 104)
+
+        mm(P(6, 0, 112), ap("I64"), ap("DW", 0, 112), True, False)
+        mask(0, 10)
         act(cand("X", t), P(4, 0, 256), AF.Relu)
         cp(ap("CS", 0, 128, 1, 0, 113), P(0, 0, 128, 1, 0, 113))
         mm(P(1, 0, 112), ap("CS", 0, 128, 1, 0, 113), ap("TN", 0, 112, 1, 0, 113), True, True)
+        mask(10, 16)
+        act(ap("DW", 0, 112), P(6, 0, 112), scale=65536.0)
         mm(P(2, 0, 128), ap("IB"), ap("F"), True, False)
 
         def fill(j):
-            if t == 0:
-                ts(cand("AF", 1 + j), cand("A", 1 + j), AO, ad)
-            if t == 1:
+            if t == 0 and j:
+                ts(cand("AF", j), cand("A", j), AO, ad)
+            if t == 1 and j < 2:
                 cp(ind(ap("R"), sl("su", "b", 8 * j, 8 * j + 8)), half("RN", j))
 
+        if t == 0:
+            nfloat(1)
+            lists(0)
+            consts_c()
         fill(0)
         cp(ap("CS2", 0, 112), P(1, 0, 112))
         mm(P(2, 0, 112), ap("TM"), ap("CS2", 0, 112), False, True)
@@ -545,8 +551,7 @@ def rank_program(g, core, T, topo):
         tt(ap("F"), P(2, 0, 128), ap("DW"), gt)
         mm(P(1, 0, 128), ap("BO"), ap("F"), True, True)
         mm(P(1, 128, 256), ap("TRI16"), ap("F"), True, True)
-        if t == 0:
-            nfloat(2)
+        fill(2)
         scan(ap("CC", 1, 129), P(1, 0, 128), ap("C256"), ad, mn)
         if t < 2:
             mm(P(2, 0, 112), ap("TRQ"), ap("F", 0, 112), True, False)
@@ -556,11 +561,11 @@ def rank_program(g, core, T, topo):
                 acc=sm("acc", c, c + 1))
         for c in range(CV):
             ts(ap("MX0", 128 * c, 128 * c + 128), ap("CC", 1, 129), ap("SCB", c, c + 1), le)
-        scan(ap("MX1", 0, 128 * CV), ap("RZ", 0, 128 * CV), ap("MX0", 0, 128 * CV), mul, ad)
-        cu, cb = sl("su", "c"), sl("sb", "c")
         tt(ap("CUM"), P(1, 128, 256), ap("CC", 0, 128), ad)
+        scan(ap("GV1", 0, 128 * CV), ap("RZ", 0, 128 * CV), ap("MX0", 0, 128 * CV), mul, ad)
+        cu, cb = sl("su", "c"), sl("sb", "c")
         ts(sl("su", "c", CV, 16), sm("acc", CV, 16), 0.5, mul, 64.0, ad)
-        cp(sl("su", "c", 0, CV), ap("MX1", 127, 128 * CV, 128))
+        cp(sl("su", "c", 0, CV), ap("GV1", 127, 128 * CV, 128))
         tt(ap("CMP"), ind(ap("CUM"), cu), ap("IOS"), le)
         cp(cb, cu)
         act(ap("CRP"), ind(ap("IOS", 0, 128), cu), AF.Copy)
@@ -574,16 +579,17 @@ def rank_program(g, core, T, topo):
                 [P(3, 0, 16)], [sm("col", 5, 6)])
             ts(sl("si", "e", 0, 1), sm("col", 5, 6), 0.5, mul)
         if t == 0:
-            nfloat(3)
+            nfloat(2)
         cp(bu, P(7, 0, 16))
         cp(ap("LBU"), ind(ap("N", 0, 2048), bu))
         act(ap("XB"), ind(xw, bu), AF.Copy)
-        act(ap("GA0", 16 * UV, 1024), ind(xw, ap("LBU", 128 + UV, 192)), AF.Copy)
-        act(ap("GA0", 1024, 2048), ind(xw, ap("LBU", 192, 256)), AF.Copy)
+        for a in (128, 192):
+            act(ap("GA0", 16 * a - 2048, 16 * a - 1024), ind(xw, ap("LBU", a, a + 64)), AF.Copy)
         ts(ap("LBH"), ap("LBU"), -CEN, ad)
         ts(ap("GH"), ap("LBU"), float(V), ge, 256.0 + G * t, mul)
-        cp(ap("GA0", 0, 16 * UV), ind(xw, ap("LBU", 128, 128 + UV)))
         cp(ap("GV0", 0, 2048), ind(xw, ap("LBU", 0, 128)))
+        if t < 2:
+            ts(sl("si", "e", 1, 2), sl("si", "e", 0, 1), 7, ALU.bitwise_and)
         for h in range(2):
             mm(P(7, 16 + 8 * h, 24 + 8 * h), half("CMP", h), b8, True, False)
             mm(P(7, 16 + 8 * h, 24 + 8 * h), half("CRP", h), b8, False, True)
@@ -598,37 +604,43 @@ def rank_program(g, core, T, topo):
             tt(ap("MX0", 128 * i, 128 * i + 128), P(2, 0, 128), ap(gb, i, 2048, 16), mx)
             mm(P(0, i, 128, 16), ap("MX0", 128 * i, 128 * i + 128), b8b, False, False)
 
-        def adiff(b, gb, i0, s0=0):
+        def rows(a, b, c=0, d=128):
+            return (T["MX1"][:, a:b, c:d] if b > a + 1 else T["MX1"][:, a, c:d], "MX1", a, b, 1)
+
+        def adiff(b, gb, i0):
             for j in range(4):
-                mm(P(b, 128 * j + s0, 128 * j + 128), ap("IB"), ap(gb, 16 * s0 + i0 + j, 2048, 16), False, j == 3)
-            act(ap("MX1", 128 * i0, 128 * i0 + 512), P(b), AF.Abs)
+                mm(P(b, 128 * j, 128 * j + 128), ap("IB"), ap(gb, i0 + j, 2048, 16), False, j == 3)
+            act(rows(i0, i0 + 4), P(b), AF.Abs)
 
-        def asum(i0, stop=False):
-            for i in range(i0, i0 + 4):
-                mm(P(1, i, 128, 16), ap("MX1", 128 * i, 128 * i + 128), b8a, False, stop and i == i0 + 3)
+        def asum(a, b, w, stop=False):
+            for i in range(a, b):
+                mm(P(1, i, 16 * w, 16), rows(i, i + 1), ap("B8J", 0, w), False, stop and i == b - 1)
 
+        for b in range(4):
+            for j in range(8):
+                mm(P(3 + b, 64 * j, 64 * j + 64), ap("NIB"), ap("XB", 128 + b // 2 * 64, 192 + b // 2 * 64), j == 0, False)
         for h in range(2):
             mm(P(h, 0, 256), ones(4), ap("KR", 0, 256, 1, 0, 4), True, False)
             mm(P(h, 0, 128), half("GH", h), ap("IB"), False, False)
             mm(P(h, 128, 256), half("LBH", h), ap("IB"), False, False)
-        mm(P(0, 0, 128), half("XB", 0), ap("NBO"), False, False)
-        mm(P(1, 0, 128), half("LBH", 1), ap("IB"), False, False)
-        preload((3, 4, 5, 6))
-        for i in range(16):
-            mm(P(3 + i // 4, 128 * (i & 3), 128 * (i & 3) + 64), ap("IB"), ap("GA0", i, 1024, 16), False, False)
-        for k in range(4):
-            adiff(3 + k, "GA0", 4 * k, 64)
-        for i in range(16):
-            mm(P(1, 128 + i, 256, 16), ap("GA0", i, 2048, 16), b8k, False, False)
+        for b in range(4):
+            if b == 2:
+                mm(P(0, 0, 128), half("XB", 0), ap("NBO"), False, False)
+                mm(P(1, 0, 128), half("LBH", 1), ap("IB"), False, False)
+                mm(P(1, 128, 256), half("XB", 1), ap("PBO"), False, False)
+            for j in range(8):
+                o = b // 2 * 1024
+                mm(P(3 + b, 64 * j, 64 * j + 64), ap("IB"), ap("GA0", o + (b & 1) * 8 + j, o + 1024, 16), False, j == 7)
+        for b in range(4):
+            act(rows((b & 1) * 8, (b & 1) * 8 + 8, b // 2 * 64, b // 2 * 64 + 64), P(3 + b), AF.Abs)
         for i in range(16):
             mm(P(0, i, 256, 16), ap("GV0", i, 2048, 16), ap("B8K"), False, False)
-        for k in range(4):
-            for i in range(4 * k, 4 * k + 4):
-                vmax("GV0", i)
-            if k < 3:
-                asum(4 * k)
-            if k == 2:
-                asum(12, True)
+        for i in range(16):
+            vmax("GV0", i)
+            if i == 5:
+                asum(0, 8, 16)
+            if i == 11:
+                asum(8, 16, 16, True)
         mm(P(0, 0, 128), half("LBH", 0), ap("IB"), False, True)
         act(sm("bT"), P(7, 16, 32), bias=-CEN)
         act(ap("BT"), ind(sm("bT"), bc), AF.Copy)
@@ -653,45 +665,43 @@ def rank_program(g, core, T, topo):
         if t < 2:
             act(ap("BM"), P(3, 0, 256), AF.Relu)
         ue, ke = ap("SC1", 15, 256, 16), ap("SC1", 271, 512, 16)
-        if t < 2:
-            ts(sl("si", "e", 1, 2), sl("si", "e", 0, 1), 7, ALU.bitwise_and)
-        cp(sl("si", "u"), ue)
+        ts(sl("si", "un"), ue, 8191, ALU.bitwise_and)
         ts(sm("xx"), ue, THR, ltn, 65536.0, mul)
-        ts(sl("si", "un"), sl("si", "u"), 8191, ALU.bitwise_and)
         if t < 2:
             cp(e8, sl("si", "e", 1, 2))
         wp = wrap(sl("si", "un"), 7, 48)
         least(256, 0, 128)
         asks = sl("sb", "asks")
         ts(sm("y1"), sl("si", "un"), 2048.0, ge)
-        ts(sl("si", "k"), ke, 65536.0, mn)
+        ts(sl("si", "k"), ke, 65536.0, mn, 0.0, mx)
         for h in range(2):
             mm(P(h, 0, 128), ones(4), ap("KR", 0, 128, 1, 0, 4), True, False)
         mm(P(0, 0, 128), half("XB", 0), ap("NBO"), False, False)
+        preload((4, 6, 3))
         uu = sl("su", "u")
         ts(uu, wp, 2047.0 + G * (t + 1), mn)
         need = sl("sb", "need")
         tt(need, sl("si", "k"), sm("xx"), ltn)
-        ts(ap("LUU"), ind(ap("N", 0, 2048 + G * (t + 1)), uu), float(W + 1), mn)
+        for h in (1, 0):
+            ts(half("LUU", h), ind(ap("N", 0, 2048 + G * (t + 1)), sl("su", "u", 8 * h, 8 * h + 8)), float(W + 1), mn)
         tt(asks, sm("y1"), need, mul)
         act(ap("GA1", 0, 2048), ind(xw, ap("LUU", 128, 256)), AF.Copy)
         act(ap("GA0", 16 * WV, 2048), ind(xw, ap("LUU", WV, 128)), AF.Copy)
         ts(ap("LUH"), ap("LUU"), -CEN, ad)
         for h in range(2):
             mm(P(5, 128 * h, 128 * h + 128), half("LUH", h), ap("IB"), True, True)
-        mm(P(6, 0, 16), ap("TRA"), asks, True, False)
-        mm(P(6, 0, 16), ap("N384"), need, False, False)
-        mm(P(6, 8, 16), ap("ONES"), sl("sb", "asks", 0, 8), False, True)
+        mm(P(5, 256, 272), ap("TRA"), asks, True, False)
+        mm(P(5, 256, 272), ap("N384"), need, False, False)
+        mm(P(5, 264, 272), ap("ONES"), sl("sb", "asks", 0, 8), False, True)
         cp(ap("GA0", 0, 16 * WV), ind(xw, ap("LUU", 0, WV)))
-        preload((4, 7, 3))
+        preload((7,))
         for r in range(17):
             if r == 0:
                 ts(sl("si", "old"), sl("si", "k"), 4095, ALU.bitwise_and)
             if r == 1:
-                ts(sm("y1"), P(6, 0, 16), -65.0, gt, -2 * THR, mul)
+                ts(sm("y1"), P(5, 256, 272), -65.0, gt, -2 * THR, mul)
             if r == 2:
                 ts(sm("fk"), sl("si", "old"), THR + YD, ad)
-                preload((6,))
             if r == 3:
                 tt(sm("fk"), sm("fk"), sm("y1"), ad)
             if r == 6:
@@ -701,10 +711,10 @@ def rank_program(g, core, T, topo):
             tt(ap("EE", 256 * r, 256 * r + 256), P(5, 0, 256), lt(r) if r < 16 else ap("BT"), eq)
             for h in range(2):
                 mm(P(h, 0, 128), ap("IBIG"), ap("EE", 256 * r + 128 * h, 256 * r + 128 * h + 128), False, False)
-            if r == 9:
+            if r == 4:
                 mm(P(1, 0, 128), half("LUH", 1), ap("IB"), False, False)
-            if 10 <= r < 14:
-                adiff((4, 7, 3, 6)[r - 10], "GA1", 4 * (r - 10))
+            if 8 <= r < 12:
+                adiff((4, 7, 3, 6)[r - 8], "GA1", 4 * (r - 8))
         tt(ap("OH"), ind(sl("si", "row"), bc), ap("IOI"), eq)
         for i in range(16):
             mm(P(0, i, 128, 16), ap("GA0", i, 2048, 16), b8n, False, False)
@@ -712,9 +722,10 @@ def rank_program(g, core, T, topo):
             for i in range(4 * k, 4 * k + 4):
                 vmax("GA0", i)
             if k < 3:
-                asum(4 * k)
+                asum(4 * k, 4 * k + 4, 8)
+            if k == 2:
+                asum(12, 16, 8, True)
         mm(P(0, 0, 128), half("LUH", 0), ap("IB"), False, True)
-        asum(12, True)
         if t < 2:
             act(ap("RG"), ind(ap("R"), bu), AF.Copy)
             act(ap("YB"), ind(yw, bu), AF.Copy)
@@ -724,8 +735,9 @@ def rank_program(g, core, T, topo):
                     mm(P(6, 8 * h, 8 * h + 8), whole("ZB", T["ZB"][:, h, 15 - q:143 - q]), ap("IB", q, 128, 16),
                        h + q == 0, h + q == 16)
         else:
-            mm(P(7, 256, 512), ap("IB"), ap("LBH"), True, False)
-        for h in range(2):
+            for h in range(2):
+                mm(P(6 + h, 0, 128), ap("IB"), half("LBH", h), True, False)
+        for h in (1, 0):
             least(0, h, 0)
         tt(sl("si", "w"), ap("SC1", 15, 256, 16), sm("fk"), mn)
         if t < 2:
@@ -741,22 +753,26 @@ def rank_program(g, core, T, topo):
                 for j in range(2):
                     mm(P(5, 128 * j + 64 * h, 128 * j + 64 * h + 64), half("PB", h), ap("JF", 64 * j, 64 * j + 64), True, True)
             mm(P(7, 256, 512), ap("IB"), ap("LBH"), True, False)
+        if t == 2:
+            for h in range(2):
+                tt(half("BC2", h), ind(sm("dv"), sl("su", "bc", 8 * h, 8 * h + 8)), half("OH", h), mul)
+                mm(P(6 + h, 0, 128), half("BC2", h), ap("IF"), False, True)
+                act(half("NL", h), P(6 + h, 0, 128), bias=CEN)
+            for h in range(2):
+                cp(ind(ap("N", 0, 2048), sl("su", "b", 8 * h, 8 * h + 8)), half("NL", h))
+            break
         tt(ap("BC2"), ind(sm("dv"), bc), ap("OH"), mul)
         newlists()
-        if t == 2:
-            ts(ap("NL"), P(7, 256, 512), CEN, ad)
-            cp(ind(ap("N", 0, 2048), bu), ap("NL"))
-            break
-        act(ap("WR"), P(5, 0, 256), scale=2.0 ** -14)
         mm(P(4, 0, 256), ap("I16"), ap("BM"), True, False)
         mm(P(4, 0, 256), ap("DQ", 128 * t, 128 * t + 128), ap("NM"), False, False)
         mm(P(0, 0, 256), ap("IB"), ap("RG"), True, False)
-        cp(sl("su", "w"), wp)
+        ts(sm("pww"), wp, 2.0 ** -14, mul)
+        act(ap("WR"), ind(sm("pww"), sl("su", "bp")), scale=2.0 ** 14)
         ts(sl("su", "wa"), wp, float(V - 1), mn)
+        cp(sl("su", "w"), wp)
         ts(sl("su", "old"), P(6, 0, 16), CEN, ad)
         act(ap("YW"), ind(ap("Y"), sl("su", "w")), AF.Copy)
         act(ap("YO"), ind(ap("Y", 0, YD), sl("su", "old")), AF.Copy)
-        ts(sm("pww"), wp, 2.0 ** -14, mul)
         ts(sm("bad"), wp, float(V), ge)
         tt(ap("X1"), ind(ap("AF", 0, V), sl("su", "wa")), ap("NM"), mul)
         tt(sm("bad"), sm("bad"), sm("pww"), ad)
@@ -765,8 +781,8 @@ def rank_program(g, core, T, topo):
         mm(P(0, 0, 256), ap("NIB"), ap("YO"), False, True)
         act(ap("NL"), P(7, 256, 512), bias=CEN)
         act(ap("AN"), P(4, 0, 256), bias=qa[t])
-        tt(ap("DE", 256, 384), ind(sm("pww"), sl("su", "bp", 8, 16)), ap("WR", 0, 128), eq)
-        tt(ap("DE", 0, 256), ind(sm("pww"), sl("su", "bp")), ap("WR"), eq)
+        tt(ap("DE", 256, 384), P(5, 0, 128), ap("WR", 128, 256), eq)
+        tt(ap("DE", 0, 256), P(5, 0, 256), ap("WR"), eq)
         scan(ap("DS", 256, 384), ap("RM"), ap("DE", 256, 384), mul, ad)
         scan(ap("DS", 0, 256), ap("DE", 0, 256), ap("MK"), ad, mul)
         bad, tg = [[ap(x[1], x[2] + j, x[3], 2) for j in range(2)] for x in (sm("bad"), sl("su", "tg"))]
@@ -786,8 +802,10 @@ def rank_program(g, core, T, topo):
         cp(ind(ap("N", 0, 2048), bu), ap("NL"))
         prep_n1(t + 1)
         tt(ind(ap("Z"), bu), ap("ZN"), ap("YB"), mul)
-        prep_n2(t + 1, lambda: None, lambda: ts(ap("AU"), cand("AF", t + 1), M1 - AO, ad, -M1, ad))
-        late = [prep_n3]
+        prep_n2(t + 1, lambda: None, masks)
+        prep_n3()
+        for a, b in ((0, 64), (64, 256)):
+            ts(ap("AU", a, b), ap("AF", t + 1 + 7 * a, t + 7 * b - 5, 7), M1 - AO, ad, -M1, ad)
 
     for k, (a, b) in enumerate(((0, 896), (896, V))):
         dma("sa"[k], T.yn[:, a:b], T["N"][:, a:b], [ap("N", a, b)], [])

@@ -1,3 +1,4 @@
+from concourse.bass import DstId, RemoteDMATransfer
 from concourse.mybir import AluOpType as ALU, AxisListType, ActivationFunctionType as AF
 
 V, G, W = 1792, 1296, 3088
@@ -11,44 +12,57 @@ AO = 32.0
 SC = 288
 PW = (192,) * 8 + (96, 96, 64)
 PV = (96, 84, 96, 92, 80, 92, 84, 84, 44, 44, 30)
-NF = (2 * SC, 1000, G, V)
-LV = ((32, 32, 32, 32), (32, 28, 32, 32), (32, 28, 32, 32))
-WV = 26
-RW = 130
-SX = (30, 63)
-CV = 8
+NF = (2 * SC, 900, G, V)
+LV = ((32, 32, 32, 32), (26, 26, 28, 32), (26, 26, 28, 32))
+GO, DP, MS = (2, 3, 0, 1, 4, 5, 6, 7), 2, 6
+DBG = []
+INIT = 1
+MORE = (0.0, 0.1, -0.1, 0.05, -0.05)
+CY, CYP, GAT, SCA, HOP, FIX, BYTE, SCHED = 0.00083, 0.00042, 1.56, 3.8, 0.2, 0.0, 0.012, 10
+GV = ((64, 40, 16, 8), (64, 40, 16, 8), (64, 40, 16, 24))
+WB, AS = 128, (8, 12)
+AB = (0, 1, 2, 3)
+WV = 24
+RL, RH = 18, 114
+RW = RL + RH
+SX = (24, 63)
+CS = 2
 
 F32, BF, F16, I32, U16 = "float32", "bfloat16", "float16", "int32", "uint16"
 SB = {
-    "NI": (V, I32), "NU": (V, U16), "N": (NW, F32), "N2": (G, F32), "A": (V, I32), "AF": (V + 32, F32),
+    "NI": (V, I32), "NU": (V, U16), "N": (NW, F32), "KV": (G, F32), "A": (V, I32), "AF": (V + 32, F32),
     "Y": (YD + YL, BF), "X": (3104, BF), "R": (2048, BF), "Z": (2048, BF), "DD": (V, BF),
-    "GV0": (2048, BF), "GV1": (128 * CV, BF), "GA0": (4608, BF), "GA1": (4608, BF),
-    "MX0": (2048, BF), "PBO": (128, BF), "B8J": (16, BF), "EE": (17 * 256, BF), "RMP": (64 * RW, BF),
+    "AG": (V + 32, F32), "GA0": (4096, BF), "GA1": (4096, BF),
+    "PBO": (128, BF), "EE": (17 * 256, BF), "RMP": (64 * RW, BF),
     "T1": (3 * SC, BF), "T2": (3 * SC, BF), "XS": (192 * 3, BF), "XL": (192 * 3, BF), "TX": (256, BF),
     "IB": (128, BF), "NIB": (128, BF), "IBIG": (128, BF), "I64": (128, BF), "I16": (128, BF),
-    "IF": (128, F32), "JF": (128, F32), "BO": (128, BF), "NBO": (128, BF),
+    "IF": (128, F32), "BO": (128, BF), "NBO": (128, BF),
     "N128": (128, BF), "DQ": (256, BF), "B8K": (16, BF), "GH": (256, BF),
-    "TRI16": (128, BF), "TRI": (128, BF), "ONES": (128, BF), "B8": (80, BF), "B8F": (16, F32), "SEL": (144, BF),
-    "WM": (256, F32), "IOI": (256, F32), "IOS": (256, F32), "RAMP": (146, BF), "TRM": (128, BF),
-    "TRA": (128, BF), "N384": (128, BF), "IO4": (64, BF), "TN": (128, F32),
-    "TM": (128, F32), "KR": (256, BF), "C15": (384, BF), "I2": (128, BF), "RB": (128, F32), "C256": (128, BF), "RZ": (128 * CV, BF),
-    "DE": (384, BF), "DS": (384, BF), "MK": (256, BF), "RM": (128, BF), "SCB": (16, BF),
+    "TQ": (256, BF), "BQ": (256, BF), "IO8": (256, BF), "SEQ": (248, BF), "TRI": (128, BF), "ONES": (128, BF), "B8": (80, BF), "B8F": (16, F32), "SEL": (144, BF),
+    "WM": (128, F32), "IOI": (128, F32), "IOS": (256, BF), "RAMP": (RW, BF), "TRM": (128, BF),
+    "TRA": (128, BF), "N384": (128, BF), "IO4": (64, BF), "TN": (224, F32), "MT": (256, BF),
+    "KR": (256, BF), "C15": (384, BF), "I2": (128, BF), "RB": (256, F32), "IA": (128, BF), "IE": (128, BF),
     "sm": (16 * 48, F32), "si": (16 * 12, I32), "su": (16 * 12, U16), "sb": (16 * 8, BF),
     "AU": (256, U16), "AH": (256, F16), "NH": (256, F16), "EB": (256, BF), "MP": (256, BF),
-    "MM": (256, BF), "RR": (256, BF), "X1": (256, F16), "X2": (256, BF), "PP": (17 * 128, BF), "DB": (256, BF),
-    "S1": (128, BF), "CS": (128, F32), "CS2": (128, F32), "DW": (128, BF), "F": (128, BF),
-    "TRQ": (128, BF), "CC": (144, BF), "CUM": (128, F32), "CMP": (256, BF), "CRP": (256, BF),
+    "RR": (256, BF), "X1": (256, F16), "X2": (256, BF), "PP": (17 * 128, BF), "DB": (256, BF),
+    "S1": (128, BF), "DW": (128, BF), "F": (128, BF),
+    "I4K": (128, BF), "FP": (144, BF), "CUM": (128, F32), "CMP": (256, BF), "CRP": (256, BF),
     "LBU": (256, U16), "LBH": (256, F16), "XB": (256, BF), "LUU": (256, U16), "LUH": (256, F16),
-    "SC1": (512, I32), "BC": (256, F32), "BC2": (256, F32), "BT": (256, F32),
+    "SC1": (256, I32), "HK": (256, F32), "BC": (256, F32), "BC2": (256, F32),
     "OH": (256, F32), "NL": (256, F32), "RG": (256, BF), "YB": (256, BF), "YW": (256, BF), "YO": (256, BF),
     "ZN": (256, BF), "RN": (256, BF), "NM": (256, BF), "BM": (256, BF), "AN": (256, F32), "PB": (256, F32),
-    "WR": (256, F32), "YC": (768, BF),
+    "YC": (768, BF), "WR": (384, F32), "DE": (384, BF), "DS": (384, BF), "MF": (192, BF),
 }
 SCRATCH = {k: ("sbuf", [128, n], d) for k, (n, d) in SB.items()}
 SCRATCH["LT"] = ("sbuf", [128, 16, 32], F32)
 SCRATCH["AT"] = ("sbuf", [128, 32, 16], BF)
-SCRATCH["MX1"] = ("sbuf", [128, 16, 128], BF)
+SCRATCH["MX0"] = SCRATCH["MX1"] = ("sbuf", [128, 16, 128], BF)
+SCRATCH["JF"] = ("sbuf", [128, 4, 48], F32)
+SCRATCH["MK"] = ("sbuf", [128, 4, 48], BF)
 SCRATCH["ZB"] = ("sbuf", [128, 2, 144], F16)
+SCRATCH["ST"] = ("sbuf", [128, 16, 17], BF)
+SCRATCH["CS"] = ("sbuf", [128, RL, 8], F32)
+SCRATCH["CM"] = ("sbuf", [128, 16, 128], BF)
 for _k in range(8):
     SCRATCH["p%d" % _k] = ("psum", [128, 512], F32)
 NDMA, NMSG = 16, 9
@@ -66,7 +80,7 @@ def rank_program(g, core, T, topo):
     engs = topo.engines(core, dst)
     engs = [engs[1::4] if 5 <= k < 8 else engs[::2] for k in range(NMSG)]
     Q = {"v": g.vector, "a": g.scalar, "p": g.tensor, "g": g, "s": g.sync}
-    ops, hist, cnt = [], {}, {"d": 0}
+    ops, hist, cnt, lands = [], {}, {"d": 0}, {}
 
     def ap(name, a=0, b=None, s=1, p0=0, p1=128):
         b = T[name].shape[-1] if b is None else b
@@ -93,9 +107,30 @@ def rank_program(g, core, T, topo):
     def sm(key, a=0, b=16):
         return sl("sm", key, a, b)
 
-    def add(q, fn, reads, writes, sem=None):
+    def cols(x):
+        if len(x) > 5:
+            return 16 * cols(x[5])
+        return len(range(x[2], x[3], x[4])) if len(SCRATCH[x[1]][1]) == 2 else 0
+
+    def lasts(q, reads, writes, two):
+        xs = [x for x in writes[:1] + reads if isinstance(x, tuple)]
+        n = ([cols(x) for x in xs if cols(x)] + [256])[0]
+        if q == "p":
+            return max(64, n) * (4 if SCRATCH[xs[1][1]][2] == F32 else 1) * CYP
+        if q == "g":
+            return 0.15 + 2 * n * CY
+        if len(xs[0]) > 5 or len(xs) > 1 and len(xs[1]) > 5:
+            return 0.06 + n * (SCA if len(xs[0]) > 5 else GAT) * CY
+        if q == "a":
+            return max(64, n) * CY + FIX
+        if two and SCRATCH[xs[1][1]][0] == SCRATCH[xs[2][1]][0]:
+            return max(64, 2 * n) * CY + FIX
+        narrow = not two and all(SCRATCH[x[1]][2] in (BF, F16, U16) for x in xs[:2])
+        return max(64, n / 2 if narrow else n) * CY + FIX
+
+    def add(q, fn, reads, writes, sem=None, two=False, t=None):
         i = len(ops)
-        deps = set()
+        deps, after = set(), set()
         acc = []
         for w, xs in ((False, reads), (True, writes)):
             for x in xs:
@@ -109,19 +144,22 @@ def rank_program(g, core, T, topo):
                 o = ops[j]
                 same = o["q"] == q and o["sem"] is None and sem is None
                 if same and q == "p":
+                    if ps:
+                        after.add(j)
                     continue
                 apart = same and s == s2 and (a - a2) % s
                 if (ps and not same) or ((w or w2) and a < b2 and a2 < b and not apart):
                     deps.add(j)
         for name, a, b, s, w in acc:
             hist.setdefault(name, []).append((a, b, s, w, i))
-        ops.append({"q": q, "fn": fn, "deps": deps, "sem": sem, "mark": False})
+        ops.append({"q": q, "fn": fn, "deps": deps, "sem": sem, "mark": False, "after": set(sorted(after)[-1:]),
+                    "t": lasts(q, reads, writes, two) if t is None else t})
 
     def x0(x):
         return x[0] if isinstance(x, tuple) else x
 
     def tt(o, a, b, op):
-        add("v", lambda: g.vector.tensor_tensor(o[0], a[0], b[0], op), [a, b], [o])
+        add("v", lambda: g.vector.tensor_tensor(o[0], a[0], b[0], op), [a, b], [o], two=True)
 
     def ts(o, a, s1, op0, s2=None, op1=None):
         if op1 is None:
@@ -145,11 +183,11 @@ def rank_program(g, core, T, topo):
     def put(o, a):
         add("a", lambda: g.scalar.activation(o[0], a[0], AF.Silu), [a], [o])
 
-    def mm(o, l, r, start, stop):
-        add("p", lambda: g.tensor.matmul(o[0], l[0], r[0], start, stop), [l, r], [o])
+    def mm(o, l, r, start, stop, also=None):
+        add("p", lambda: g.tensor.matmul(o[0], l[0], r[0], start, stop), [l, r, also], [o])
 
     def iota(o, pat, base, cm=0):
-        if SB[o[1]][1] == I32:
+        if SCRATCH[o[1]][2] == I32:
             add("g", lambda: g.iota(o[0], pat, base, cm), [], [o])
         else:
             add("g", lambda: g.iota(o[0], pat, base, cm, allow_small_or_imprecise_dtypes=True), [], [o])
@@ -160,15 +198,25 @@ def rank_program(g, core, T, topo):
     def dma(q, o, a, reads, writes, **how):
         s = "d%d" % cnt["d"]
         cnt["d"] += 1
-        add(q, lambda: Q[q].dma_start(o, a, **how), reads, writes, sem=(s, 16, True))
+        add(q, lambda: Q[q].dma_start(o, a, **how), reads, writes, sem=(s, 16, True),
+            t=1.5 + sum(cols(x) * (2 if SCRATCH[x[1]][2] == BF else 4) for x in (writes or reads)) * BYTE / 16)
 
-    def send(k, o, a):
+    def send(k, o, a, plus=None):
         mask = sum(1 << e for e in engs[k])
-        add("g", lambda: g.remote_dma(o[0], a[0], T.sem["r%d" % k], T.sem["l%d" % k], pid, rid, mask), [a], [],
-            sem=("l%d" % k, len(engs[k]), False))
+        t = 2.0 + cols(a) * (2 if SCRATCH[a[1]][2] == BF else 4) * BYTE / len(engs[k])
+        ops[lands[k]]["after"].add(len(ops))
+        if plus is None:
+            add("g", lambda: g.remote_dma(o[0], a[0], T.sem["r%d" % k], T.sem["l%d" % k], pid, rid, mask), [a], [],
+                sem=("l%d" % k, len(engs[k]), False), t=t)
+        else:
+            fold = RemoteDMATransfer(dst_ids=[DstId(rid=rid, pnc=pid)], dma_engine_mask=mask, remote_sem=T.sem["r%d" % k],
+                                     srcs=[a[0], plus[0]], dsts=[o[0]], alu_op=1)
+            add("g", lambda: g.remote_dma_fused([fold], local_sem=T.sem["l%d" % k]), [a, plus], [],
+                sem=("l%d" % k, len(engs[k]), False), t=2 * t)
 
     def landed(k, o):
-        add("x", None, [], [o], sem=("r%d" % k, len(engs[k]), False))
+        lands[k] = len(ops)
+        add("x", None, [], [o], sem=("r%d" % k, len(engs[k]), False), t=0.5)
 
     def P(k, a=0, b=512, s=1, p0=0, p1=128):
         return ap("p%d" % k, a, b, s, p0, p1)
@@ -210,8 +258,10 @@ def rank_program(g, core, T, topo):
     block(b8, 1, [[16, 8]])
     send(0, ap("Y", V, V + G // 2), ap("Y", 0, G // 2))
     send(8, ap("Y", V + G // 2, W), ap("Y", G // 2, G))
-    first = len(ops) - 1
-    iota(ap("IOI"), [[0, 16], [1, 16]], 0)
+    first = sent = len(ops) - 1
+    iota(ap("IOI"), [[0, 8], [1, 16]], 0)
+    iota(ap("IO8", 0, 128), [[0, 16], [1, 8]], 0)
+    iota(ap("IO8", 128, 256), [[1, 8], [0, 16]], 0)
     for a, b in pieces[1:]:
         dma("s", T["NI"][:, a:b], T.nb[:, a:b], [], [ap("NI", a, b)])
         ops[-1]["deps"].add(first)
@@ -222,19 +272,22 @@ def rank_program(g, core, T, topo):
     ms(ap("X", W, W + 1), 0.0)
     ms(ap("X", W + 1, 3104), 63.0)
     ms(ap("SEL"), 0.0)
+    ms(ap("SEQ"), 0.0)
     e8 = sm("col", 4, 5)
     ms(e8, 0.0)
-    ms(ap("CC", 0, 1), 0.0)
+    ms(ap("FP", 0, 1), 0.0)
     ms(ap("DW"), 0.0)
     ts(sl("si", "q", 0, 1), sl("si", "p", 0, 1), 15, ALU.bitwise_and)
     ts(ap("NIB"), ap("IB"), -1.0, mul)
     qf = sm("col", 0, 1)
     cp(qf, sl("si", "q", 0, 1))
     cp(ap("SEL", 15, 143, 16), b8)
+    ts(sl("si", "q", 1, 2), sl("si", "p", 0, 1), 7, ALU.bitwise_and)
+    cp(ap("SEQ", 120, 128), b8)
+    cp(sm("col", 7, 8), sl("si", "q", 1, 2))
     m0 = sm("col", 1, 2)
     ts(m0, qf, 0.0, eq)
-    for o, val in ((ap("B8J", 0, 8), DK), (ap("B8J", 8, 16), -4096), (b8b, 2 * DK), (b8n, -DK), (ap("B8K", 0, 8), -DK),
-                   (ap("B8K", 8, 16), 512), (ap("B8F", 0, 8), 1)):
+    for o, val in ((b8b, 2 * DK), (ap("B8K", 0, 8), -DK), (ap("B8K", 8, 16), 512), (ap("B8F", 0, 8), 1)):
         ts(o, b8, float(val), mul)
     ts(sm("col", 2, 3), m0, 16.0, mul, qf, ad)
     ms(whole("ZB", T["ZB"][:, :, :]), 0.0)
@@ -242,25 +295,32 @@ def rank_program(g, core, T, topo):
     qt = [qf, sm("col", 2, 3)]
     nq, qa, dum = [[sm(k, j, j + 1) for j in range(2)] for k in ("nq", "qa", "dum")]
     for j in range(2):
-        ts(nq[j], qt[j], -1.0, mul)
+        ts(nq[j], qt[j], 1.0, ge)
         ts(qa[j], qt[j], AO, ad)
         ts(dum[j], qf, float(V + 16 * j), ad)
+    ts(sm("col", 6, 7), sl("si", "p", 0, 1), 16.0 * CS, ltn, 64.0, mul)
     for name, val in (("I64", 1.0 / 64), ("I16", 16.0), ("IBIG", 2.0 ** 26), ("N128", -128.0), ("N384", -384.0),
-                      ("IF", 1.0), ("I2", 2.0)):
+                      ("IF", 1.0), ("I2", 2.0), ("I4K", 4096.0), ("IA", -65.0 / 64), ("IE", -1.0 / 128)):
         act(ap(name), ap("IB"), scale=val)
+    tt(ap("MT", 1, 128), ap("IB", 1, 128), ap("IB", 0, 127), sub)
+    cp(ap("MT", 0, 128, 16), ap("IB", 0, 128, 16))
+    cp(ap("MT", 129, 256), ap("MT", 0, 127))
+    cp(ap("MT", 128, 256, 16), ap("MT", 15, 128, 16))
     for j in range(2):
-        ts(ap("DQ", 128 * j, 128 * j + 128), ap("NIB"), qa[j], mul)
+        ts(ap("DQ", 128 * j, 128 * j + 128), ap("NIB"), (qt, qa)[j][j], mul)
     cp(ap("NU", *pieces[0]), ap("NI", *pieces[0]))
     cp(ap("N", *pieces[0]), ap("NI", *pieces[0]))
     io16 = ap("IOI", 0, 16)
     bc = sl("su", "bc")
     cp(bc, io16)
-    for j in range(2):
-        ts(sl("su", "bp", 8 * j, 8 * j + 8), ap("IOI", 0, 8), 2.0, mul, float(j), ad)
-    ts(ap("SCB"), io16, 16.0, mul, qf, ad)
     ts(ap("WM"), ap("IOI"), qf, eq)
-    ts(sm("sh"), ap("SCB"), 0.5, ad)
-    ts(ap("MK"), ap("IOI"), qf, ad, 15.0, gt)
+    ts(whole("MK", T["MK"][:, :, 0:32]), ap("IOI"), qf, ad, 15.0, gt)
+    ms(whole("MK", T["MK"][:, :, 32:48]), 1.0)
+    cp(ap("MF"), whole("MK", T["MK"][:, :, :]))
+    bp = sl("su", "bp", 0, 12)
+    for j in range(3):
+        ts(ap("su", bp[2] + j, bp[3], 3), ap("IOI", 0, 4), 2.0, mul, float(j > 0), ad)
+    ts(ap("BQ"), ap("IO8"), sm("col", 7, 8), eq)
 
     def pick(q):
         return ap("SEL", 15 - q, 143 - q)
@@ -271,46 +331,30 @@ def rank_program(g, core, T, topo):
         sel(ap("TRM"), ap("TRI"), [[-1, 128]], ne, -255, 0, 1)
         sel(ap("TRA"), ap("TRI"), [[-1, 128]], ne, 256, 0, 1)
         iota(ap("IO4"), [[2, 64]], -510)
-        iota(ap("C15", 0, 256), [[0, 256]], -15)
-        iota(ap("RAMP", 0, 16), [[2, 16]], -15)
-        iota(ap("RAMP", 16, 130), [[32, 114]], 32)
-        iota(ap("RAMP", 130, 146), [[2, 16]], -13)
+        iota(ap("C15", 0, 256, 1, 0, 2), [[0, 256]], -15, 4111)
+        iota(ap("RAMP", 0, RL), [[2, RL]], -17)
+        iota(ap("RAMP", RL, RW), [[32, RH]], 4096)
         for t in range(3):
             sel(ap("YC", 256 * t, 256 * t + 256), cand("Y", t), [[0, 256]], ge, 0, 0, 0)
         iota(ap("PP"), [[0, 17 * 128]], 0)
-        iota(ap("DD"), [[0, V]], 0)
         dma("g", T["X"][:, 0:V], T.xf[:, :], [], [ap("X", 0, V)], accum_op=ad)
         ops[-1]["deps"].add(first)
-        iota(ap("XS"), [[0, 192 * 3]], 0)
 
     def consts_b():
         iota(ap("F", 0, 112), [[0, 112]], 0)
         iota(ap("F", 112, 128), [[0, 16]], 1)
-        diag("TN", 2.0 / 32)
-        sel(ap("TN"), ap("TN"), [[-1, 128]], ne, -1.0 / 32, 1, 1)
-        sel(ap("TN"), ap("TN"), [[-1, 128]], ne, -1.0 / 32, -1, 1)
-        diag("TM", -2.0)
-        sel(ap("TM"), ap("TM"), [[-1, 128]], ne, 1.0, 1, 1)
-        sel(ap("TM"), ap("TM"), [[-1, 128]], ne, 1.0, -1, 1)
-        for col, off, val in ((0, 0, -1.0), (0, 1, 0.0), (15, 0, -13.0), (15, 1, 15.0), (15, -1, 0.0)):
-            sel(ap("TM", col, 128, 16), ap("TM", col, 128, 16), [[-16, 8]], ne, val, off - col, 1)
-        ta = ap("TM", 0, 32, 1, 0, 32)
-        iota(ta, [[0, 32]], 0)
+        tn = ap("TN", 0, 112)
+        iota(tn, [[0, 112]], 0)
         for off, val in enumerate((-1.0, 2.0, -1.0)):
-            sel(ta, ta, [[-1, 32]], ne, val, off, 1)
-        sel(ta, ta, [[-16, 2], [0, 16]], ge, 0, 0, 1)
+            sel(tn, tn, [[-1, 112]], ne, val / 32, -off, 1)
         block(ap("BO"), 1, [[16, 8], [0, 16]])
-        sel(ap("TRI16"), ap("BO"), [[1, 128]], ge, 0, 0, -1)
-        sel(ap("TRQ"), ap("TRI16"), [[-1, 128]], ne, 256, 0, 1)
-        iota(ap("C256"), [[0, 128]], 256)
-        iota(ap("RZ"), [[0, 128 * CV]], 1)
-        iota(ap("RZ", 0, 128 * CV, 128), [[0, CV]], 0)
+        sel(ap("TQ", 0, 128), ap("BQ", 0, 128), [[1, 128]], ge, 0, 0, -1)
+        sel(ap("TQ", 128, 256), ap("BQ", 128, 256), [[0, 8], [8, 16]], ge, 0, 7, -1)
         iota(ap("IOS"), [[1, 256]], 0)
+        iota(ap("KV"), [[0, G]], V)
         send(1, ap("X", V, W), ap("X", 0, G))
         iota(ap("N", V, 2048), [[0, 256]], W + 1)
         iota(ap("R", V, 2048), [[0, 256]], 0)
-        block(ap("NBO"), -DK, [[16, 8], [0, 16]])
-        block(ap("PBO"), 4096, [[16, 8], [0, 16]])
 
     def consts_c():
         kinds = [[1, 2], [0, 128]]
@@ -319,17 +363,20 @@ def rank_program(g, core, T, topo):
         sel(ap("KR"), ap("KR"), kinds, ne, -120 * DK, -4, 2)
         sel(ap("KR"), ap("KR"), kinds, ne, 0, -5, 2)
         sel(ap("KR"), ap("KR"), kinds, ne, 0, -7, 2)
-        iota(ap("RB"), [[0, 128]], 0)
-        sel(ap("RB", 0, 128, 16), ap("RB", 0, 128, 16), [[0, 8]], ne, 2.0 ** 30, 0, 0)
-        iota(ap("JF"), [[0, 128]], 0)
-        sel(ap("JF"), ap("JF"), [[-16, 2], [-32, 4], [1, 16]], ne, 1, -15, 1)
-        iota(ap("RM"), [[0, 128]], 1)
-        iota(ap("RM", 0, 128, 16), [[0, 8]], 0)
-        iota(ap("Y", W, YD), [[0, YD - W]], 0)
-        sel(ap("Y", YD, YD + YL), ap("Y", 0, YL), [[0, YL]], ge, 0, 0, 0)
+        iota(ap("RB", 0, 128), [[0, 128]], 0)
+        iota(ap("RB", 128, 256), [[0, 128]], -2 ** 23)
+        for o, val in ((0, 2.0 ** 30), (128, 65536.0)):
+            sel(ap("RB", o, o + 128, 16), ap("RB", o, o + 128, 16), [[0, 8]], ne, val, 0, 0)
+        iota((T["ST"][:, :, 0], "ST", 0, 2, 1), [[0, 16]], 0)
+        iota(whole("JF", T["JF"][:, :, :]), [[0, 192]], 0)
+        for a, b in ((0, 32), (32, 48)):
+            x = whole("JF", T["JF"][:, :, a:b])
+            sel(x, x, [[-32, 4], [-16, (b - a) // 16], [1, 16]], ne, 1, -15, 1)
 
     consts_a()
     consts_b()
+    iota(ap("Y", W, YD), [[0, YD - W]], 0)
+    dma("s", T["Y"][:, YD:YD + YL], T["Y"][:, 0:YL], [ap("Y", 0, YL)], [ap("Y", YD, YD + YL)])
 
     def zfrom(src, w, ycols, zout, bank):
         o = SC * (bank - 2)
@@ -354,18 +401,17 @@ def rank_program(g, core, T, topo):
 
     def masks():
         ts(ap("MP"), ap("EB"), 2.0, eq, -1.0, mul)
-        ts(ap("MM"), ap("EB"), -2.0, eq)
 
     def prep_n3():
-        mm(P(5, 0, 256), ap("NIB"), ap("MP"), True, False)
-        mm(P(5, 0, 256), ap("I64"), ap("MM"), False, True)
+        mm(P(5, 0, 256), ap("IA"), ap("MP"), True, False)
+        mm(P(5, 0, 256), ap("IE"), ap("EB"), False, True)
 
     def prep_a(t):
-        if t:
-            ts(ap("AH"), cand("AF", t), M1 + 16 - AO, ad, -M1, ad)
-        mm(P(6, 0, 256), ap("ONES", 0, 128, 1, 0, 1), ap("C15", 0, 256, 1, 0, 1), True, False)
-        for h in range(2):
-            mm(P(6, 128 * h, 128 * h + 128), ap("AH", 128 * h, 128 * h + 128), ap("I2"), False, h == 1)
+        ts(ap("AH"), ap("AU"), 16.0, ad)
+        for k in (6, 2):
+            mm(P(k, 0, 256), ap("ONES", 0, 128, 1, 0, 2), ap("C15", 0, 256, 1, 0, 2), True, False)
+            for h in range(2):
+                mm(P(k, 128 * h, 128 * h + 128), ap("AH", 128 * h, 128 * h + 128), ap("I2"), False, k == 6 and h == 1)
 
     late = []
     last = len(PW) - 1
@@ -410,7 +456,6 @@ def rank_program(g, core, T, topo):
     zpiece(last - 1, P(banks[last - 1], 0, PW[last - 1]), 3 - (last & 1))
     rcopy(last - 1)
     late.pop(0)()
-    ts(ap("AH"), cand("A", 0), 16.0, ad)
     zpiece(last, P(7, 0, PW[last]), 4)
     late.pop(0)()
     masks()
@@ -433,8 +478,7 @@ def rank_program(g, core, T, topo):
     bu = sl("su", "b")
 
     def lists(t):
-        act(ap("N2"), ap("N", 0, G), bias=float(V))
-        send(2 + t, ap("N", 2048 + G * t, 2048 + G * (t + 1)), ap("N2"))
+        send(2 + t, ap("N", 2048 + G * t, 2048 + G * (t + 1)), ap("N", 0, G), ap("KV"))
 
     def newlists():
         for h in range(2):
@@ -445,36 +489,47 @@ def rank_program(g, core, T, topo):
         for k in range(4):
             a, m, b = 64 * k, 64 * k + LV[t][k], 64 * k + 64
             cp(ap("RMP", 16 * a, 16 * m), ind(zw, ap("AU", a, m)))
+            if t and k == 0:
+                prep_n2(t, lambda: None, lambda: None)
+            if t and k == 1:
+                masks()
             act(ap("RMP", 16 * m, 16 * b), ind(zw, ap("AU", m, b)), AF.Copy)
             for i in range(16):
                 mm(P(k // 3, a, b), ap("IB"), ap("RMP", 16 * a + i, 16 * b, 16), k % 3 + i == 0, k > 1 and i == 15)
             if k == 1:
                 prep_a(t)
+            if t and k == 2:
+                prep_n3()
+        act(whole("AT", T["AT"][:, :, 8:16]), P(6, 0, 256), AF.Copy)
         if t == 0:
             rcopy(last)
-        else:
-            lists(t)
+            act(ap("TN", 112, 224), ap("TN", 0, 112), scale=-2.0)
+            act(ap("NBO"), ap("BO"), scale=-float(DK))
+            act(ap("PBO"), ap("BO"), scale=float(DK))
+        mm(P(2, 0, 256), ap("NIB"), whole("AT", T["AT"][:, :, 8:16]), False, True)
+        act(whole("AT", T["AT"][:, :, 0:8]), P(2, 0, 256), AF.Copy)
         for k, a, b in ((0, 0, 192), (1, 192, 256)):
             ts(ap("RR", a, b), P(k, a, b), M64, ad, -M64, ad)
             tt(ap("X1", a, b), P(k, a, b), ap("MP", a, b), mul)
-            if k:
-                ts(whole("AT", T["AT"][:, :, 8:16]), P(6, 0, 256), M32, ad, -M32, ad)
             tt(ap("X2", a, b), P(5, a, b), ap("RR", a, b), mul)
-        tt(whole("AT", T["AT"][:, :, 0:8]), P(6, 0, 256), whole("AT", T["AT"][:, :, 8:16]), sub)
         for h in range(2):
             mm(P(3, 8 * h, 8 * h + 8), half("X1", h), b8, h == 0, False)
             mm(P(3, 8 * h, 8 * h + 8), half("X2", h), b8, False, h == 1)
         will = sl("sb", "will")
+        if t == 0:
+            nfloat(0)
         ts(will, P(3, 0, 16), e8, le, 2.0, mul)
         mm(P(3, 16, 32), ap("TRM"), will, True, False)
         mm(P(3, 24, 32), ap("ONES"), sl("sb", "will", 0, 8), False, True)
         if t == 0:
-            nfloat(0)
+            nfloat(1)
+            lists(0)
         die = sl("sb", "die")
         ng = len(range(t, G, 7))
-        ts(die, P(3, 16, 32), -384.0, le, 2.0, mul)
-        act(ap("DB"), ind(die, bc), AF.Copy)
-        for gi in (2, 3, 0, 1, 4, 5, 6, 7):
+        for gi in GO:
+            if gi == GO[DP]:
+                ts(die, P(3, 16, 32), -384.0, le, 2.0, mul)
+                act(ap("DB"), ind(die, bc), AF.Copy)
             for h in range(2):
                 c = 8 * h + gi
                 ts(ap("PP", 128 * c + 64, 128 * c + 128), ap("IO4"), P(3, 16 + c, 17 + c), eq)
@@ -486,17 +541,18 @@ def rank_program(g, core, T, topo):
                        whole("AT", T["AT"][:, 2 * c + j, :]), gi in (0, 2, 4) and h + j == 0, gi in (1, 3, 7) and h + j == 2)
             if gi == 5:
                 cp(ap("S1", 32, 64), P(1, 32, 64))
-        act(ap("S1", 0, 32), P(2, 0, 32), scale=-1.0)
+            if gi == 1:
+                act(ap("S1", 0, 32), P(2, 0, 32), scale=-1.0)
         for h in range(2):
             mm(P(5, 128 * h, 128 * h + 128), half("DB", h), ap("IB"), True, True)
         mm(P(4, 0, 256), ap("IB"), cand("X", t), True, False)
         for h in range(2):
             mm(P(4, 128 * h, 128 * h + 128), half("DB", h), ap("N128"), False, h == 1)
 
-        def count(c, stop=False):
+        def count(c):
             o = RW * c
-            mm(P(0, c >> 3 << 4, (c >> 3 << 4) + 16, 1, 0, 113), ap("RMP", o + 16, o + 129), ap("RMP", o, o + 16),
-               c == 16, stop)
+            sums = P(2, c >> 3, 2 * RL, 2, 0, RH) if c < 16 else P(0, (c >> 3) - 2, 6 * RL, 6, 0, RH)
+            mm(sums, ap("RMP", o + RL, o + RW), ap("RMP", o, o + RL), c in (0, 16), c in (15, 63))
 
         def digit(c, j):
             a = (c >> 3 << 4) + 8 * j + (c & 7)
@@ -506,99 +562,319 @@ def rank_program(g, core, T, topo):
             o = RW * c
             if c == 24:
                 cp(ap("S1", 64, 128), P(7, 64, 128))
-            ts(ap("RMP", o, o + 129), ap("RAMP", 0, 129), digit(c, 0), mx, digit(c, 1), mn)
+            ts(ap("RMP", o, o + RW), ap("RAMP"), digit(c, 0), mx, digit(c, 1), mn)
             count(c)
             if c % 3 == 0:
                 k = c // 3 - 6
                 o = RW * k
-                act(ap("RMP", o, o + 16), ap("RAMP", 130, 146), AF.Relu, bias=digit(k, 0))
-                act(ap("RMP", o + 16, o + 129), ap("RAMP", 16, 129), AF.Relu, bias=digit(k, 1))
-                count(k, k == 15)
+                act(ap("RMP", o, o + RL), ap("RAMP", 0, RL), AF.Relu, bias=digit(k, 0))
+                act(ap("RMP", o + RL, o + RW), ap("RAMP", RL, RW), AF.Relu, bias=digit(k, 1))
+                count(k)
             if c == SX[0]:
                 act(cand("DD", t), P(5, 0, 256), scale=(t + 1) / 2.0)
+            if c == SX[0] + MS:
+                mm(P(6, 0, 112), ap("I64"), ap("DW", 0, 112), True, False)
+                mm(P(1, 0, 128), ap("IB"), ap("F"), True, False)
+                if t < 2:
+                    mm(P(3, 0, 16), ap("ONES"), die, True, True)
+            if 0 < c - SX[0] - MS <= 16:
+                v = t + 7 * (c - SX[0] - MS - 1)
+                mm(P(6, v >> 4, 112, 7), ap("SEQ", 120 - 8 * (v & 15), 248 - 8 * (v & 15)), ap("DD", v, V, 112), False, v > 104)
             if c == SX[1]:
-                act(ap("XS", 192 * t, 192 * t + ng), P(4, 0, ng), AF.Relu)
+                act(ap("XS", 192 * t, 192 * t + 192), P(4, 0, 192), AF.Relu)
                 send(5 + t, ap("XL", 192 * t, 192 * t + 192), ap("XS", 192 * t, 192 * t + 192))
-        def mask(a, b):
-            for v in range(t + 7 * a, 7 * b, 7):
-                mm(P(6, v >> 4, 112, 7), pick(v & 15), ap("DD", v, V, 112), False, v > 104)
-
-        mm(P(6, 0, 112), ap("I64"), ap("DW", 0, 112), True, False)
-        mask(0, 10)
-        act(cand("X", t), P(4, 0, 256), AF.Relu)
-        cp(ap("CS", 0, 128, 1, 0, 113), P(0, 0, 128, 1, 0, 113))
-        mm(P(1, 0, 112), ap("CS", 0, 128, 1, 0, 113), ap("TN", 0, 112, 1, 0, 113), True, True)
-        mask(10, 16)
+        if t == 0:
+            consts_c()
+        cp((T["CS"][0:RH, :, 2:8], "CS", 2, 8, 1), P(0, 0, 6 * RL, 1, 0, RH))
+        act((T["CS"][0:RH, :, 0:2], "CS", 0, 2, 1), P(2, 0, 2 * RL, 1, 0, RH), scale=-1.0)
+        for j in range(3):
+            mm(P(1, 0, 112), (T["CS"][0:RH, j:j + 16, :], "CS", 0, 8, 1), ap("TN", 112 * (j & 1), 112 * (j & 1) + 112, 1, 0, RH),
+               False, j == 2)
         act(ap("DW", 0, 112), P(6, 0, 112), scale=65536.0)
-        mm(P(2, 0, 128), ap("IB"), ap("F"), True, False)
+        act(cand("X", t), P(4, 0, 256), AF.Relu)
 
         def fill(j):
-            if t == 0 and j:
-                ts(cand("AF", j), cand("A", j), AO, ad)
-            if t == 1 and j < 2:
-                cp(ind(ap("R"), sl("su", "b", 8 * j, 8 * j + 8)), half("RN", j))
+            if t == 0 and j < 2:
+                ts(cand("AF", j + 1), cand("A", j + 1), AO, ad)
+            if t == 1 and j != 1:
+                cp(ind(ap("R"), sl("su", "b", 4 * j, 4 * j + 8)), half("RN", j // 2))
 
-        if t == 0:
-            nfloat(1)
-            lists(0)
-            consts_c()
+        if t < 2:
+            add("v", lambda: g.vector.tensor_reduce(sm("col", 5, 6)[0], P(3, 0, 16)[0], AxisListType.X, ad),
+                [P(3, 0, 16)], [sm("col", 5, 6)])
         fill(0)
-        cp(ap("CS2", 0, 112), P(1, 0, 112))
-        mm(P(2, 0, 112), ap("TM"), ap("CS2", 0, 112), False, True)
+        if t < 2:
+            ts(sl("si", "e", 0, 1), sm("col", 5, 6), 0.5, mul)
+        tt(ap("F"), P(1, 0, 128), ap("DW"), gt)
+        if t < 2:
+            ts(sl("si", "e", 1, 2), sl("si", "e", 0, 1), 7, ALU.bitwise_and)
+        scan(ap("FP", 1, 129), ap("F"), zero, ad, ad)
+        mm(P(2, 0, 128), half("TQ", 1), ap("F"), True, False)
+        mm(P(0, 0, 8), ap("FP", 1, 129), ap("BQ", 0, 8), True, True)
+        mm(P(2, 0, 128), half("BQ", 1), ap("FP", 0, 128), False, True)
+        if t < 2:
+            mm(P(6, 0, 112), half("TQ", 0), ap("F", 0, 112), True, False)
+            mm(P(6, 0, 112), half("BQ", 0), ap("FP", 0, 112), False, False)
+            mm(P(6, 0, 112), ap("I4K"), ap("F", 0, 112), False, True)
+        if t < 2:
+            cp(e8, sl("si", "e", 1, 2))
+        ts(sl("sb", "cc", 0, 8), P(0, 0, 8), 256.0, mn)
+        ts(sm("ncc", 0, CS), P(0, 0, CS), -1.0, mul, 0.5, ad)
+        act(ap("CUM"), P(2, 0, 128), AF.Copy)
+        def hs(buf, key, h):
+            return sl(buf, key, 8 * h, 8 * h + 8)
+
+        def part(name, h, a, b):
+            return (T[name][:, 8 * h:8 * h + 8, a:b], name, h, h + 1, 1)
+
+        def spread(src):
+            return ind(src, sl("su", "bc", 0, 8))
+
+        def wrap(src, h, a):
+            tt(half("BC", h), spread(src), ap("WM"), mul)
+            mm(P(7, a, a + 8), half("BC", h), ap("B8F", 0, 8), True, True)
+            return P(7, a, a + 8)
+
+        def treated(h):
+            for gi in range(8):
+                o = (T["CM"][:, 8 * h:8 * h + 8, 16 * gi:16 * gi + 16], "CM", 8 * h + gi, 8 * h + gi + 1, 1)
+                if gi < CS:
+                    act(o, half("IOS", h), AF.Sign, bias=sm("ncc", gi, gi + 1))
+                else:
+                    ts(o, half("IOS", h), sl("sb", "cc", gi, gi + 1), ge, 2.0, mul)
+            for k in range(8):
+                mm(P(h, 2 * k, 2 * k + 2), (T["CM"][:, 8 * h + k, :], "CM", 8 * h, 8 * h + 8, 1), ap("ONES", 0, 2), k == 0, k == 7)
+            cu, bk = hs("su", "c", h), (3, 7)[h]
+            ts(cu, P(h, 0, 16, 2), 0.5, mul, sm("col", 6, 7), ad)
+            tt(half("CMP", h), ind(ap("CUM"), cu), half("IOS", h), le)
+            cp(hs("sb", "c", h), cu)
+            act(half("CRP", h), ind(ap("IOS", 0, 128), cu), bias=-CEN / 16)
+            mm(P(bk, 0, 8), ap("I16"), hs("sb", "c", h), True, False)
+            for q in range(16):
+                mm(P(bk, 0, 8), pick(q), ap("CMP", 128 * h + q, 128 * h + 128, 16), False, q == 15)
+            cp(hs("su", "b", h), P(bk, 0, 8))
+            cp(half("LBU", h), ind(ap("N", 0, 2048), hs("su", "b", h)))
+            act(half("XB", h), ind(xw, hs("su", "b", h)), AF.Copy)
+            ts(half("LBH", h), half("LBU", h), -CEN, ad)
+            ts(half("GH", h), half("LBU", h), float(V), ge, 256.0 + G * t, mul)
+
+        def mx_(h, a, b, c):
+            return (T["MX%d" % h][:, a:b, 64 * c:64 * c + 64], "MX%d" % h, 16 * c + a, 16 * c + b, 1)
+
+        def keys(h, d, names):
+            gb, o, sv, w = "GA%d" % h, 2048 * d, GV[t][2 * d + 1 - h], 256 >> d
+            cp(ap(gb, o, o + 16 * sv), ind(xw, ap(names, 128 * h, 128 * h + sv)))
+            for a, b in ((sv, 64), (max(sv, 64), 128)):
+                if a < b:
+                    act(ap(gb, o + 16 * a, o + 16 * b), ind(xw, ap(names, 128 * h + a, 128 * h + b)), AF.Copy)
+            mm(P(h, 0, w), ones(4), ap("KR", 0, w, 1, 0, 4), True, False)
+            mm(P(h, 0, 128, 1, 0, 64), ap("XB", 128 * h, 128 * h + 64), ap("NBO"), False, False)
+            mm(P(h, 0, 128, 1, 64, 128), ap("XB", 128 * h + 64, 128 * h + 128), ap("PBO"), False, False)
+            if not d:
+                mm(P(h, 0, 128), half("GH", h), ap("IB"), False, False)
+                mm(P(h, 128, 256), half("LBH", h), ap("IB"), False, False)
+            for b in range(2):
+                for j in range(8):
+                    mm(P(4 + 2 * b, 64 * j, 64 * j + 64), ap("NIB"), ap("XB", 128 * h + 64, 128 * h + 128), j == 0, False)
+                for j in range(8):
+                    mm(P(4 + 2 * b, 64 * j, 64 * j + 64), ap("IB"), ap(gb, o + 1024 + 8 * b + j, o + 2048, 16), False, j == 7)
+                act(mx_(h, 8 * b, 8 * b + 8, 1), P(4 + 2 * b), AF.Relu)
+            if d:
+                offers(h)
+            for i in range(16):
+                mm(P(h, i, w, 16), ap(gb, o + i, o + 2048, 16), ap("B8K", 0, w // 16), False, False)
+            for i in range(16):
+                tt(mx_(h, i, i + 1, 0), P(2, 64 * h, 64 * h + 64), ap(gb, o + i, o + 1024, 16), mx)
+                mm(P(h, i, 128, 16), (T["MX%d" % h][:, i, :], "MX%d" % h, i, i + 1, 1), b8b, False, False, mx_(h, i, i + 1, 1))
+            mm(P(h, 0, 128), half(("LBH", "LUH")[d], h), ap("IB"), False, True)
+            scan(half("SC1", h), ap("RB", 0, 128), P(h, 0, 128), ad, mn)
+            return ap("SC1", 128 * h + 15, 128 * h + 128, 16)
+
+        def near(h):
+            lu = (3, 5)[h]
+            ue = keys(h, 0, "LBU")
+            ts(hs("si", "un", h), ue, 8191, ALU.bitwise_and)
+            scan(half("HK", h), ap("RB", 128, 256), P(h, 128, 256), mx, mn)
+            ts(hs("sm", "xx", h), ue, THR, ltn, 65536.0, mul)
+            mm(P(lu, 0, 128), half("LBH", h), ap("IB"), True, t == 2)
+            if t < 2:
+                mm(P(lu, 128, 256), half("MT", t), half("CMP", h), False, True)
+            act(part("LT", h, 0, 16), P(lu, 0, 128), AF.Copy)
+            sel(part("LT", h, 16, 32), part("LT", h, 0, 16), [[0, 128]], ge, 0, 0, 0)
+            if t < 2:
+                act(half("NM", h), P(lu, 128, 256), bias=nq[t])
+                mm(P(lu, 256, 384), ap("IB"), half("CRP", h), True, False)
+                mm(P(lu, 256, 384), ap("N128"), half("NM", h), False, True)
+                act(half("BM", h), P(lu, 256, 384), AF.Relu, bias=CEN / 16)
+            act(part("ST", h, 1, 17), half("HK", h), AF.Sign, bias=65536.0, scale=-1.0)
+
+        def fetch(h):
+            ts(hs("su", "u", h), wrap(hs("si", "un", h), h, 16), 2047.0 + G * (t + 1), mn)
+            ts(half("LUU", h), ind(ap("N", 0, 2048 + G * (t + 1)), hs("su", "u", h)), float(W + 1), mn)
+            ts(half("LUH", h), half("LUU", h), -CEN, ad)
+
+        def offers(h):
+            lu = (3, 5)[h]
+            mm(P(lu, 0, 128), half("LUH", h), ap("IB"), True, False)
+            mm(P(lu, 128, 256), ap("IB"), part("ST", h, 1, 17), False, False)
+            mm(P(lu, 128, 256), ap("NIB"), part("ST", h, 0, 16), False, True)
+            tt(half("EE", 32 + h), P(2, 256 + 128 * h, 384 + 128 * h), half("LUH", h), eq)
+            mm(P(h, 0, 128), half("EE", 32 + h), ap("IBIG"), False, False)
+            for r in range(16):
+                tt(half("EE", 2 * r + h), P(lu, 0, 128), part("LT", h, r, r + 16), eq)
+                mm(P(h, 0, 128), ap("IBIG"), half("EE", 2 * r + h), False, False)
+            act(half("OH", h), P(lu, 128, 256), AF.Copy)
+
+        def aside():
+            asks, need = sl("sb", "asks"), sl("sb", "need")
+            ts(sl("si", "k"), ap("HK", 15, 256, 16), 0.0, mx)
+            ts(sm("y1"), sl("si", "un"), 2048.0, ge)
+            tt(need, sl("si", "k"), sm("xx"), ltn)
+            ts(sl("si", "old"), sl("si", "k"), 4095, ALU.bitwise_and)
+            tt(asks, sm("y1"), need, mul)
+            ts(sm("fk"), sl("si", "old"), THR + YD, ad)
+            mm(P(7, 32, 48), ap("TRA"), asks, True, False)
+            mm(P(7, 32, 48), ap("N384"), need, False, False)
+            mm(P(7, 40, 48), ap("ONES"), sl("sb", "asks", 0, 8), False, True)
+            ts(sm("y2"), P(7, 32, 48), -65.0, gt, -2 * THR, mul)
+            tt(sm("fk"), sm("fk"), sm("y2"), ad)
+            if t < 2:
+                ts((T["ZB"][:, :, 15:143:16], "ZB", 0, 1, 1), sl("si", "old"), -CEN, ad)
+                for h in range(2):
+                    for q in range(16):
+                        mm(P(7, 48 + 8 * h, 56 + 8 * h), whole("ZB", T["ZB"][:, h, 15 - q:143 - q]), ap("IB", q, 128, 16),
+                           h + q == 0, h + q == 16)
+                ts(sl("su", "old"), P(7, 48, 64), CEN, ad)
+                act(ap("YO"), ind(ap("Y", 0, YD), sl("su", "old")), AF.Copy)
+                act(ap("RG"), ind(ap("R"), bu), AF.Copy)
+                act(ap("YB"), ind(yw, bu), AF.Copy)
+
+        def change(h, we):
+            bn, ba, br = ((P(4, 0, 128), P(6, 0, 128), P(3, 0, 128)), (P(5, 0, 128), P(5, 128, 256), P(5, 256, 384)))[h]
+            w, pw, wn, dv, b = hs("si", "w", h), hs("si", "pw", h), hs("si", "wn", h), hs("sm", "dv", h), hs("su", "b", h)
+            tt(w, we, hs("sm", "fk", h), mn)
+            if t < 2:
+                ts(pw, w, 8191, ALU.bitwise_and)
+            ts(wn, w, 4095, ALU.bitwise_and)
+            if t < 2:
+                cp(hs("sm", "pw", h), pw)
+                act(half("PB", h), spread(hs("sm", "pw", h)), AF.Copy)
+                wp = wrap(pw, h, 64)
+                mm(P(h, 128, 320), half("PB", h), whole("JF", T["JF"][:, :, :]), True, True)
+            tt(dv, wn, hs("si", "old", h), sub)
+            tt(half("BC2", h), spread(dv), half("OH", h), mul)
+            mm(bn, ap("IB"), half("LBH", h), True, False)
+            mm(bn, half("BC2", h), ap("IF"), False, t == 2 or h == 0)
+            if t < 2:
+                pww, bad, table = hs("sm", "pww", h), hs("sm", "bad", h), ap(("AF", "AG")[t])
+                ts(pww, wp, 2.0 ** -14, mul)
+                act(ap("WR", 192 * h, 192 * h + 192), ind(pww, sl("su", "bp", 0, 12)), scale=2.0 ** 14)
+                ts(hs("su", "wa", h), wp, float(V - 1), mn)
+                cp(hs("su", "w", h), wp)
+                ts(bad, wp, float(V), ge)
+                act(half("YW", h), ind(ap("Y"), hs("su", "w", h)), AF.Copy)
+                tt(half("X1", h), ind(ap(("A", "AF")[t], 0, V), hs("su", "wa", h)), half("NM", h), mul)
+                tt(bad, bad, pww, ad)
+                mm(ba, ap("I16"), half("BM", h), h == 0, False)
+                mm(ba, half("DQ", t), half("NM", h), False, False)
+                mm(ba, ap("IB"), half("X1", h), False, h == 0)
+                mm(br, ap("IB"), half("RG", h), h == 0, False)
+                mm(br, ap("NIB"), half("YO", h), False, False)
+                mm(br, ap("IB"), half("YW", h), False, True)
+                act(half("AN", h), ba, bias=qa[t])
+                o = 192 * h
+                tt(ap("DE", o, o + 192), P(h, 128, 320), ap("WR", o, o + 192), eq)
+                scan(ap("DS", o, o + 192), ap("DE", o, o + 192), ap("MF"), ad, mul)
+                tg = hs("su", "tg", h)
+                bad = [ap(bad[1], bad[2] + j, bad[3], 2) for j in range(2)]
+                for j in (1, 0):
+                    tt(bad[j], bad[j], ap("DS", o + 15 + 32 * j, o + 192, 48), ad)
+                for j in (1, 0):
+                    ts(ap(tg[1], tg[2] + j, tg[3], 2), bad[j], 16384.0, mul, dum[j], mn)
+                for k in range(4 * h + 3, 4 * h - 1, -1):
+                    put(ind(table, sl("su", "tg", 2 * k, 2 * k + 2)), ap("AN", 32 * k, 32 * k + 32))
+                act(half("TX", h), br, AF.Square, bias=-3.5, scale=4.5)
+                act(half("ZN", h), half("TX", h), AF.Relu, bias=65.0, scale=-1.0)
+                if t == 0:
+                    act(half("RN", h), br, AF.Copy)
+                tt(ind(ap("Z"), b), half("ZN", h), half("YB", h), mul)
+            act(half("NL", h), bn, bias=CEN)
+            cp(ind(ap("N", 0, 2048), b), half("NL", h))
+
         fill(1)
-        if t < 2:
-            mm(P(3, 0, 16), ap("ONES"), die, True, True)
-        tt(ap("F"), P(2, 0, 128), ap("DW"), gt)
-        mm(P(1, 0, 128), ap("BO"), ap("F"), True, True)
-        mm(P(1, 128, 256), ap("TRI16"), ap("F"), True, True)
         fill(2)
-        scan(ap("CC", 1, 129), P(1, 0, 128), ap("C256"), ad, mn)
+        if t == 0:
+            nfloat(2)
+        act(ap("X", V + t, W, 7), ap("XL", 192 * t, 192 * t + ng), AF.Copy)
+        for h in (1, 0):
+            treated(h)
         if t < 2:
-            mm(P(2, 0, 112), ap("TRQ"), ap("F", 0, 112), True, False)
-            mm(P(2, 0, 112), ap("IB"), ap("CC", 0, 112), False, True)
-        for c in range(CV, 16):
-            act(ap("GA0", 128 * c, 128 * c + 128), ap("CC", 1, 129), AF.Sign, bias=sm("sh", c, c + 1), scale=-1.0,
-                acc=sm("acc", c, c + 1))
-        for c in range(CV):
-            ts(ap("MX0", 128 * c, 128 * c + 128), ap("CC", 1, 129), ap("SCB", c, c + 1), le)
-        tt(ap("CUM"), P(1, 128, 256), ap("CC", 0, 128), ad)
-        scan(ap("GV1", 0, 128 * CV), ap("RZ", 0, 128 * CV), ap("MX0", 0, 128 * CV), mul, ad)
+            act(ap("F", 0, 112), P(6, 0, 112), AF.Relu, bias=-4352.0)
+        for h in (1, 0):
+            mm(P(2, 256 + 128 * h, 384 + 128 * h), ap("I16"), half("CRP", h), h == 1, False)
+            mm(P(2, 256 + 128 * h, 384 + 128 * h), ap("BO"), half("CMP", h), False, False)
+            mm(P(2, 64 * h, 64 * h + 64), ap("IB"), ap("XB", 128 * h, 128 * h + 64), False, h == 0)
+        near(1)
+        fetch(1)
+        near(0)
+        fetch(0)
+        aside()
+        we = [keys(h, 1, "LUU") for h in (1, 0)]
+        change(1, we[0])
+        change(0, we[1])
+        if t == 0:
+            for j in range(3, 7):
+                iota(cand("DD", j), [[0, 256]], 0)
+            sel(cand("AG", 2), cand("AF", 2), [[0, 256]], ge, 0, 0, 0)
+        if t < 2:
+            lists(t + 1)
+            prep_n1(t + 1)
+            for a, b in ((0, 64), (64, 256)):
+                ts(ap("AU", a, b), ap(("AF", "AG")[t], t + 1 + 7 * a, t + 7 * b - 5, 7), M1 - AO, ad, -M1, ad)
+        continue
+        for h in range(2):
+            for gi in range(8):
+                o = (T["CM"][:, 8 * h:8 * h + 8, 16 * gi:16 * gi + 16], "CM", 8 * h + gi, 8 * h + gi + 1, 1)
+                if gi < CS:
+                    act(o, half("IOS", h), AF.Sign, bias=sm("ncc", gi, gi + 1))
+                else:
+                    ts(o, half("IOS", h), sl("sb", "cc", gi, gi + 1), ge, 2.0, mul)
+            for k in range(8 * h, 8 * h + 8):
+                mm(P(1, 2 * k, 2 * k + 2), (T["CM"][:, k, :], "CM", 8 * h, 8 * h + 8, 1), ap("ONES", 0, 2), k == 0, k == 15)
         cu, cb = sl("su", "c"), sl("sb", "c")
-        ts(sl("su", "c", CV, 16), sm("acc", CV, 16), 0.5, mul, 64.0, ad)
-        cp(sl("su", "c", 0, CV), ap("GV1", 127, 128 * CV, 128))
+        fill(1)
+        ts(cu, P(1, 0, 32, 2), 0.5, mul, sm("col", 6, 7), ad)
         tt(ap("CMP"), ind(ap("CUM"), cu), ap("IOS"), le)
         cp(cb, cu)
-        act(ap("CRP"), ind(ap("IOS", 0, 128), cu), AF.Copy)
+        act(ap("CRP"), ind(ap("IOS", 0, 128), cu), bias=-CEN / 16)
         act(ap("X", V + t, W, 7), ap("XL", 192 * t, 192 * t + ng), AF.Copy)
         for q in range(16):
             mm(P(7, 0, 16), pick(q), ap("CMP", q, 256, 16), q == 0, False)
         mm(P(7, 0, 16), ap("I16"), cb, False, True)
         if t < 2:
-            act(ap("F", 0, 112), P(2, 0, 112), AF.Relu, bias=-511.0)
-            add("v", lambda: g.vector.tensor_reduce(sm("col", 5, 6)[0], P(3, 0, 16)[0], AxisListType.X, ad),
-                [P(3, 0, 16)], [sm("col", 5, 6)])
-            ts(sl("si", "e", 0, 1), sm("col", 5, 6), 0.5, mul)
+            act(ap("F", 0, 112), P(6, 0, 112), AF.Relu, bias=-4352.0)
+        fill(2)
         if t == 0:
             nfloat(2)
         cp(bu, P(7, 0, 16))
-        cp(ap("LBU"), ind(ap("N", 0, 2048), bu))
+        for h in (1, 0):
+            cp(half("LBU", h), ind(ap("N", 0, 2048), sl("su", "b", 8 * h, 8 * h + 8)))
         act(ap("XB"), ind(xw, bu), AF.Copy)
         for a in (128, 192):
             act(ap("GA0", 16 * a - 2048, 16 * a - 1024), ind(xw, ap("LBU", a, a + 64)), AF.Copy)
-        ts(ap("LBH"), ap("LBU"), -CEN, ad)
+            if a == 128 and WB < 128:
+                act(ap("GV0", 16 * WB, 2048), ind(xw, ap("LBU", WB, 128)), AF.Copy)
+        ts(ap("LBH", 128, 256), ap("LBU", 128, 256), -CEN, ad)
+        cp(ap("GV0", 0, 16 * WB), ind(xw, ap("LBU", 0, WB)))
+        ts(ap("LBH", 0, 128), ap("LBU", 0, 128), -CEN, ad)
         ts(ap("GH"), ap("LBU"), float(V), ge, 256.0 + G * t, mul)
-        cp(ap("GV0", 0, 2048), ind(xw, ap("LBU", 0, 128)))
-        if t < 2:
-            ts(sl("si", "e", 1, 2), sl("si", "e", 0, 1), 7, ALU.bitwise_and)
-        for h in range(2):
-            mm(P(7, 16 + 8 * h, 24 + 8 * h), half("CMP", h), b8, True, False)
-            mm(P(7, 16 + 8 * h, 24 + 8 * h), half("CRP", h), b8, False, True)
-        mm(P(2, 0, 128), ap("IB"), half("XB", 0), True, True)
+        mm(P(2, 256, 512), ap("I16"), ap("CRP"), True, False)
+        mm(P(2, 256, 512), ap("BO"), ap("CMP"), False, False)
+        mm(P(2, 0, 128), ap("IB"), half("XB", 0), False, True)
 
-        def preload(banks):
-            for b in banks:
-                for j in range(4):
-                    mm(P(b, 128 * j, 128 * j + 128), ap("NIB"), half("XB", 1), j == 0, False)
+        def preload(banks, b):
+            for j in range(8):
+                mm(P(banks[b], 64 * j, 64 * j + 64), ap("NIB"), ap("XB", 128 + b // 2 * 64, 192 + b // 2 * 64), j == 0, False)
 
         def vmax(gb, i):
             tt(ap("MX0", 128 * i, 128 * i + 128), P(2, 0, 128), ap(gb, i, 2048, 16), mx)
@@ -607,137 +883,149 @@ def rank_program(g, core, T, topo):
         def rows(a, b, c=0, d=128):
             return (T["MX1"][:, a:b, c:d] if b > a + 1 else T["MX1"][:, a, c:d], "MX1", a, b, 1)
 
-        def adiff(b, gb, i0):
-            for j in range(4):
-                mm(P(b, 128 * j, 128 * j + 128), ap("IB"), ap(gb, i0 + j, 2048, 16), False, j == 3)
-            act(rows(i0, i0 + 4), P(b), AF.Abs)
+        def adiff(banks, b, gb):
+            for j in range(8):
+                o = b // 2 * 1024
+                mm(P(banks[b], 64 * j, 64 * j + 64), ap("IB"), ap(gb, o + (b & 1) * 8 + j, o + 1024, 16), False, j == 7)
+
+        def aabs(banks):
+            for b in AB:
+                act(rows((b & 1) * 8, (b & 1) * 8 + 8, b // 2 * 64, b // 2 * 64 + 64), P(banks[b]), AF.Abs)
 
         def asum(a, b, w, stop=False):
             for i in range(a, b):
                 mm(P(1, i, 16 * w, 16), rows(i, i + 1), ap("B8J", 0, w), False, stop and i == b - 1)
 
+        bb = (3, 4, 5, 6)
         for b in range(4):
-            for j in range(8):
-                mm(P(3 + b, 64 * j, 64 * j + 64), ap("NIB"), ap("XB", 128 + b // 2 * 64, 192 + b // 2 * 64), j == 0, False)
+            preload(bb, b)
         for h in range(2):
             mm(P(h, 0, 256), ones(4), ap("KR", 0, 256, 1, 0, 4), True, False)
-            mm(P(h, 0, 128), half("GH", h), ap("IB"), False, False)
-            mm(P(h, 128, 256), half("LBH", h), ap("IB"), False, False)
+        if t < 2:
+            mm(P(7, 256, 512), half("MT", t), ap("CMP"), True, False)
+        mm(P(7, 128, 256), half("LBH", 1), ap("IB"), t == 2, False)
+        mm(P(0, 0, 128), half("XB", 0), ap("NBO"), False, False)
+        for a in (0, 128):
+            mm(P(1, a, a + 128), half("LBH", 1), ap("IB"), False, False)
+        mm(P(1, 128, 256), half("XB", 1), ap("PBO"), False, False)
         for b in range(4):
-            if b == 2:
-                mm(P(0, 0, 128), half("XB", 0), ap("NBO"), False, False)
-                mm(P(1, 0, 128), half("LBH", 1), ap("IB"), False, False)
-                mm(P(1, 128, 256), half("XB", 1), ap("PBO"), False, False)
-            for j in range(8):
-                o = b // 2 * 1024
-                mm(P(3 + b, 64 * j, 64 * j + 64), ap("IB"), ap("GA0", o + (b & 1) * 8 + j, o + 1024, 16), False, j == 7)
-        for b in range(4):
-            act(rows((b & 1) * 8, (b & 1) * 8 + 8, b // 2 * 64, b // 2 * 64 + 64), P(3 + b), AF.Abs)
+            adiff(bb, b, "GA0")
+        aabs(bb)
         for i in range(16):
             mm(P(0, i, 256, 16), ap("GV0", i, 2048, 16), ap("B8K"), False, False)
+        mm(P(7, 0, 128), half("LBH", 0), ap("IB"), False, True)
+        mm(P(0, 128, 256), half("LBH", 0), ap("IB"), False, False)
+        for h in range(2):
+            mm(P(h, 0, 128), half("GH", h), ap("IB"), False, False)
         for i in range(16):
             vmax("GV0", i)
-            if i == 5:
+            if i == AS[0]:
                 asum(0, 8, 16)
-            if i == 11:
-                asum(8, 16, 16, True)
         mm(P(0, 0, 128), half("LBH", 0), ap("IB"), False, True)
-        act(sm("bT"), P(7, 16, 32), bias=-CEN)
-        act(ap("BT"), ind(sm("bT"), bc), AF.Copy)
-        if t < 2:
-            mm(P(2, 256, 512), ap("BO"), ap("CMP"), True, True)
-        for h in range(2):
-            mm(P(5, 256 + 128 * h, 384 + 128 * h), half("LBH", h), ap("IB"), True, True)
+        asum(8, 16, 16, True)
+        act(lt(0), P(7, 0, 256), AF.Copy)
+        sel(lt(16), lt(0), [[0, 256]], ge, 0, 0, 0)
+        if t == 0:
+            for j in range(3, 7):
+                iota(cand("DD", j), [[0, 256]], 0)
 
         def least(o, h, a):
-            scan(ap("SC1", o + 128 * h, o + 128 * h + 128), ap("RB"), P(h, a, a + 128), ad, mn)
+            scan(ap("SC1", o + 128 * h, o + 128 * h + 128), ap("RB", 0, 128), P(h, a, a + 128), ad, mn)
 
-        least(0, 1, 0)
-        least(256, 1, 128)
+        def holes(h):
+            scan(half("HK", h), ap("RB", 128, 256), P(h, 128, 256), mx, mn)
+
         least(0, 0, 0)
+        holes(0)
+        least(0, 1, 0)
+        holes(1)
         if t < 2:
-            act(ap("TX"), P(2, 256, 512), AF.Abs, bias=nq[t])
-            act(ap("NM"), ap("TX"), AF.Sign)
+            act(ap("NM"), P(7, 256, 512), bias=nq[t])
             mm(P(3, 0, 256), ap("IB"), ap("CRP"), True, False)
             mm(P(3, 0, 256), ap("N128"), ap("NM"), False, True)
-        act(lt(0), P(5, 256, 512), AF.Copy)
-        act(lt(16), P(5, 256, 512), AF.Copy)
-        if t < 2:
-            act(ap("BM"), P(3, 0, 256), AF.Relu)
-        ue, ke = ap("SC1", 15, 256, 16), ap("SC1", 271, 512, 16)
+            act(ap("RG"), ind(ap("R"), bu), AF.Copy)
+            act(ap("BM"), P(3, 0, 256), AF.Relu, bias=CEN / 16)
+            act(ap("YB"), ind(yw, bu), AF.Copy)
+        ue, ke = ap("SC1", 15, 256, 16), ap("HK", 15, 256, 16)
         ts(sl("si", "un"), ue, 8191, ALU.bitwise_and)
         ts(sm("xx"), ue, THR, ltn, 65536.0, mul)
-        if t < 2:
-            cp(e8, sl("si", "e", 1, 2))
         wp = wrap(sl("si", "un"), 7, 48)
-        least(256, 0, 128)
         asks = sl("sb", "asks")
         ts(sm("y1"), sl("si", "un"), 2048.0, ge)
-        ts(sl("si", "k"), ke, 65536.0, mn, 0.0, mx)
+        ts(sl("si", "k"), ke, 0.0, mx)
+        act(whole("ST", T["ST"][:, :, 1:17]), ap("HK"), AF.Sign, bias=65536.0, scale=-1.0)
         for h in range(2):
             mm(P(h, 0, 128), ones(4), ap("KR", 0, 128, 1, 0, 4), True, False)
         mm(P(0, 0, 128), half("XB", 0), ap("NBO"), False, False)
-        preload((4, 6, 3))
+        bd = (4, 6, 3, 7)
+        for b in range(3):
+            preload(bd, b)
         uu = sl("su", "u")
-        ts(uu, wp, 2047.0 + G * (t + 1), mn)
         need = sl("sb", "need")
         tt(need, sl("si", "k"), sm("xx"), ltn)
+        ts(sl("si", "old"), sl("si", "k"), 4095, ALU.bitwise_and)
+        ts(uu, wp, 2047.0 + G * (t + 1), mn)
+        ts(sm("fk"), sl("si", "old"), THR + YD, ad)
         for h in (1, 0):
             ts(half("LUU", h), ind(ap("N", 0, 2048 + G * (t + 1)), sl("su", "u", 8 * h, 8 * h + 8)), float(W + 1), mn)
         tt(asks, sm("y1"), need, mul)
-        act(ap("GA1", 0, 2048), ind(xw, ap("LUU", 128, 256)), AF.Copy)
+        act(ap("GA1", 0, 1024), ind(xw, ap("LUU", 128, 192)), AF.Copy)
         act(ap("GA0", 16 * WV, 2048), ind(xw, ap("LUU", WV, 128)), AF.Copy)
+        act(ap("GA1", 1024, 2048), ind(xw, ap("LUU", 192, 256)), AF.Copy)
         ts(ap("LUH"), ap("LUU"), -CEN, ad)
         for h in range(2):
             mm(P(5, 128 * h, 128 * h + 128), half("LUH", h), ap("IB"), True, True)
+        if t < 2:
+            ts(whole("ZB", T["ZB"][:, :, 15:143:16]), sl("si", "old"), -CEN, ad)
+        tt(ap("EE", 4096, 4352), P(2, 256, 512), ap("LUH"), eq)
         mm(P(5, 256, 272), ap("TRA"), asks, True, False)
         mm(P(5, 256, 272), ap("N384"), need, False, False)
         mm(P(5, 264, 272), ap("ONES"), sl("sb", "asks", 0, 8), False, True)
         cp(ap("GA0", 0, 16 * WV), ind(xw, ap("LUU", 0, WV)))
-        preload((7,))
-        for r in range(17):
-            if r == 0:
-                ts(sl("si", "old"), sl("si", "k"), 4095, ALU.bitwise_and)
+        preload(bd, 3)
+        for r in range(16):
             if r == 1:
                 ts(sm("y1"), P(5, 256, 272), -65.0, gt, -2 * THR, mul)
-            if r == 2:
-                ts(sm("fk"), sl("si", "old"), THR + YD, ad)
             if r == 3:
                 tt(sm("fk"), sm("fk"), sm("y1"), ad)
-            if r == 6:
-                ts(sl("si", "row"), sl("si", "k"), 12, ALU.logical_shift_right)
-            if r == 7 and t < 2:
-                ts(whole("ZB", T["ZB"][:, :, 15:143:16]), sl("si", "old"), -CEN, ad)
-            tt(ap("EE", 256 * r, 256 * r + 256), P(5, 0, 256), lt(r) if r < 16 else ap("BT"), eq)
+            tt(ap("EE", 256 * r, 256 * r + 256), P(5, 0, 256), lt(r), eq)
             for h in range(2):
                 mm(P(h, 0, 128), ap("IBIG"), ap("EE", 256 * r + 128 * h, 256 * r + 128 * h + 128), False, False)
+            if r == 0:
+                for h in range(2):
+                    mm(P(h, 0, 128), ap("EE", 4096 + 128 * h, 4224 + 128 * h), ap("IBIG"), False, False)
             if r == 4:
                 mm(P(1, 0, 128), half("LUH", 1), ap("IB"), False, False)
-            if 8 <= r < 12:
-                adiff((4, 7, 3, 6)[r - 8], "GA1", 4 * (r - 8))
-        tt(ap("OH"), ind(sl("si", "row"), bc), ap("IOI"), eq)
+            if t < 2 and 1 <= r < 5:
+                h = (r - 1) // 2
+                for q in range(8 * (r & 1 ^ 1), 8 * (r & 1 ^ 1) + 8):
+                    mm(P(2, 128 + 8 * h, 136 + 8 * h), whole("ZB", T["ZB"][:, h, 15 - q:143 - q]), ap("IB", q, 128, 16),
+                       h + q == 0, h + q == 16)
+            if t < 2 and r == 9:
+                ts(sl("su", "old"), P(2, 128, 144), CEN, ad)
+            if r in (6, 8):
+                adiff(bd, r // 2 - 3, "GA1")
         for i in range(16):
             mm(P(0, i, 128, 16), ap("GA0", i, 2048, 16), b8n, False, False)
-        for k in range(4):
-            for i in range(4 * k, 4 * k + 4):
-                vmax("GA0", i)
-            if k < 3:
-                asum(4 * k, 4 * k + 4, 8)
-            if k == 2:
-                asum(12, 16, 8, True)
+        for i in range(16):
+            vmax("GA0", i)
+            if i in (1, 3):
+                adiff(bd, 2 + i // 2, "GA1")
+            if i == 3:
+                aabs(bd)
+            if i == AS[1]:
+                asum(0, 8, 8)
         mm(P(0, 0, 128), half("LUH", 0), ap("IB"), False, True)
+        asum(8, 16, 8, True)
+        mm(P(5, 256, 512), ap("IB"), whole("ST", T["ST"][:, :, 1:17]), True, False)
+        mm(P(5, 256, 512), ap("NIB"), whole("ST", T["ST"][:, :, 0:16]), False, True)
+        act(ap("OH"), P(5, 256, 512), AF.Copy)
         if t < 2:
-            act(ap("RG"), ind(ap("R"), bu), AF.Copy)
-            act(ap("YB"), ind(yw, bu), AF.Copy)
-        if t < 2:
-            for h in range(2):
-                for q in range(16):
-                    mm(P(6, 8 * h, 8 * h + 8), whole("ZB", T["ZB"][:, h, 15 - q:143 - q]), ap("IB", q, 128, 16),
-                       h + q == 0, h + q == 16)
+            act(ap("YO"), ind(ap("Y", 0, YD), sl("su", "old")), AF.Copy)
         else:
             for h in range(2):
                 mm(P(6 + h, 0, 128), ap("IB"), half("LBH", h), True, False)
-        for h in (1, 0):
+        for h in range(2):
             least(0, h, 0)
         tt(sl("si", "w"), ap("SC1", 15, 256, 16), sm("fk"), mn)
         if t < 2:
@@ -746,9 +1034,9 @@ def rank_program(g, core, T, topo):
         if t < 2:
             cp(sm("pw"), sl("si", "pw"))
             act(ap("PB"), ind(sm("pw"), bc), AF.Copy)
+            wp = wrap(sl("si", "pw"), 3, 0)
         tt(sm("dv"), sl("si", "wn"), sl("si", "old"), sub)
         if t < 2:
-            wp = wrap(sl("si", "pw"), 3, 0)
             for h in range(2):
                 for j in range(2):
                     mm(P(5, 128 * j + 64 * h, 128 * j + 64 * h + 64), half("PB", h), ap("JF", 64 * j, 64 * j + 64), True, True)
@@ -770,9 +1058,7 @@ def rank_program(g, core, T, topo):
         act(ap("WR"), ind(sm("pww"), sl("su", "bp")), scale=2.0 ** 14)
         ts(sl("su", "wa"), wp, float(V - 1), mn)
         cp(sl("su", "w"), wp)
-        ts(sl("su", "old"), P(6, 0, 16), CEN, ad)
         act(ap("YW"), ind(ap("Y"), sl("su", "w")), AF.Copy)
-        act(ap("YO"), ind(ap("Y", 0, YD), sl("su", "old")), AF.Copy)
         ts(sm("bad"), wp, float(V), ge)
         tt(ap("X1"), ind(ap("AF", 0, V), sl("su", "wa")), ap("NM"), mul)
         tt(sm("bad"), sm("bad"), sm("pww"), ad)
@@ -800,16 +1086,68 @@ def rank_program(g, core, T, topo):
             if k == 5 and t == 0:
                 act(ap("RN"), P(0, 0, 256), AF.Copy)
         cp(ind(ap("N", 0, 2048), bu), ap("NL"))
-        prep_n1(t + 1)
+        lists(t + 1)
         tt(ind(ap("Z"), bu), ap("ZN"), ap("YB"), mul)
-        prep_n2(t + 1, lambda: None, masks)
-        prep_n3()
+        prep_n1(t + 1)
         for a, b in ((0, 64), (64, 256)):
             ts(ap("AU", a, b), ap("AF", t + 1 + 7 * a, t + 7 * b - 5, 7), M1 - AO, ad, -M1, ad)
 
     for k, (a, b) in enumerate(((0, 896), (896, V))):
         dma("sa"[k], T.yn[:, a:b], T["N"][:, a:b], [ap("N", a, b)], [])
     dma("g", T.yd[:, :], T["DD"][0:128:16, :], [ap("DD")], [])
+
+    hold = [o["t"] if o["sem"] is None else {"x": 0.0, "g": 0.3}.get(o["q"], 0.05) for o in ops]
+    before, behind, dmas = [[] for o in ops], [[] for o in ops], {}
+    for i, o in enumerate(ops):
+        lag = {j: ops[j]["t"] for j in o["after"]}
+        if o["sem"] is not None and o["q"] != "x":
+            if o["q"] in dmas:
+                lag[dmas[o["q"]]] = hold[dmas[o["q"]]]
+            dmas[o["q"]] = i
+        if o["q"] == "g" and i > sent:
+            lag[sent] = 2.0
+        lag.update({j: ops[j]["t"] + HOP for j in o["deps"]})
+        for j, d in lag.items():
+            before[i].append((j, d, j in o["deps"]))
+            behind[j].append((i, d + hold[i] - hold[j], j in o["deps"]))
+
+    def lay(seq, waits, gaps, more=0.0):
+        at, busy = {}, {q: [] for q in "vapgsx"}
+        for i in seq:
+            s = max([at[j] + d + more * w for j, d, w in waits[i]] + [0.0])
+            row = busy[ops[i]["q"]]
+            k = len(row)
+            while gaps and k and row[k - 1][0] > s:
+                k -= 1
+            if k:
+                s = max(s, row[k - 1][1])
+            while k < len(row) and s + hold[i] > row[k][0] + 1e-9:
+                s = row[k][1]
+                k += 1
+            row.insert(k, (s, s + hold[i]))
+            at[i] = s
+        return at
+
+    seq = [i for i, o in enumerate(ops) if o["q"] != "x"]
+    for i in lands.values():
+        seq.insert(seq.index(min(ops[i]["after"])) + 1, i)
+    at = lay(seq, before, INIT > 0)
+
+    def tighten(at, more):
+        back = lay(sorted(seq, key=lambda i: (-at[i] - hold[i], -i)), behind, True, more)
+        return lay(sorted(seq, key=lambda i: (-back[i] - hold[i], i)), before, True, more)
+
+    best = (1e9, at)
+    for k in range(SCHED):
+        at = tighten(tighten(best[1], MORE[k % len(MORE)]), 0.0)
+        best = min(best, (max(at[i] + ops[i]["t"] for i in seq), at), key=lambda x: x[0])
+        DBG.append(best[0])
+    if SCHED:
+        seq.sort(key=lambda i: (best[1][i], i))
+        place = {i: k for k, i in enumerate(seq)}
+        ops = [ops[i] for i in seq]
+        for o in ops:
+            o["deps"] = {place[j] for j in o["deps"]}
 
     for o in ops:
         best = {}

@@ -4,65 +4,53 @@ from concourse.mybir import AluOpType as ALU, AxisListType, ActivationFunctionTy
 V, G, W = 1792, 1296, 3088
 CEN = 1552.0
 NW = 2048 + 3 * G
-YD, YL = 4096, 3104
+YL = 3104
+Y0 = 800
 DK = 2 ** 17
 THR = 121.0 * DK
-M1, M32, M64 = 1.5 * 2 ** 23, 1.5 * 2 ** 28, 1.5 * 2 ** 29
+M1 = 1.5 * 2 ** 23
 AO = 32.0
 SC = 288
-PW = (192,) * 8 + (96, 96, 64)
-PV = (96, 84, 96, 92, 80, 92, 84, 84, 44, 44, 30)
+PW = (192,) * 8 + (128, 64, 64)
+PV = (96, 86, 90, 86, 86, 86, 86, 86, 58, 30, 30)
 NF = (2 * SC, 900, G, V)
-LV = ((32, 32, 32, 32), (26, 26, 28, 32), (26, 26, 28, 32))
-GO, DP, MS = (2, 3, 0, 1, 4, 5, 6, 7), 2, 6
-DBG = []
-INIT = 1
-MORE = (0.0, 0.1, -0.1, 0.05, -0.05)
-CY, CYP, GAT, SCA, HOP, FIX, BYTE, SCHED = 0.00083, 0.00042, 1.56, 3.8, 0.2, 0.0, 0.012, 10
-GV = ((64, 40, 16, 8), (64, 40, 16, 8), (64, 40, 16, 24))
-WB, AS = 128, (8, 12)
-AB = (0, 1, 2, 3)
-WV = 24
+LV = ((34, 32, 32, 32), (28, 28, 28, 32), (28, 28, 28, 32))
+GV = ((64, 48, 20, 8), (64, 48, 20, 8), (64, 48, 20, 24))
 RL, RH = 18, 114
 RW = RL + RH
-SX = (24, 63)
 CS = 2
+HOP, BYTE = 0.2, 0.012
+PACES = ((0.00083, 1.56, 3.8), (0.00085, 1.15, 2.2), (0.00105, 1.9, 5.2), (0.0009, 1.7, 4.2))
+PASSES, MORE = 44, (0.1, -0.1, 0.2, -0.15, 0.05, -0.05, 0.3, 0.15)
+ORDER = []
 
 F32, BF, F16, I32, U16 = "float32", "bfloat16", "float16", "int32", "uint16"
 SB = {
-    "NI": (V, I32), "NU": (V, U16), "N": (NW, F32), "KV": (G, F32), "A": (V, I32), "AF": (V + 32, F32),
-    "Y": (YD + YL, BF), "X": (3104, BF), "R": (2048, BF), "Z": (2048, BF), "DD": (V, BF),
-    "AG": (V + 32, F32), "GA0": (4096, BF), "GA1": (4096, BF),
-    "PBO": (128, BF), "EE": (17 * 256, BF), "RMP": (64 * RW, BF),
-    "T1": (3 * SC, BF), "T2": (3 * SC, BF), "XS": (192 * 3, BF), "XL": (192 * 3, BF), "TX": (256, BF),
-    "IB": (128, BF), "NIB": (128, BF), "IBIG": (128, BF), "I64": (128, BF), "I16": (128, BF),
-    "IF": (128, F32), "BO": (128, BF), "NBO": (128, BF),
-    "N128": (128, BF), "DQ": (256, BF), "B8K": (16, BF), "GH": (256, BF),
-    "TQ": (256, BF), "BQ": (256, BF), "IO8": (256, BF), "SEQ": (248, BF), "TRI": (128, BF), "ONES": (128, BF), "B8": (80, BF), "B8F": (16, F32), "SEL": (144, BF),
-    "WM": (128, F32), "IOI": (128, F32), "IOS": (256, BF), "RAMP": (RW, BF), "TRM": (128, BF),
-    "TRA": (128, BF), "N384": (128, BF), "IO4": (64, BF), "TN": (224, F32), "MT": (256, BF),
-    "KR": (256, BF), "C15": (384, BF), "I2": (128, BF), "RB": (256, F32), "IA": (128, BF), "IE": (128, BF),
-    "sm": (16 * 48, F32), "si": (16 * 12, I32), "su": (16 * 12, U16), "sb": (16 * 8, BF),
-    "AU": (256, U16), "AH": (256, F16), "NH": (256, F16), "EB": (256, BF), "MP": (256, BF),
-    "RR": (256, BF), "X1": (256, F16), "X2": (256, BF), "PP": (17 * 128, BF), "DB": (256, BF),
-    "S1": (128, BF), "DW": (128, BF), "F": (128, BF),
-    "I4K": (128, BF), "FP": (144, BF), "CUM": (128, F32), "CMP": (256, BF), "CRP": (256, BF),
+    "NI": (V, I32), "NU": (V, U16), "N": (NW, F32), "KV": (G, F32), "A": (YL, I32), "AF": (YL + 32, F32),
+    "AG": (YL + 32, F32), "Y": (YL, BF), "X": (YL, BF), "R": (2048, BF), "Z": (2048, BF), "DD": (V, BF),
+    "GA0": (4096, BF), "GA1": (4096, BF), "RMP": (64 * RW, BF), "PP": (17 * 128, BF),
+    "T1": (3 * SC, BF), "T2": (3 * SC, BF), "XS": (192 * 3, BF), "XL": (192 * 3, BF), "YC": (768, BF),
+    "IB": (128, BF), "NIB": (128, BF), "IBIG": (128, BF), "I64": (128, BF), "I16": (128, BF), "I2": (128, BF),
+    "I4K": (128, BF), "IA": (128, BF), "IE": (128, BF), "N12": (128, BF), "N128": (128, BF), "N384": (128, BF),
+    "BO": (128, BF), "NBO": (128, BF), "PBO": (128, BF), "B8": (80, BF), "B8K": (16, BF), "B8F": (16, F32),
+    "TQ": (256, BF), "BQ": (256, BF), "IO8": (256, BF), "SEL": (144, BF), "SEQ": (248, BF), "DQ": (256, BF),
+    "TRI": (128, BF), "TRM": (128, BF), "TRA": (128, BF), "ONES": (128, BF), "MT": (256, BF), "MF": (192, BF),
+    "WM": (128, F32), "IOI": (128, F32), "IOS": (256, BF), "IO4": (64, BF), "RAMP": (RW, BF), "TN": (224, F32),
+    "KR": (256, BF), "C15": (384, BF), "C12": (128, BF), "RB": (392, F32),
+    "sm": (16 * 16, F32), "si": (16 * 12, I32), "su": (16 * 12, U16), "sb": (16 * 8, BF),
+    "AU": (256, U16), "AH": (256, F16), "NH": (256, F16), "EB": (256, BF), "MP": (256, BF), "M5": (256, BF),
+    "X1": (256, F16), "X2": (256, BF), "S1": (128, BF), "DW": (128, BF), "F": (128, BF), "FP": (144, BF),
+    "CUM": (128, F32), "CMP": (256, BF), "CRP": (256, BF), "GH": (256, BF),
     "LBU": (256, U16), "LBH": (256, F16), "XB": (256, BF), "LUU": (256, U16), "LUH": (256, F16),
-    "SC1": (256, I32), "HK": (256, F32), "BC": (256, F32), "BC2": (256, F32),
-    "OH": (256, F32), "NL": (256, F32), "RG": (256, BF), "YB": (256, BF), "YW": (256, BF), "YO": (256, BF),
-    "ZN": (256, BF), "RN": (256, BF), "NM": (256, BF), "BM": (256, BF), "AN": (256, F32), "PB": (256, F32),
-    "YC": (768, BF), "WR": (384, F32), "DE": (384, BF), "DS": (384, BF), "MF": (192, BF),
+    "SC1": (272, I32), "HK": (256, F32), "BC": (256, F32), "BC2": (256, F32), "OH": (256, BF), "NL": (256, F32),
+    "RG": (256, BF), "YB": (256, BF), "YW": (256, BF), "YO": (256, BF), "TX": (256, BF), "ZN": (256, BF), "RN": (256, BF),
+    "NM": (256, BF), "BM": (256, BF), "AN": (256, F32), "PB": (256, F16), "DE": (384, BF), "DS": (384, BF),
 }
 SCRATCH = {k: ("sbuf", [128, n], d) for k, (n, d) in SB.items()}
-SCRATCH["LT"] = ("sbuf", [128, 16, 32], F32)
-SCRATCH["AT"] = ("sbuf", [128, 32, 16], BF)
-SCRATCH["MX0"] = SCRATCH["MX1"] = ("sbuf", [128, 16, 128], BF)
-SCRATCH["JF"] = ("sbuf", [128, 4, 48], F32)
-SCRATCH["MK"] = ("sbuf", [128, 4, 48], BF)
-SCRATCH["ZB"] = ("sbuf", [128, 2, 144], F16)
-SCRATCH["ST"] = ("sbuf", [128, 16, 17], BF)
-SCRATCH["CS"] = ("sbuf", [128, RL, 8], F32)
-SCRATCH["CM"] = ("sbuf", [128, 16, 128], BF)
+for _k, _a, _b, _d in (("LT", 16, 32, F32), ("AT", 32, 16, BF), ("MX0", 16, 128, BF), ("MX1", 16, 128, BF),
+                       ("JF", 4, 48, BF), ("JR", 4, 48, F32), ("MK", 4, 48, BF), ("EE", 256, 17, BF), ("C17", 40, 17, BF),
+                       ("ZB", 2, 144, F16), ("ST", 16, 17, BF), ("CS", RL, 8, F32), ("CM", 16, 128, BF)):
+    SCRATCH[_k] = ("sbuf", [128, _a, _b], _d)
 for _k in range(8):
     SCRATCH["p%d" % _k] = ("psum", [128, 512], F32)
 NDMA, NMSG = 16, 9
@@ -78,9 +66,9 @@ def rank_program(g, core, T, topo):
     dst = T.cores[(rank - 1) % n]
     rid, pid = topo.addr(dst)[0], topo.addr(dst)[1]
     engs = topo.engines(core, dst)
-    engs = [engs[1::4] if 5 <= k < 8 else engs[::2] for k in range(NMSG)]
+    engs = [engs[1::4] if 5 <= k < 8 else engs[k // 8::2] for k in range(NMSG)]
     Q = {"v": g.vector, "a": g.scalar, "p": g.tensor, "g": g, "s": g.sync}
-    ops, hist, cnt, lands = [], {}, {"d": 0}, {}
+    ops, hist, cnt, lands, groups = [], {}, {"d": 0}, {}, {}
 
     def ap(name, a=0, b=None, s=1, p0=0, p1=128):
         b = T[name].shape[-1] if b is None else b
@@ -95,8 +83,11 @@ def rank_program(g, core, T, topo):
     def whole(name, pattern):
         return (pattern, name, 0, 1, 1)
 
-    def lt(a):
-        return whole("LT", T["LT"][:, :, a:a + 16])
+    def half(name, h):
+        return ap(name, 128 * h, 128 * h + 128)
+
+    def part(name, h, a, b):
+        return (T[name][:, 8 * h:8 * h + 8, a:b], name, h, h + 1, 1)
 
     slots = {"sm": {}, "si": {}, "su": {}, "sb": {}}
 
@@ -107,30 +98,33 @@ def rank_program(g, core, T, topo):
     def sm(key, a=0, b=16):
         return sl("sm", key, a, b)
 
+    def hs(buf, key, h):
+        return sl(buf, key, 8 * h, 8 * h + 8)
+
     def cols(x):
         if len(x) > 5:
             return 16 * cols(x[5])
         return len(range(x[2], x[3], x[4])) if len(SCRATCH[x[1]][1]) == 2 else 0
 
-    def lasts(q, reads, writes, two):
+    def lasts(q, reads, writes, two, cy, gat, sca):
         xs = [x for x in writes[:1] + reads if isinstance(x, tuple)]
         n = ([cols(x) for x in xs if cols(x)] + [256])[0]
         if q == "p":
-            return max(64, n) * (4 if SCRATCH[xs[1][1]][2] == F32 else 1) * CYP
+            return max(64, n) * (4 if SCRATCH[xs[1][1]][2] == F32 else 1) * cy / 1.7
         if q == "g":
-            return 0.15 + 2 * n * CY
+            return 0.15 + 2 * n * cy
         if len(xs[0]) > 5 or len(xs) > 1 and len(xs[1]) > 5:
-            return 0.06 + n * (SCA if len(xs[0]) > 5 else GAT) * CY
+            return 0.06 + n * (sca if len(xs[0]) > 5 else gat) * cy
         if q == "a":
-            return max(64, n) * CY + FIX
+            return max(64, n) * cy
         if two and SCRATCH[xs[1][1]][0] == SCRATCH[xs[2][1]][0]:
-            return max(64, 2 * n) * CY + FIX
-        narrow = not two and all(SCRATCH[x[1]][2] in (BF, F16, U16) for x in xs[:2])
-        return max(64, n / 2 if narrow else n) * CY + FIX
+            return max(64, 2 * n) * cy
+        narrow = not two and all(SCRATCH[x[1]][2] in (BF, F16, U16) for x in xs)
+        return max(64, n / 2 if narrow else n) * cy
 
     def add(q, fn, reads, writes, sem=None, two=False, t=None):
         i = len(ops)
-        deps, after = set(), set()
+        deps = set()
         acc = []
         for w, xs in ((False, reads), (True, writes)):
             for x in xs:
@@ -144,16 +138,14 @@ def rank_program(g, core, T, topo):
                 o = ops[j]
                 same = o["q"] == q and o["sem"] is None and sem is None
                 if same and q == "p":
-                    if ps:
-                        after.add(j)
                     continue
                 apart = same and s == s2 and (a - a2) % s
                 if (ps and not same) or ((w or w2) and a < b2 and a2 < b and not apart):
                     deps.add(j)
         for name, a, b, s, w in acc:
             hist.setdefault(name, []).append((a, b, s, w, i))
-        ops.append({"q": q, "fn": fn, "deps": deps, "sem": sem, "mark": False, "after": set(sorted(after)[-1:]),
-                    "t": lasts(q, reads, writes, two) if t is None else t})
+        ops.append({"q": q, "fn": fn, "deps": deps, "sem": sem, "mark": False, "after": set(),
+                    "t": [lasts(q, reads, writes, two, *x) if t is None else t for x in PACES]})
 
     def x0(x):
         return x[0] if isinstance(x, tuple) else x
@@ -176,15 +168,19 @@ def rank_program(g, core, T, topo):
     def ms(o, c):
         add("v", lambda: g.vector.memset(o[0], c), [], [o])
 
-    def act(o, a, f=AF.Identity, bias=0.0, scale=1.0, acc=None):
-        add("a", lambda: g.scalar.activation(o[0], a[0], f, bias=x0(bias), scale=scale, accum_out=x0(acc)),
-            [a, bias], [o, acc])
+    def act(o, a, f=AF.Identity, bias=0.0, scale=1.0):
+        add("a", lambda: g.scalar.activation(o[0], a[0], f, bias=x0(bias), scale=scale), [a, bias], [o])
 
     def put(o, a):
         add("a", lambda: g.scalar.activation(o[0], a[0], AF.Silu), [a], [o])
 
     def mm(o, l, r, start, stop, also=None):
         add("p", lambda: g.tensor.matmul(o[0], l[0], r[0], start, stop), [l, r, also], [o])
+        group = groups.setdefault(o[1], [])
+        ops[-1]["after"].update(group if start or stop else group[:1])
+        if start or stop:
+            group.clear()
+        group.append(len(ops) - 1)
 
     def iota(o, pat, base, cm=0):
         if SCRATCH[o[1]][2] == I32:
@@ -203,7 +199,7 @@ def rank_program(g, core, T, topo):
 
     def send(k, o, a, plus=None):
         mask = sum(1 << e for e in engs[k])
-        t = 2.0 + cols(a) * (2 if SCRATCH[a[1]][2] == BF else 4) * BYTE / len(engs[k])
+        t = 3.0 + cols(a) * (2 if SCRATCH[a[1]][2] == BF else 4) * BYTE / len(engs[k])
         ops[lands[k]]["after"].add(len(ops))
         if plus is None:
             add("g", lambda: g.remote_dma(o[0], a[0], T.sem["r%d" % k], T.sem["l%d" % k], pid, rid, mask), [a], [],
@@ -212,7 +208,7 @@ def rank_program(g, core, T, topo):
             fold = RemoteDMATransfer(dst_ids=[DstId(rid=rid, pnc=pid)], dma_engine_mask=mask, remote_sem=T.sem["r%d" % k],
                                      srcs=[a[0], plus[0]], dsts=[o[0]], alu_op=1)
             add("g", lambda: g.remote_dma_fused([fold], local_sem=T.sem["l%d" % k]), [a, plus], [],
-                sem=("l%d" % k, len(engs[k]), False), t=2 * t)
+                sem=("l%d" % k, len(engs[k]), False), t=1.1 * t)
 
     def landed(k, o):
         lands[k] = len(ops)
@@ -225,13 +221,6 @@ def rank_program(g, core, T, topo):
     ad, sub, mul, mx, mn = ALU.add, ALU.subtract, ALU.mult, ALU.max, ALU.min
     zero = ap("C15", 256, 384)
 
-    def diag(name, val, base=0, step=-1):
-        src = zero
-        if SB[name][1] != BF:
-            src = ap(name)
-            iota(src, [[0, 128]], 0)
-        sel(ap(name), src, [[step, 128]], ne, val, base, 1)
-
     def block(o, val, pat):
         c = 1
         for x in pat:
@@ -240,25 +229,44 @@ def rank_program(g, core, T, topo):
         sel(o, o, [[-x[0], x[1]] for x in pat], ge, 0, 0, 1)
         sel(o, o, pat, ge, 0, 15, -1)
 
-    landed(0, ap("Y", V, V + G // 2))
-    landed(8, ap("Y", V + G // 2, W))
+    def ones(k):
+        return ap("ONES", 0, 128, 1, 0, k)
+
+    def pick(q):
+        return ap("SEL", 15 - q, 143 - q)
+
+    def c17(k, rows=128):
+        return whole("C17", T["C17"][0:rows, 8 * k:8 * k + 8, :])
+
+    def spread(src):
+        return ind(src, sl("su", "bc", 0, 8))
+
+    def wrap(src, h, a, bank=7):
+        tt(half("BC", h), spread(src), ap("WM"), mul)
+        mm(P(bank, a, a + 8), half("BC", h), ap("B8F", 0, 8), True, True)
+        return P(bank, a, a + 8)
+
+    landed(0, ap("Y", V, V + Y0))
+    landed(8, ap("Y", V + Y0, W))
     landed(1, ap("X", V, W))
     for t in range(3):
         landed(2 + t, ap("N", 2048 + G * t, 2048 + G * (t + 1)))
         landed(5 + t, ap("XL", 192 * t, 192 * t + 192))
     pieces = ((0, 2 * SC), (2 * SC, 4 * SC), (4 * SC, V))
-    for a, b in ((0, G // 2), (G // 2, G)):
+    for a, b in ((0, Y0), (Y0, G)):
         dma("s", T["Y"][:, a:b], T.lab[:, a:b], [], [ap("Y", a, b)])
     dma("s", T["NI"][:, 0:2 * SC], T.nb[:, 0:2 * SC], [], [ap("NI", 0, 2 * SC)])
     dma("s", T["Y"][:, G:V], T.lab[:, G:V], [], [ap("Y", G, V)])
-    b8, b8b, b8n = [ap("B8", 16 * k, 16 * k + 8) for k in range(3)]
+    b8, b8b = ap("B8", 0, 8), ap("B8", 16, 24)
+    lead = len(ops)
     ms(zero, 0.0)
     iota(sl("si", "p", 0, 1), [[0, 1]], 0, 1)
-    diag("IB", 1.0)
+    sel(ap("IB"), zero, [[-1, 128]], ne, 1.0, 0, 1)
+    send(0, ap("Y", V, V + Y0), ap("Y", 0, Y0))
+    send(8, ap("Y", V + Y0, W), ap("Y", Y0, G))
+    first = len(ops) - 1
+    sent = [first]
     block(b8, 1, [[16, 8]])
-    send(0, ap("Y", V, V + G // 2), ap("Y", 0, G // 2))
-    send(8, ap("Y", V + G // 2, W), ap("Y", G // 2, G))
-    first = sent = len(ops) - 1
     iota(ap("IOI"), [[0, 8], [1, 16]], 0)
     iota(ap("IO8", 0, 128), [[0, 16], [1, 8]], 0)
     iota(ap("IO8", 128, 256), [[1, 8], [0, 16]], 0)
@@ -268,9 +276,10 @@ def rank_program(g, core, T, topo):
     dma("s", T["A"][:, 0:V], T.asc[:, :], [], [ap("A", 0, V)])
     first = len(ops) - 1
     ms(ap("X", 0, V), 16.0)
+    ops[-1]["after"].add(lead)
     act(ap("AF", 0, V), ap("X", 0, V), AF.Silu, scale=AO / 16)
     ms(ap("X", W, W + 1), 0.0)
-    ms(ap("X", W + 1, 3104), 63.0)
+    ms(ap("X", W + 1, YL), 63.0)
     ms(ap("SEL"), 0.0)
     ms(ap("SEQ"), 0.0)
     e8 = sm("col", 4, 5)
@@ -283,11 +292,12 @@ def rank_program(g, core, T, topo):
     cp(qf, sl("si", "q", 0, 1))
     cp(ap("SEL", 15, 143, 16), b8)
     ts(sl("si", "q", 1, 2), sl("si", "p", 0, 1), 7, ALU.bitwise_and)
-    cp(ap("SEQ", 120, 128), b8)
+    cp(ap("SEQ", 120, 128), ap("IB", 0, 8))
     cp(sm("col", 7, 8), sl("si", "q", 1, 2))
     m0 = sm("col", 1, 2)
     ts(m0, qf, 0.0, eq)
-    for o, val in ((b8b, 2 * DK), (ap("B8K", 0, 8), -DK), (ap("B8K", 8, 16), 512), (ap("B8F", 0, 8), 1)):
+    for o, val in ((b8b, 2 * DK), (ap("B8K", 0, 8), -DK), (ap("B8K", 8, 16), 512), (ap("B8F", 0, 8), 1),
+                   (ap("B8", 48, 56), 192), (ap("B8", 64, 72), 96)):
         ts(o, b8, float(val), mul)
     ts(sm("col", 2, 3), m0, 16.0, mul, qf, ad)
     ms(whole("ZB", T["ZB"][:, :, :]), 0.0)
@@ -297,86 +307,80 @@ def rank_program(g, core, T, topo):
     for j in range(2):
         ts(nq[j], qt[j], 1.0, ge)
         ts(qa[j], qt[j], AO, ad)
-        ts(dum[j], qf, float(V + 16 * j), ad)
+        ts(dum[j], qf, float(YL + 16 * j), ad)
     ts(sm("col", 6, 7), sl("si", "p", 0, 1), 16.0 * CS, ltn, 64.0, mul)
     for name, val in (("I64", 1.0 / 64), ("I16", 16.0), ("IBIG", 2.0 ** 26), ("N128", -128.0), ("N384", -384.0),
-                      ("IF", 1.0), ("I2", 2.0), ("I4K", 4096.0), ("IA", -65.0 / 64), ("IE", -1.0 / 128)):
+                      ("I2", 2.0), ("I4K", 4096.0), ("N12", -12288.0), ("IA", -65.0 / 64), ("IE", -1.0 / 128)):
         act(ap(name), ap("IB"), scale=val)
     tt(ap("MT", 1, 128), ap("IB", 1, 128), ap("IB", 0, 127), sub)
     cp(ap("MT", 0, 128, 16), ap("IB", 0, 128, 16))
     cp(ap("MT", 129, 256), ap("MT", 0, 127))
     cp(ap("MT", 128, 256, 16), ap("MT", 15, 128, 16))
     for j in range(2):
-        ts(ap("DQ", 128 * j, 128 * j + 128), ap("NIB"), (qt, qa)[j][j], mul)
+        ts(half("DQ", j), ap("NIB"), (qt, qa)[j][j], mul)
     cp(ap("NU", *pieces[0]), ap("NI", *pieces[0]))
-    cp(ap("N", *pieces[0]), ap("NI", *pieces[0]))
-    io16 = ap("IOI", 0, 16)
-    bc = sl("su", "bc")
-    cp(bc, io16)
+    ts(ap("N", *pieces[0]), ap("NI", *pieces[0]), AO, ad)
+    cp(sl("su", "bc"), ap("IOI", 0, 16))
     ts(ap("WM"), ap("IOI"), qf, eq)
     ts(whole("MK", T["MK"][:, :, 0:32]), ap("IOI"), qf, ad, 15.0, gt)
     ms(whole("MK", T["MK"][:, :, 32:48]), 1.0)
     cp(ap("MF"), whole("MK", T["MK"][:, :, :]))
-    bp = sl("su", "bp", 0, 12)
-    for j in range(3):
-        ts(ap("su", bp[2] + j, bp[3], 3), ap("IOI", 0, 4), 2.0, mul, float(j > 0), ad)
     ts(ap("BQ"), ap("IO8"), sm("col", 7, 8), eq)
 
-    def pick(q):
-        return ap("SEL", 15 - q, 143 - q)
+    iota(ap("ONES"), [[0, 128]], 1)
+    sel(ap("TRI"), ap("ONES"), [[1, 128]], ge, 0, 0, -1)
+    sel(ap("TRM"), ap("TRI"), [[-1, 128]], ne, -255, 0, 1)
+    iota(ap("IO4"), [[2, 64]], -510)
+    iota(ap("C15", 0, 256, 1, 0, 2), [[0, 256]], -15, 4111)
+    iota(ap("C12", 0, 128, 1, 0, 2), [[0, 128]], 12288, int(CEN + AO) - 12288)
+    iota(ap("RAMP", 0, RL), [[2, RL]], -17)
+    iota(ap("RAMP", RL, RW), [[32, RH]], 4096)
+    sel(ap("YC", 0, 256), cand("Y", 0), [[0, 256]], ge, 0, 0, 0)
+    iota(ap("PP"), [[0, 17 * 128]], 0)
+    dma("g", T["X"][:, 0:V], T.xf[:, :], [], [ap("X", 0, V)], accum_op=ad)
+    ops[-1]["deps"].add(first)
+    iota(ap("F", 0, 112), [[0, 112]], 0)
+    iota(ap("F", 112, 128), [[0, 16]], 1)
+    tn = ap("TN", 0, 112)
+    iota(tn, [[0, 112]], 0)
+    for off, val in enumerate((-1.0, 2.0, -1.0)):
+        sel(tn, tn, [[-1, 112]], ne, val / 32, -off, 1)
+    block(ap("BO"), 1, [[16, 8], [0, 16]])
+    sel(ap("TQ", 0, 128), ap("BQ", 0, 128), [[1, 128]], ge, 0, 0, -1)
+    sel(ap("TQ", 128, 256), ap("BQ", 128, 256), [[0, 8], [8, 16]], ge, 0, 7, -1)
+    iota(ap("IOS"), [[1, 256]], 0)
+    iota(ap("KV"), [[0, G]], V)
+    send(1, ap("X", V, W), ap("X", 0, G))
+    iota(ap("N", V, 2048), [[0, 256]], W + 1 + int(AO))
+    kinds = [[1, 2], [0, 128]]
+    iota(ap("KR"), [[0, 16], [4096, 16]], 0)
+    sel(ap("KR"), ap("KR"), [[0, 256]], ne, CEN, -1, 1)
+    sel(ap("KR"), ap("KR"), kinds, ne, -120 * DK, -4, 2)
+    sel(ap("KR"), ap("KR"), kinds, ne, 0, -5, 2)
+    sel(ap("KR"), ap("KR"), kinds, ne, 0, -7, 2)
+    iota(ap("RB", 0, 128), [[0, 128]], 0)
+    iota(ap("RB", 128, 256), [[0, 128]], -2 ** 23)
+    for o, val in ((0, 2.0 ** 30), (128, 65536.0 + W)):
+        sel(ap("RB", o, o + 128, 16), ap("RB", o, o + 128, 16), [[0, 8]], ne, val, 0, 0)
+    iota(ap("RB", 256, 392), [[0, 136]], 0)
+    sel(ap("RB", 256, 392, 17), ap("RB", 256, 392, 17), [[0, 8]], ne, 2.0 ** 30, 0, 0)
+    iota((T["ST"][:, :, 0], "ST", 0, 2, 1), [[0, 16]], 0)
+    iota(ap("Y", W, YL), [[0, YL - W]], 0)
 
-    def consts_a():
-        iota(ap("ONES"), [[0, 128]], 1)
-        sel(ap("TRI"), ap("ONES"), [[1, 128]], ge, 0, 0, -1)
-        sel(ap("TRM"), ap("TRI"), [[-1, 128]], ne, -255, 0, 1)
+    def later():
         sel(ap("TRA"), ap("TRI"), [[-1, 128]], ne, 256, 0, 1)
-        iota(ap("IO4"), [[2, 64]], -510)
-        iota(ap("C15", 0, 256, 1, 0, 2), [[0, 256]], -15, 4111)
-        iota(ap("RAMP", 0, RL), [[2, RL]], -17)
-        iota(ap("RAMP", RL, RW), [[32, RH]], 4096)
-        for t in range(3):
-            sel(ap("YC", 256 * t, 256 * t + 256), cand("Y", t), [[0, 256]], ge, 0, 0, 0)
-        iota(ap("PP"), [[0, 17 * 128]], 0)
-        dma("g", T["X"][:, 0:V], T.xf[:, :], [], [ap("X", 0, V)], accum_op=ad)
-        ops[-1]["deps"].add(first)
-
-    def consts_b():
-        iota(ap("F", 0, 112), [[0, 112]], 0)
-        iota(ap("F", 112, 128), [[0, 16]], 1)
-        tn = ap("TN", 0, 112)
-        iota(tn, [[0, 112]], 0)
-        for off, val in enumerate((-1.0, 2.0, -1.0)):
-            sel(tn, tn, [[-1, 112]], ne, val / 32, -off, 1)
-        block(ap("BO"), 1, [[16, 8], [0, 16]])
-        sel(ap("TQ", 0, 128), ap("BQ", 0, 128), [[1, 128]], ge, 0, 0, -1)
-        sel(ap("TQ", 128, 256), ap("BQ", 128, 256), [[0, 8], [8, 16]], ge, 0, 7, -1)
-        iota(ap("IOS"), [[1, 256]], 0)
-        iota(ap("KV"), [[0, G]], V)
-        send(1, ap("X", V, W), ap("X", 0, G))
-        iota(ap("N", V, 2048), [[0, 256]], W + 1)
         iota(ap("R", V, 2048), [[0, 256]], 0)
-
-    def consts_c():
-        kinds = [[1, 2], [0, 128]]
-        iota(ap("KR"), [[0, 16], [4096, 16]], 0)
-        sel(ap("KR"), ap("KR"), [[0, 256]], ne, CEN, -1, 1)
-        sel(ap("KR"), ap("KR"), kinds, ne, -120 * DK, -4, 2)
-        sel(ap("KR"), ap("KR"), kinds, ne, 0, -5, 2)
-        sel(ap("KR"), ap("KR"), kinds, ne, 0, -7, 2)
-        iota(ap("RB", 0, 128), [[0, 128]], 0)
-        iota(ap("RB", 128, 256), [[0, 128]], -2 ** 23)
-        for o, val in ((0, 2.0 ** 30), (128, 65536.0)):
-            sel(ap("RB", o, o + 128, 16), ap("RB", o, o + 128, 16), [[0, 8]], ne, val, 0, 0)
-        iota((T["ST"][:, :, 0], "ST", 0, 2, 1), [[0, 16]], 0)
+        for t in (1, 2):
+            sel(ap("YC", 256 * t, 256 * t + 256), cand("Y", t), [[0, 256]], ge, 0, 0, 0)
         iota(whole("JF", T["JF"][:, :, :]), [[0, 192]], 0)
         for a, b in ((0, 32), (32, 48)):
             x = whole("JF", T["JF"][:, :, a:b])
-            sel(x, x, [[-32, 4], [-16, (b - a) // 16], [1, 16]], ne, 1, -15, 1)
-
-    consts_a()
-    consts_b()
-    iota(ap("Y", W, YD), [[0, YD - W]], 0)
-    dma("s", T["Y"][:, YD:YD + YL], T["Y"][:, 0:YL], [ap("Y", 0, YL)], [ap("Y", YD, YD + YL)])
+            sel(x, x, [[-32, 4], [-16, (b - a) // 16], [1, 16]], ne, -1, -15, 1)
+        iota(whole("JR", T["JR"][:, :, :]), [[0, 192]], 1)
+        for a, b in ((0, 16), (16, 48)):
+            x = whole("JR", T["JR"][:, :, a:b])
+            sel(x, x, [[-32, 4], [0, b - a]], ge, 0, -a, 1)
+            sel(x, x, [[32, 4], [0, b - a]], ge, 0, a + 15, -1)
 
     def zfrom(src, w, ycols, zout, bank):
         o = SC * (bank - 2)
@@ -389,29 +393,18 @@ def rank_program(g, core, T, topo):
     yw = ap("Y", 0, W)
 
     def prep_n1(t):
-        ts(ap("NH"), cand("N" if t else "NI", t), -CEN, ad, m0, mul)
+        ts(ap("NH"), cand("N" if t else "NI", t), -CEN - AO * (t > 0), ad, m0, mul)
         for q in range(16):
             mm(P(4, 0, 16), pick(q), ap("NH", q, 256, 16), q == 0, q == 15)
 
-    def prep_n2(t, fill1, fill2):
-        ts(sl("su", "n"), P(4, 0, 16), CEN, ad)
-        fill1()
+    def prep_n2(t):
+        ts(sl("su", "n"), P(4, 0, 16), CEN + 0.25, ad)
         tt(ap("EB"), ind(yw, sl("su", "n")), ap("YC", 256 * t, 256 * t + 256), sub)
-        fill2()
-
-    def masks():
-        ts(ap("MP"), ap("EB"), 2.0, eq, -1.0, mul)
 
     def prep_n3():
+        ts(ap("MP"), ap("EB"), 2.0, eq, -1.0, mul)
         mm(P(5, 0, 256), ap("IA"), ap("MP"), True, False)
         mm(P(5, 0, 256), ap("IE"), ap("EB"), False, True)
-
-    def prep_a(t):
-        ts(ap("AH"), ap("AU"), 16.0, ad)
-        for k in (6, 2):
-            mm(P(k, 0, 256), ap("ONES", 0, 128, 1, 0, 2), ap("C15", 0, 256, 1, 0, 2), True, False)
-            for h in range(2):
-                mm(P(k, 128 * h, 128 * h + 128), ap("AH", 128 * h, 128 * h + 128), ap("I2"), False, k == 6 and h == 1)
 
     late = []
     last = len(PW) - 1
@@ -425,7 +418,7 @@ def rank_program(g, core, T, topo):
         act(ap("R", at[c], at[c + 1]), P(banks[c], 0, PW[c]), AF.Copy)
 
     def nfloat(k):
-        cp(ap("N", NF[k], NF[k + 1]), ap("NI", NF[k], NF[k + 1]))
+        ts(ap("N", NF[k], NF[k + 1]), ap("NI", NF[k], NF[k + 1]), AO, ad)
 
     for c in range(last + 1):
         a, w, sv, bank = at[c], PW[c], PV[c], banks[c]
@@ -451,103 +444,89 @@ def rank_program(g, core, T, topo):
         if c == last - 4:
             prep_n1(0)
         if c == last - 3:
-            prep_n2(0, lambda: None, lambda: None)
+            prep_n2(0)
     cp(ap("AU"), cand("A", 0))
     zpiece(last - 1, P(banks[last - 1], 0, PW[last - 1]), 3 - (last & 1))
     rcopy(last - 1)
     late.pop(0)()
     zpiece(last, P(7, 0, PW[last]), 4)
     late.pop(0)()
-    masks()
     late.pop(0)()
     prep_n3()
 
-    def wrap(src, bank, a):
-        tt(ap("BC"), ind(src, bc), ap("WM"), mul)
-        for h in range(2):
-            mm(P(bank, a + 8 * h, a + 8 * h + 8), ap("BC", 128 * h, 128 * h + 128), ap("B8F", 0, 8), True, True)
-        return P(bank, a, a + 16)
-
-    def half(name, h):
-        return ap(name, 128 * h, 128 * h + 128)
-
-    def ones(k):
-        return ap("ONES", 0, 128, 1, 0, k)
-
     xw = ap("X", 0, W + 2)
+    zw = ap("Z", 0, V)
     bu = sl("su", "b")
 
     def lists(t):
         send(2 + t, ap("N", 2048 + G * t, 2048 + G * (t + 1)), ap("N", 0, G), ap("KV"))
 
-    def newlists():
-        for h in range(2):
-            mm(P(7, 256 + 128 * h, 384 + 128 * h), half("BC2", h), ap("IF"), False, h == 1)
-
     for t in range(3):
-        zw = ap("Z", 0, V)
-        for k in range(4):
+        def quarter(k):
             a, m, b = 64 * k, 64 * k + LV[t][k], 64 * k + 64
             cp(ap("RMP", 16 * a, 16 * m), ind(zw, ap("AU", a, m)))
-            if t and k == 0:
-                prep_n2(t, lambda: None, lambda: None)
-            if t and k == 1:
-                masks()
             act(ap("RMP", 16 * m, 16 * b), ind(zw, ap("AU", m, b)), AF.Copy)
+            zb = (0, 0, 1, 7)[k]
+            mm(P(zb, a, b), ones(1), ap("C12", 0, 64, 1, 0, 1), k != 1, False)
             for i in range(16):
-                mm(P(k // 3, a, b), ap("IB"), ap("RMP", 16 * a + i, 16 * b, 16), k % 3 + i == 0, k > 1 and i == 15)
-            if k == 1:
-                prep_a(t)
-            if t and k == 2:
-                prep_n3()
-        act(whole("AT", T["AT"][:, :, 8:16]), P(6, 0, 256), AF.Copy)
-        if t == 0:
+                mm(P(zb, a, b), ap("IB"), ap("RMP", 16 * a + i, 16 * b, 16), False, k > 0 and i == 15)
+
+        ts(ap("AH"), ap("AU"), 16.0, ad)
+        for k in (6, 2):
+            mm(P(k, 0, 256), ones(2), ap("C15", 0, 256, 1, 0, 2), True, False)
+            for h in range(2):
+                mm(P(k, 128 * h, 128 * h + 128), half("AH", h), ap("I2"), False, k == 6 and h == 1)
+        if t:
+            prep_n2(t)
+            prep_n3()
+        else:
             rcopy(last)
+        quarter(0)
+        act(whole("AT", T["AT"][:, :, 8:16]), P(6, 0, 256), AF.Copy)
+        act(ap("M5"), P(5, 0, 256), AF.Copy)
+        quarter(1)
+        mm(P(2, 0, 256), ap("NIB"), whole("AT", T["AT"][:, :, 8:16]), False, True)
+        act(whole("AT", T["AT"][:, :, 0:8]), P(2, 0, 256), AF.Copy)
+        for h in range(2):
+            if h:
+                quarter(2)
+                quarter(3)
+            for k, a, b in (((0, 0, 128),), ((1, 128, 192), (7, 192, 256)))[h]:
+                tt(ap("BC2", a, b), P(k, a, b), ap("MP", a, b), mul)
+                tt(ap("X2", a, b), P(k, a, b), ap("M5", a, b), mul)
+            mm(P(3 + h, 0, 8), half("MP", h), ap("B8", 48, 56), True, False)
+            mm(P(3 + h, 0, 8), half("EB", h), ap("B8", 64, 72), False, False)
+            mm(P(3 + h, 0, 8), half("X2", h), b8, False, False)
+            mm(P(3 + h, 0, 8), half("BC2", h), ap("B8F", 0, 8), False, True)
+            will = hs("sb", "will", h)
+            ts(will, P(3 + h, 0, 8), e8, le, 2.0, mul)
+            if h:
+                mm(P(4, 16, 24), ap("ONES"), hs("sb", "will", 0), True, False)
+            mm(P(3 + h, 16, 24), ap("TRM"), will, h == 0, True)
+            for gi in (2, 3, 0, 1, 4, 5, 6, 7):
+                c = 8 * h + gi
+                ts(ap("PP", 128 * c + 64, 128 * c + 128), ap("IO4"), P(3 + h, 16 + gi, 17 + gi), eq)
+                for j in range(2):
+                    o = 128 * c + 64 - 64 * j
+                    mm(P((2, 6, 5, 5)[gi // 2], 16 * gi, 16 * gi + 16), ap("PP", o, o + 128),
+                       whole("AT", T["AT"][:, 2 * c + j, :]), gi in (0, 2, 4) and h + j == 0, gi in (1, 3, 7) and h + j == 2)
+            act(hs("sb", "die", h), P(3 + h, 16, 24), AF.Sign, bias=-383.0, scale=-1.0)
+        if t == 0:
             act(ap("TN", 112, 224), ap("TN", 0, 112), scale=-2.0)
             act(ap("NBO"), ap("BO"), scale=-float(DK))
             act(ap("PBO"), ap("BO"), scale=float(DK))
-        mm(P(2, 0, 256), ap("NIB"), whole("AT", T["AT"][:, :, 8:16]), False, True)
-        act(whole("AT", T["AT"][:, :, 0:8]), P(2, 0, 256), AF.Copy)
-        for k, a, b in ((0, 0, 192), (1, 192, 256)):
-            ts(ap("RR", a, b), P(k, a, b), M64, ad, -M64, ad)
-            tt(ap("X1", a, b), P(k, a, b), ap("MP", a, b), mul)
-            tt(ap("X2", a, b), P(5, a, b), ap("RR", a, b), mul)
-        for h in range(2):
-            mm(P(3, 8 * h, 8 * h + 8), half("X1", h), b8, h == 0, False)
-            mm(P(3, 8 * h, 8 * h + 8), half("X2", h), b8, False, h == 1)
-        will = sl("sb", "will")
-        if t == 0:
             nfloat(0)
-        ts(will, P(3, 0, 16), e8, le, 2.0, mul)
-        mm(P(3, 16, 32), ap("TRM"), will, True, False)
-        mm(P(3, 24, 32), ap("ONES"), sl("sb", "will", 0, 8), False, True)
-        if t == 0:
             nfloat(1)
             lists(0)
-        die = sl("sb", "die")
-        ng = len(range(t, G, 7))
-        for gi in GO:
-            if gi == GO[DP]:
-                ts(die, P(3, 16, 32), -384.0, le, 2.0, mul)
-                act(ap("DB"), ind(die, bc), AF.Copy)
-            for h in range(2):
-                c = 8 * h + gi
-                ts(ap("PP", 128 * c + 64, 128 * c + 128), ap("IO4"), P(3, 16 + c, 17 + c), eq)
-            for h in range(2):
-                c = 8 * h + gi
-                for j in range(2):
-                    o = 128 * c + 64 - 64 * j
-                    mm(P((2, 1, 7, 7)[gi // 2], 16 * gi, 16 * gi + 16), ap("PP", o, o + 128),
-                       whole("AT", T["AT"][:, 2 * c + j, :]), gi in (0, 2, 4) and h + j == 0, gi in (1, 3, 7) and h + j == 2)
-            if gi == 5:
-                cp(ap("S1", 32, 64), P(1, 32, 64))
-            if gi == 1:
-                act(ap("S1", 0, 32), P(2, 0, 32), scale=-1.0)
+        act(ap("S1", 0, 32), P(2, 0, 32), scale=-1.0)
+        act(ap("S1", 32, 64), P(6, 32, 64))
+        act(ap("S1", 64, 128), P(5, 64, 128))
+        dd = ap("DD", t, t + 7 * 255 + 1, 7, 0, 8)
         for h in range(2):
-            mm(P(5, 128 * h, 128 * h + 128), half("DB", h), ap("IB"), True, True)
-        mm(P(4, 0, 256), ap("IB"), cand("X", t), True, False)
-        for h in range(2):
-            mm(P(4, 128 * h, 128 * h + 128), half("DB", h), ap("N128"), False, h == 1)
+            mm(P(7, 128 * h, 128 * h + 128, 1, 0, 8), hs("sb", "die", h), ap("IB"), h == 0, h == 1)
+        act(dd, P(7, 0, 256, 1, 0, 8), bias=(t + 1) / 2.0, scale=(t + 1) / 2.0)
+        mm(P(1, 0, 256), ap("IE"), cand("X", t), True, False)
+        mm(P(1, 0, 256), ap("BQ", 128, 256, 1, 0, 8), dd, False, True)
 
         def count(c):
             o = RW * c
@@ -560,8 +539,6 @@ def rank_program(g, core, T, topo):
 
         for c in range(16, 64):
             o = RW * c
-            if c == 24:
-                cp(ap("S1", 64, 128), P(7, 64, 128))
             ts(ap("RMP", o, o + RW), ap("RAMP"), digit(c, 0), mx, digit(c, 1), mn)
             count(c)
             if c % 3 == 0:
@@ -570,44 +547,32 @@ def rank_program(g, core, T, topo):
                 act(ap("RMP", o, o + RL), ap("RAMP", 0, RL), AF.Relu, bias=digit(k, 0))
                 act(ap("RMP", o + RL, o + RW), ap("RAMP", RL, RW), AF.Relu, bias=digit(k, 1))
                 count(k)
-            if c == SX[0]:
-                act(cand("DD", t), P(5, 0, 256), scale=(t + 1) / 2.0)
-            if c == SX[0] + MS:
-                mm(P(6, 0, 112), ap("I64"), ap("DW", 0, 112), True, False)
-                mm(P(1, 0, 128), ap("IB"), ap("F"), True, False)
-                if t < 2:
-                    mm(P(3, 0, 16), ap("ONES"), die, True, True)
-            if 0 < c - SX[0] - MS <= 16:
-                v = t + 7 * (c - SX[0] - MS - 1)
-                mm(P(6, v >> 4, 112, 7), ap("SEQ", 120 - 8 * (v & 15), 248 - 8 * (v & 15)), ap("DD", v, V, 112), False, v > 104)
-            if c == SX[1]:
-                act(ap("XS", 192 * t, 192 * t + 192), P(4, 0, 192), AF.Relu)
-                send(5 + t, ap("XL", 192 * t, 192 * t + 192), ap("XS", 192 * t, 192 * t + 192))
+        mm(P(6, 0, 112), ap("I64"), ap("DW", 0, 112), True, False)
+        mm(P(4, 0, 128), ap("IB"), ap("F"), True, False)
+        if t < 2:
+            mm(P(3, 0, 16), ap("ONES"), sl("sb", "die"), True, True)
+        for v in range(t, 112, 7):
+            mm(P(6, v >> 4, 112, 7), ap("SEQ", 120 - 8 * (v & 15), 248 - 8 * (v & 15), 1, 0, 8), ap("DD", v, V, 112, 0, 8),
+               False, v > 104)
+        act(ap("XS", 192 * t, 192 * t + 192), P(1, 0, 192), AF.Relu, scale=-128.0)
+        send(5 + t, ap("XL", 192 * t, 192 * t + 192), ap("XS", 192 * t, 192 * t + 192))
         if t == 0:
-            consts_c()
+            sent.append(len(ops) - 1)
+            later()
         cp((T["CS"][0:RH, :, 2:8], "CS", 2, 8, 1), P(0, 0, 6 * RL, 1, 0, RH))
         act((T["CS"][0:RH, :, 0:2], "CS", 0, 2, 1), P(2, 0, 2 * RL, 1, 0, RH), scale=-1.0)
         for j in range(3):
-            mm(P(1, 0, 112), (T["CS"][0:RH, j:j + 16, :], "CS", 0, 8, 1), ap("TN", 112 * (j & 1), 112 * (j & 1) + 112, 1, 0, RH),
+            mm(P(4, 0, 112), (T["CS"][0:RH, j:j + 16, :], "CS", 0, 8, 1), ap("TN", 112 * (j & 1), 112 * (j & 1) + 112, 1, 0, RH),
                False, j == 2)
         act(ap("DW", 0, 112), P(6, 0, 112), scale=65536.0)
-        act(cand("X", t), P(4, 0, 256), AF.Relu)
-
-        def fill(j):
-            if t == 0 and j < 2:
-                ts(cand("AF", j + 1), cand("A", j + 1), AO, ad)
-            if t == 1 and j != 1:
-                cp(ind(ap("R"), sl("su", "b", 4 * j, 4 * j + 8)), half("RN", j // 2))
-
+        act(cand("X", t), P(1, 0, 256), AF.Relu, scale=-128.0)
         if t < 2:
             add("v", lambda: g.vector.tensor_reduce(sm("col", 5, 6)[0], P(3, 0, 16)[0], AxisListType.X, ad),
                 [P(3, 0, 16)], [sm("col", 5, 6)])
-        fill(0)
-        if t < 2:
-            ts(sl("si", "e", 0, 1), sm("col", 5, 6), 0.5, mul)
-        tt(ap("F"), P(1, 0, 128), ap("DW"), gt)
-        if t < 2:
+            ts(sl("si", "e", 0, 1), sm("col", 5, 6), 0.5, mul, 1024.0, ad)
             ts(sl("si", "e", 1, 2), sl("si", "e", 0, 1), 7, ALU.bitwise_and)
+            cp(e8, sl("si", "e", 1, 2))
+        tt(ap("F"), P(4, 0, 128), ap("DW"), gt)
         scan(ap("FP", 1, 129), ap("F"), zero, ad, ad)
         mm(P(2, 0, 128), half("TQ", 1), ap("F"), True, False)
         mm(P(0, 0, 8), ap("FP", 1, 129), ap("BQ", 0, 8), True, True)
@@ -616,24 +581,17 @@ def rank_program(g, core, T, topo):
             mm(P(6, 0, 112), half("TQ", 0), ap("F", 0, 112), True, False)
             mm(P(6, 0, 112), half("BQ", 0), ap("FP", 0, 112), False, False)
             mm(P(6, 0, 112), ap("I4K"), ap("F", 0, 112), False, True)
-        if t < 2:
-            cp(e8, sl("si", "e", 1, 2))
         ts(sl("sb", "cc", 0, 8), P(0, 0, 8), 256.0, mn)
         ts(sm("ncc", 0, CS), P(0, 0, CS), -1.0, mul, 0.5, ad)
         act(ap("CUM"), P(2, 0, 128), AF.Copy)
-        def hs(buf, key, h):
-            return sl(buf, key, 8 * h, 8 * h + 8)
 
-        def part(name, h, a, b):
-            return (T[name][:, 8 * h:8 * h + 8, a:b], name, h, h + 1, 1)
-
-        def spread(src):
-            return ind(src, sl("su", "bc", 0, 8))
-
-        def wrap(src, h, a):
-            tt(half("BC", h), spread(src), ap("WM"), mul)
-            mm(P(7, a, a + 8), half("BC", h), ap("B8F", 0, 8), True, True)
-            return P(7, a, a + 8)
+        def row(h, k):
+            if t < 2:
+                mm(P(k, 0, 128), half("MT", t), half("CMP", h), True, True)
+                act(half("NM", h), P(k, 0, 128), bias=nq[t])
+                mm(P(k, 256, 384), ap("IB"), half("CRP", h), True, False)
+                mm(P(k, 256, 384), ap("N128"), half("NM", h), False, True)
+                act(half("BM", h), P(k, 256, 384), AF.Relu, bias=CEN / 16)
 
         def treated(h):
             for gi in range(8):
@@ -649,12 +607,14 @@ def rank_program(g, core, T, topo):
             tt(half("CMP", h), ind(ap("CUM"), cu), half("IOS", h), le)
             cp(hs("sb", "c", h), cu)
             act(half("CRP", h), ind(ap("IOS", 0, 128), cu), bias=-CEN / 16)
-            mm(P(bk, 0, 8), ap("I16"), hs("sb", "c", h), True, False)
             for q in range(16):
-                mm(P(bk, 0, 8), pick(q), ap("CMP", 128 * h + q, 128 * h + 128, 16), False, q == 15)
+                mm(P(bk, 0, 8), pick(q), ap("CMP", 128 * h + q, 128 * h + 128, 16), q == 0, False)
+            mm(P(bk, 0, 8), ap("I16"), hs("sb", "c", h), False, True)
+            if h:
+                row(h, 5)
             cp(hs("su", "b", h), P(bk, 0, 8))
-            cp(half("LBU", h), ind(ap("N", 0, 2048), hs("su", "b", h)))
-            act(half("XB", h), ind(xw, hs("su", "b", h)), AF.Copy)
+            ts(half("LBU", h), ind(ap("N", 0, 2048), hs("su", "b", h)), 0.25 - AO, ad)
+            (cp, act)[h](half("XB", h), ind(xw, hs("su", "b", h)))
             ts(half("LBH", h), half("LBU", h), -CEN, ad)
             ts(half("GH", h), half("LBU", h), float(V), ge, 256.0 + G * t, mul)
 
@@ -662,15 +622,20 @@ def rank_program(g, core, T, topo):
             return (T["MX%d" % h][:, a:b, 64 * c:64 * c + 64], "MX%d" % h, 16 * c + a, 16 * c + b, 1)
 
         def keys(h, d, names):
-            gb, o, sv, w = "GA%d" % h, 2048 * d, GV[t][2 * d + 1 - h], 256 >> d
+            gb, o, sv, w = "GA%d" % h, 2048 * d, GV[t][2 * d + 1 - h], (256, 136)[d]
+            st, kw = 16 + d, 128 + 8 * d
+            kr, nbo, pbo, ib = ((ap("KR", 0, 256, 1, 0, 4), ap("NBO"), ap("PBO"), ap("IB")), (c17(4, 4), c17(0), c17(1), c17(2)))[d]
             cp(ap(gb, o, o + 16 * sv), ind(xw, ap(names, 128 * h, 128 * h + sv)))
-            for a, b in ((sv, 64), (max(sv, 64), 128)):
+            for a, b in ((sv, 64), (64, 128)):
                 if a < b:
                     act(ap(gb, o + 16 * a, o + 16 * b), ind(xw, ap(names, 128 * h + a, 128 * h + b)), AF.Copy)
-            mm(P(h, 0, w), ones(4), ap("KR", 0, w, 1, 0, 4), True, False)
-            mm(P(h, 0, 128, 1, 0, 64), ap("XB", 128 * h, 128 * h + 64), ap("NBO"), False, False)
-            mm(P(h, 0, 128, 1, 64, 128), ap("XB", 128 * h + 64, 128 * h + 128), ap("PBO"), False, False)
-            if not d:
+            mm(P(h, 0, w), ones(4), kr, True, False)
+            mm(P(h, 0, kw, 1, 0, 64), ap("XB", 128 * h, 128 * h + 64), nbo, False, False)
+            mm(P(h, 0, kw, 1, 64, 128), ap("XB", 128 * h + 64, 128 * h + 128), pbo, False, False)
+            if d:
+                mm(P(h, 16, kw, st), ap("IB"), hs("sb", "off", h), False, False)
+                mm(P(h, 16, kw, st), ap("IB"), whole("ZB", T["ZB"][:, h, 15:143:16]), False, False)
+            else:
                 mm(P(h, 0, 128), half("GH", h), ap("IB"), False, False)
                 mm(P(h, 128, 256), half("LBH", h), ap("IB"), False, False)
             for b in range(2):
@@ -682,13 +647,13 @@ def rank_program(g, core, T, topo):
             if d:
                 offers(h)
             for i in range(16):
-                mm(P(h, i, w, 16), ap(gb, o + i, o + 2048, 16), ap("B8K", 0, w // 16), False, False)
+                mm(P(h, i, w, st), ap(gb, o + i, o + 2048, 16), ap("B8K", 0, w // 16), False, False)
             for i in range(16):
                 tt(mx_(h, i, i + 1, 0), P(2, 64 * h, 64 * h + 64), ap(gb, o + i, o + 1024, 16), mx)
-                mm(P(h, i, 128, 16), (T["MX%d" % h][:, i, :], "MX%d" % h, i, i + 1, 1), b8b, False, False, mx_(h, i, i + 1, 1))
-            mm(P(h, 0, 128), half(("LBH", "LUH")[d], h), ap("IB"), False, True)
-            scan(half("SC1", h), ap("RB", 0, 128), P(h, 0, 128), ad, mn)
-            return ap("SC1", 128 * h + 15, 128 * h + 128, 16)
+                mm(P(h, i, kw, st), (T["MX%d" % h][:, i, :], "MX%d" % h, i, i + 1, 1), b8b, False, False, mx_(h, i, i + 1, 1))
+            mm(P(h, 0, kw), half(("LBH", "LUH")[d], h), ib, False, True)
+            scan(ap("SC1", 136 * h, 136 * h + kw), ap("RB", 256 * d, 256 * d + kw), P(h, 0, kw), ad, mn)
+            return ap("SC1", 136 * h + st - 1, 136 * h + kw, st)
 
         def near(h):
             lu = (3, 5)[h]
@@ -696,21 +661,14 @@ def rank_program(g, core, T, topo):
             ts(hs("si", "un", h), ue, 8191, ALU.bitwise_and)
             scan(half("HK", h), ap("RB", 128, 256), P(h, 128, 256), mx, mn)
             ts(hs("sm", "xx", h), ue, THR, ltn, 65536.0, mul)
-            mm(P(lu, 0, 128), half("LBH", h), ap("IB"), True, t == 2)
-            if t < 2:
-                mm(P(lu, 128, 256), half("MT", t), half("CMP", h), False, True)
+            mm(P(lu, 0, 128), half("LBH", h), ap("IB"), True, True)
             act(part("LT", h, 0, 16), P(lu, 0, 128), AF.Copy)
             sel(part("LT", h, 16, 32), part("LT", h, 0, 16), [[0, 128]], ge, 0, 0, 0)
-            if t < 2:
-                act(half("NM", h), P(lu, 128, 256), bias=nq[t])
-                mm(P(lu, 256, 384), ap("IB"), half("CRP", h), True, False)
-                mm(P(lu, 256, 384), ap("N128"), half("NM", h), False, True)
-                act(half("BM", h), P(lu, 256, 384), AF.Relu, bias=CEN / 16)
-            act(part("ST", h, 1, 17), half("HK", h), AF.Sign, bias=65536.0, scale=-1.0)
+            act(part("ST", h, 1, 17), half("HK", h), AF.Sign, bias=65536.0 + W, scale=-1.0)
 
         def fetch(h):
             ts(hs("su", "u", h), wrap(hs("si", "un", h), h, 16), 2047.0 + G * (t + 1), mn)
-            ts(half("LUU", h), ind(ap("N", 0, 2048 + G * (t + 1)), hs("su", "u", h)), float(W + 1), mn)
+            ts(half("LUU", h), ind(ap("N", 0, 2048 + G * (t + 1)), hs("su", "u", h)), 0.25 - AO, ad, W + 1.25, mn)
             ts(half("LUH", h), half("LUU", h), -CEN, ad)
 
         def offers(h):
@@ -718,12 +676,17 @@ def rank_program(g, core, T, topo):
             mm(P(lu, 0, 128), half("LUH", h), ap("IB"), True, False)
             mm(P(lu, 128, 256), ap("IB"), part("ST", h, 1, 17), False, False)
             mm(P(lu, 128, 256), ap("NIB"), part("ST", h, 0, 16), False, True)
-            tt(half("EE", 32 + h), P(2, 256 + 128 * h, 384 + 128 * h), half("LUH", h), eq)
-            mm(P(h, 0, 128), half("EE", 32 + h), ap("IBIG"), False, False)
+            tt(half("TX", h), P(2, 256 + 128 * h, 384 + 128 * h), half("LUH", h), eq)
+            mm(P(h, 0, 136), half("TX", h), c17(3), False, False)
             for r in range(16):
-                tt(half("EE", 2 * r + h), P(lu, 0, 128), part("LT", h, r, r + 16), eq)
-                mm(P(h, 0, 128), ap("IBIG"), half("EE", 2 * r + h), False, False)
+                tt(part("EE", 2 * r + h, 0, 16), P(lu, 0, 128), part("LT", h, r, r + 16), eq)
+                mm(P(h, 0, 136), ap("IBIG"), part("EE", 2 * r + h, 0, 17), False, False)
             act(half("OH", h), P(lu, 128, 256), AF.Copy)
+            mm(P(lu, 256, 384), ap("IB"), half("LBH", h), True, False)
+            mm(P(lu, 256, 384), half("OH", h), ap("I4K"), False, True)
+            act(half("NL", h), P(lu, 256, 384), bias=CEN + AO)
+            if not h:
+                row(h, lu)
 
         def aside():
             asks, need = sl("sb", "asks"), sl("sb", "need")
@@ -732,80 +695,92 @@ def rank_program(g, core, T, topo):
             tt(need, sl("si", "k"), sm("xx"), ltn)
             ts(sl("si", "old"), sl("si", "k"), 4095, ALU.bitwise_and)
             tt(asks, sm("y1"), need, mul)
-            ts(sm("fk"), sl("si", "old"), THR + YD, ad)
+            ts(whole("ZB", T["ZB"][:, :, 15:143:16]), sl("si", "old"), -CEN, ad)
             mm(P(7, 32, 48), ap("TRA"), asks, True, False)
             mm(P(7, 32, 48), ap("N384"), need, False, False)
-            mm(P(7, 40, 48), ap("ONES"), sl("sb", "asks", 0, 8), False, True)
-            ts(sm("y2"), P(7, 32, 48), -65.0, gt, -2 * THR, mul)
-            tt(sm("fk"), sm("fk"), sm("y2"), ad)
-            if t < 2:
-                ts((T["ZB"][:, :, 15:143:16], "ZB", 0, 1, 1), sl("si", "old"), -CEN, ad)
-                for h in range(2):
-                    for q in range(16):
-                        mm(P(7, 48 + 8 * h, 56 + 8 * h), whole("ZB", T["ZB"][:, h, 15 - q:143 - q]), ap("IB", q, 128, 16),
-                           h + q == 0, h + q == 16)
-                ts(sl("su", "old"), P(7, 48, 64), CEN, ad)
-                act(ap("YO"), ind(ap("Y", 0, YD), sl("su", "old")), AF.Copy)
-                act(ap("RG"), ind(ap("R"), bu), AF.Copy)
-                act(ap("YB"), ind(yw, bu), AF.Copy)
+            mm(P(7, 40, 48), ap("ONES"), hs("sb", "asks", 0), False, True)
+            ts(sl("sb", "off"), P(7, 32, 48), -65.0, gt, -2 * THR, mul)
+
+        def olds():
+            for h in range(2):
+                for q in range(16):
+                    mm(P(7, 48 + 8 * h, 56 + 8 * h), whole("ZB", T["ZB"][:, h, 15 - q:143 - q]), ap("IB", q, 128, 16),
+                       h + q == 0, h + q == 16)
+            ts(sl("su", "old"), P(7, 48, 64), CEN, ad)
+            act(ap("YO"), ind(ap("Y"), sl("su", "old")), AF.Copy)
+            act(ap("RG"), ind(ap("R"), bu), AF.Copy)
+            act(ap("YB"), ind(yw, bu), AF.Copy)
 
         def change(h, we):
-            bn, ba, br = ((P(4, 0, 128), P(6, 0, 128), P(3, 0, 128)), (P(5, 0, 128), P(5, 128, 256), P(5, 256, 384)))[h]
-            w, pw, wn, dv, b = hs("si", "w", h), hs("si", "pw", h), hs("si", "wn", h), hs("sm", "dv", h), hs("su", "b", h)
-            tt(w, we, hs("sm", "fk", h), mn)
-            if t < 2:
-                ts(pw, w, 8191, ALU.bitwise_and)
-            ts(wn, w, 4095, ALU.bitwise_and)
-            if t < 2:
-                cp(hs("sm", "pw", h), pw)
-                act(half("PB", h), spread(hs("sm", "pw", h)), AF.Copy)
-                wp = wrap(pw, h, 64)
-                mm(P(h, 128, 320), half("PB", h), whole("JF", T["JF"][:, :, :]), True, True)
-            tt(dv, wn, hs("si", "old", h), sub)
-            tt(half("BC2", h), spread(dv), half("OH", h), mul)
-            mm(bn, ap("IB"), half("LBH", h), True, False)
-            mm(bn, half("BC2", h), ap("IF"), False, t == 2 or h == 0)
-            if t < 2:
-                pww, bad, table = hs("sm", "pww", h), hs("sm", "bad", h), ap(("AF", "AG")[t])
-                ts(pww, wp, 2.0 ** -14, mul)
-                act(ap("WR", 192 * h, 192 * h + 192), ind(pww, sl("su", "bp", 0, 12)), scale=2.0 ** 14)
-                ts(hs("su", "wa", h), wp, float(V - 1), mn)
-                cp(hs("su", "w", h), wp)
-                ts(bad, wp, float(V), ge)
-                act(half("YW", h), ind(ap("Y"), hs("su", "w", h)), AF.Copy)
-                tt(half("X1", h), ind(ap(("A", "AF")[t], 0, V), hs("su", "wa", h)), half("NM", h), mul)
-                tt(bad, bad, pww, ad)
-                mm(ba, ap("I16"), half("BM", h), h == 0, False)
-                mm(ba, half("DQ", t), half("NM", h), False, False)
-                mm(ba, ap("IB"), half("X1", h), False, h == 0)
-                mm(br, ap("IB"), half("RG", h), h == 0, False)
-                mm(br, ap("NIB"), half("YO", h), False, False)
-                mm(br, ap("IB"), half("YW", h), False, True)
-                act(half("AN", h), ba, bias=qa[t])
-                o = 192 * h
-                tt(ap("DE", o, o + 192), P(h, 128, 320), ap("WR", o, o + 192), eq)
-                scan(ap("DS", o, o + 192), ap("DE", o, o + 192), ap("MF"), ad, mul)
-                tg = hs("su", "tg", h)
-                bad = [ap(bad[1], bad[2] + j, bad[3], 2) for j in range(2)]
-                for j in (1, 0):
-                    tt(bad[j], bad[j], ap("DS", o + 15 + 32 * j, o + 192, 48), ad)
-                for j in (1, 0):
-                    ts(ap(tg[1], tg[2] + j, tg[3], 2), bad[j], 16384.0, mul, dum[j], mn)
-                for k in range(4 * h + 3, 4 * h - 1, -1):
-                    put(ind(table, sl("su", "tg", 2 * k, 2 * k + 2)), ap("AN", 32 * k, 32 * k + 32))
-                act(half("TX", h), br, AF.Square, bias=-3.5, scale=4.5)
-                act(half("ZN", h), half("TX", h), AF.Relu, bias=65.0, scale=-1.0)
-                if t == 0:
-                    act(half("RN", h), br, AF.Copy)
-                tt(ind(ap("Z"), b), half("ZN", h), half("YB", h), mul)
-            act(half("NL", h), bn, bias=CEN)
-            cp(ind(ap("N", 0, 2048), b), half("NL", h))
+            ba, br = ((P(6, 0, 128), P(4, 0, 128)), (P(5, 0, 128), P(5, 128, 256)))[h]
+            wn, b = hs("si", "wn", h), hs("su", "b", h)
 
-        fill(1)
-        fill(2)
+            def newlist():
+                x = P(h, 320, 448)
+                mm(x, ones(2), ap("C12", 0, 128, 1, 0, 2), True, False)
+                mm(x, half("OH", h), ap("N12"), False, False)
+                mm(x, half("PB", h), ap("IB"), False, True)
+                tt(half("BC2", h), x, half("NL", h), mn)
+                if t == 2:
+                    ts(ind(ap("AF", 0, 2048), b), half("BC2", h), 1.0, mul, -AO, ad)
+                else:
+                    (cp, put)[h](ind(ap("N", 0, 2048), b), half("BC2", h))
+
+            ts(wn, we, 4095, ALU.bitwise_and)
+            if t == 2:
+                ts(half("PB", h), spread(wn), -CEN, ad)
+                return newlist()
+            wp = wrap(wn, h, 128, (2, 7)[h])
+            ts(half("PB", h), spread(wn), -CEN, ad)
+            mm(P(h, 128, 320), half("BC", h), whole("JR", T["JR"][:, :, :]), True, False)
+            mm(P(h, 128, 320), half("PB", h), whole("JF", T["JF"][:, :, :]), False, True)
+            cp(hs("su", "w", h), wp)
+            act(half("YW", h), ind(ap("Y"), hs("su", "w", h)), AF.Copy)
+            tt(half("X1", h), ind(ap(("A", "AF")[t], 0, YL), hs("su", "w", h)), half("NM", h), mul)
+            mm(ba, ap("I16"), half("BM", h), True, False)
+            mm(ba, half("DQ", t), half("NM", h), False, False)
+            mm(ba, ap("IB"), half("X1", h), False, True)
+            act(half("AN", h), ba, bias=qa[t])
+            o = 192 * h
+            ts(ap("DE", o, o + 192), P(h, 128, 320), CEN, eq, 4096.0, mul)
+            newlist()
+            mm(br, ap("IB"), half("RG", h), True, False)
+            mm(br, ap("NIB"), half("YO", h), False, False)
+            mm(br, ap("IB"), half("YW", h), False, True)
+            scan(ap("DS", o, o + 192), ap("DE", o, o + 192), ap("MF"), ad, mul)
+            bad, tg = [[ap(x[1], x[2] + j, x[3], 2) for j in range(2)] for x in (hs("sm", "bad", h), hs("su", "tg", h))]
+            for j in (1, 0):
+                tt(bad[j], P((2, 7)[h], 128 + j, 136, 2), ap("DS", o + 15 + 32 * j, o + 192, 48), ad)
+            for j in (1, 0):
+                ts(tg[j], bad[j], dum[j], mn)
+            for k in range(4 * h + 3, 4 * h - 1, -1):
+                put(ind(ap(("AF", "AG")[t]), sl("su", "tg", 2 * k, 2 * k + 2)), ap("AN", 32 * k, 32 * k + 32))
+            act(half("TX", h), br, AF.Square, bias=-3.5, scale=4.5)
+            act(half("ZN", h), half("TX", h), AF.Relu, bias=65.0, scale=-1.0)
+            if t == 0:
+                act(half("RN", h), br, AF.Copy)
+            tt(ind(ap("Z"), b), half("ZN", h), half("YB", h), mul)
+
         if t == 0:
+            for j in (1, 2):
+                ts(cand("AF", j), cand("A", j), AO, ad)
             nfloat(2)
-        act(ap("X", V + t, W, 7), ap("XL", 192 * t, 192 * t + ng), AF.Copy)
+            iota((T["EE"][:, :, 16], "EE", 0, 32, 1), [[0, 256]], 0)
+            iota(whole("C17", T["C17"][:, :, 16]), [[0, 40]], 0)
+            for k, name in enumerate(("NBO", "PBO", "IB", "IBIG", "KR")):
+                sel(whole("C17", T["C17"][:, 8 * k:8 * k + 8, 0:16]), ap(name, 0, 128), [[0, 128]], ge, 0, 0, 0)
+            for k, val in enumerate((THR, CEN)):
+                x = whole("C17", T["C17"][:, 32:40, 16])
+                sel(x, x, [[0, 8]], ne, val, -k, 1)
+            iota(ap("A", V, YL), [[0, YL - V]], 0)
+            iota(ap("AF", V, YL), [[0, YL - V]], int(AO))
+        if t == 1:
+            for h in range(2):
+                cp(ind(ap("R"), hs("su", "b", h)), half("RN", h))
+        if t == 2:
+            for a in range(0, V, 256):
+                ts(ap("AF", a, a + 256), ap("N", a, a + 256), M1 - AO, ad, -M1, ad)
+        act(ap("X", V + t, W, 7), ap("XL", 192 * t, 192 * t + len(range(t, G, 7))), AF.Copy)
         for h in (1, 0):
             treated(h)
         if t < 2:
@@ -814,14 +789,15 @@ def rank_program(g, core, T, topo):
             mm(P(2, 256 + 128 * h, 384 + 128 * h), ap("I16"), half("CRP", h), h == 1, False)
             mm(P(2, 256 + 128 * h, 384 + 128 * h), ap("BO"), half("CMP", h), False, False)
             mm(P(2, 64 * h, 64 * h + 64), ap("IB"), ap("XB", 128 * h, 128 * h + 64), False, h == 0)
-        near(1)
-        fetch(1)
-        near(0)
-        fetch(0)
+        for h in (1, 0):
+            near(h)
+            fetch(h)
         aside()
-        we = [keys(h, 1, "LUU") for h in (1, 0)]
-        change(1, we[0])
-        change(0, we[1])
+        if t < 2:
+            olds()
+        we = {h: keys(h, 1, "LUU") for h in (1, 0)}
+        for h in (1, 0):
+            change(h, we[h])
         if t == 0:
             for j in range(3, 7):
                 iota(cand("DD", j), [[0, 256]], 0)
@@ -831,330 +807,95 @@ def rank_program(g, core, T, topo):
             prep_n1(t + 1)
             for a, b in ((0, 64), (64, 256)):
                 ts(ap("AU", a, b), ap(("AF", "AG")[t], t + 1 + 7 * a, t + 7 * b - 5, 7), M1 - AO, ad, -M1, ad)
-        continue
-        for h in range(2):
-            for gi in range(8):
-                o = (T["CM"][:, 8 * h:8 * h + 8, 16 * gi:16 * gi + 16], "CM", 8 * h + gi, 8 * h + gi + 1, 1)
-                if gi < CS:
-                    act(o, half("IOS", h), AF.Sign, bias=sm("ncc", gi, gi + 1))
-                else:
-                    ts(o, half("IOS", h), sl("sb", "cc", gi, gi + 1), ge, 2.0, mul)
-            for k in range(8 * h, 8 * h + 8):
-                mm(P(1, 2 * k, 2 * k + 2), (T["CM"][:, k, :], "CM", 8 * h, 8 * h + 8, 1), ap("ONES", 0, 2), k == 0, k == 15)
-        cu, cb = sl("su", "c"), sl("sb", "c")
-        fill(1)
-        ts(cu, P(1, 0, 32, 2), 0.5, mul, sm("col", 6, 7), ad)
-        tt(ap("CMP"), ind(ap("CUM"), cu), ap("IOS"), le)
-        cp(cb, cu)
-        act(ap("CRP"), ind(ap("IOS", 0, 128), cu), bias=-CEN / 16)
-        act(ap("X", V + t, W, 7), ap("XL", 192 * t, 192 * t + ng), AF.Copy)
-        for q in range(16):
-            mm(P(7, 0, 16), pick(q), ap("CMP", q, 256, 16), q == 0, False)
-        mm(P(7, 0, 16), ap("I16"), cb, False, True)
-        if t < 2:
-            act(ap("F", 0, 112), P(6, 0, 112), AF.Relu, bias=-4352.0)
-        fill(2)
-        if t == 0:
-            nfloat(2)
-        cp(bu, P(7, 0, 16))
-        for h in (1, 0):
-            cp(half("LBU", h), ind(ap("N", 0, 2048), sl("su", "b", 8 * h, 8 * h + 8)))
-        act(ap("XB"), ind(xw, bu), AF.Copy)
-        for a in (128, 192):
-            act(ap("GA0", 16 * a - 2048, 16 * a - 1024), ind(xw, ap("LBU", a, a + 64)), AF.Copy)
-            if a == 128 and WB < 128:
-                act(ap("GV0", 16 * WB, 2048), ind(xw, ap("LBU", WB, 128)), AF.Copy)
-        ts(ap("LBH", 128, 256), ap("LBU", 128, 256), -CEN, ad)
-        cp(ap("GV0", 0, 16 * WB), ind(xw, ap("LBU", 0, WB)))
-        ts(ap("LBH", 0, 128), ap("LBU", 0, 128), -CEN, ad)
-        ts(ap("GH"), ap("LBU"), float(V), ge, 256.0 + G * t, mul)
-        mm(P(2, 256, 512), ap("I16"), ap("CRP"), True, False)
-        mm(P(2, 256, 512), ap("BO"), ap("CMP"), False, False)
-        mm(P(2, 0, 128), ap("IB"), half("XB", 0), False, True)
-
-        def preload(banks, b):
-            for j in range(8):
-                mm(P(banks[b], 64 * j, 64 * j + 64), ap("NIB"), ap("XB", 128 + b // 2 * 64, 192 + b // 2 * 64), j == 0, False)
-
-        def vmax(gb, i):
-            tt(ap("MX0", 128 * i, 128 * i + 128), P(2, 0, 128), ap(gb, i, 2048, 16), mx)
-            mm(P(0, i, 128, 16), ap("MX0", 128 * i, 128 * i + 128), b8b, False, False)
-
-        def rows(a, b, c=0, d=128):
-            return (T["MX1"][:, a:b, c:d] if b > a + 1 else T["MX1"][:, a, c:d], "MX1", a, b, 1)
-
-        def adiff(banks, b, gb):
-            for j in range(8):
-                o = b // 2 * 1024
-                mm(P(banks[b], 64 * j, 64 * j + 64), ap("IB"), ap(gb, o + (b & 1) * 8 + j, o + 1024, 16), False, j == 7)
-
-        def aabs(banks):
-            for b in AB:
-                act(rows((b & 1) * 8, (b & 1) * 8 + 8, b // 2 * 64, b // 2 * 64 + 64), P(banks[b]), AF.Abs)
-
-        def asum(a, b, w, stop=False):
-            for i in range(a, b):
-                mm(P(1, i, 16 * w, 16), rows(i, i + 1), ap("B8J", 0, w), False, stop and i == b - 1)
-
-        bb = (3, 4, 5, 6)
-        for b in range(4):
-            preload(bb, b)
-        for h in range(2):
-            mm(P(h, 0, 256), ones(4), ap("KR", 0, 256, 1, 0, 4), True, False)
-        if t < 2:
-            mm(P(7, 256, 512), half("MT", t), ap("CMP"), True, False)
-        mm(P(7, 128, 256), half("LBH", 1), ap("IB"), t == 2, False)
-        mm(P(0, 0, 128), half("XB", 0), ap("NBO"), False, False)
-        for a in (0, 128):
-            mm(P(1, a, a + 128), half("LBH", 1), ap("IB"), False, False)
-        mm(P(1, 128, 256), half("XB", 1), ap("PBO"), False, False)
-        for b in range(4):
-            adiff(bb, b, "GA0")
-        aabs(bb)
-        for i in range(16):
-            mm(P(0, i, 256, 16), ap("GV0", i, 2048, 16), ap("B8K"), False, False)
-        mm(P(7, 0, 128), half("LBH", 0), ap("IB"), False, True)
-        mm(P(0, 128, 256), half("LBH", 0), ap("IB"), False, False)
-        for h in range(2):
-            mm(P(h, 0, 128), half("GH", h), ap("IB"), False, False)
-        for i in range(16):
-            vmax("GV0", i)
-            if i == AS[0]:
-                asum(0, 8, 16)
-        mm(P(0, 0, 128), half("LBH", 0), ap("IB"), False, True)
-        asum(8, 16, 16, True)
-        act(lt(0), P(7, 0, 256), AF.Copy)
-        sel(lt(16), lt(0), [[0, 256]], ge, 0, 0, 0)
-        if t == 0:
-            for j in range(3, 7):
-                iota(cand("DD", j), [[0, 256]], 0)
-
-        def least(o, h, a):
-            scan(ap("SC1", o + 128 * h, o + 128 * h + 128), ap("RB", 0, 128), P(h, a, a + 128), ad, mn)
-
-        def holes(h):
-            scan(half("HK", h), ap("RB", 128, 256), P(h, 128, 256), mx, mn)
-
-        least(0, 0, 0)
-        holes(0)
-        least(0, 1, 0)
-        holes(1)
-        if t < 2:
-            act(ap("NM"), P(7, 256, 512), bias=nq[t])
-            mm(P(3, 0, 256), ap("IB"), ap("CRP"), True, False)
-            mm(P(3, 0, 256), ap("N128"), ap("NM"), False, True)
-            act(ap("RG"), ind(ap("R"), bu), AF.Copy)
-            act(ap("BM"), P(3, 0, 256), AF.Relu, bias=CEN / 16)
-            act(ap("YB"), ind(yw, bu), AF.Copy)
-        ue, ke = ap("SC1", 15, 256, 16), ap("HK", 15, 256, 16)
-        ts(sl("si", "un"), ue, 8191, ALU.bitwise_and)
-        ts(sm("xx"), ue, THR, ltn, 65536.0, mul)
-        wp = wrap(sl("si", "un"), 7, 48)
-        asks = sl("sb", "asks")
-        ts(sm("y1"), sl("si", "un"), 2048.0, ge)
-        ts(sl("si", "k"), ke, 0.0, mx)
-        act(whole("ST", T["ST"][:, :, 1:17]), ap("HK"), AF.Sign, bias=65536.0, scale=-1.0)
-        for h in range(2):
-            mm(P(h, 0, 128), ones(4), ap("KR", 0, 128, 1, 0, 4), True, False)
-        mm(P(0, 0, 128), half("XB", 0), ap("NBO"), False, False)
-        bd = (4, 6, 3, 7)
-        for b in range(3):
-            preload(bd, b)
-        uu = sl("su", "u")
-        need = sl("sb", "need")
-        tt(need, sl("si", "k"), sm("xx"), ltn)
-        ts(sl("si", "old"), sl("si", "k"), 4095, ALU.bitwise_and)
-        ts(uu, wp, 2047.0 + G * (t + 1), mn)
-        ts(sm("fk"), sl("si", "old"), THR + YD, ad)
-        for h in (1, 0):
-            ts(half("LUU", h), ind(ap("N", 0, 2048 + G * (t + 1)), sl("su", "u", 8 * h, 8 * h + 8)), float(W + 1), mn)
-        tt(asks, sm("y1"), need, mul)
-        act(ap("GA1", 0, 1024), ind(xw, ap("LUU", 128, 192)), AF.Copy)
-        act(ap("GA0", 16 * WV, 2048), ind(xw, ap("LUU", WV, 128)), AF.Copy)
-        act(ap("GA1", 1024, 2048), ind(xw, ap("LUU", 192, 256)), AF.Copy)
-        ts(ap("LUH"), ap("LUU"), -CEN, ad)
-        for h in range(2):
-            mm(P(5, 128 * h, 128 * h + 128), half("LUH", h), ap("IB"), True, True)
-        if t < 2:
-            ts(whole("ZB", T["ZB"][:, :, 15:143:16]), sl("si", "old"), -CEN, ad)
-        tt(ap("EE", 4096, 4352), P(2, 256, 512), ap("LUH"), eq)
-        mm(P(5, 256, 272), ap("TRA"), asks, True, False)
-        mm(P(5, 256, 272), ap("N384"), need, False, False)
-        mm(P(5, 264, 272), ap("ONES"), sl("sb", "asks", 0, 8), False, True)
-        cp(ap("GA0", 0, 16 * WV), ind(xw, ap("LUU", 0, WV)))
-        preload(bd, 3)
-        for r in range(16):
-            if r == 1:
-                ts(sm("y1"), P(5, 256, 272), -65.0, gt, -2 * THR, mul)
-            if r == 3:
-                tt(sm("fk"), sm("fk"), sm("y1"), ad)
-            tt(ap("EE", 256 * r, 256 * r + 256), P(5, 0, 256), lt(r), eq)
-            for h in range(2):
-                mm(P(h, 0, 128), ap("IBIG"), ap("EE", 256 * r + 128 * h, 256 * r + 128 * h + 128), False, False)
-            if r == 0:
-                for h in range(2):
-                    mm(P(h, 0, 128), ap("EE", 4096 + 128 * h, 4224 + 128 * h), ap("IBIG"), False, False)
-            if r == 4:
-                mm(P(1, 0, 128), half("LUH", 1), ap("IB"), False, False)
-            if t < 2 and 1 <= r < 5:
-                h = (r - 1) // 2
-                for q in range(8 * (r & 1 ^ 1), 8 * (r & 1 ^ 1) + 8):
-                    mm(P(2, 128 + 8 * h, 136 + 8 * h), whole("ZB", T["ZB"][:, h, 15 - q:143 - q]), ap("IB", q, 128, 16),
-                       h + q == 0, h + q == 16)
-            if t < 2 and r == 9:
-                ts(sl("su", "old"), P(2, 128, 144), CEN, ad)
-            if r in (6, 8):
-                adiff(bd, r // 2 - 3, "GA1")
-        for i in range(16):
-            mm(P(0, i, 128, 16), ap("GA0", i, 2048, 16), b8n, False, False)
-        for i in range(16):
-            vmax("GA0", i)
-            if i in (1, 3):
-                adiff(bd, 2 + i // 2, "GA1")
-            if i == 3:
-                aabs(bd)
-            if i == AS[1]:
-                asum(0, 8, 8)
-        mm(P(0, 0, 128), half("LUH", 0), ap("IB"), False, True)
-        asum(8, 16, 8, True)
-        mm(P(5, 256, 512), ap("IB"), whole("ST", T["ST"][:, :, 1:17]), True, False)
-        mm(P(5, 256, 512), ap("NIB"), whole("ST", T["ST"][:, :, 0:16]), False, True)
-        act(ap("OH"), P(5, 256, 512), AF.Copy)
-        if t < 2:
-            act(ap("YO"), ind(ap("Y", 0, YD), sl("su", "old")), AF.Copy)
-        else:
-            for h in range(2):
-                mm(P(6 + h, 0, 128), ap("IB"), half("LBH", h), True, False)
-        for h in range(2):
-            least(0, h, 0)
-        tt(sl("si", "w"), ap("SC1", 15, 256, 16), sm("fk"), mn)
-        if t < 2:
-            ts(sl("si", "pw"), sl("si", "w"), 8191, ALU.bitwise_and)
-        ts(sl("si", "wn"), sl("si", "w"), 4095, ALU.bitwise_and)
-        if t < 2:
-            cp(sm("pw"), sl("si", "pw"))
-            act(ap("PB"), ind(sm("pw"), bc), AF.Copy)
-            wp = wrap(sl("si", "pw"), 3, 0)
-        tt(sm("dv"), sl("si", "wn"), sl("si", "old"), sub)
-        if t < 2:
-            for h in range(2):
-                for j in range(2):
-                    mm(P(5, 128 * j + 64 * h, 128 * j + 64 * h + 64), half("PB", h), ap("JF", 64 * j, 64 * j + 64), True, True)
-            mm(P(7, 256, 512), ap("IB"), ap("LBH"), True, False)
-        if t == 2:
-            for h in range(2):
-                tt(half("BC2", h), ind(sm("dv"), sl("su", "bc", 8 * h, 8 * h + 8)), half("OH", h), mul)
-                mm(P(6 + h, 0, 128), half("BC2", h), ap("IF"), False, True)
-                act(half("NL", h), P(6 + h, 0, 128), bias=CEN)
-            for h in range(2):
-                cp(ind(ap("N", 0, 2048), sl("su", "b", 8 * h, 8 * h + 8)), half("NL", h))
-            break
-        tt(ap("BC2"), ind(sm("dv"), bc), ap("OH"), mul)
-        newlists()
-        mm(P(4, 0, 256), ap("I16"), ap("BM"), True, False)
-        mm(P(4, 0, 256), ap("DQ", 128 * t, 128 * t + 128), ap("NM"), False, False)
-        mm(P(0, 0, 256), ap("IB"), ap("RG"), True, False)
-        ts(sm("pww"), wp, 2.0 ** -14, mul)
-        act(ap("WR"), ind(sm("pww"), sl("su", "bp")), scale=2.0 ** 14)
-        ts(sl("su", "wa"), wp, float(V - 1), mn)
-        cp(sl("su", "w"), wp)
-        act(ap("YW"), ind(ap("Y"), sl("su", "w")), AF.Copy)
-        ts(sm("bad"), wp, float(V), ge)
-        tt(ap("X1"), ind(ap("AF", 0, V), sl("su", "wa")), ap("NM"), mul)
-        tt(sm("bad"), sm("bad"), sm("pww"), ad)
-        mm(P(0, 0, 256), ap("IB"), ap("YW"), False, False)
-        mm(P(4, 0, 256), ap("IB"), ap("X1"), False, True)
-        mm(P(0, 0, 256), ap("NIB"), ap("YO"), False, True)
-        act(ap("NL"), P(7, 256, 512), bias=CEN)
-        act(ap("AN"), P(4, 0, 256), bias=qa[t])
-        tt(ap("DE", 256, 384), P(5, 0, 128), ap("WR", 128, 256), eq)
-        tt(ap("DE", 0, 256), P(5, 0, 256), ap("WR"), eq)
-        scan(ap("DS", 256, 384), ap("RM"), ap("DE", 256, 384), mul, ad)
-        scan(ap("DS", 0, 256), ap("DE", 0, 256), ap("MK"), ad, mul)
-        bad, tg = [[ap(x[1], x[2] + j, x[3], 2) for j in range(2)] for x in (sm("bad"), sl("su", "tg"))]
-        tt(bad[1], bad[1], ap("DS", 271, 384, 16), ad)
-        for j in range(2):
-            tt(bad[j], bad[j], ap("DS", 128 * j + 15, 128 * j + 128, 16), ad)
-        for j in range(2):
-            ts(tg[j], bad[j], 16384.0, mul, dum[j], mn)
-        for k in range(7, -1, -1):
-            put(ind(ap("AF"), sl("su", "tg", 2 * k, 2 * k + 2)), ap("AN", 32 * k, 32 * k + 32))
-            if k == 7:
-                act(ap("TX"), P(0, 0, 256), AF.Square, bias=-3.5, scale=4.5)
-            if k == 6:
-                act(ap("ZN"), ap("TX"), AF.Relu, bias=65.0, scale=-1.0)
-            if k == 5 and t == 0:
-                act(ap("RN"), P(0, 0, 256), AF.Copy)
-        cp(ind(ap("N", 0, 2048), bu), ap("NL"))
-        lists(t + 1)
-        tt(ind(ap("Z"), bu), ap("ZN"), ap("YB"), mul)
-        prep_n1(t + 1)
-        for a, b in ((0, 64), (64, 256)):
-            ts(ap("AU", a, b), ap("AF", t + 1 + 7 * a, t + 7 * b - 5, 7), M1 - AO, ad, -M1, ad)
 
     for k, (a, b) in enumerate(((0, 896), (896, V))):
-        dma("sa"[k], T.yn[:, a:b], T["N"][:, a:b], [ap("N", a, b)], [])
-    dma("g", T.yd[:, :], T["DD"][0:128:16, :], [ap("DD")], [])
-
-    hold = [o["t"] if o["sem"] is None else {"x": 0.0, "g": 0.3}.get(o["q"], 0.05) for o in ops]
-    before, behind, dmas = [[] for o in ops], [[] for o in ops], {}
-    for i, o in enumerate(ops):
-        lag = {j: ops[j]["t"] for j in o["after"]}
-        if o["sem"] is not None and o["q"] != "x":
-            if o["q"] in dmas:
-                lag[dmas[o["q"]]] = hold[dmas[o["q"]]]
-            dmas[o["q"]] = i
-        if o["q"] == "g" and i > sent:
-            lag[sent] = 2.0
-        lag.update({j: ops[j]["t"] + HOP for j in o["deps"]})
-        for j, d in lag.items():
-            before[i].append((j, d, j in o["deps"]))
-            behind[j].append((i, d + hold[i] - hold[j], j in o["deps"]))
-
-    def lay(seq, waits, gaps, more=0.0):
-        at, busy = {}, {q: [] for q in "vapgsx"}
-        for i in seq:
-            s = max([at[j] + d + more * w for j, d, w in waits[i]] + [0.0])
-            row = busy[ops[i]["q"]]
-            k = len(row)
-            while gaps and k and row[k - 1][0] > s:
-                k -= 1
-            if k:
-                s = max(s, row[k - 1][1])
-            while k < len(row) and s + hold[i] > row[k][0] + 1e-9:
-                s = row[k][1]
-                k += 1
-            row.insert(k, (s, s + hold[i]))
-            at[i] = s
-        return at
+        dma("sa"[k], T.yn[:, a:b], T["AF"][:, a:b], [ap("AF", a, b)], [])
+    dma("g", T.yd[:, :], T["DD"][0:8, :], [ap("DD")], [])
 
     seq = [i for i, o in enumerate(ops) if o["q"] != "x"]
     for i in lands.values():
         seq.insert(seq.index(min(ops[i]["after"])) + 1, i)
-    at = lay(seq, before, INIT > 0)
+    above = {}
+    for i in seq:
+        far = 0
+        for j in ops[i]["deps"] | ops[i]["after"]:
+            far |= above[j]
+        ops[i]["near"] = {j for j in ops[i]["deps"] if not far >> j & 1}
+        above[i] = far | sum(1 << j for j in ops[i]["near"])
+    graphs = []
+    for m in range(len(PACES)):
+        hold = [o["t"][m] if o["sem"] is None else {"x": 0.0, "g": 0.3}.get(o["q"], 0.05) for o in ops]
+        before, behind, dmas = [[] for o in ops], [[] for o in ops], {}
+        for i, o in enumerate(ops):
+            lag = {j: ops[j]["t"][m] for j in o["after"]}
+            if o["sem"] is not None and o["q"] != "x":
+                if o["q"] in dmas:
+                    lag[dmas[o["q"]]] = hold[dmas[o["q"]]]
+                dmas[o["q"]] = i
+            for j in sent if o["q"] == "g" else ():
+                if i > j:
+                    lag[j] = 2.0 if j == sent[0] else hold[j]
+            lag.update({j: ops[j]["t"][m] + HOP for j in o["near"]})
+            for j, d in lag.items():
+                before[i].append((j, d, j in o["near"]))
+                behind[j].append((i, d + hold[i] - hold[j], j in o["near"]))
+        graphs.append((hold, before, behind))
 
-    def tighten(at, more):
-        back = lay(sorted(seq, key=lambda i: (-at[i] - hold[i], -i)), behind, True, more)
-        return lay(sorted(seq, key=lambda i: (-back[i] - hold[i], i)), before, True, more)
+    def lay(seq, hold, waits, gaps, more=0.0):
+        at, busy = {}, {q: [] for q in "vapgsx"}
+        for i in seq:
+            s = max([at[j] + d + more * w for j, d, w in waits[i]] + [0.0])
+            line = busy[ops[i]["q"]]
+            k = len(line)
+            while gaps and k and line[k - 1][0] > s:
+                k -= 1
+            if k:
+                s = max(s, line[k - 1][1])
+            while k < len(line) and s + hold[i] > line[k][0] + 1e-9:
+                s = line[k][1]
+                k += 1
+            line.insert(k, (s, s + hold[i]))
+            at[i] = s
+        return at
 
-    best = (1e9, at)
-    for k in range(SCHED):
-        at = tighten(tighten(best[1], MORE[k % len(MORE)]), 0.0)
-        best = min(best, (max(at[i] + ops[i]["t"] for i in seq), at), key=lambda x: x[0])
-        DBG.append(best[0])
-    if SCHED:
-        seq.sort(key=lambda i: (best[1][i], i))
-        place = {i: k for k, i in enumerate(seq)}
-        ops = [ops[i] for i in seq]
-        for o in ops:
-            o["deps"] = {place[j] for j in o["deps"]}
+    def tighten(at, m, more):
+        hold, before, behind = graphs[m]
+        back = lay(sorted(seq, key=lambda i: (-at[i] - hold[i], -i)), hold, behind, True, more)
+        return lay(sorted(seq, key=lambda i: (-back[i] - hold[i], i)), hold, before, True, more)
 
+    best = now = (1e99, seq)
+    for k in range(0 if ORDER else PASSES):
+        m = 3 * (k & 1)
+        at = lay(now[1], graphs[m][0], graphs[m][1], k == 0)
+        at = tighten(tighten(at, m, MORE[k % len(MORE)]), m, 0.0)
+        new = sorted(seq, key=lambda i: (at[i], i))
+        score = 1.0
+        for hold, before, behind in graphs:
+            score *= max(lay(new, hold, before, False).values())
+        if score < now[0] * 1.02:
+            now = (score, new)
+        best = min(best, now, key=lambda x: x[0])
+    if not ORDER:
+        ORDER.extend(best[1])
+    place = {i: k for k, i in enumerate(ORDER)}
+    ops = [ops[i] for i in ORDER]
     for o in ops:
+        o["deps"] = {place[j] for j in o["deps"]}
+
+    knows = {q: {} for q in Q}
+    for i, o in enumerate(ops):
         best = {}
         for j in o["deps"]:
-            if ops[j]["sem"] is None:
-                best[ops[j]["q"]] = max(best.get(ops[j]["q"], -1), j)
-        o["deps"] = [j for j in o["deps"] if ops[j]["sem"] is not None] + list(best.values())
+            k = ops[j]["q"] if ops[j]["sem"] is None else j
+            best[k] = max(best.get(k, -1), j)
+        o["deps"] = []
+        for k, j in sorted(best.items(), key=lambda x: -x[1]) if o["q"] != "x" else ():
+            if knows[o["q"]].get(k, -1) < j:
+                o["deps"].append(j)
+                knows[o["q"]][k] = j
+                for k2, j2 in ops[j]["knew"].items():
+                    knows[o["q"]][k2] = max(knows[o["q"]].get(k2, -1), j2)
+        o["knew"] = dict(knows.get(o["q"], {}))
     done = {q: {} for q in Q}
     for o in ops:
         if o["q"] != "x":

@@ -1,3 +1,4 @@
+import numpy as np
 from concourse.bass import DstId, RemoteDMATransfer
 from concourse.mybir import AluOpType as ALU, AxisListType, ActivationFunctionType as AF
 
@@ -10,46 +11,53 @@ DK = 2 ** 17
 THR = 121.0 * DK
 M1 = 1.5 * 2 ** 23
 AO = 32.0
-SC = 288
-PW = (192,) * 8 + (128, 64, 64)
-PV = (96, 86, 90, 86, 86, 86, 86, 86, 58, 30, 30)
+SC = 256
+PW = (256,) * 6 + (128, 64, 64)
+PV = (128, 114, 118, 114, 116, 118, 60, 30, 30)
 NF = (2 * SC, 900, G, V)
 LV = ((34, 32, 32, 32), (28, 28, 28, 32), (28, 28, 28, 32))
 GV = ((64, 48, 20, 8), (64, 48, 20, 8), (64, 48, 20, 24))
-RL, RH = 18, 114
-RW = RL + RH
+RH = 57
+FA = 31
+MV = ((0, 0, 0, 0),) * 3
 CS = 2
-HOP, BYTE = 0.2, 0.012
-PACES = ((0.00083, 1.56, 3.8), (0.00085, 1.15, 2.2), (0.00105, 1.9, 5.2), (0.0009, 1.7, 4.2))
-PASSES, MORE = 44, (0.1, -0.1, 0.2, -0.15, 0.05, -0.05, 0.3, 0.15)
+BYTE = 0.012
+PACES = ((0.00083, 1.56, 3.8, 1.8, 0.18), (0.00085, 1.15, 2.2, 1.8, 0.2), (0.00105, 1.9, 5.2, 1.9, 0.2),
+         (0.0009, 1.5, 4.2, 1.7, 0.14))
+PASSES, MORE = 8, (0.1, -0.05, 0.2, 0.0, 0.05, -0.05, 0.15, 0.0)
+SEED, AMP, SIZE, TRIES, ROUNDS = 1, 1.6, 300, 12, 900
 ORDER = []
 
 F32, BF, F16, I32, U16 = "float32", "bfloat16", "float16", "int32", "uint16"
 SB = {
-    "NI": (V, I32), "NU": (V, U16), "N": (NW, F32), "KV": (G, F32), "A": (YL, I32), "AF": (YL + 32, F32),
-    "AG": (YL + 32, F32), "Y": (YL, BF), "X": (YL, BF), "R": (2048, BF), "Z": (2048, BF), "DD": (V, BF),
-    "GA0": (4096, BF), "GA1": (4096, BF), "RMP": (64 * RW, BF), "PP": (17 * 128, BF),
+    "NI": (V, I32), "NU": (V, U16), "N": (NW, F32), "KV": (G, F32), "A": (YL, I32), "AF": (YL + 256, F32),
+    "AG": (YL + 256, F32), "Y": (YL, BF), "X": (YL, BF), "R": (2048, BF), "RF": (2048, F32),
+    "Z": (2048, BF), "DD": (V, BF),
+    "GA0": (4096, BF), "GA1": (4096, BF), "RMP": (4096, BF), "PP": (17 * 128, BF),
     "T1": (3 * SC, BF), "T2": (3 * SC, BF), "XS": (192 * 3, BF), "XL": (192 * 3, BF), "YC": (768, BF),
     "IB": (128, BF), "NIB": (128, BF), "IBIG": (128, BF), "I64": (128, BF), "I16": (128, BF), "I2": (128, BF),
-    "I4K": (128, BF), "IA": (128, BF), "IE": (128, BF), "N12": (128, BF), "N128": (128, BF), "N384": (128, BF),
+    "I4K": (128, BF), "IE": (128, BF), "N12": (128, BF), "I12": (128, BF), "N384": (128, BF),
     "BO": (128, BF), "NBO": (128, BF), "PBO": (128, BF), "B8": (80, BF), "B8K": (16, BF), "B8F": (16, F32),
     "TQ": (256, BF), "BQ": (256, BF), "IO8": (256, BF), "SEL": (144, BF), "SEQ": (248, BF), "DQ": (256, BF),
-    "TRI": (128, BF), "TRM": (128, BF), "TRA": (128, BF), "ONES": (128, BF), "MT": (256, BF), "MF": (192, BF),
-    "WM": (128, F32), "IOI": (128, F32), "IOS": (256, BF), "IO4": (64, BF), "RAMP": (RW, BF), "TN": (224, F32),
-    "KR": (256, BF), "C15": (384, BF), "C12": (128, BF), "RB": (392, F32),
+    "TRI": (128, BF), "TRM": (128, BF), "TRA": (128, BF), "ONES": (128, BF), "MT": (256, BF), "MF": (256, BF),
+    "WM": (128, F32), "IOI": (128, F32), "IOS": (256, BF), "IO4": (64, BF), "RAMP": (128, BF),
+    "IH": (256, BF), "HH": (256, BF),
+    "KR": (256, BF), "C15": (384, BF), "C12": (128, BF), "RB": (512, F32),
     "sm": (16 * 16, F32), "si": (16 * 12, I32), "su": (16 * 12, U16), "sb": (16 * 8, BF),
     "AU": (256, U16), "AH": (256, F16), "NH": (256, F16), "EB": (256, BF), "MP": (256, BF), "M5": (256, BF),
-    "X1": (256, F16), "X2": (256, BF), "S1": (128, BF), "DW": (128, BF), "F": (128, BF), "FP": (144, BF),
+    "X1": (256, F16), "X2": (256, BF), "DW": (128, BF), "F": (128, BF), "FP": (144, BF),
     "CUM": (128, F32), "CMP": (256, BF), "CRP": (256, BF), "GH": (256, BF),
     "LBU": (256, U16), "LBH": (256, F16), "XB": (256, BF), "LUU": (256, U16), "LUH": (256, F16),
-    "SC1": (272, I32), "HK": (256, F32), "BC": (256, F32), "BC2": (256, F32), "OH": (256, BF), "NL": (256, F32),
-    "RG": (256, BF), "YB": (256, BF), "YW": (256, BF), "YO": (256, BF), "TX": (256, BF), "ZN": (256, BF), "RN": (256, BF),
-    "NM": (256, BF), "BM": (256, BF), "AN": (256, F32), "PB": (256, F16), "DE": (384, BF), "DS": (384, BF),
+    "SC1": (272, I32), "HK": (256, F32), "BC": (256, F32), "BC2": (256, F32), "NL": (256, F32),
+    "RG": (256, BF), "YB": (256, BF), "YW": (256, BF), "YO": (256, BF), "TX": (256, BF), "ZN": (256, BF), "RN": (256, F32),
+    "NM": (256, F32), "AN": (256, F32), "PB": (256, F16), "DE": (512, BF), "DS": (512, BF), "BW": (256, F16),
+    "ST": (288, BF), "SU": (256, BF),
 }
 SCRATCH = {k: ("sbuf", [128, n], d) for k, (n, d) in SB.items()}
-for _k, _a, _b, _d in (("LT", 16, 32, F32), ("AT", 32, 16, BF), ("MX0", 16, 128, BF), ("MX1", 16, 128, BF),
-                       ("JF", 4, 48, BF), ("JR", 4, 48, F32), ("MK", 4, 48, BF), ("EE", 256, 17, BF), ("C17", 40, 17, BF),
-                       ("ZB", 2, 144, F16), ("ST", 16, 17, BF), ("CS", RL, 8, F32), ("CM", 16, 128, BF)):
+for _k, _a, _b, _d in (("LT", 16, 32, F32), ("AT", 32, 40, BF), ("S1", 8, 40, BF), ("OL", 32, 64, BF), ("CS", 64, 4, F16),
+                       ("MX0", 16, 128, BF), ("MX1", 16, 128, BF),
+                       ("JF", 4, 64, BF), ("JR", 4, 64, BF), ("MK", 4, 64, BF), ("EE", 256, 17, BF), ("C17", 40, 17, BF),
+                       ("ZB", 2, 144, F16), ("CM", 16, 128, BF)):
     SCRATCH[_k] = ("sbuf", [128, _a, _b], _d)
 for _k in range(8):
     SCRATCH["p%d" % _k] = ("psum", [128, 512], F32)
@@ -66,7 +74,7 @@ def rank_program(g, core, T, topo):
     dst = T.cores[(rank - 1) % n]
     rid, pid = topo.addr(dst)[0], topo.addr(dst)[1]
     engs = topo.engines(core, dst)
-    engs = [engs[1::4] if 5 <= k < 8 else engs[k // 8::2] for k in range(NMSG)]
+    engs = [engs[1::2] if 5 <= k < 8 else engs[k // 8::2] for k in range(NMSG)]
     Q = {"v": g.vector, "a": g.scalar, "p": g.tensor, "g": g, "s": g.sync}
     ops, hist, cnt, lands, groups = [], {}, {"d": 0}, {}, {}
 
@@ -104,19 +112,19 @@ def rank_program(g, core, T, topo):
     def cols(x):
         if len(x) > 5:
             return 16 * cols(x[5])
-        return len(range(x[2], x[3], x[4])) if len(SCRATCH[x[1]][1]) == 2 else 0
+        return len(range(x[2], x[3], x[4])) * (1 if len(SCRATCH[x[1]][1]) == 2 else {"OL": 128, "S1": 40, "CS": 128}.get(x[1], 0))
 
-    def lasts(q, reads, writes, two, cy, gat, sca):
+    def lasts(q, reads, writes, two, cy, gat, sca, pe, hop):
         xs = [x for x in writes[:1] + reads if isinstance(x, tuple)]
         n = ([cols(x) for x in xs if cols(x)] + [256])[0]
         if q == "p":
-            return max(64, n) * (4 if SCRATCH[xs[1][1]][2] == F32 else 1) * cy / 1.7
+            return max(64, n) * (4 if SCRATCH[xs[1][1]][2] == F32 else 1) * cy / pe
         if q == "g":
             return 0.15 + 2 * n * cy
         if len(xs[0]) > 5 or len(xs) > 1 and len(xs[1]) > 5:
             return 0.06 + n * (sca if len(xs[0]) > 5 else gat) * cy
         if q == "a":
-            return max(64, n) * cy
+            return max(64, n) * cy + 0.015
         if two and SCRATCH[xs[1][1]][0] == SCRATCH[xs[2][1]][0]:
             return max(64, 2 * n) * cy
         narrow = not two and all(SCRATCH[x[1]][2] in (BF, F16, U16) for x in xs)
@@ -145,6 +153,7 @@ def rank_program(g, core, T, topo):
         for name, a, b, s, w in acc:
             hist.setdefault(name, []).append((a, b, s, w, i))
         ops.append({"q": q, "fn": fn, "deps": deps, "sem": sem, "mark": False, "after": set(),
+                    "kin": (q, ([x[1] for x in writes] + [""])[0]),
                     "t": [lasts(q, reads, writes, two, *x) if t is None else t for x in PACES]})
 
     def x0(x):
@@ -199,7 +208,7 @@ def rank_program(g, core, T, topo):
 
     def send(k, o, a, plus=None):
         mask = sum(1 << e for e in engs[k])
-        t = 3.0 + cols(a) * (2 if SCRATCH[a[1]][2] == BF else 4) * BYTE / len(engs[k])
+        t = 3.0 + 0.6 * (5 <= k < 8) + cols(a) * (2 if SCRATCH[a[1]][2] == BF else 4) * BYTE / len(engs[k])
         ops[lands[k]]["after"].add(len(ops))
         if plus is None:
             add("g", lambda: g.remote_dma(o[0], a[0], T.sem["r%d" % k], T.sem["l%d" % k], pid, rid, mask), [a], [],
@@ -286,6 +295,7 @@ def rank_program(g, core, T, topo):
     ms(e8, 0.0)
     ms(ap("FP", 0, 1), 0.0)
     ms(ap("DW"), 0.0)
+    ms((T["CS"][:, :, :], "CS", 0, 2, 1), 0.0)
     ts(sl("si", "q", 0, 1), sl("si", "p", 0, 1), 15, ALU.bitwise_and)
     ts(ap("NIB"), ap("IB"), -1.0, mul)
     qf = sm("col", 0, 1)
@@ -296,8 +306,8 @@ def rank_program(g, core, T, topo):
     cp(sm("col", 7, 8), sl("si", "q", 1, 2))
     m0 = sm("col", 1, 2)
     ts(m0, qf, 0.0, eq)
-    for o, val in ((b8b, 2 * DK), (ap("B8K", 0, 8), -DK), (ap("B8K", 8, 16), 512), (ap("B8F", 0, 8), 1),
-                   (ap("B8", 48, 56), 192), (ap("B8", 64, 72), 96)):
+    for o, val in ((b8b, 2 * DK), (ap("B8K", 0, 8), -DK), (ap("B8K", 8, 16), 512), (ap("B8F", 0, 8), 1), (ap("B8", 32, 40), -1),
+                   (ap("B8", 48, 56), -12288)):
         ts(o, b8, float(val), mul)
     ts(sm("col", 2, 3), m0, 16.0, mul, qf, ad)
     ms(whole("ZB", T["ZB"][:, :, :]), 0.0)
@@ -305,26 +315,34 @@ def rank_program(g, core, T, topo):
     qt = [qf, sm("col", 2, 3)]
     nq, qa, dum = [[sm(k, j, j + 1) for j in range(2)] for k in ("nq", "qa", "dum")]
     for j in range(2):
-        ts(nq[j], qt[j], 1.0, ge)
-        ts(qa[j], qt[j], AO, ad)
-        ts(dum[j], qf, float(YL + 16 * j), ad)
+        ts(qa[j], qt[j], 1.0, ge, 4096.0, mul)
+        ts(nq[j], qa[j], qt[j], ad, CEN - 2048, ad)
+        ts(qa[j], qt[j], 1.0, ltn, 2048.0 + AO * j, mul)
+        ts(qa[j], qa[j], AO * (1 - j), ad)
+        ts(dum[j], qf, -8.0, mul, CEN - YL - 128 * j, ad)
     ts(sm("col", 6, 7), sl("si", "p", 0, 1), 16.0 * CS, ltn, 64.0, mul)
-    for name, val in (("I64", 1.0 / 64), ("I16", 16.0), ("IBIG", 2.0 ** 26), ("N128", -128.0), ("N384", -384.0),
-                      ("I2", 2.0), ("I4K", 4096.0), ("N12", -12288.0), ("IA", -65.0 / 64), ("IE", -1.0 / 128)):
+    for name, val in (("I64", 1.0 / 64), ("I16", 16.0), ("IBIG", 2.0 ** 26), ("I12", 12288.0), ("N384", -384.0),
+                      ("I2", 2.0), ("I4K", 4096.0), ("N12", -12288.0), ("IE", -1.0 / 128)):
         act(ap(name), ap("IB"), scale=val)
+    for j in range(2):
+        act(half("IH", j), ap("IB"), scale=-1792.0 + 32 * j)
     tt(ap("MT", 1, 128), ap("IB", 1, 128), ap("IB", 0, 127), sub)
     cp(ap("MT", 0, 128, 16), ap("IB", 0, 128, 16))
     cp(ap("MT", 129, 256), ap("MT", 0, 127))
     cp(ap("MT", 128, 256, 16), ap("MT", 15, 128, 16))
     for j in range(2):
-        ts(half("DQ", j), ap("NIB"), (qt, qa)[j][j], mul)
+        ts(half("DQ", j), half("MT", j), -2048.0 - AO * j, mul)
+    ts(ap("MT"), ap("MT"), 4096.0, mul)
     cp(ap("NU", *pieces[0]), ap("NI", *pieces[0]))
     ts(ap("N", *pieces[0]), ap("NI", *pieces[0]), AO, ad)
     cp(sl("su", "bc"), ap("IOI", 0, 16))
     ts(ap("WM"), ap("IOI"), qf, eq)
-    ts(whole("MK", T["MK"][:, :, 0:32]), ap("IOI"), qf, ad, 15.0, gt)
-    ms(whole("MK", T["MK"][:, :, 32:48]), 1.0)
-    cp(ap("MF"), whole("MK", T["MK"][:, :, :]))
+    ms(whole("MK", T["MK"][:, :, 0:16]), 1.0)
+    ts(whole("MK", T["MK"][:, :, 16:48]), ap("IOI"), qf, ad, 15.0, le)
+    ms(whole("MK", T["MK"][:, :, 48:64]), 0.0)
+    ts(ap("MF"), whole("MK", T["MK"][:, :, :]), 8192.0, mul)
+    for j in range(2):
+        ts(ap("MF", 31 + 32 * j, 256, 64), ap("MF", 31 + 32 * j, 256, 64), dum[j], ad)
     ts(ap("BQ"), ap("IO8"), sm("col", 7, 8), eq)
 
     iota(ap("ONES"), [[0, 128]], 1)
@@ -333,18 +351,19 @@ def rank_program(g, core, T, topo):
     iota(ap("IO4"), [[2, 64]], -510)
     iota(ap("C15", 0, 256, 1, 0, 2), [[0, 256]], -15, 4111)
     iota(ap("C12", 0, 128, 1, 0, 2), [[0, 128]], 12288, int(CEN + AO) - 12288)
-    iota(ap("RAMP", 0, RL), [[2, RL]], -17)
-    iota(ap("RAMP", RL, RW), [[32, RH]], 4096)
-    sel(ap("YC", 0, 256), cand("Y", 0), [[0, 256]], ge, 0, 0, 0)
+    iota(ap("RAMP", 0, RH), [[32, RH]], 4128)
+    iota(ap("RB", 392, 392 + RH), [[32, RH]], 4112)
+    for j in range(3):
+        act(ap("YC", 256 * j, 256 * j + 256), cand("Y", j), bias=63.0 / 128, scale=-65.0 / 128)
     iota(ap("PP"), [[0, 17 * 128]], 0)
     dma("g", T["X"][:, 0:V], T.xf[:, :], [], [ap("X", 0, V)], accum_op=ad)
     ops[-1]["deps"].add(first)
     iota(ap("F", 0, 112), [[0, 112]], 0)
     iota(ap("F", 112, 128), [[0, 16]], 1)
-    tn = ap("TN", 0, 112)
-    iota(tn, [[0, 112]], 0)
-    for off, val in enumerate((-1.0, 2.0, -1.0)):
-        sel(tn, tn, [[-1, 112]], ne, val / 32, -off, 1)
+    tn = ap("RAMP", 64, 120)
+    iota(tn, [[0, 56]], 0)
+    for off, val in ((0, 0.5), (1, -0.5), (64, 0.5), (65, -0.5)):
+        sel(tn, tn, [[-1, 56]], ne, val, -off, 1)
     block(ap("BO"), 1, [[16, 8], [0, 16]])
     sel(ap("TQ", 0, 128), ap("BQ", 0, 128), [[1, 128]], ge, 0, 0, -1)
     sel(ap("TQ", 128, 256), ap("BQ", 128, 256), [[0, 8], [8, 16]], ge, 0, 7, -1)
@@ -364,28 +383,29 @@ def rank_program(g, core, T, topo):
         sel(ap("RB", o, o + 128, 16), ap("RB", o, o + 128, 16), [[0, 8]], ne, val, 0, 0)
     iota(ap("RB", 256, 392), [[0, 136]], 0)
     sel(ap("RB", 256, 392, 17), ap("RB", 256, 392, 17), [[0, 8]], ne, 2.0 ** 30, 0, 0)
-    iota((T["ST"][:, :, 0], "ST", 0, 2, 1), [[0, 16]], 0)
+    iota(ap("ST", 15, 288, 144), [[0, 2]], 0)
     iota(ap("Y", W, YL), [[0, YL - W]], 0)
 
     def later():
         sel(ap("TRA"), ap("TRI"), [[-1, 128]], ne, 256, 0, 1)
-        iota(ap("R", V, 2048), [[0, 256]], 0)
-        for t in (1, 2):
-            sel(ap("YC", 256 * t, 256 * t + 256), cand("Y", t), [[0, 256]], ge, 0, 0, 0)
-        iota(whole("JF", T["JF"][:, :, :]), [[0, 192]], 0)
-        for a, b in ((0, 32), (32, 48)):
+        iota(ap("R", V, 2048), [[0, 256]], 64)
+        for a in range(0, 2048, 256):
+            sel(ap("RF", a, a + 256), ap("R", a, a + 256), [[0, 256]], ge, 0, 0, 0)
+        iota(whole("JF", T["JF"][:, :, :]), [[0, 256]], 0)
+        for a, b in ((16, 48), (48, 64)):
             x = whole("JF", T["JF"][:, :, a:b])
             sel(x, x, [[-32, 4], [-16, (b - a) // 16], [1, 16]], ne, -1, -15, 1)
-        iota(whole("JR", T["JR"][:, :, :]), [[0, 192]], 1)
-        for a, b in ((0, 16), (16, 48)):
-            x = whole("JR", T["JR"][:, :, a:b])
-            sel(x, x, [[-32, 4], [0, b - a]], ge, 0, -a, 1)
-            sel(x, x, [[32, 4], [0, b - a]], ge, 0, a + 15, -1)
+        iota(whole("JR", T["JR"][:, :, :]), [[0, 256]], 1)
+        for a in (0, 16):
+            x = whole("JR", T["JR"][:, :, 2 * a:2 * a + 32])
+            sel(x, x, [[-32, 4], [0, 32]], ge, 0, -a, 1)
+            sel(x, x, [[32, 4], [0, 32]], ge, 0, a + 15, -1)
 
     def zfrom(src, w, ycols, zout, bank):
         o = SC * (bank - 2)
-        ts(ap("T1", o, o + w), src, 1.0, eq, 64.0, mul)
-        ts(ap("T2", o, o + w), src, -1.0, eq)
+        up = 64.0 * (src[1] == "R")
+        ts(ap("T1", o, o + w), src, up + 1, eq, 64.0, mul)
+        ts(ap("T2", o, o + w), src, up - 1, eq)
         mm(P(bank, 0, w), ap("IB"), ap("T1", o, o + w), True, False)
         mm(P(bank, 0, w), ap("IB"), ap("T2", o, o + w), False, True)
         return lambda: tt(zout, P(bank, 0, w), ycols, mul)
@@ -399,12 +419,11 @@ def rank_program(g, core, T, topo):
 
     def prep_n2(t):
         ts(sl("su", "n"), P(4, 0, 16), CEN + 0.25, ad)
-        tt(ap("EB"), ind(yw, sl("su", "n")), ap("YC", 256 * t, 256 * t + 256), sub)
+        tt(ap("EB"), ind(yw, sl("su", "n")), ap("YC", 256 * t, 256 * t + 256), mul)
 
     def prep_n3():
-        ts(ap("MP"), ap("EB"), 2.0, eq, -1.0, mul)
-        mm(P(5, 0, 256), ap("IA"), ap("MP"), True, False)
-        mm(P(5, 0, 256), ap("IE"), ap("EB"), False, True)
+        ts(ap("MP"), ap("EB"), 1.0, eq, -1.0, mul)
+        ts(ap("M5"), ap("EB"), 0.0, mx)
 
     late = []
     last = len(PW) - 1
@@ -415,7 +434,7 @@ def rank_program(g, core, T, topo):
         late.append(zfrom(src, PW[c], ap("Y", at[c], at[c + 1]), ap("Z", at[c], at[c + 1]), bank))
 
     def rcopy(c):
-        act(ap("R", at[c], at[c + 1]), P(banks[c], 0, PW[c]), AF.Copy)
+        act(ap("R", at[c], at[c + 1]), P(banks[c], 0, PW[c]), bias=64.0)
 
     def nfloat(k):
         ts(ap("N", NF[k], NF[k + 1]), ap("NI", NF[k], NF[k + 1]), AO, ad)
@@ -472,9 +491,11 @@ def rank_program(g, core, T, topo):
                 mm(P(zb, a, b), ap("IB"), ap("RMP", 16 * a + i, 16 * b, 16), False, k > 0 and i == 15)
 
         ts(ap("AH"), ap("AU"), 16.0, ad)
+        ts(ap("HH"), ap("AU"), 896.0, ge)
         for k in (6, 2):
             mm(P(k, 0, 256), ones(2), ap("C15", 0, 256, 1, 0, 2), True, False)
             for h in range(2):
+                mm(P(k, 128 * h, 128 * h + 128), half("HH", h), half("IH", k == 2), False, False)
                 mm(P(k, 128 * h, 128 * h + 128), half("AH", h), ap("I2"), False, k == 6 and h == 1)
         if t:
             prep_n2(t)
@@ -482,11 +503,11 @@ def rank_program(g, core, T, topo):
         else:
             rcopy(last)
         quarter(0)
-        act(whole("AT", T["AT"][:, :, 8:16]), P(6, 0, 256), AF.Copy)
-        act(ap("M5"), P(5, 0, 256), AF.Copy)
+        act((T["AT"][:, :, 0:8], "AT", 0, 8, 1), P(6, 0, 256), AF.Copy)
         quarter(1)
-        mm(P(2, 0, 256), ap("NIB"), whole("AT", T["AT"][:, :, 8:16]), False, True)
-        act(whole("AT", T["AT"][:, :, 0:8]), P(2, 0, 256), AF.Copy)
+        mm(P(2, 0, 256), ap("NIB"), (T["AT"][:, :, 0:8], "AT", 0, 8, 1), False, True)
+        for j in range(4):
+            act((T["AT"][:, :, 8 + 8 * j:16 + 8 * j], "AT", 8 + 8 * j, 16 + 8 * j, 1), P(2, 0, 256), bias=-2.0 * j)
         for h in range(2):
             if h:
                 quarter(2)
@@ -495,7 +516,7 @@ def rank_program(g, core, T, topo):
                 tt(ap("BC2", a, b), P(k, a, b), ap("MP", a, b), mul)
                 tt(ap("X2", a, b), P(k, a, b), ap("M5", a, b), mul)
             mm(P(3 + h, 0, 8), half("MP", h), ap("B8", 48, 56), True, False)
-            mm(P(3 + h, 0, 8), half("EB", h), ap("B8", 64, 72), False, False)
+            mm(P(3 + h, 0, 8), half("M5", h), ap("B8", 48, 56), False, False)
             mm(P(3 + h, 0, 8), half("X2", h), b8, False, False)
             mm(P(3 + h, 0, 8), half("BC2", h), ap("B8F", 0, 8), False, True)
             will = hs("sb", "will", h)
@@ -508,19 +529,17 @@ def rank_program(g, core, T, topo):
                 ts(ap("PP", 128 * c + 64, 128 * c + 128), ap("IO4"), P(3 + h, 16 + gi, 17 + gi), eq)
                 for j in range(2):
                     o = 128 * c + 64 - 64 * j
-                    mm(P((2, 6, 5, 5)[gi // 2], 16 * gi, 16 * gi + 16), ap("PP", o, o + 128),
-                       whole("AT", T["AT"][:, 2 * c + j, :]), gi in (0, 2, 4) and h + j == 0, gi in (1, 3, 7) and h + j == 2)
+                    mm(P((2, 6, 5, 5)[gi // 2], 40 * gi, 40 * gi + 40), ap("PP", o, o + 128),
+                       (T["AT"][:, 2 * c + j, :], "AT", 0, 40, 1), gi in (0, 2, 4) and h + j == 0, gi in (1, 3, 7) and h + j == 2)
             act(hs("sb", "die", h), P(3 + h, 16, 24), AF.Sign, bias=-383.0, scale=-1.0)
         if t == 0:
-            act(ap("TN", 112, 224), ap("TN", 0, 112), scale=-2.0)
             act(ap("NBO"), ap("BO"), scale=-float(DK))
             act(ap("PBO"), ap("BO"), scale=float(DK))
             nfloat(0)
             nfloat(1)
             lists(0)
-        act(ap("S1", 0, 32), P(2, 0, 32), scale=-1.0)
-        act(ap("S1", 32, 64), P(6, 32, 64))
-        act(ap("S1", 64, 128), P(5, 64, 128))
+        for k, a, b in ((6, 2, 4), (2, 0, 2), (5, 4, 8)):
+            act((T["S1"][:, a:b, :], "S1", a, b, 1), P(k, 40 * a, 40 * b))
         dd = ap("DD", t, t + 7 * 255 + 1, 7, 0, 8)
         for h in range(2):
             mm(P(7, 128 * h, 128 * h + 128, 1, 0, 8), hs("sb", "die", h), ap("IB"), h == 0, h == 1)
@@ -528,25 +547,22 @@ def rank_program(g, core, T, topo):
         mm(P(1, 0, 256), ap("IE"), cand("X", t), True, False)
         mm(P(1, 0, 256), ap("BQ", 128, 256, 1, 0, 8), dd, False, True)
 
-        def count(c):
-            o = RW * c
-            sums = P(2, c >> 3, 2 * RL, 2, 0, RH) if c < 16 else P(0, (c >> 3) - 2, 6 * RL, 6, 0, RH)
-            mm(sums, ap("RMP", o + RL, o + RW), ap("RMP", o, o + RL), c in (0, 16), c in (15, 63))
-
-        def digit(c, j):
-            a = (c >> 3 << 4) + 8 * j + (c & 7)
-            return ap("S1", a, a + 1)
-
-        for c in range(16, 64):
-            o = RW * c
-            ts(ap("RMP", o, o + RW), ap("RAMP"), digit(c, 0), mx, digit(c, 1), mn)
-            count(c)
-            if c % 3 == 0:
-                k = c // 3 - 6
-                o = RW * k
-                act(ap("RMP", o, o + RL), ap("RAMP", 0, RL), AF.Relu, bias=digit(k, 0))
-                act(ap("RMP", o + RL, o + RW), ap("RAMP", RL, RW), AF.Relu, bias=digit(k, 1))
-                count(k)
+        for k in range(16):
+            a = k // 8
+            ts((T["OL"][:, k + 8 * a:16 * a + 16:8, :], "OL", k, k + 1, 1),
+               (T["S1"][:, 4 * a:4 * a + 4, 8:40], "S1", 4 * a, 4 * a + 4, 1), 8.0 * (k & 7) - 15, eq)
+        turn = [c for x in range(32) for c in (x + (x & 16) + 16, x + (x & 16))]
+        for k, c in enumerate(turn):
+            gi, o = c >> 3, 128 * (k >> 1) + 64 * (c >> 4 & 1)
+            high = (T["S1"][:, gi, c & 7:(c & 7) + 1], "S1", gi, gi + 1, 1)
+            if (k + 1) * FA // 64 > k * FA // 64:
+                act(ap("RMP", o, o + RH), ap("RB", 392, 392 + RH), AF.Sign, bias=high, scale=-1.0)
+            else:
+                ts(ap("RMP", o, o + RH), ap("RAMP", 0, RH), high, le, 2.0, mul)
+            if k & 1:
+                a, b = k >> 5, 32 * (gi & 1) + (c & 7)
+                mm(P(0, k >> 4, 256, 4, 0, 64 + RH), ap("RMP", o, o + 64 + RH),
+                   (T["OL"][:, 16 * a:16 * a + 16, b:b + 25:8], "OL", 8 * a, 8 * a + 8, 1), k == 1, k == 63)
         mm(P(6, 0, 112), ap("I64"), ap("DW", 0, 112), True, False)
         mm(P(4, 0, 128), ap("IB"), ap("F"), True, False)
         if t < 2:
@@ -559,11 +575,12 @@ def rank_program(g, core, T, topo):
         if t == 0:
             sent.append(len(ops) - 1)
             later()
-        cp((T["CS"][0:RH, :, 2:8], "CS", 2, 8, 1), P(0, 0, 6 * RL, 1, 0, RH))
-        act((T["CS"][0:RH, :, 0:2], "CS", 0, 2, 1), P(2, 0, 2 * RL, 1, 0, RH), scale=-1.0)
-        for j in range(3):
-            mm(P(4, 0, 112), (T["CS"][0:RH, j:j + 16, :], "CS", 0, 8, 1), ap("TN", 112 * (j & 1), 112 * (j & 1) + 112, 1, 0, RH),
-               False, j == 2)
+        for j in range(2):
+            cp((T["CS"][64 * j:64 * j + RH, :, 2 * j:2 * j + 2], "CS", j, j + 1, 1),
+               P(0, 128 * j, 128 * j + 128, 1, 64 * j, 64 * j + RH))
+        for j in range(2):
+            mm(P(4, 56 * j, 56 * j + 56), (T["CS"][0:64 + RH, 32 * j:32 * j + 32, :], "CS", 0, 2, 1),
+               ap("RAMP", 64, 120, 1, 0, 64 + RH), False, j == 1)
         act(ap("DW", 0, 112), P(6, 0, 112), scale=65536.0)
         act(cand("X", t), P(1, 0, 256), AF.Relu, scale=-128.0)
         if t < 2:
@@ -581,17 +598,16 @@ def rank_program(g, core, T, topo):
             mm(P(6, 0, 112), half("TQ", 0), ap("F", 0, 112), True, False)
             mm(P(6, 0, 112), half("BQ", 0), ap("FP", 0, 112), False, False)
             mm(P(6, 0, 112), ap("I4K"), ap("F", 0, 112), False, True)
+        mm(P(3, 32, 40), ap("FP", 1, 129), ap("BQ", 0, 8), True, True)
         ts(sl("sb", "cc", 0, 8), P(0, 0, 8), 256.0, mn)
-        ts(sm("ncc", 0, CS), P(0, 0, CS), -1.0, mul, 0.5, ad)
+        act(sm("ncc", 0, CS), P(3, 32, 32 + CS), scale=-1.0, bias=0.5)
         act(ap("CUM"), P(2, 0, 128), AF.Copy)
 
         def row(h, k):
             if t < 2:
-                mm(P(k, 0, 128), half("MT", t), half("CMP", h), True, True)
+                mm(P(k, 0, 128), half("MT", t), half("CMP", h), True, False)
+                mm(P(k, 0, 128), ap("I16"), half("CRP", h), False, True)
                 act(half("NM", h), P(k, 0, 128), bias=nq[t])
-                mm(P(k, 256, 384), ap("IB"), half("CRP", h), True, False)
-                mm(P(k, 256, 384), ap("N128"), half("NM", h), False, True)
-                act(half("BM", h), P(k, 256, 384), AF.Relu, bias=CEN / 16)
 
         def treated(h):
             for gi in range(8):
@@ -601,9 +617,9 @@ def rank_program(g, core, T, topo):
                 else:
                     ts(o, half("IOS", h), sl("sb", "cc", gi, gi + 1), ge, 2.0, mul)
             for k in range(8):
-                mm(P(h, 2 * k, 2 * k + 2), (T["CM"][:, 8 * h + k, :], "CM", 8 * h, 8 * h + 8, 1), ap("ONES", 0, 2), k == 0, k == 7)
+                mm(P((4, 1)[h], 2 * k, 2 * k + 2), (T["CM"][:, 8 * h + k, :], "CM", 8 * h, 8 * h + 8, 1), ap("ONES", 0, 2), k == 0, k == 7)
             cu, bk = hs("su", "c", h), (3, 7)[h]
-            ts(cu, P(h, 0, 16, 2), 0.5, mul, sm("col", 6, 7), ad)
+            ts(cu, P((4, 1)[h], 0, 16, 2), 0.5, mul, sm("col", 6, 7), ad)
             tt(half("CMP", h), ind(ap("CUM"), cu), half("IOS", h), le)
             cp(hs("sb", "c", h), cu)
             act(half("CRP", h), ind(ap("IOS", 0, 128), cu), bias=-CEN / 16)
@@ -623,6 +639,7 @@ def rank_program(g, core, T, topo):
 
         def keys(h, d, names):
             gb, o, sv, w = "GA%d" % h, 2048 * d, GV[t][2 * d + 1 - h], (256, 136)[d]
+            both = MV[t][2 * d + 1 - h]
             st, kw = 16 + d, 128 + 8 * d
             kr, nbo, pbo, ib = ((ap("KR", 0, 256, 1, 0, 4), ap("NBO"), ap("PBO"), ap("IB")), (c17(4, 4), c17(0), c17(1), c17(2)))[d]
             cp(ap(gb, o, o + 16 * sv), ind(xw, ap(names, 128 * h, 128 * h + sv)))
@@ -631,14 +648,14 @@ def rank_program(g, core, T, topo):
                     act(ap(gb, o + 16 * a, o + 16 * b), ind(xw, ap(names, 128 * h + a, 128 * h + b)), AF.Copy)
             mm(P(h, 0, w), ones(4), kr, True, False)
             mm(P(h, 0, kw, 1, 0, 64), ap("XB", 128 * h, 128 * h + 64), nbo, False, False)
-            mm(P(h, 0, kw, 1, 64, 128), ap("XB", 128 * h + 64, 128 * h + 128), pbo, False, False)
+            mm(P(h, 0, kw, 1, 64, 128), ap("XB", 128 * h + 64, 128 * h + 128), nbo if both else pbo, False, False)
             if d:
                 mm(P(h, 16, kw, st), ap("IB"), hs("sb", "off", h), False, False)
                 mm(P(h, 16, kw, st), ap("IB"), whole("ZB", T["ZB"][:, h, 15:143:16]), False, False)
             else:
                 mm(P(h, 0, 128), half("GH", h), ap("IB"), False, False)
                 mm(P(h, 128, 256), half("LBH", h), ap("IB"), False, False)
-            for b in range(2):
+            for b in range(0 if both else 2):
                 for j in range(8):
                     mm(P(4 + 2 * b, 64 * j, 64 * j + 64), ap("NIB"), ap("XB", 128 * h + 64, 128 * h + 128), j == 0, False)
                 for j in range(8):
@@ -649,11 +666,16 @@ def rank_program(g, core, T, topo):
             for i in range(16):
                 mm(P(h, i, w, st), ap(gb, o + i, o + 2048, 16), ap("B8K", 0, w // 16), False, False)
             for i in range(16):
-                tt(mx_(h, i, i + 1, 0), P(2, 64 * h, 64 * h + 64), ap(gb, o + i, o + 1024, 16), mx)
+                for c in range(1 + both):
+                    tt(mx_(h, i, i + 1, c), P(2, 128 * h + 64 * c, 128 * h + 64 * c + 64),
+                       ap(gb, o + 1024 * c + i, o + 1024 * c + 1024, 16), mx)
                 mm(P(h, i, kw, st), (T["MX%d" % h][:, i, :], "MX%d" % h, i, i + 1, 1), b8b, False, False, mx_(h, i, i + 1, 1))
             mm(P(h, 0, kw), half(("LBH", "LUH")[d], h), ib, False, True)
             scan(ap("SC1", 136 * h, 136 * h + kw), ap("RB", 256 * d, 256 * d + kw), P(h, 0, kw), ad, mn)
             return ap("SC1", 136 * h + st - 1, 136 * h + kw, st)
+
+        def step(h, back=0):
+            return ap("ST", 144 * h + 16 - back, 144 * h + 144 - back)
 
         def near(h):
             lu = (3, 5)[h]
@@ -664,7 +686,8 @@ def rank_program(g, core, T, topo):
             mm(P(lu, 0, 128), half("LBH", h), ap("IB"), True, True)
             act(part("LT", h, 0, 16), P(lu, 0, 128), AF.Copy)
             sel(part("LT", h, 16, 32), part("LT", h, 0, 16), [[0, 128]], ge, 0, 0, 0)
-            act(part("ST", h, 1, 17), half("HK", h), AF.Sign, bias=65536.0 + W, scale=-1.0)
+            act(step(h), half("HK", h), AF.Sign, bias=65536.0 + W, scale=-1.0)
+            sel(half("SU", h), step(h, 1), [[0, 8], [1, 16]], ge, 0, -1, 0)
 
         def fetch(h):
             ts(hs("su", "u", h), wrap(hs("si", "un", h), h, 16), 2047.0 + G * (t + 1), mn)
@@ -673,17 +696,15 @@ def rank_program(g, core, T, topo):
 
         def offers(h):
             lu = (3, 5)[h]
-            mm(P(lu, 0, 128), half("LUH", h), ap("IB"), True, False)
-            mm(P(lu, 128, 256), ap("IB"), part("ST", h, 1, 17), False, False)
-            mm(P(lu, 128, 256), ap("NIB"), part("ST", h, 0, 16), False, True)
+            mm(P(lu, 0, 128), half("LUH", h), ap("IB"), True, True)
             tt(half("TX", h), P(2, 256 + 128 * h, 384 + 128 * h), half("LUH", h), eq)
             mm(P(h, 0, 136), half("TX", h), c17(3), False, False)
             for r in range(16):
                 tt(part("EE", 2 * r + h, 0, 16), P(lu, 0, 128), part("LT", h, r, r + 16), eq)
                 mm(P(h, 0, 136), ap("IBIG"), part("EE", 2 * r + h, 0, 17), False, False)
-            act(half("OH", h), P(lu, 128, 256), AF.Copy)
             mm(P(lu, 256, 384), ap("IB"), half("LBH", h), True, False)
-            mm(P(lu, 256, 384), half("OH", h), ap("I4K"), False, True)
+            mm(P(lu, 256, 384), step(h), ap("I12"), False, False)
+            mm(P(lu, 256, 384), half("SU", h), ap("N12"), False, True)
             act(half("NL", h), P(lu, 256, 384), bias=CEN + AO)
             if not h:
                 row(h, lu)
@@ -708,7 +729,7 @@ def rank_program(g, core, T, topo):
                        h + q == 0, h + q == 16)
             ts(sl("su", "old"), P(7, 48, 64), CEN, ad)
             act(ap("YO"), ind(ap("Y"), sl("su", "old")), AF.Copy)
-            act(ap("RG"), ind(ap("R"), bu), AF.Copy)
+            act(ap("RG"), ind(ap(("R", "RF")[t]), bu), AF.Copy)
             act(ap("YB"), ind(yw, bu), AF.Copy)
 
         def change(h, we):
@@ -716,9 +737,10 @@ def rank_program(g, core, T, topo):
             wn, b = hs("si", "wn", h), hs("su", "b", h)
 
             def newlist():
-                x = P(h, 320, 448)
+                x = P(h, 384, 512)
                 mm(x, ones(2), ap("C12", 0, 128, 1, 0, 2), True, False)
-                mm(x, half("OH", h), ap("N12"), False, False)
+                mm(x, step(h), ap("N12"), False, False)
+                mm(x, half("SU", h), ap("I12"), False, False)
                 mm(x, half("PB", h), ap("IB"), False, True)
                 tt(half("BC2", h), x, half("NL", h), mn)
                 if t == 2:
@@ -730,32 +752,31 @@ def rank_program(g, core, T, topo):
             if t == 2:
                 ts(half("PB", h), spread(wn), -CEN, ad)
                 return newlist()
-            wp = wrap(wn, h, 128, (2, 7)[h])
+            wc, wp = hs("sm", "wc", h), P((3, 7)[h], 128, 136)
+            ts(wc, wn, -CEN, ad)
+            tt(half("BW", h), spread(wc), ap("WM"), mul)
+            mm(wp, half("BW", h), ap("B8", 32, 40), True, True)
             ts(half("PB", h), spread(wn), -CEN, ad)
-            mm(P(h, 128, 320), half("BC", h), whole("JR", T["JR"][:, :, :]), True, False)
-            mm(P(h, 128, 320), half("PB", h), whole("JF", T["JF"][:, :, :]), False, True)
-            cp(hs("su", "w", h), wp)
-            act(half("YW", h), ind(ap("Y"), hs("su", "w", h)), AF.Copy)
-            tt(half("X1", h), ind(ap(("A", "AF")[t], 0, YL), hs("su", "w", h)), half("NM", h), mul)
-            mm(ba, ap("I16"), half("BM", h), True, False)
-            mm(ba, half("DQ", t), half("NM", h), False, False)
+            mm(P(h, 128, 384), half("BW", h), whole("JR", T["JR"][:, :, :]), True, False)
+            mm(P(h, 128, 384), half("PB", h), whole("JF", T["JF"][:, :, :]), False, True)
+            ts(hs("su", "w", h), wp, -1.0, mul, CEN, ad)
+            (cp, act)[h](half("YW", h), ind(ap("Y"), hs("su", "w", h)))
+            tt(half("X1", h), ind(ap(("A", "AF")[t], 0, YL), hs("su", "w", h)), half("NM", h), mn)
+            mm(ba, half("DQ", t), half("CMP", h), True, False)
             mm(ba, ap("IB"), half("X1", h), False, True)
             act(half("AN", h), ba, bias=qa[t])
-            o = 192 * h
-            ts(ap("DE", o, o + 192), P(h, 128, 320), CEN, eq, 4096.0, mul)
+            o = 256 * h
+            act(ap("DE", o, o + 256), P(h, 128, 384), AF.Abs, scale=4096.0)
             newlist()
             mm(br, ap("IB"), half("RG", h), True, False)
             mm(br, ap("NIB"), half("YO", h), False, False)
             mm(br, ap("IB"), half("YW", h), False, True)
-            scan(ap("DS", o, o + 192), ap("DE", o, o + 192), ap("MF"), ad, mul)
-            bad, tg = [[ap(x[1], x[2] + j, x[3], 2) for j in range(2)] for x in (hs("sm", "bad", h), hs("su", "tg", h))]
-            for j in (1, 0):
-                tt(bad[j], P((2, 7)[h], 128 + j, 136, 2), ap("DS", o + 15 + 32 * j, o + 192, 48), ad)
-            for j in (1, 0):
-                ts(tg[j], bad[j], dum[j], mn)
+            scan(ap("DS", o, o + 256), ap("DE", o, o + 256), ap("MF"), mn, ad)
+            tt(hs("sm", "bad", h), wp, ap("DS", o + 31, o + 256, 32), mn)
+            ts(hs("su", "tg", h), hs("sm", "bad", h), -1.0, mul, CEN, ad)
             for k in range(4 * h + 3, 4 * h - 1, -1):
                 put(ind(ap(("AF", "AG")[t]), sl("su", "tg", 2 * k, 2 * k + 2)), ap("AN", 32 * k, 32 * k + 32))
-            act(half("TX", h), br, AF.Square, bias=-3.5, scale=4.5)
+            act(half("TX", h), br, AF.Square, bias=-291.5, scale=4.5)
             act(half("ZN", h), half("TX", h), AF.Relu, bias=65.0, scale=-1.0)
             if t == 0:
                 act(half("RN", h), br, AF.Copy)
@@ -776,7 +797,7 @@ def rank_program(g, core, T, topo):
             iota(ap("AF", V, YL), [[0, YL - V]], int(AO))
         if t == 1:
             for h in range(2):
-                cp(ind(ap("R"), hs("su", "b", h)), half("RN", h))
+                put(ind(ap("RF"), hs("su", "b", h)), half("RN", h))
         if t == 2:
             for a in range(0, V, 256):
                 ts(ap("AF", a, a + 256), ap("N", a, a + 256), M1 - AO, ad, -M1, ad)
@@ -788,7 +809,7 @@ def rank_program(g, core, T, topo):
         for h in (1, 0):
             mm(P(2, 256 + 128 * h, 384 + 128 * h), ap("I16"), half("CRP", h), h == 1, False)
             mm(P(2, 256 + 128 * h, 384 + 128 * h), ap("BO"), half("CMP", h), False, False)
-            mm(P(2, 64 * h, 64 * h + 64), ap("IB"), ap("XB", 128 * h, 128 * h + 64), False, h == 0)
+            mm(P(2, 128 * h, 128 * h + 128), ap("IB"), half("XB", h), False, h == 0)
         for h in (1, 0):
             near(h)
             fetch(h)
@@ -808,8 +829,7 @@ def rank_program(g, core, T, topo):
             for a, b in ((0, 64), (64, 256)):
                 ts(ap("AU", a, b), ap(("AF", "AG")[t], t + 1 + 7 * a, t + 7 * b - 5, 7), M1 - AO, ad, -M1, ad)
 
-    for k, (a, b) in enumerate(((0, 896), (896, V))):
-        dma("sa"[k], T.yn[:, a:b], T["AF"][:, a:b], [ap("AF", a, b)], [])
+    dma("s", T.yn[:, :], T["AF"][:, 0:V], [ap("AF", 0, V)], [])
     dma("g", T.yd[:, :], T["DD"][0:8, :], [ap("DD")], [])
 
     seq = [i for i, o in enumerate(ops) if o["q"] != "x"]
@@ -835,7 +855,7 @@ def rank_program(g, core, T, topo):
             for j in sent if o["q"] == "g" else ():
                 if i > j:
                     lag[j] = 2.0 if j == sent[0] else hold[j]
-            lag.update({j: ops[j]["t"][m] + HOP for j in o["near"]})
+            lag.update({j: ops[j]["t"][m] + PACES[m][4] for j in o["near"]})
             for j, d in lag.items():
                 before[i].append((j, d, j in o["near"]))
                 behind[j].append((i, d + hold[i] - hold[j], j in o["near"]))
@@ -875,8 +895,111 @@ def rank_program(g, core, T, topo):
         if score < now[0] * 1.02:
             now = (score, new)
         best = min(best, now, key=lambda x: x[0])
+
+    def refine(order):
+        qs, nm, rnd = [o["q"] for o in ops], len(PACES), np.random.default_rng(SEED)
+
+        def rate(order):
+            hd, tl = [], []
+            for hold, before, behind in graphs:
+                at, free = [0.0] * len(ops), dict.fromkeys("vapgsx", 0.0)
+                for i in order:
+                    s = free[qs[i]]
+                    for j, d, w in before[i]:
+                        if at[j] + d > s:
+                            s = at[j] + d
+                    at[i] = s
+                    free[qs[i]] = s + hold[i]
+                to, nxt = list(hold), dict.fromkeys("vapgsx", 0.0)
+                for i in reversed(order):
+                    if hold[i] + nxt[qs[i]] > to[i]:
+                        to[i] = hold[i] + nxt[qs[i]]
+                    nxt[qs[i]] = x = to[i]
+                    for j, d, w in before[i]:
+                        if x + d > to[j]:
+                            to[j] = x + d
+                hd.append(at)
+                tl.append(to)
+            return hd, tl, [max(x) for x in tl]
+
+        def fit(piece, hold, waits, ready, free, gaps):
+            at, busy = {}, {q: [(-1.0, free[q])] for q in free}
+            for i in piece:
+                s = ready[i]
+                for j, d in waits[i]:
+                    if at[j] + d > s:
+                        s = at[j] + d
+                line, h = busy[qs[i]], hold[i]
+                k = len(line)
+                while gaps and k > 1 and line[k - 1][0] > s:
+                    k -= 1
+                if line[k - 1][1] > s:
+                    s = line[k - 1][1]
+                while k < len(line) and s + h > line[k][0] + 1e-9:
+                    s = line[k][1]
+                    k += 1
+                line.insert(k, (s, s + h))
+                at[i] = s
+            return at
+
+        hd, tl, span = rate(order)
+        for k in range(ROUNDS):
+            size = int(rnd.integers(SIZE // 3, SIZE))
+            a = max(0, int(rnd.integers(-size // 2, len(order) - size // 2)))
+            old = order[a:a + size]
+            inside = set(old)
+            edge = []
+            for m, (hold, before, behind) in enumerate(graphs):
+                h, t = hd[m], tl[m]
+                free, nxt = dict.fromkeys("vapgsx", 0.0), dict.fromkeys("vapgsx", 0.0)
+                for i in order[:a]:
+                    free[qs[i]] = h[i] + hold[i]
+                for i in reversed(order[a + size:]):
+                    nxt[qs[i]] = t[i]
+                ready = {i: max([h[j] + d for j, d, w in before[i] if j not in inside] + [0.0]) for i in old}
+                rest = {i: max([t[j] + d - hold[j] for j, d, w in behind[i] if j not in inside] + [0.0]) for i in old}
+                waits = {i: [(j, d) for j, d, w in before[i] if j in inside] for i in old}
+                edge.append((hold, waits, ready, rest, free, nxt))
+
+            def ends(piece):
+                x = 1.0
+                for m, (hold, waits, ready, rest, free, nxt) in enumerate(edge):
+                    at = fit(piece, hold, waits, ready, free, False)
+                    last = {qs[i]: at[i] + hold[i] for i in piece}
+                    far = max(max(at[i] + hold[i] + rest[i] for i in piece), max(last[q] + nxt[q] for q in last))
+                    x *= max(far / span[m], 0.998)
+                return x
+
+            best = (ends(old) - 1e-7, None)
+            for tries in range(TRIES):
+                hold, waits, ready, rest, free, nxt = edge[int(rnd.integers(nm))]
+                r = dict(zip(old, (1 + AMP * rnd.random() * (rnd.random(len(old)) - 0.5)).tolist()))
+                if tries & 1:
+                    kin = {ops[i]["kin"]: r[i] ** 2 for i in old}
+                    r = {i: kin[ops[i]["kin"]] for i in old}
+                new = best[1] or old
+                for shaken in (True, False):
+                    h2 = {i: hold[i] * r[i] for i in old} if shaken else hold
+                    w2 = {i: [(j, d * r[j]) for j, d in waits[i]] for i in old} if shaken else waits
+                    back = {i: [] for i in old}
+                    for i in old:
+                        for j, d in w2[i]:
+                            back[j].append((i, d + h2[i] - h2[j]))
+                    at = fit(new, h2, w2, ready, free, False)
+                    at = fit(sorted(old, key=lambda i: (-at[i] - h2[i], -i)), h2, back, rest, nxt, True)
+                    at = fit(sorted(old, key=lambda i: (-at[i] - h2[i], i)), h2, w2, ready, free, True)
+                    new = sorted(old, key=lambda i: (at[i], i))
+                x = ends(new)
+                if x < best[0]:
+                    best = (x, new)
+            if best[1]:
+                order = order[:a] + best[1] + order[a + size:]
+                hd, tl, span = rate(order)
+                order.sort(key=lambda i: hd[k % nm][i])
+        return order
+
     if not ORDER:
-        ORDER.extend(best[1])
+        ORDER.extend(refine(best[1]))
     place = {i: k for k, i in enumerate(ORDER)}
     ops = [ops[i] for i in ORDER]
     for o in ops:

import numpy as np
from concourse.bass import DstId, RemoteDMATransfer
from concourse.mybir import AluOpType as ALU, AxisListType, ActivationFunctionType as AF

V, G, W = 1792, 1296, 3088
CEN = 1552.0
NW = 2048 + 3 * G
YL = 3104
Y0 = 800
DK = 2 ** 17
THR = 121.0 * DK
M1 = 1.5 * 2 ** 23
AO = 32.0
SC = 256
PW = (256,) * 6 + (128, 64, 64)
PV = (128, 114, 118, 114, 116, 118, 60, 30, 30)
NF = (2 * SC, 900, G, V)
LV = ((34, 32, 32, 32), (28, 28, 28, 32), (28, 28, 28, 32))
GV = ((64, 48, 20, 8), (64, 48, 20, 8), (64, 48, 20, 24))
RH = 57
FA = 31
MV = ((0, 0, 0, 0),) * 3
CS = 2
BYTE = 0.012
PACES = ((0.00083, 1.56, 3.8, 1.8, 0.18), (0.00085, 1.15, 2.2, 1.8, 0.2), (0.00105, 1.9, 5.2, 1.9, 0.2),
         (0.0009, 1.5, 4.2, 1.7, 0.14))
PASSES, MORE = 8, (0.1, -0.05, 0.2, 0.0, 0.05, -0.05, 0.15, 0.0)
SEED, AMP, SIZE, TRIES, ROUNDS = 1, 1.6, 300, 12, 900
ORDER = []

F32, BF, F16, I32, U16 = "float32", "bfloat16", "float16", "int32", "uint16"
SB = {
    "NI": (V, I32), "NU": (V, U16), "N": (NW, F32), "KV": (G, F32), "A": (YL, I32), "AF": (YL + 256, F32),
    "AG": (YL + 256, F32), "Y": (YL, BF), "X": (YL, BF), "R": (2048, BF), "RF": (2048, F32),
    "Z": (2048, BF), "DD": (V, BF),
    "GA0": (4096, BF), "GA1": (4096, BF), "RMP": (4096, BF), "PP": (17 * 128, BF),
    "T1": (3 * SC, BF), "T2": (3 * SC, BF), "XS": (192 * 3, BF), "XL": (192 * 3, BF), "YC": (768, BF),
    "IB": (128, BF), "NIB": (128, BF), "IBIG": (128, BF), "I64": (128, BF), "I16": (128, BF), "I2": (128, BF),
    "I4K": (128, BF), "IE": (128, BF), "N12": (128, BF), "I12": (128, BF), "N384": (128, BF),
    "BO": (128, BF), "NBO": (128, BF), "PBO": (128, BF), "B8": (80, BF), "B8K": (16, BF), "B8F": (16, F32),
    "TQ": (256, BF), "BQ": (256, BF), "IO8": (256, BF), "SEL": (144, BF), "SEQ": (248, BF), "DQ": (256, BF),
    "TRI": (128, BF), "TRM": (128, BF), "TRA": (128, BF), "ONES": (128, BF), "MT": (256, BF), "MF": (256, BF),
    "WM": (128, F32), "IOI": (128, F32), "IOS": (256, BF), "IO4": (64, BF), "RAMP": (128, BF),
    "IH": (256, BF), "HH": (256, BF),
    "KR": (256, BF), "C15": (384, BF), "C12": (128, BF), "RB": (512, F32),
    "sm": (16 * 16, F32), "si": (16 * 12, I32), "su": (16 * 12, U16), "sb": (16 * 8, BF),
    "AU": (256, U16), "AH": (256, F16), "NH": (256, F16), "EB": (256, BF), "MP": (256, BF), "M5": (256, BF),
    "X1": (256, F16), "X2": (256, BF), "DW": (128, BF), "F": (128, BF), "FP": (144, BF),
    "CUM": (128, F32), "CMP": (256, BF), "CRP": (256, BF), "GH": (256, BF),
    "LBU": (256, U16), "LBH": (256, F16), "XB": (256, BF), "LUU": (256, U16), "LUH": (256, F16),
    "SC1": (272, I32), "HK": (256, F32), "BC": (256, F32), "BC2": (256, F32), "NL": (256, F32),
    "RG": (256, BF), "YB": (256, BF), "YW": (256, BF), "YO": (256, BF), "TX": (256, BF), "ZN": (256, BF), "RN": (256, F32),
    "NM": (256, F32), "AN": (256, F32), "PB": (256, F16), "DE": (512, BF), "DS": (512, BF), "BW": (256, F16),
    "ST": (288, BF), "SU": (256, BF),
}
SCRATCH = {k: ("sbuf", [128, n], d) for k, (n, d) in SB.items()}
for _k, _a, _b, _d in (("LT", 16, 32, F32), ("AT", 32, 40, BF), ("S1", 8, 40, BF), ("OL", 32, 64, BF), ("CS", 64, 4, F16),
                       ("MX0", 16, 128, BF), ("MX1", 16, 128, BF),
                       ("JF", 4, 64, BF), ("JR", 4, 64, BF), ("MK", 4, 64, BF), ("EE", 256, 17, BF), ("C17", 40, 17, BF),
                       ("ZB", 2, 144, F16), ("CM", 16, 128, BF)):
    SCRATCH[_k] = ("sbuf", [128, _a, _b], _d)
for _k in range(8):
    SCRATCH["p%d" % _k] = ("psum", [128, 512], F32)
NDMA, NMSG = 16, 9
SEMAPHORES = ["cv", "ca", "cp", "cg"] + ["d%d" % k for k in range(NDMA)] + ["r%d" % k for k in range(NMSG)] + \
             ["l%d" % k for k in range(NMSG)]


def rank_program(g, core, T, topo):
    rank = T.rank_of(core)
    if rank is None:
        return
    n = len(T.cores)
    dst = T.cores[(rank - 1) % n]
    rid, pid = topo.addr(dst)[0], topo.addr(dst)[1]
    engs = topo.engines(core, dst)
    engs = [engs[1::2] if 5 <= k < 8 else engs[k // 8::2] for k in range(NMSG)]
    Q = {"v": g.vector, "a": g.scalar, "p": g.tensor, "g": g, "s": g.sync}
    ops, hist, cnt, lands, groups = [], {}, {"d": 0}, {}, {}

    def ap(name, a=0, b=None, s=1, p0=0, p1=128):
        b = T[name].shape[-1] if b is None else b
        return (T[name][p0:p1, a:b:s] if s > 1 else T[name][p0:p1, a:b], name, a, b, s)

    def ind(win, off):
        return (win[0].indirect(off[0]), win[1], win[2], win[3], 1, off)

    def cand(name, t):
        return ap(name, t, t + 7 * 255 + 1, 7)

    def whole(name, pattern):
        return (pattern, name, 0, 1, 1)

    def half(name, h):
        return ap(name, 128 * h, 128 * h + 128)

    def part(name, h, a, b):
        return (T[name][:, 8 * h:8 * h + 8, a:b], name, h, h + 1, 1)

    slots = {"sm": {}, "si": {}, "su": {}, "sb": {}}

    def sl(buf, key, a=0, b=16):
        k = slots[buf].setdefault(key, len(slots[buf]))
        return ap(buf, 16 * k + a, 16 * k + b)

    def sm(key, a=0, b=16):
        return sl("sm", key, a, b)

    def hs(buf, key, h):
        return sl(buf, key, 8 * h, 8 * h + 8)

    def cols(x):
        if len(x) > 5:
            return 16 * cols(x[5])
        return len(range(x[2], x[3], x[4])) * (1 if len(SCRATCH[x[1]][1]) == 2 else {"OL": 128, "S1": 40, "CS": 128}.get(x[1], 0))

    def lasts(q, reads, writes, two, cy, gat, sca, pe, hop):
        xs = [x for x in writes[:1] + reads if isinstance(x, tuple)]
        n = ([cols(x) for x in xs if cols(x)] + [256])[0]
        if q == "p":
            return max(64, n) * (4 if SCRATCH[xs[1][1]][2] == F32 else 1) * cy / pe
        if q == "g":
            return 0.15 + 2 * n * cy
        if len(xs[0]) > 5 or len(xs) > 1 and len(xs[1]) > 5:
            return 0.06 + n * (sca if len(xs[0]) > 5 else gat) * cy
        if q == "a":
            return max(64, n) * cy + 0.015
        if two and SCRATCH[xs[1][1]][0] == SCRATCH[xs[2][1]][0]:
            return max(64, 2 * n) * cy
        narrow = not two and all(SCRATCH[x[1]][2] in (BF, F16, U16) for x in xs)
        return max(64, n / 2 if narrow else n) * cy

    def add(q, fn, reads, writes, sem=None, two=False, t=None):
        i = len(ops)
        deps = set()
        acc = []
        for w, xs in ((False, reads), (True, writes)):
            for x in xs:
                if isinstance(x, tuple):
                    acc.append(x[1:5] + (w,))
                    if len(x) > 5:
                        acc.append(x[5][1:5] + (False,))
        for name, a, b, s, w in acc:
            ps = name[0] == "p" and name[1:].isdigit()
            for (a2, b2, s2, w2, j) in hist.get(name, []):
                o = ops[j]
                same = o["q"] == q and o["sem"] is None and sem is None
                if same and q == "p":
                    continue
                apart = same and s == s2 and (a - a2) % s
                if (ps and not same) or ((w or w2) and a < b2 and a2 < b and not apart):
                    deps.add(j)
        for name, a, b, s, w in acc:
            hist.setdefault(name, []).append((a, b, s, w, i))
        ops.append({"q": q, "fn": fn, "deps": deps, "sem": sem, "mark": False, "after": set(),
                    "kin": (q, ([x[1] for x in writes] + [""])[0]),
                    "t": [lasts(q, reads, writes, two, *x) if t is None else t for x in PACES]})

    def x0(x):
        return x[0] if isinstance(x, tuple) else x

    def tt(o, a, b, op):
        add("v", lambda: g.vector.tensor_tensor(o[0], a[0], b[0], op), [a, b], [o], two=True)

    def ts(o, a, s1, op0, s2=None, op1=None):
        if op1 is None:
            add("v", lambda: g.vector.tensor_scalar(o[0], a[0], x0(s1), None, op0), [a, s1], [o])
        else:
            add("v", lambda: g.vector.tensor_scalar(o[0], a[0], x0(s1), x0(s2), op0, op1), [a, s1, s2], [o])

    def cp(o, a):
        add("v", lambda: g.vector.tensor_copy(o[0], a[0]), [a], [o])

    def scan(o, d0, d1, op0, op1):
        add("v", lambda: g.vector.tensor_tensor_scan(o[0], d0[0], d1[0], 0.0, op0, op1), [d0, d1], [o])

    def ms(o, c):
        add("v", lambda: g.vector.memset(o[0], c), [], [o])

    def act(o, a, f=AF.Identity, bias=0.0, scale=1.0):
        add("a", lambda: g.scalar.activation(o[0], a[0], f, bias=x0(bias), scale=scale), [a, bias], [o])

    def put(o, a):
        add("a", lambda: g.scalar.activation(o[0], a[0], AF.Silu), [a], [o])

    def mm(o, l, r, start, stop, also=None):
        add("p", lambda: g.tensor.matmul(o[0], l[0], r[0], start, stop), [l, r, also], [o])
        group = groups.setdefault(o[1], [])
        ops[-1]["after"].update(group if start or stop else group[:1])
        if start or stop:
            group.clear()
        group.append(len(ops) - 1)

    def iota(o, pat, base, cm=0):
        if SCRATCH[o[1]][2] == I32:
            add("g", lambda: g.iota(o[0], pat, base, cm), [], [o])
        else:
            add("g", lambda: g.iota(o[0], pat, base, cm, allow_small_or_imprecise_dtypes=True), [], [o])

    def sel(o, a, pat, op, fill, base, cm):
        add("g", lambda: g.affine_select(o[0], a[0], pat, op, float(fill), base, cm), [a], [o])

    def dma(q, o, a, reads, writes, **how):
        s = "d%d" % cnt["d"]
        cnt["d"] += 1
        add(q, lambda: Q[q].dma_start(o, a, **how), reads, writes, sem=(s, 16, True),
            t=1.5 + sum(cols(x) * (2 if SCRATCH[x[1]][2] == BF else 4) for x in (writes or reads)) * BYTE / 16)

    def send(k, o, a, plus=None):
        mask = sum(1 << e for e in engs[k])
        t = 3.0 + 0.6 * (5 <= k < 8) + cols(a) * (2 if SCRATCH[a[1]][2] == BF else 4) * BYTE / len(engs[k])
        ops[lands[k]]["after"].add(len(ops))
        if plus is None:
            add("g", lambda: g.remote_dma(o[0], a[0], T.sem["r%d" % k], T.sem["l%d" % k], pid, rid, mask), [a], [],
                sem=("l%d" % k, len(engs[k]), False), t=t)
        else:
            fold = RemoteDMATransfer(dst_ids=[DstId(rid=rid, pnc=pid)], dma_engine_mask=mask, remote_sem=T.sem["r%d" % k],
                                     srcs=[a[0], plus[0]], dsts=[o[0]], alu_op=1)
            add("g", lambda: g.remote_dma_fused([fold], local_sem=T.sem["l%d" % k]), [a, plus], [],
                sem=("l%d" % k, len(engs[k]), False), t=1.1 * t)

    def landed(k, o):
        lands[k] = len(ops)
        add("x", None, [], [o], sem=("r%d" % k, len(engs[k]), False), t=0.5)

    def P(k, a=0, b=512, s=1, p0=0, p1=128):
        return ap("p%d" % k, a, b, s, p0, p1)

    eq, ge, gt, le, ltn, ne = ALU.is_equal, ALU.is_ge, ALU.is_gt, ALU.is_le, ALU.is_lt, ALU.not_equal
    ad, sub, mul, mx, mn = ALU.add, ALU.subtract, ALU.mult, ALU.max, ALU.min
    zero = ap("C15", 256, 384)

    def block(o, val, pat):
        c = 1
        for x in pat:
            c *= x[1]
        iota(o, [[0, c]], val)
        sel(o, o, [[-x[0], x[1]] for x in pat], ge, 0, 0, 1)
        sel(o, o, pat, ge, 0, 15, -1)

    def ones(k):
        return ap("ONES", 0, 128, 1, 0, k)

    def pick(q):
        return ap("SEL", 15 - q, 143 - q)

    def c17(k, rows=128):
        return whole("C17", T["C17"][0:rows, 8 * k:8 * k + 8, :])

    def spread(src):
        return ind(src, sl("su", "bc", 0, 8))

    def wrap(src, h, a, bank=7):
        tt(half("BC", h), spread(src), ap("WM"), mul)
        mm(P(bank, a, a + 8), half("BC", h), ap("B8F", 0, 8), True, True)
        return P(bank, a, a + 8)

    landed(0, ap("Y", V, V + Y0))
    landed(8, ap("Y", V + Y0, W))
    landed(1, ap("X", V, W))
    for t in range(3):
        landed(2 + t, ap("N", 2048 + G * t, 2048 + G * (t + 1)))
        landed(5 + t, ap("XL", 192 * t, 192 * t + 192))
    pieces = ((0, 2 * SC), (2 * SC, 4 * SC), (4 * SC, V))
    for a, b in ((0, Y0), (Y0, G)):
        dma("s", T["Y"][:, a:b], T.lab[:, a:b], [], [ap("Y", a, b)])
    dma("s", T["NI"][:, 0:2 * SC], T.nb[:, 0:2 * SC], [], [ap("NI", 0, 2 * SC)])
    dma("s", T["Y"][:, G:V], T.lab[:, G:V], [], [ap("Y", G, V)])
    b8, b8b = ap("B8", 0, 8), ap("B8", 16, 24)
    lead = len(ops)
    ms(zero, 0.0)
    iota(sl("si", "p", 0, 1), [[0, 1]], 0, 1)
    sel(ap("IB"), zero, [[-1, 128]], ne, 1.0, 0, 1)
    send(0, ap("Y", V, V + Y0), ap("Y", 0, Y0))
    send(8, ap("Y", V + Y0, W), ap("Y", Y0, G))
    first = len(ops) - 1
    sent = [first]
    block(b8, 1, [[16, 8]])
    iota(ap("IOI"), [[0, 8], [1, 16]], 0)
    iota(ap("IO8", 0, 128), [[0, 16], [1, 8]], 0)
    iota(ap("IO8", 128, 256), [[1, 8], [0, 16]], 0)
    for a, b in pieces[1:]:
        dma("s", T["NI"][:, a:b], T.nb[:, a:b], [], [ap("NI", a, b)])
        ops[-1]["deps"].add(first)
    dma("s", T["A"][:, 0:V], T.asc[:, :], [], [ap("A", 0, V)])
    first = len(ops) - 1
    ms(ap("X", 0, V), 16.0)
    ops[-1]["after"].add(lead)
    act(ap("AF", 0, V), ap("X", 0, V), AF.Silu, scale=AO / 16)
    ms(ap("X", W, W + 1), 0.0)
    ms(ap("X", W + 1, YL), 63.0)
    ms(ap("SEL"), 0.0)
    ms(ap("SEQ"), 0.0)
    e8 = sm("col", 4, 5)
    ms(e8, 0.0)
    ms(ap("FP", 0, 1), 0.0)
    ms(ap("DW"), 0.0)
    ms((T["CS"][:, :, :], "CS", 0, 2, 1), 0.0)
    ts(sl("si", "q", 0, 1), sl("si", "p", 0, 1), 15, ALU.bitwise_and)
    ts(ap("NIB"), ap("IB"), -1.0, mul)
    qf = sm("col", 0, 1)
    cp(qf, sl("si", "q", 0, 1))
    cp(ap("SEL", 15, 143, 16), b8)
    ts(sl("si", "q", 1, 2), sl("si", "p", 0, 1), 7, ALU.bitwise_and)
    cp(ap("SEQ", 120, 128), ap("IB", 0, 8))
    cp(sm("col", 7, 8), sl("si", "q", 1, 2))
    m0 = sm("col", 1, 2)
    ts(m0, qf, 0.0, eq)
    for o, val in ((b8b, 2 * DK), (ap("B8K", 0, 8), -DK), (ap("B8K", 8, 16), 512), (ap("B8F", 0, 8), 1), (ap("B8", 32, 40), -1),
                   (ap("B8", 48, 56), -12288)):
        ts(o, b8, float(val), mul)
    ts(sm("col", 2, 3), m0, 16.0, mul, qf, ad)
    ms(whole("ZB", T["ZB"][:, :, :]), 0.0)
    ts(sm("col", 2, 3), sm("col", 2, 3), -1.0, ad)
    qt = [qf, sm("col", 2, 3)]
    nq, qa, dum = [[sm(k, j, j + 1) for j in range(2)] for k in ("nq", "qa", "dum")]
    for j in range(2):
        ts(qa[j], qt[j], 1.0, ge, 4096.0, mul)
        ts(nq[j], qa[j], qt[j], ad, CEN - 2048, ad)
        ts(qa[j], qt[j], 1.0, ltn, 2048.0 + AO * j, mul)
        ts(qa[j], qa[j], AO * (1 - j), ad)
        ts(dum[j], qf, -8.0, mul, CEN - YL - 128 * j, ad)
    ts(sm("col", 6, 7), sl("si", "p", 0, 1), 16.0 * CS, ltn, 64.0, mul)
    for name, val in (("I64", 1.0 / 64), ("I16", 16.0), ("IBIG", 2.0 ** 26), ("I12", 12288.0), ("N384", -384.0),
                      ("I2", 2.0), ("I4K", 4096.0), ("N12", -12288.0), ("IE", -1.0 / 128)):
        act(ap(name), ap("IB"), scale=val)
    for j in range(2):
        act(half("IH", j), ap("IB"), scale=-1792.0 + 32 * j)
    tt(ap("MT", 1, 128), ap("IB", 1, 128), ap("IB", 0, 127), sub)
    cp(ap("MT", 0, 128, 16), ap("IB", 0, 128, 16))
    cp(ap("MT", 129, 256), ap("MT", 0, 127))
    cp(ap("MT", 128, 256, 16), ap("MT", 15, 128, 16))
    for j in range(2):
        ts(half("DQ", j), half("MT", j), -2048.0 - AO * j, mul)
    ts(ap("MT"), ap("MT"), 4096.0, mul)
    cp(ap("NU", *pieces[0]), ap("NI", *pieces[0]))
    ts(ap("N", *pieces[0]), ap("NI", *pieces[0]), AO, ad)
    cp(sl("su", "bc"), ap("IOI", 0, 16))
    ts(ap("WM"), ap("IOI"), qf, eq)
    ms(whole("MK", T["MK"][:, :, 0:16]), 1.0)
    ts(whole("MK", T["MK"][:, :, 16:48]), ap("IOI"), qf, ad, 15.0, le)
    ms(whole("MK", T["MK"][:, :, 48:64]), 0.0)
    ts(ap("MF"), whole("MK", T["MK"][:, :, :]), 8192.0, mul)
    for j in range(2):
        ts(ap("MF", 31 + 32 * j, 256, 64), ap("MF", 31 + 32 * j, 256, 64), dum[j], ad)
    ts(ap("BQ"), ap("IO8"), sm("col", 7, 8), eq)

    iota(ap("ONES"), [[0, 128]], 1)
    sel(ap("TRI"), ap("ONES"), [[1, 128]], ge, 0, 0, -1)
    sel(ap("TRM"), ap("TRI"), [[-1, 128]], ne, -255, 0, 1)
    iota(ap("IO4"), [[2, 64]], -510)
    iota(ap("C15", 0, 256, 1, 0, 2), [[0, 256]], -15, 4111)
    iota(ap("C12", 0, 128, 1, 0, 2), [[0, 128]], 12288, int(CEN + AO) - 12288)
    iota(ap("RAMP", 0, RH), [[32, RH]], 4128)
    iota(ap("RB", 392, 392 + RH), [[32, RH]], 4112)
    for j in range(3):
        act(ap("YC", 256 * j, 256 * j + 256), cand("Y", j), bias=63.0 / 128, scale=-65.0 / 128)
    iota(ap("PP"), [[0, 17 * 128]], 0)
    dma("g", T["X"][:, 0:V], T.xf[:, :], [], [ap("X", 0, V)], accum_op=ad)
    ops[-1]["deps"].add(first)
    iota(ap("F", 0, 112), [[0, 112]], 0)
    iota(ap("F", 112, 128), [[0, 16]], 1)
    tn = ap("RAMP", 64, 120)
    iota(tn, [[0, 56]], 0)
    for off, val in ((0, 0.5), (1, -0.5), (64, 0.5), (65, -0.5)):
        sel(tn, tn, [[-1, 56]], ne, val, -off, 1)
    block(ap("BO"), 1, [[16, 8], [0, 16]])
    sel(ap("TQ", 0, 128), ap("BQ", 0, 128), [[1, 128]], ge, 0, 0, -1)
    sel(ap("TQ", 128, 256), ap("BQ", 128, 256), [[0, 8], [8, 16]], ge, 0, 7, -1)
    iota(ap("IOS"), [[1, 256]], 0)
    iota(ap("KV"), [[0, G]], V)
    send(1, ap("X", V, W), ap("X", 0, G))
    iota(ap("N", V, 2048), [[0, 256]], W + 1 + int(AO))
    kinds = [[1, 2], [0, 128]]
    iota(ap("KR"), [[0, 16], [4096, 16]], 0)
    sel(ap("KR"), ap("KR"), [[0, 256]], ne, CEN, -1, 1)
    sel(ap("KR"), ap("KR"), kinds, ne, -120 * DK, -4, 2)
    sel(ap("KR"), ap("KR"), kinds, ne, 0, -5, 2)
    sel(ap("KR"), ap("KR"), kinds, ne, 0, -7, 2)
    iota(ap("RB", 0, 128), [[0, 128]], 0)
    iota(ap("RB", 128, 256), [[0, 128]], -2 ** 23)
    for o, val in ((0, 2.0 ** 30), (128, 65536.0 + W)):
        sel(ap("RB", o, o + 128, 16), ap("RB", o, o + 128, 16), [[0, 8]], ne, val, 0, 0)
    iota(ap("RB", 256, 392), [[0, 136]], 0)
    sel(ap("RB", 256, 392, 17), ap("RB", 256, 392, 17), [[0, 8]], ne, 2.0 ** 30, 0, 0)
    iota(ap("ST", 15, 288, 144), [[0, 2]], 0)
    iota(ap("Y", W, YL), [[0, YL - W]], 0)

    def later():
        sel(ap("TRA"), ap("TRI"), [[-1, 128]], ne, 256, 0, 1)
        iota(ap("R", V, 2048), [[0, 256]], 64)
        for a in range(0, 2048, 256):
            sel(ap("RF", a, a + 256), ap("R", a, a + 256), [[0, 256]], ge, 0, 0, 0)
        iota(whole("JF", T["JF"][:, :, :]), [[0, 256]], 0)
        for a, b in ((16, 48), (48, 64)):
            x = whole("JF", T["JF"][:, :, a:b])
            sel(x, x, [[-32, 4], [-16, (b - a) // 16], [1, 16]], ne, -1, -15, 1)
        iota(whole("JR", T["JR"][:, :, :]), [[0, 256]], 1)
        for a in (0, 16):
            x = whole("JR", T["JR"][:, :, 2 * a:2 * a + 32])
            sel(x, x, [[-32, 4], [0, 32]], ge, 0, -a, 1)
            sel(x, x, [[32, 4], [0, 32]], ge, 0, a + 15, -1)

    def zfrom(src, w, ycols, zout, bank):
        o = SC * (bank - 2)
        up = 64.0 * (src[1] == "R")
        ts(ap("T1", o, o + w), src, up + 1, eq, 64.0, mul)
        ts(ap("T2", o, o + w), src, up - 1, eq)
        mm(P(bank, 0, w), ap("IB"), ap("T1", o, o + w), True, False)
        mm(P(bank, 0, w), ap("IB"), ap("T2", o, o + w), False, True)
        return lambda: tt(zout, P(bank, 0, w), ycols, mul)

    yw = ap("Y", 0, W)

    def prep_n1(t):
        ts(ap("NH"), cand("N" if t else "NI", t), -CEN - AO * (t > 0), ad, m0, mul)
        for q in range(16):
            mm(P(4, 0, 16), pick(q), ap("NH", q, 256, 16), q == 0, q == 15)

    def prep_n2(t):
        ts(sl("su", "n"), P(4, 0, 16), CEN + 0.25, ad)
        tt(ap("EB"), ind(yw, sl("su", "n")), ap("YC", 256 * t, 256 * t + 256), mul)

    def prep_n3():
        ts(ap("MP"), ap("EB"), 1.0, eq, -1.0, mul)
        ts(ap("M5"), ap("EB"), 0.0, mx)

    late = []
    last = len(PW) - 1
    at = [sum(PW[:c]) for c in range(last + 2)]
    banks = [c & 1 for c in range(last)] + [7]

    def zpiece(c, src, bank):
        late.append(zfrom(src, PW[c], ap("Y", at[c], at[c + 1]), ap("Z", at[c], at[c + 1]), bank))

    def rcopy(c):
        act(ap("R", at[c], at[c + 1]), P(banks[c], 0, PW[c]), bias=64.0)

    def nfloat(k):
        ts(ap("N", NF[k], NF[k + 1]), ap("NI", NF[k], NF[k + 1]), AO, ad)

    for c in range(last + 1):
        a, w, sv, bank = at[c], PW[c], PV[c], banks[c]
        one = w < 128
        gb = ("GA0", "GA1", "RMP")[c % 3]
        cp(ap(gb, 0, 16 * sv), ind(yw, ap("NU", a, a + sv)))
        act(ap(gb, 16 * sv, 16 * w), ind(yw, ap("NU", a + sv, a + w)), AF.Copy)
        if 0 < c < last:
            rcopy(c - 1)
        mm(P(bank, 0, w), ap("NIB"), ap("Y", a, a + w), True, False)
        for i in range(0 if one else 16):
            mm(P(bank, 0, sv), ap("IB"), ap(gb, i, 16 * sv, 16), False, False)
        while late:
            late.pop()()
        if c > 1:
            zpiece(c - 2, ap("R", at[c - 2], at[c - 1]), 2 + (c & 1))
        o = 0 if one else sv
        for i in range(16):
            mm(P(bank, o, w), ap("IB"), ap(gb, 16 * o + i, 16 * w, 16), False, i == 15)
        for a, b in pieces[1:]:
            if c < last and a == at[c + 2]:
                cp(ap("NU", a, b), ap("NI", a, b))
        if c == last - 4:
            prep_n1(0)
        if c == last - 3:
            prep_n2(0)
    cp(ap("AU"), cand("A", 0))
    zpiece(last - 1, P(banks[last - 1], 0, PW[last - 1]), 3 - (last & 1))
    rcopy(last - 1)
    late.pop(0)()
    zpiece(last, P(7, 0, PW[last]), 4)
    late.pop(0)()
    late.pop(0)()
    prep_n3()

    xw = ap("X", 0, W + 2)
    zw = ap("Z", 0, V)
    bu = sl("su", "b")

    def lists(t):
        send(2 + t, ap("N", 2048 + G * t, 2048 + G * (t + 1)), ap("N", 0, G), ap("KV"))

    for t in range(3):
        def quarter(k):
            a, m, b = 64 * k, 64 * k + LV[t][k], 64 * k + 64
            cp(ap("RMP", 16 * a, 16 * m), ind(zw, ap("AU", a, m)))
            act(ap("RMP", 16 * m, 16 * b), ind(zw, ap("AU", m, b)), AF.Copy)
            zb = (0, 0, 1, 7)[k]
            mm(P(zb, a, b), ones(1), ap("C12", 0, 64, 1, 0, 1), k != 1, False)
            for i in range(16):
                mm(P(zb, a, b), ap("IB"), ap("RMP", 16 * a + i, 16 * b, 16), False, k > 0 and i == 15)

        ts(ap("AH"), ap("AU"), 16.0, ad)
        ts(ap("HH"), ap("AU"), 896.0, ge)
        for k in (6, 2):
            mm(P(k, 0, 256), ones(2), ap("C15", 0, 256, 1, 0, 2), True, False)
            for h in range(2):
                mm(P(k, 128 * h, 128 * h + 128), half("HH", h), half("IH", k == 2), False, False)
                mm(P(k, 128 * h, 128 * h + 128), half("AH", h), ap("I2"), False, k == 6 and h == 1)
        if t:
            prep_n2(t)
            prep_n3()
        else:
            rcopy(last)
        quarter(0)
        act((T["AT"][:, :, 0:8], "AT", 0, 8, 1), P(6, 0, 256), AF.Copy)
        quarter(1)
        mm(P(2, 0, 256), ap("NIB"), (T["AT"][:, :, 0:8], "AT", 0, 8, 1), False, True)
        for j in range(4):
            act((T["AT"][:, :, 8 + 8 * j:16 + 8 * j], "AT", 8 + 8 * j, 16 + 8 * j, 1), P(2, 0, 256), bias=-2.0 * j)
        for h in range(2):
            if h:
                quarter(2)
                quarter(3)
            for k, a, b in (((0, 0, 128),), ((1, 128, 192), (7, 192, 256)))[h]:
                tt(ap("BC2", a, b), P(k, a, b), ap("MP", a, b), mul)
                tt(ap("X2", a, b), P(k, a, b), ap("M5", a, b), mul)
            mm(P(3 + h, 0, 8), half("MP", h), ap("B8", 48, 56), True, False)
            mm(P(3 + h, 0, 8), half("M5", h), ap("B8", 48, 56), False, False)
            mm(P(3 + h, 0, 8), half("X2", h), b8, False, False)
            mm(P(3 + h, 0, 8), half("BC2", h), ap("B8F", 0, 8), False, True)
            will = hs("sb", "will", h)
            ts(will, P(3 + h, 0, 8), e8, le, 2.0, mul)
            if h:
                mm(P(4, 16, 24), ap("ONES"), hs("sb", "will", 0), True, False)
            mm(P(3 + h, 16, 24), ap("TRM"), will, h == 0, True)
            for gi in (2, 3, 0, 1, 4, 5, 6, 7):
                c = 8 * h + gi
                ts(ap("PP", 128 * c + 64, 128 * c + 128), ap("IO4"), P(3 + h, 16 + gi, 17 + gi), eq)
                for j in range(2):
                    o = 128 * c + 64 - 64 * j
                    mm(P((2, 6, 5, 5)[gi // 2], 40 * gi, 40 * gi + 40), ap("PP", o, o + 128),
                       (T["AT"][:, 2 * c + j, :], "AT", 0, 40, 1), gi in (0, 2, 4) and h + j == 0, gi in (1, 3, 7) and h + j == 2)
            act(hs("sb", "die", h), P(3 + h, 16, 24), AF.Sign, bias=-383.0, scale=-1.0)
        if t == 0:
            act(ap("NBO"), ap("BO"), scale=-float(DK))
            act(ap("PBO"), ap("BO"), scale=float(DK))
            nfloat(0)
            nfloat(1)
            lists(0)
        for k, a, b in ((6, 2, 4), (2, 0, 2), (5, 4, 8)):
            act((T["S1"][:, a:b, :], "S1", a, b, 1), P(k, 40 * a, 40 * b))
        dd = ap("DD", t, t + 7 * 255 + 1, 7, 0, 8)
        for h in range(2):
            mm(P(7, 128 * h, 128 * h + 128, 1, 0, 8), hs("sb", "die", h), ap("IB"), h == 0, h == 1)
        act(dd, P(7, 0, 256, 1, 0, 8), bias=(t + 1) / 2.0, scale=(t + 1) / 2.0)
        mm(P(1, 0, 256), ap("IE"), cand("X", t), True, False)
        mm(P(1, 0, 256), ap("BQ", 128, 256, 1, 0, 8), dd, False, True)

        for k in range(16):
            a = k // 8
            ts((T["OL"][:, k + 8 * a:16 * a + 16:8, :], "OL", k, k + 1, 1),
               (T["S1"][:, 4 * a:4 * a + 4, 8:40], "S1", 4 * a, 4 * a + 4, 1), 8.0 * (k & 7) - 15, eq)
        turn = [c for x in range(32) for c in (x + (x & 16) + 16, x + (x & 16))]
        for k, c in enumerate(turn):
            gi, o = c >> 3, 128 * (k >> 1) + 64 * (c >> 4 & 1)
            high = (T["S1"][:, gi, c & 7:(c & 7) + 1], "S1", gi, gi + 1, 1)
            if (k + 1) * FA // 64 > k * FA // 64:
                act(ap("RMP", o, o + RH), ap("RB", 392, 392 + RH), AF.Sign, bias=high, scale=-1.0)
            else:
                ts(ap("RMP", o, o + RH), ap("RAMP", 0, RH), high, le, 2.0, mul)
            if k & 1:
                a, b = k >> 5, 32 * (gi & 1) + (c & 7)
                mm(P(0, k >> 4, 256, 4, 0, 64 + RH), ap("RMP", o, o + 64 + RH),
                   (T["OL"][:, 16 * a:16 * a + 16, b:b + 25:8], "OL", 8 * a, 8 * a + 8, 1), k == 1, k == 63)
        mm(P(6, 0, 112), ap("I64"), ap("DW", 0, 112), True, False)
        mm(P(4, 0, 128), ap("IB"), ap("F"), True, False)
        if t < 2:
            mm(P(3, 0, 16), ap("ONES"), sl("sb", "die"), True, True)
        for v in range(t, 112, 7):
            mm(P(6, v >> 4, 112, 7), ap("SEQ", 120 - 8 * (v & 15), 248 - 8 * (v & 15), 1, 0, 8), ap("DD", v, V, 112, 0, 8),
               False, v > 104)
        act(ap("XS", 192 * t, 192 * t + 192), P(1, 0, 192), AF.Relu, scale=-128.0)
        send(5 + t, ap("XL", 192 * t, 192 * t + 192), ap("XS", 192 * t, 192 * t + 192))
        if t == 0:
            sent.append(len(ops) - 1)
            later()
        for j in range(2):
            cp((T["CS"][64 * j:64 * j + RH, :, 2 * j:2 * j + 2], "CS", j, j + 1, 1),
               P(0, 128 * j, 128 * j + 128, 1, 64 * j, 64 * j + RH))
        for j in range(2):
            mm(P(4, 56 * j, 56 * j + 56), (T["CS"][0:64 + RH, 32 * j:32 * j + 32, :], "CS", 0, 2, 1),
               ap("RAMP", 64, 120, 1, 0, 64 + RH), False, j == 1)
        act(ap("DW", 0, 112), P(6, 0, 112), scale=65536.0)
        act(cand("X", t), P(1, 0, 256), AF.Relu, scale=-128.0)
        if t < 2:
            add("v", lambda: g.vector.tensor_reduce(sm("col", 5, 6)[0], P(3, 0, 16)[0], AxisListType.X, ad),
                [P(3, 0, 16)], [sm("col", 5, 6)])
            ts(sl("si", "e", 0, 1), sm("col", 5, 6), 0.5, mul, 1024.0, ad)
            ts(sl("si", "e", 1, 2), sl("si", "e", 0, 1), 7, ALU.bitwise_and)
            cp(e8, sl("si", "e", 1, 2))
        tt(ap("F"), P(4, 0, 128), ap("DW"), gt)
        scan(ap("FP", 1, 129), ap("F"), zero, ad, ad)
        mm(P(2, 0, 128), half("TQ", 1), ap("F"), True, False)
        mm(P(0, 0, 8), ap("FP", 1, 129), ap("BQ", 0, 8), True, True)
        mm(P(2, 0, 128), half("BQ", 1), ap("FP", 0, 128), False, True)
        if t < 2:
            mm(P(6, 0, 112), half("TQ", 0), ap("F", 0, 112), True, False)
            mm(P(6, 0, 112), half("BQ", 0), ap("FP", 0, 112), False, False)
            mm(P(6, 0, 112), ap("I4K"), ap("F", 0, 112), False, True)
        mm(P(3, 32, 40), ap("FP", 1, 129), ap("BQ", 0, 8), True, True)
        ts(sl("sb", "cc", 0, 8), P(0, 0, 8), 256.0, mn)
        act(sm("ncc", 0, CS), P(3, 32, 32 + CS), scale=-1.0, bias=0.5)
        act(ap("CUM"), P(2, 0, 128), AF.Copy)

        def row(h, k):
            if t < 2:
                mm(P(k, 0, 128), half("MT", t), half("CMP", h), True, False)
                mm(P(k, 0, 128), ap("I16"), half("CRP", h), False, True)
                act(half("NM", h), P(k, 0, 128), bias=nq[t])

        def treated(h):
            for gi in range(8):
                o = (T["CM"][:, 8 * h:8 * h + 8, 16 * gi:16 * gi + 16], "CM", 8 * h + gi, 8 * h + gi + 1, 1)
                if gi < CS:
                    act(o, half("IOS", h), AF.Sign, bias=sm("ncc", gi, gi + 1))
                else:
                    ts(o, half("IOS", h), sl("sb", "cc", gi, gi + 1), ge, 2.0, mul)
            for k in range(8):
                mm(P((4, 1)[h], 2 * k, 2 * k + 2), (T["CM"][:, 8 * h + k, :], "CM", 8 * h, 8 * h + 8, 1), ap("ONES", 0, 2), k == 0, k == 7)
            cu, bk = hs("su", "c", h), (3, 7)[h]
            ts(cu, P((4, 1)[h], 0, 16, 2), 0.5, mul, sm("col", 6, 7), ad)
            tt(half("CMP", h), ind(ap("CUM"), cu), half("IOS", h), le)
            cp(hs("sb", "c", h), cu)
            act(half("CRP", h), ind(ap("IOS", 0, 128), cu), bias=-CEN / 16)
            for q in range(16):
                mm(P(bk, 0, 8), pick(q), ap("CMP", 128 * h + q, 128 * h + 128, 16), q == 0, False)
            mm(P(bk, 0, 8), ap("I16"), hs("sb", "c", h), False, True)
            if h:
                row(h, 5)
            cp(hs("su", "b", h), P(bk, 0, 8))
            ts(half("LBU", h), ind(ap("N", 0, 2048), hs("su", "b", h)), 0.25 - AO, ad)
            (cp, act)[h](half("XB", h), ind(xw, hs("su", "b", h)))
            ts(half("LBH", h), half("LBU", h), -CEN, ad)
            ts(half("GH", h), half("LBU", h), float(V), ge, 256.0 + G * t, mul)

        def mx_(h, a, b, c):
            return (T["MX%d" % h][:, a:b, 64 * c:64 * c + 64], "MX%d" % h, 16 * c + a, 16 * c + b, 1)

        def keys(h, d, names):
            gb, o, sv, w = "GA%d" % h, 2048 * d, GV[t][2 * d + 1 - h], (256, 136)[d]
            both = MV[t][2 * d + 1 - h]
            st, kw = 16 + d, 128 + 8 * d
            kr, nbo, pbo, ib = ((ap("KR", 0, 256, 1, 0, 4), ap("NBO"), ap("PBO"), ap("IB")), (c17(4, 4), c17(0), c17(1), c17(2)))[d]
            cp(ap(gb, o, o + 16 * sv), ind(xw, ap(names, 128 * h, 128 * h + sv)))
            for a, b in ((sv, 64), (64, 128)):
                if a < b:
                    act(ap(gb, o + 16 * a, o + 16 * b), ind(xw, ap(names, 128 * h + a, 128 * h + b)), AF.Copy)
            mm(P(h, 0, w), ones(4), kr, True, False)
            mm(P(h, 0, kw, 1, 0, 64), ap("XB", 128 * h, 128 * h + 64), nbo, False, False)
            mm(P(h, 0, kw, 1, 64, 128), ap("XB", 128 * h + 64, 128 * h + 128), nbo if both else pbo, False, False)
            if d:
                mm(P(h, 16, kw, st), ap("IB"), hs("sb", "off", h), False, False)
                mm(P(h, 16, kw, st), ap("IB"), whole("ZB", T["ZB"][:, h, 15:143:16]), False, False)
            else:
                mm(P(h, 0, 128), half("GH", h), ap("IB"), False, False)
                mm(P(h, 128, 256), half("LBH", h), ap("IB"), False, False)
            for b in range(0 if both else 2):
                for j in range(8):
                    mm(P(4 + 2 * b, 64 * j, 64 * j + 64), ap("NIB"), ap("XB", 128 * h + 64, 128 * h + 128), j == 0, False)
                for j in range(8):
                    mm(P(4 + 2 * b, 64 * j, 64 * j + 64), ap("IB"), ap(gb, o + 1024 + 8 * b + j, o + 2048, 16), False, j == 7)
                act(mx_(h, 8 * b, 8 * b + 8, 1), P(4 + 2 * b), AF.Relu)
            if d:
                offers(h)
            for i in range(16):
                mm(P(h, i, w, st), ap(gb, o + i, o + 2048, 16), ap("B8K", 0, w // 16), False, False)
            for i in range(16):
                for c in range(1 + both):
                    tt(mx_(h, i, i + 1, c), P(2, 128 * h + 64 * c, 128 * h + 64 * c + 64),
                       ap(gb, o + 1024 * c + i, o + 1024 * c + 1024, 16), mx)
                mm(P(h, i, kw, st), (T["MX%d" % h][:, i, :], "MX%d" % h, i, i + 1, 1), b8b, False, False, mx_(h, i, i + 1, 1))
            mm(P(h, 0, kw), half(("LBH", "LUH")[d], h), ib, False, True)
            scan(ap("SC1", 136 * h, 136 * h + kw), ap("RB", 256 * d, 256 * d + kw), P(h, 0, kw), ad, mn)
            return ap("SC1", 136 * h + st - 1, 136 * h + kw, st)

        def step(h, back=0):
            return ap("ST", 144 * h + 16 - back, 144 * h + 144 - back)

        def near(h):
            lu = (3, 5)[h]
            ue = keys(h, 0, "LBU")
            ts(hs("si", "un", h), ue, 8191, ALU.bitwise_and)
            scan(half("HK", h), ap("RB", 128, 256), P(h, 128, 256), mx, mn)
            ts(hs("sm", "xx", h), ue, THR, ltn, 65536.0, mul)
            mm(P(lu, 0, 128), half("LBH", h), ap("IB"), True, True)
            act(part("LT", h, 0, 16), P(lu, 0, 128), AF.Copy)
            sel(part("LT", h, 16, 32), part("LT", h, 0, 16), [[0, 128]], ge, 0, 0, 0)
            act(step(h), half("HK", h), AF.Sign, bias=65536.0 + W, scale=-1.0)
            sel(half("SU", h), step(h, 1), [[0, 8], [1, 16]], ge, 0, -1, 0)

        def fetch(h):
            ts(hs("su", "u", h), wrap(hs("si", "un", h), h, 16), 2047.0 + G * (t + 1), mn)
            ts(half("LUU", h), ind(ap("N", 0, 2048 + G * (t + 1)), hs("su", "u", h)), 0.25 - AO, ad, W + 1.25, mn)
            ts(half("LUH", h), half("LUU", h), -CEN, ad)

        def offers(h):
            lu = (3, 5)[h]
            mm(P(lu, 0, 128), half("LUH", h), ap("IB"), True, True)
            tt(half("TX", h), P(2, 256 + 128 * h, 384 + 128 * h), half("LUH", h), eq)
            mm(P(h, 0, 136), half("TX", h), c17(3), False, False)
            for r in range(16):
                tt(part("EE", 2 * r + h, 0, 16), P(lu, 0, 128), part("LT", h, r, r + 16), eq)
                mm(P(h, 0, 136), ap("IBIG"), part("EE", 2 * r + h, 0, 17), False, False)
            mm(P(lu, 256, 384), ap("IB"), half("LBH", h), True, False)
            mm(P(lu, 256, 384), step(h), ap("I12"), False, False)
            mm(P(lu, 256, 384), half("SU", h), ap("N12"), False, True)
            act(half("NL", h), P(lu, 256, 384), bias=CEN + AO)
            if not h:
                row(h, lu)

        def aside():
            asks, need = sl("sb", "asks"), sl("sb", "need")
            ts(sl("si", "k"), ap("HK", 15, 256, 16), 0.0, mx)
            ts(sm("y1"), sl("si", "un"), 2048.0, ge)
            tt(need, sl("si", "k"), sm("xx"), ltn)
            ts(sl("si", "old"), sl("si", "k"), 4095, ALU.bitwise_and)
            tt(asks, sm("y1"), need, mul)
            ts(whole("ZB", T["ZB"][:, :, 15:143:16]), sl("si", "old"), -CEN, ad)
            mm(P(7, 32, 48), ap("TRA"), asks, True, False)
            mm(P(7, 32, 48), ap("N384"), need, False, False)
            mm(P(7, 40, 48), ap("ONES"), hs("sb", "asks", 0), False, True)
            ts(sl("sb", "off"), P(7, 32, 48), -65.0, gt, -2 * THR, mul)

        def olds():
            for h in range(2):
                for q in range(16):
                    mm(P(7, 48 + 8 * h, 56 + 8 * h), whole("ZB", T["ZB"][:, h, 15 - q:143 - q]), ap("IB", q, 128, 16),
                       h + q == 0, h + q == 16)
            ts(sl("su", "old"), P(7, 48, 64), CEN, ad)
            act(ap("YO"), ind(ap("Y"), sl("su", "old")), AF.Copy)
            act(ap("RG"), ind(ap(("R", "RF")[t]), bu), AF.Copy)
            act(ap("YB"), ind(yw, bu), AF.Copy)

        def change(h, we):
            ba, br = ((P(6, 0, 128), P(4, 0, 128)), (P(5, 0, 128), P(5, 128, 256)))[h]
            wn, b = hs("si", "wn", h), hs("su", "b", h)

            def newlist():
                x = P(h, 384, 512)
                mm(x, ones(2), ap("C12", 0, 128, 1, 0, 2), True, False)
                mm(x, step(h), ap("N12"), False, False)
                mm(x, half("SU", h), ap("I12"), False, False)
                mm(x, half("PB", h), ap("IB"), False, True)
                tt(half("BC2", h), x, half("NL", h), mn)
                if t == 2:
                    ts(ind(ap("AF", 0, 2048), b), half("BC2", h), 1.0, mul, -AO, ad)
                else:
                    (cp, put)[h](ind(ap("N", 0, 2048), b), half("BC2", h))

            ts(wn, we, 4095, ALU.bitwise_and)
            if t == 2:
                ts(half("PB", h), spread(wn), -CEN, ad)
                return newlist()
            wc, wp = hs("sm", "wc", h), P((3, 7)[h], 128, 136)
            ts(wc, wn, -CEN, ad)
            tt(half("BW", h), spread(wc), ap("WM"), mul)
            mm(wp, half("BW", h), ap("B8", 32, 40), True, True)
            ts(half("PB", h), spread(wn), -CEN, ad)
            mm(P(h, 128, 384), half("BW", h), whole("JR", T["JR"][:, :, :]), True, False)
            mm(P(h, 128, 384), half("PB", h), whole("JF", T["JF"][:, :, :]), False, True)
            ts(hs("su", "w", h), wp, -1.0, mul, CEN, ad)
            (cp, act)[h](half("YW", h), ind(ap("Y"), hs("su", "w", h)))
            tt(half("X1", h), ind(ap(("A", "AF")[t], 0, YL), hs("su", "w", h)), half("NM", h), mn)
            mm(ba, half("DQ", t), half("CMP", h), True, False)
            mm(ba, ap("IB"), half("X1", h), False, True)
            act(half("AN", h), ba, bias=qa[t])
            o = 256 * h
            act(ap("DE", o, o + 256), P(h, 128, 384), AF.Abs, scale=4096.0)
            newlist()
            mm(br, ap("IB"), half("RG", h), True, False)
            mm(br, ap("NIB"), half("YO", h), False, False)
            mm(br, ap("IB"), half("YW", h), False, True)
            scan(ap("DS", o, o + 256), ap("DE", o, o + 256), ap("MF"), mn, ad)
            tt(hs("sm", "bad", h), wp, ap("DS", o + 31, o + 256, 32), mn)
            ts(hs("su", "tg", h), hs("sm", "bad", h), -1.0, mul, CEN, ad)
            for k in range(4 * h + 3, 4 * h - 1, -1):
                put(ind(ap(("AF", "AG")[t]), sl("su", "tg", 2 * k, 2 * k + 2)), ap("AN", 32 * k, 32 * k + 32))
            act(half("TX", h), br, AF.Square, bias=-291.5, scale=4.5)
            act(half("ZN", h), half("TX", h), AF.Relu, bias=65.0, scale=-1.0)
            if t == 0:
                act(half("RN", h), br, AF.Copy)
            tt(ind(ap("Z"), b), half("ZN", h), half("YB", h), mul)

        if t == 0:
            for j in (1, 2):
                ts(cand("AF", j), cand("A", j), AO, ad)
            nfloat(2)
            iota((T["EE"][:, :, 16], "EE", 0, 32, 1), [[0, 256]], 0)
            iota(whole("C17", T["C17"][:, :, 16]), [[0, 40]], 0)
            for k, name in enumerate(("NBO", "PBO", "IB", "IBIG", "KR")):
                sel(whole("C17", T["C17"][:, 8 * k:8 * k + 8, 0:16]), ap(name, 0, 128), [[0, 128]], ge, 0, 0, 0)
            for k, val in enumerate((THR, CEN)):
                x = whole("C17", T["C17"][:, 32:40, 16])
                sel(x, x, [[0, 8]], ne, val, -k, 1)
            iota(ap("A", V, YL), [[0, YL - V]], 0)
            iota(ap("AF", V, YL), [[0, YL - V]], int(AO))
        if t == 1:
            for h in range(2):
                put(ind(ap("RF"), hs("su", "b", h)), half("RN", h))
        if t == 2:
            for a in range(0, V, 256):
                ts(ap("AF", a, a + 256), ap("N", a, a + 256), M1 - AO, ad, -M1, ad)
        act(ap("X", V + t, W, 7), ap("XL", 192 * t, 192 * t + len(range(t, G, 7))), AF.Copy)
        for h in (1, 0):
            treated(h)
        if t < 2:
            act(ap("F", 0, 112), P(6, 0, 112), AF.Relu, bias=-4352.0)
        for h in (1, 0):
            mm(P(2, 256 + 128 * h, 384 + 128 * h), ap("I16"), half("CRP", h), h == 1, False)
            mm(P(2, 256 + 128 * h, 384 + 128 * h), ap("BO"), half("CMP", h), False, False)
            mm(P(2, 128 * h, 128 * h + 128), ap("IB"), half("XB", h), False, h == 0)
        for h in (1, 0):
            near(h)
            fetch(h)
        aside()
        if t < 2:
            olds()
        we = {h: keys(h, 1, "LUU") for h in (1, 0)}
        for h in (1, 0):
            change(h, we[h])
        if t == 0:
            for j in range(3, 7):
                iota(cand("DD", j), [[0, 256]], 0)
            sel(cand("AG", 2), cand("AF", 2), [[0, 256]], ge, 0, 0, 0)
        if t < 2:
            lists(t + 1)
            prep_n1(t + 1)
            for a, b in ((0, 64), (64, 256)):
                ts(ap("AU", a, b), ap(("AF", "AG")[t], t + 1 + 7 * a, t + 7 * b - 5, 7), M1 - AO, ad, -M1, ad)

    dma("s", T.yn[:, :], T["AF"][:, 0:V], [ap("AF", 0, V)], [])
    dma("g", T.yd[:, :], T["DD"][0:8, :], [ap("DD")], [])

    seq = [i for i, o in enumerate(ops) if o["q"] != "x"]
    for i in lands.values():
        seq.insert(seq.index(min(ops[i]["after"])) + 1, i)
    above = {}
    for i in seq:
        far = 0
        for j in ops[i]["deps"] | ops[i]["after"]:
            far |= above[j]
        ops[i]["near"] = {j for j in ops[i]["deps"] if not far >> j & 1}
        above[i] = far | sum(1 << j for j in ops[i]["near"])
    graphs = []
    for m in range(len(PACES)):
        hold = [o["t"][m] if o["sem"] is None else {"x": 0.0, "g": 0.3}.get(o["q"], 0.05) for o in ops]
        before, behind, dmas = [[] for o in ops], [[] for o in ops], {}
        for i, o in enumerate(ops):
            lag = {j: ops[j]["t"][m] for j in o["after"]}
            if o["sem"] is not None and o["q"] != "x":
                if o["q"] in dmas:
                    lag[dmas[o["q"]]] = hold[dmas[o["q"]]]
                dmas[o["q"]] = i
            for j in sent if o["q"] == "g" else ():
                if i > j:
                    lag[j] = 2.0 if j == sent[0] else hold[j]
            lag.update({j: ops[j]["t"][m] + PACES[m][4] for j in o["near"]})
            for j, d in lag.items():
                before[i].append((j, d, j in o["near"]))
                behind[j].append((i, d + hold[i] - hold[j], j in o["near"]))
        graphs.append((hold, before, behind))

    def lay(seq, hold, waits, gaps, more=0.0):
        at, busy = {}, {q: [] for q in "vapgsx"}
        for i in seq:
            s = max([at[j] + d + more * w for j, d, w in waits[i]] + [0.0])
            line = busy[ops[i]["q"]]
            k = len(line)
            while gaps and k and line[k - 1][0] > s:
                k -= 1
            if k:
                s = max(s, line[k - 1][1])
            while k < len(line) and s + hold[i] > line[k][0] + 1e-9:
                s = line[k][1]
                k += 1
            line.insert(k, (s, s + hold[i]))
            at[i] = s
        return at

    def tighten(at, m, more):
        hold, before, behind = graphs[m]
        back = lay(sorted(seq, key=lambda i: (-at[i] - hold[i], -i)), hold, behind, True, more)
        return lay(sorted(seq, key=lambda i: (-back[i] - hold[i], i)), hold, before, True, more)

    best = now = (1e99, seq)
    for k in range(0 if ORDER else PASSES):
        m = 3 * (k & 1)
        at = lay(now[1], graphs[m][0], graphs[m][1], k == 0)
        at = tighten(tighten(at, m, MORE[k % len(MORE)]), m, 0.0)
        new = sorted(seq, key=lambda i: (at[i], i))
        score = 1.0
        for hold, before, behind in graphs:
            score *= max(lay(new, hold, before, False).values())
        if score < now[0] * 1.02:
            now = (score, new)
        best = min(best, now, key=lambda x: x[0])

    def refine(order):
        qs, nm, rnd = [o["q"] for o in ops], len(PACES), np.random.default_rng(SEED)

        def rate(order):
            hd, tl = [], []
            for hold, before, behind in graphs:
                at, free = [0.0] * len(ops), dict.fromkeys("vapgsx", 0.0)
                for i in order:
                    s = free[qs[i]]
                    for j, d, w in before[i]:
                        if at[j] + d > s:
                            s = at[j] + d
                    at[i] = s
                    free[qs[i]] = s + hold[i]
                to, nxt = list(hold), dict.fromkeys("vapgsx", 0.0)
                for i in reversed(order):
                    if hold[i] + nxt[qs[i]] > to[i]:
                        to[i] = hold[i] + nxt[qs[i]]
                    nxt[qs[i]] = x = to[i]
                    for j, d, w in before[i]:
                        if x + d > to[j]:
                            to[j] = x + d
                hd.append(at)
                tl.append(to)
            return hd, tl, [max(x) for x in tl]

        def fit(piece, hold, waits, ready, free, gaps):
            at, busy = {}, {q: [(-1.0, free[q])] for q in free}
            for i in piece:
                s = ready[i]
                for j, d in waits[i]:
                    if at[j] + d > s:
                        s = at[j] + d
                line, h = busy[qs[i]], hold[i]
                k = len(line)
                while gaps and k > 1 and line[k - 1][0] > s:
                    k -= 1
                if line[k - 1][1] > s:
                    s = line[k - 1][1]
                while k < len(line) and s + h > line[k][0] + 1e-9:
                    s = line[k][1]
                    k += 1
                line.insert(k, (s, s + h))
                at[i] = s
            return at

        hd, tl, span = rate(order)
        for k in range(ROUNDS):
            size = int(rnd.integers(SIZE // 3, SIZE))
            a = max(0, int(rnd.integers(-size // 2, len(order) - size // 2)))
            old = order[a:a + size]
            inside = set(old)
            edge = []
            for m, (hold, before, behind) in enumerate(graphs):
                h, t = hd[m], tl[m]
                free, nxt = dict.fromkeys("vapgsx", 0.0), dict.fromkeys("vapgsx", 0.0)
                for i in order[:a]:
                    free[qs[i]] = h[i] + hold[i]
                for i in reversed(order[a + size:]):
                    nxt[qs[i]] = t[i]
                ready = {i: max([h[j] + d for j, d, w in before[i] if j not in inside] + [0.0]) for i in old}
                rest = {i: max([t[j] + d - hold[j] for j, d, w in behind[i] if j not in inside] + [0.0]) for i in old}
                waits = {i: [(j, d) for j, d, w in before[i] if j in inside] for i in old}
                edge.append((hold, waits, ready, rest, free, nxt))

            def ends(piece):
                x = 1.0
                for m, (hold, waits, ready, rest, free, nxt) in enumerate(edge):
                    at = fit(piece, hold, waits, ready, free, False)
                    last = {qs[i]: at[i] + hold[i] for i in piece}
                    far = max(max(at[i] + hold[i] + rest[i] for i in piece), max(last[q] + nxt[q] for q in last))
                    x *= max(far / span[m], 0.998)
                return x

            best = (ends(old) - 1e-7, None)
            for tries in range(TRIES):
                hold, waits, ready, rest, free, nxt = edge[int(rnd.integers(nm))]
                r = dict(zip(old, (1 + AMP * rnd.random() * (rnd.random(len(old)) - 0.5)).tolist()))
                if tries & 1:
                    kin = {ops[i]["kin"]: r[i] ** 2 for i in old}
                    r = {i: kin[ops[i]["kin"]] for i in old}
                new = best[1] or old
                for shaken in (True, False):
                    h2 = {i: hold[i] * r[i] for i in old} if shaken else hold
                    w2 = {i: [(j, d * r[j]) for j, d in waits[i]] for i in old} if shaken else waits
                    back = {i: [] for i in old}
                    for i in old:
                        for j, d in w2[i]:
                            back[j].append((i, d + h2[i] - h2[j]))
                    at = fit(new, h2, w2, ready, free, False)
                    at = fit(sorted(old, key=lambda i: (-at[i] - h2[i], -i)), h2, back, rest, nxt, True)
                    at = fit(sorted(old, key=lambda i: (-at[i] - h2[i], i)), h2, w2, ready, free, True)
                    new = sorted(old, key=lambda i: (at[i], i))
                x = ends(new)
                if x < best[0]:
                    best = (x, new)
            if best[1]:
                order = order[:a] + best[1] + order[a + size:]
                hd, tl, span = rate(order)
                order.sort(key=lambda i: hd[k % nm][i])
        return order

    if not ORDER:
        ORDER.extend(refine(best[1]))
    place = {i: k for k, i in enumerate(ORDER)}
    ops = [ops[i] for i in ORDER]
    for o in ops:
        o["deps"] = {place[j] for j in o["deps"]}

    knows = {q: {} for q in Q}
    for i, o in enumerate(ops):
        best = {}
        for j in o["deps"]:
            k = ops[j]["q"] if ops[j]["sem"] is None else j
            best[k] = max(best.get(k, -1), j)
        o["deps"] = []
        for k, j in sorted(best.items(), key=lambda x: -x[1]) if o["q"] != "x" else ():
            if knows[o["q"]].get(k, -1) < j:
                o["deps"].append(j)
                knows[o["q"]][k] = j
                for k2, j2 in ops[j]["knew"].items():
                    knows[o["q"]][k2] = max(knows[o["q"]].get(k2, -1), j2)
        o["knew"] = dict(knows.get(o["q"], {}))
    done = {q: {} for q in Q}
    for o in ops:
        if o["q"] != "x":
            for j in o["deps"]:
                if ops[j]["sem"] is None and done[o["q"]].get(ops[j]["q"], -1) < j:
                    done[o["q"]][ops[j]["q"]] = j
                    ops[j]["mark"] = True
    num, run = {}, {"v": 0, "a": 0, "p": 0, "g": 0}
    for i, o in enumerate(ops):
        if o["sem"] is None:
            run[o["q"]] += o["mark"]
            num[i] = run[o["q"]]
    seen = {q: {} for q in Q}
    waited = set()
    for i, o in enumerate(ops):
        q = o["q"]
        if q == "x":
            continue
        for j in sorted(o["deps"]):
            d = ops[j]
            s, c = ("c" + d["q"], num[j]) if d["sem"] is None else d["sem"][:2]
            if seen[q].get(s, 0) < c:
                Q[q].wait_ge(T.sem[s], c)
                seen[q][s] = c
                waited.add(s)
        h = o["fn"]()
        if o["sem"] is not None:
            if o["sem"][2]:
                h.then_inc(T.sem[o["sem"][0]], 16)
        elif o["mark"]:
            h.then_inc(T.sem["c" + q], 1)
    for o in ops:
        if o["sem"] is not None and o["sem"][0] not in waited:
            Q["g" if o["q"] == "x" else o["q"]].wait_ge(T.sem[o["sem"][0]], o["sem"][1])
